import numpy as np
import ml_dtypes


def mxq(x, axis, fmt="e4m3"):
    dtype, down = {"e4m3": (ml_dtypes.float8_e4m3fn, 7), "e5m2": (ml_dtypes.float8_e5m2, 14)}[fmt]
    v = np.moveaxis(np.asarray(x, np.float32).astype(ml_dtypes.bfloat16).astype(np.float64), axis, -1)
    blocks = v.reshape(v.shape[:-1] + (-1, 32))
    amax = np.abs(blocks).max(-1, keepdims=True)
    byte = np.maximum(np.where(amax > 0, np.frexp(amax)[1] - 1 + 127, 0) - down, 1)
    scale = np.exp2(byte - 127.0)
    codes = (blocks / scale).astype(np.float32).astype(dtype).astype(np.float64)
    return np.moveaxis((codes * scale).reshape(v.shape), -1, axis)


WIDE = False


def mx_kscale(k):
    if not WIDE:
        return np.ones(k)
    levels = np.array([10, -10, 5, -5, 0])
    if k % 512:
        return np.exp2(np.random.permutation(np.resize(levels, k // 32))).repeat(32)
    a = np.empty((k // 512, 16))
    for p in range(k // 512):
        a[p, :8] = np.random.permutation(np.resize(levels, 8))
        for g in range(8):
            far = levels[np.abs(levels - a[p, g]) >= 10]
            a[p, g + 8] = far[np.random.randint(len(far))]
    return np.exp2(a.ravel()).repeat(32)


def f64(x):
    return np.asarray(x).astype(np.float64)


def striped(idx):
    return np.tile(idx.reshape(-1, 16).T, (8, 1)).astype(np.uint16)


def unstriped(offs):
    return offs[:16].T.reshape(-1).astype(np.int64)


E2M1 = np.array([0.0, 0.5, 1.0, 1.5, 2.0, 3.0, 4.0, 6.0, -0.0, -0.5, -1.0, -1.5, -2.0, -3.0, -4.0, -6.0])


def pack_weight(w, fmt):
    k, n = w.shape
    w = f64(np.asarray(w, np.float32).astype(ml_dtypes.bfloat16)).reshape(k // 32, 32, n)
    amax = np.abs(w).max(1)
    if fmt == "e4m3":
        byte = np.frexp(amax)[1] - 1 + 127 - 7
    else:
        mant, ex = np.frexp(amax / 6.0)
        byte = np.where(mant > 0.5, ex, ex - 1) + 127
    byte = np.clip(np.where(amax > 0, byte, 1), 1, 254)
    scaled = (w * np.exp2(127.0 - byte)[:, None, :]).reshape(k, n).astype(np.float32)
    by_word = np.ascontiguousarray(scaled.reshape(k // 512, 128, 4, n).transpose(0, 1, 3, 2))
    if fmt == "e4m3":
        words = by_word.astype(ml_dtypes.float8_e4m3fn).view(np.uint8)
    else:
        c = by_word.astype(ml_dtypes.float4_e2m1fn).view(np.uint8) & 0xF
        words = (c[..., 0::2] | (c[..., 1::2] << 4)).reshape(k // 512, 128, 2 * n)
    return np.ascontiguousarray(words), np.ascontiguousarray(byte.astype(np.uint8).reshape(k // 512, 16, n))


def unpack_weight(words, scales, fmt):
    g, _, n = scales.shape
    words = np.ascontiguousarray(words).reshape(g, 128, n, -1)
    if fmt == "e4m3":
        vals = words.view(ml_dtypes.float8_e4m3fn).astype(np.float64)
    else:
        nib = np.empty((g, 128, n, 4), np.uint8)
        nib[..., 0::2] = words & 0xF
        nib[..., 1::2] = words >> 4
        vals = E2M1[nib]
    vals = vals * np.repeat(np.exp2(scales.astype(np.float64) - 127.0), 8, axis=1)[..., None]
    return vals.transpose(0, 1, 3, 2).reshape(g * 512, n)


def relu(v):
    return np.maximum(v, 0.0)


K, T, E, C, F, D, H = 512, 1024, 12, 256, 2, 256, 512
N, TOP = 512, 3


def by_expert(wq, xq, E, C):
    return np.concatenate([wq[e].T @ xq[:, e * C:(e + 1) * C] for e in range(E)], axis=1)


def setup_inputs():
    n = np.random.standard_normal
    s = mx_kscale(K)
    u = mx_kscale(H)
    deal = np.repeat(np.arange(E), C).reshape(TOP, T)[:, np.random.permutation(T)]
    deal = np.take_along_axis(deal, np.argsort(np.random.rand(TOP, T), axis=0), axis=0)
    for _ in range(8):
        s_, t_ = np.random.permutation(T).reshape(2, -1); r = np.random.randint(TOP, size=T // 2); x, y = deal[r, s_].copy(), deal[r, t_].copy()
        ok = ~((deal[:, s_] == y).any(0) | (deal[:, t_] == x).any(0)); deal[r[ok], s_[ok]] = y[ok]; deal[r[ok], t_[ok]] = x[ok]
    order = np.lexsort((np.random.rand(TOP * T), deal.reshape(-1)))
    slot_token = order % T; pos = np.empty(TOP * T, np.int64); pos[order] = np.arange(TOP * T); pos = pos.reshape(TOP, T)
    g = np.random.uniform(0.5, 1.5, (TOP, T)); g = g / g.sum(0)
    slots2 = np.random.permutation(T)[:F * D]
    x = pack_weight(n((K, T)) * s[:, None], "e4m3")
    w = [pack_weight(m, "e2m1") for m in n((E, K, N)) / np.sqrt(K) / s[None, :, None]]
    wa = [pack_weight(m, "e2m1") for m in n((F, K, H)) / np.sqrt(K) / s[None, :, None] * u]
    wb = [pack_weight(m, "e2m1") for m in n((F, H, N)) / np.sqrt(H) / u[None, :, None]]
    return {
        "x_words": x[0],
        "x_scales": x[1],
        "w_words": np.stack([m[0] for m in w]),
        "w_scales": np.stack([m[1] for m in w]),
        "wa_words": np.stack([m[0] for m in wa]),
        "wa_scales": np.stack([m[1] for m in wa]),
        "wb_words": np.stack([m[0] for m in wb]),
        "wb_scales": np.stack([m[1] for m in wb]),
        "gate": np.stack([np.tile(r, (128, 1)) for r in g]).astype(np.float32),
        "gate2": (np.tile(np.random.uniform(0.2, 1.0, F * D), (128, 1))).astype(np.float32),
        "offs": striped(slot_token),
        "pos1": striped(pos[0]),
        "pos2": striped(pos[1]),
        "pos3": striped(pos[2]),
        "offs2": striped(slots2),
    }


def reference(x_words, x_scales, w_words, w_scales, wa_words, wa_scales, wb_words, wb_scales, gate, gate2, offs, pos1, pos2, pos3, offs2):
    w = np.stack([unpack_weight(w_words[e], w_scales[e], "e2m1") for e in range(E)])
    wa = np.stack([unpack_weight(wa_words[e], wa_scales[e], "e2m1") for e in range(F)])
    wb = np.stack([unpack_weight(wb_words[e], wb_scales[e], "e2m1") for e in range(F)])
    idx, idx2 = unstriped(offs), unstriped(offs2)
    x = unpack_weight(x_words, x_scales, "e4m3")
    y = by_expert(w, x[:, idx], E, C)
    h = relu(by_expert(wa, x[:, idx2], F, D))
    z = by_expert(wb, mxq(h, 0, "e4m3"), F, D)
    out = sum(f64(gate[r, :1]) * y[:, unstriped(p)] for r, p in enumerate((pos1, pos2, pos3)))
    out[:, idx2] += f64(gate2[:1]) * z
    return out

@@ -1,0 +1,178 @@
+from contextlib import ExitStack
+
+import concourse.mybir as mybir
+from concourse.masks import make_identity
+
+K, T, E, C, F, D, H, N, TOP = 512, 1024, 12, 256, 2, 256, 512, 512, 3
+FLOPS = 2 * K * N * E * C + 2 * K * H * F * D + 2 * H * N * F * D
+
+F32 = mybir.dt.float32
+BF16 = mybir.dt.bfloat16
+I32 = mybir.dt.int32
+U32 = mybir.dt.uint32
+U16 = mybir.dt.uint16
+U8 = mybir.dt.uint8
+FP8X4 = mybir.dt.float8_e4m3fn_x4
+FP4X4 = mybir.dt.float4_e2m1fn_x4
+MULT = mybir.AluOpType.mult
+RELU = mybir.ActivationFunctionType.Relu
+
+P = 128
+BANK = 512
+SLOTS = E * C
+ASLOTS = F * D
+BLOCKS = N // P
+PIECE = 3 * C
+PIECES = SLOTS // PIECE
+LAST_CUTS = (512, 256, 256)
+
+
+def load_scale_rows(nc, plane, rows):
+    by_row = rows.rearrange("g (q r) n -> r q g n", r=4)
+    for r in range(4):
+        nc.sync.dma_start(plane[r:P:32, :, :].bitcast(I32), by_row[r].bitcast(I32))
+
+
+def tile_moe_mlr_relu_kernel(
+    tc, x_words, x_scales, w_words, w_scales, wa_words, wa_scales, wb_words, wb_scales,
+    gate, gate2, offs, pos1, pos2, pos3, offs2, out,
+):
+    nc = tc.nc
+    with ExitStack() as ctx:
+        keep = ctx.enter_context(tc.tile_pool(name="keep", bufs=1))
+        ring = ctx.enter_context(tc.tile_pool(name="ring", bufs=6))
+        stage = ctx.enter_context(tc.tile_pool(name="stage", bufs=3))
+        psum_mm = ctx.enter_context(tc.psum_pool(name="psum_mm", bufs=4))
+        psum_sum = ctx.enter_context(tc.psum_pool(name="psum_sum", bufs=2))
+
+        offs_sb = keep.tile([P, SLOTS // 16], U16, name="offs_sb")
+        offs2_sb = keep.tile([P, ASLOTS // 16], U16, name="offs2_sb")
+        pos_sb = [keep.tile([P, T // 16], U16, name=f"pos_sb{r}") for r in range(TOP)]
+        xw = keep.tile([P, T], I32, name="xw", align_bytes=64)
+        xs = keep.tile([P, T], U8, name="xs", align_bytes=64)
+        wa_w = keep.tile([P, F, 2 * H], U8, name="wa_w", align_bytes=64)
+        wa_s = keep.tile([P, F, H], U8, name="wa_s", align_bytes=64)
+        wb_w = keep.tile([P, F, 2 * N], U8, name="wb_w", align_bytes=64)
+        wb_s = keep.tile([P, F, N], U8, name="wb_s", align_bytes=64)
+        w_w = [keep.tile([P, 3, 2 * N], U8, name=f"w_w{c}", align_bytes=64) for c in range(PIECES)]
+        w_s = keep.tile([P, E, N], U8, name="w_s", align_bytes=64)
+        gate_sb = [keep.tile([P, T], F32, name=f"gate_sb{r}") for r in range(TOP)]
+        gate2_sb = keep.tile([P, ASLOTS], F32, name="gate2_sb")
+        ident = keep.tile([P, P], F32, name="ident")
+        scat = [keep.tile([P, T], F32, name=f"scat{b}") for b in range(BLOCKS)]
+        y = [keep.tile([P, SLOTS], F32, name=f"y{b}") for b in range(BLOCKS)]
+
+        nc.vector.memset(xs[:].bitcast(I32), 0)
+        nc.vector.memset(wa_s[:].bitcast(I32), 0)
+        nc.vector.memset(wb_s[:].bitcast(I32), 0)
+        nc.vector.memset(w_s[:].bitcast(I32), 0)
+        nc.vector.memset(scat[0][:], 0.0)
+        for b in range(1, BLOCKS):
+            nc.scalar.activation(scat[b][:], scat[0][:], RELU)
+        make_identity(nc, ident[:])
+
+        nc.sync.dma_start(offs2_sb[:], offs2)
+        x_rows = x_scales[0].rearrange("(q r) t -> r q t", r=4)
+        for r in range(4):
+            nc.sync.dma_start(xs[r:P:32, :].bitcast(I32), x_rows[r].bitcast(I32))
+        nc.sync.dma_start(xw[:], x_words[0].rearrange("p t d -> p (t d)").bitcast(I32))
+        nc.sync.dma_start(offs_sb[:], offs)
+        nc.sync.dma_start(wa_w[:].bitcast(I32), wa_words[:, 0].rearrange("f p n -> p f n").bitcast(I32))
+        load_scale_rows(nc, wa_s, wa_scales[:, 0])
+        load_scale_rows(nc, wb_s, wb_scales[:, 0])
+        nc.sync.dma_start(wb_w[:].bitcast(I32), wb_words[:, 0].rearrange("f p n -> p f n").bitcast(I32))
+        load_scale_rows(nc, w_s, w_scales[:, 0])
+        for c in range(PIECES):
+            nc.sync.dma_start(w_w[c][:].bitcast(I32), w_words[3 * c:3 * c + 3, 0].rearrange("e p n -> p e n").bitcast(I32))
+        nc.sync.dma_start(gate2_sb[:], gate2)
+        for r, pos in enumerate((pos1, pos2, pos3)):
+            nc.sync.dma_start(pos_sb[r][:], pos)
+            nc.sync.dma_start(gate_sb[r][:], gate[r])
+
+        def gather_tokens(lst, count, name, tag):
+            scales = keep.tile([P, count], U8, name=name + "_s", align_bytes=64)
+            nc.vector.tensor_copy(scales[:], xs[:].indirect(lst))
+            words = keep.tile([P, count], U32, name=name + "_w", tag=tag, align_bytes=64)
+            nc.vector.tensor_copy(words[:], xw[:].bitcast(U32).indirect(lst))
+            return words, scales
+
+        xa_w, xa_s = gather_tokens(offs2_sb[:], ASLOTS, "xa", "xa_w")
+        h_in = keep.tile([P, ASLOTS, 4], BF16, name="h_in", tag="held", align_bytes=64)
+        for f in range(F):
+            turned = psum_sum.tile([P, 2, 2, P], F32, name="turned", tag="back")
+            for half in range(2):
+                cols = slice(f * D + half * P, f * D + (half + 1) * P)
+                bank = psum_mm.tile([P, BANK], F32, name="bank")
+                nc.tensor.matmul_mx(bank[:], lhsT=xa_w[:, cols].bitcast(FP8X4), lhsT_scale=xa_s[:, cols],
+                                    rhs=wa_w[:, f, :].bitcast(FP4X4), rhs_scale=wa_s[:, f, :], start=True, stop=True)
+                h_rows = stage.tile([P, H], BF16, name="h_rows")
+                nc.scalar.activation(h_rows[:], bank[:], RELU)
+                pairs = h_rows[:].bitcast(F32)
+                for u in range(2):
+                    nc.tensor.transpose(turned[:, half, u, :], pairs[:, u:H // 2:2], ident[:])
+            dst = h_in[:, f * D:(f + 1) * D, :].rearrange("p m j -> p (m j)").bitcast(F32)
+            nc.scalar.copy(dst.rearrange("p (a m u) -> p a m u", a=2, u=2), turned[:].rearrange("p a u m -> p a m u"))
+        h_w = keep.tile([P, ASLOTS], U32, name="h_w", align_bytes=64)
+        h_s = keep.tile([P, ASLOTS], U8, name="h_s", align_bytes=64)
+        nc.vector.quantize_mx(out=h_w[:].bitcast(FP8X4), scales=h_s[:], in_=h_in[:].rearrange("p m j -> p (m j)"))
+
+        for b in range(BLOCKS):
+            bank = psum_mm.tile([P, BANK], F32, name="bank")
+            for f in range(F):
+                cols = slice(f * D, (f + 1) * D)
+                nc.tensor.matmul_mx(bank[:, cols], lhsT=wb_w[:, f, 2 * P * b:2 * P * (b + 1)].bitcast(FP4X4),
+                                    lhsT_scale=wb_s[:, f, P * b:P * (b + 1)],
+                                    rhs=h_w[:, cols].bitcast(FP8X4), rhs_scale=h_s[:, cols], start=True, stop=True)
+            z = keep.tile([P, ASLOTS], F32, name=f"z{b}")
+            nc.scalar.copy(z[:], bank[:])
+            nc.vector.tensor_tensor(scat[b][:].indirect(offs2_sb[:]), z[:], gate2_sb[:], MULT)
+
+        xg = []
+        for c in range(PIECES):
+            lst = offs_sb[:, c * PIECE // 16:(c + 1) * PIECE // 16]
+            xg.append(gather_tokens(lst, PIECE, f"xg{c}", "held" if c == PIECES - 1 else f"xg{c}_w"))
+        for pair in range(E // 2):
+            for b in range(BLOCKS):
+                bank = psum_mm.tile([P, BANK], F32, name="bank")
+                for half in range(2):
+                    e = 2 * pair + half
+                    words, scales = xg[e // 3]
+                    cols = slice((e % 3) * C, (e % 3 + 1) * C)
+                    nc.tensor.matmul_mx(bank[:, half * C:(half + 1) * C],
+                                        lhsT=w_w[e // 3][:, e % 3, 2 * P * b:2 * P * (b + 1)].bitcast(FP4X4),
+                                        lhsT_scale=w_s[:, e, P * b:P * (b + 1)],
+                                        rhs=words[:, cols].bitcast(FP8X4), rhs_scale=scales[:, cols], start=True, stop=True)
+                nc.scalar.copy(y[b][:, pair * BANK:(pair + 1) * BANK], bank[:])
+
+        def add_turned(acc, term, t0, width, first, last):
+            for a in range(width // P):
+                nc.tensor.matmul(acc[:, a * P:(a + 1) * P], term[:, t0 + a * P:t0 + (a + 1) * P], ident[:],
+                                 is_transpose=True, start=(first and a == 0), stop=(last and a == width // P - 1))
+
+        def finish(acc, b, t0, width):
+            total = stage.tile([P, BANK], F32, name="total")
+            nc.scalar.copy(total[:, :width], acc[:, :width])
+            back = psum_sum.tile([P, BANK], F32, name="back", tag="back")
+            for a in range(width // P):
+                nc.tensor.transpose(back[:, a * P:(a + 1) * P], total[:, a * P:(a + 1) * P], ident[:])
+            res = stage.tile([P, BANK], F32, name="res")
+            nc.scalar.copy(res[:, :width], back[:, :width])
+            nc.sync.dma_start(out[P * b:P * (b + 1), t0:t0 + width], res[:, :width])
+
+        for b in range(BLOCKS):
+            cuts = LAST_CUTS if b == BLOCKS - 1 else (T,)
+            start = 0
+            for cut in cuts:
+                spans = [(t0, min(BANK, cut)) for t0 in range(start, start + cut, BANK)]
+                accs = [psum_sum.tile([P, BANK], F32, name="acc", tag="acc") for span in spans]
+                for acc, (t0, width) in zip(accs, spans):
+                    add_turned(acc, scat[b], t0, width, True, False)
+                for r in range(TOP):
+                    term = ring.tile([P, T], F32, name="term")
+                    lst = pos_sb[r][:, start // 16:(start + cut) // 16]
+                    nc.vector.tensor_tensor(term[:, :cut], y[b][:].indirect(lst), gate_sb[r][:, start:start + cut], MULT)
+                    for acc, (t0, width) in zip(accs, spans):
+                        add_turned(acc, term, t0 - start, width, False, r == TOP - 1)
+                for acc, (t0, width) in zip(accs, spans):
+                    finish(acc, b, t0, width)
+                start += cut

@@ -24,7 +24,8 @@ ASLOTS = F * D
 BLOCKS = N // P
 PIECE = 3 * C
 PIECES = SLOTS // PIECE
-LAST_CUTS = (512, 256, 256)
+LAST_STORE = 256
+ADD = mybir.AluOpType.add
 
 
 def load_scale_rows(nc, plane, rows):
@@ -40,7 +41,7 @@ def tile_moe_mlr_relu_kernel(
     nc = tc.nc
     with ExitStack() as ctx:
         keep = ctx.enter_context(tc.tile_pool(name="keep", bufs=1))
-        ring = ctx.enter_context(tc.tile_pool(name="ring", bufs=6))
+        ring = ctx.enter_context(tc.tile_pool(name="ring", bufs=4))
         stage = ctx.enter_context(tc.tile_pool(name="stage", bufs=3))
         psum_mm = ctx.enter_context(tc.psum_pool(name="psum_mm", bufs=4))
         psum_sum = ctx.enter_context(tc.psum_pool(name="psum_sum", bufs=2))
@@ -59,17 +60,16 @@ def tile_moe_mlr_relu_kernel(
         gate_sb = [keep.tile([P, T], F32, name=f"gate_sb{r}") for r in range(TOP)]
         gate2_sb = keep.tile([P, ASLOTS], F32, name="gate2_sb")
         ident = keep.tile([P, P], F32, name="ident")
-        scat = [keep.tile([P, T], F32, name=f"scat{b}") for b in range(BLOCKS)]
+        scat = [keep.tile([P, T], F32, name=f"scat{a}") for a in range(2)]
         y = [keep.tile([P, SLOTS], F32, name=f"y{b}") for b in range(BLOCKS)]
 
-        nc.vector.memset(xs[:].bitcast(I32), 0)
-        nc.vector.memset(wa_s[:].bitcast(I32), 0)
-        nc.vector.memset(wb_s[:].bitcast(I32), 0)
+        nc.gpsimd.memset(xs[:].bitcast(I32), 0)
+        nc.gpsimd.memset(wa_s[:].bitcast(I32), 0)
+        nc.gpsimd.memset(wb_s[:].bitcast(I32), 0)
+        make_identity(nc, ident[:])
         nc.vector.memset(w_s[:].bitcast(I32), 0)
         nc.vector.memset(scat[0][:], 0.0)
-        for b in range(1, BLOCKS):
-            nc.scalar.activation(scat[b][:], scat[0][:], RELU)
-        make_identity(nc, ident[:])
+        nc.scalar.activation(scat[1][:], scat[0][:], RELU)
 
         nc.sync.dma_start(offs2_sb[:], offs2)
         x_rows = x_scales[0].rearrange("(q r) t -> r q t", r=4)
@@ -116,23 +116,27 @@ def tile_moe_mlr_relu_kernel(
         h_s = keep.tile([P, ASLOTS], U8, name="h_s", align_bytes=64)
         nc.vector.quantize_mx(out=h_w[:].bitcast(FP8X4), scales=h_s[:], in_=h_in[:].rearrange("p m j -> p (m j)"))
 
-        for b in range(BLOCKS):
+        xg = []
+        for c in range(PIECES):
+            lst = offs_sb[:, c * PIECE // 16:(c + 1) * PIECE // 16]
+            xg.append(gather_tokens(lst, PIECE, f"xg{c}", "held" if c == PIECES - 1 else f"xg{c}_w"))
+
+        def adapter_rows(b, tag):
             bank = psum_mm.tile([P, BANK], F32, name="bank")
             for f in range(F):
                 cols = slice(f * D, (f + 1) * D)
                 nc.tensor.matmul_mx(bank[:, cols], lhsT=wb_w[:, f, 2 * P * b:2 * P * (b + 1)].bitcast(FP4X4),
                                     lhsT_scale=wb_s[:, f, P * b:P * (b + 1)],
                                     rhs=h_w[:, cols].bitcast(FP8X4), rhs_scale=h_s[:, cols], start=True, stop=True)
-            z = keep.tile([P, ASLOTS], F32, name=f"z{b}")
+            z = keep.tile([P, ASLOTS], F32, name=f"z{b}", tag=tag)
             nc.scalar.copy(z[:], bank[:])
-            nc.vector.tensor_tensor(scat[b][:].indirect(offs2_sb[:]), z[:], gate2_sb[:], MULT)
+            return z
 
-        xg = []
-        for c in range(PIECES):
-            lst = offs_sb[:, c * PIECE // 16:(c + 1) * PIECE // 16]
-            xg.append(gather_tokens(lst, PIECE, f"xg{c}", "held" if c == PIECES - 1 else f"xg{c}_w"))
-        for pair in range(E // 2):
-            for b in range(BLOCKS):
+        def scatter(b, z):
+            nc.vector.tensor_tensor(scat[b % 2][:].indirect(offs2_sb[:]), z[:], gate2_sb[:], MULT)
+
+        def expert_rows(b, pairs):
+            for pair in pairs:
                 bank = psum_mm.tile([P, BANK], F32, name="bank")
                 for half in range(2):
                     e = 2 * pair + half
@@ -144,35 +148,57 @@ def tile_moe_mlr_relu_kernel(
                                         rhs=words[:, cols].bitcast(FP8X4), rhs_scale=scales[:, cols], start=True, stop=True)
                 nc.scalar.copy(y[b][:, pair * BANK:(pair + 1) * BANK], bank[:])
 
-        def add_turned(acc, term, t0, width, first, last):
-            for a in range(width // P):
-                nc.tensor.matmul(acc[:, a * P:(a + 1) * P], term[:, t0 + a * P:t0 + (a + 1) * P], ident[:],
-                                 is_transpose=True, start=(first and a == 0), stop=(last and a == width // P - 1))
+        def add_turned(accs, term, first, last):
+            for h, acc in enumerate(accs):
+                for a in range(BANK // P):
+                    t0 = h * BANK + a * P
+                    nc.tensor.matmul(acc[:, a * P:(a + 1) * P], term[:, t0:t0 + P], ident[:],
+                                     is_transpose=True, start=(first and a == 0), stop=(last and a == BANK // P - 1))
 
-        def finish(acc, b, t0, width):
-            total = stage.tile([P, BANK], F32, name="total")
-            nc.scalar.copy(total[:, :width], acc[:, :width])
+        def add_expert(accs, b, r, first):
+            term = keep.tile([P, T], F32, name=f"term{b}_{r}")
+            nc.vector.tensor_tensor(term[:], y[b][:].indirect(pos_sb[r][:]), gate_sb[r][:], MULT)
+            add_turned(accs, term, first, r == TOP - 1)
+
+        def turn_back(acc, total):
+            nc.scalar.copy(total[:], acc[:])
             back = psum_sum.tile([P, BANK], F32, name="back", tag="back")
-            for a in range(width // P):
+            for a in range(BANK // P):
                 nc.tensor.transpose(back[:, a * P:(a + 1) * P], total[:, a * P:(a + 1) * P], ident[:])
-            res = stage.tile([P, BANK], F32, name="res")
-            nc.scalar.copy(res[:, :width], back[:, :width])
-            nc.sync.dma_start(out[P * b:P * (b + 1), t0:t0 + width], res[:, :width])
+            return back
 
+        early = (PIECES - 1) * PIECE // BANK
+        for pair in range(early):
+            for b in range(BLOCKS):
+                expert_rows(b, [pair])
+        zs = []
         for b in range(BLOCKS):
-            cuts = LAST_CUTS if b == BLOCKS - 1 else (T,)
-            start = 0
-            for cut in cuts:
-                spans = [(t0, min(BANK, cut)) for t0 in range(start, start + cut, BANK)]
-                accs = [psum_sum.tile([P, BANK], F32, name="acc", tag="acc") for span in spans]
-                for acc, (t0, width) in zip(accs, spans):
-                    add_turned(acc, scat[b], t0, width, True, False)
-                for r in range(TOP):
-                    term = ring.tile([P, T], F32, name="term")
-                    lst = pos_sb[r][:, start // 16:(start + cut) // 16]
-                    nc.vector.tensor_tensor(term[:, :cut], y[b][:].indirect(lst), gate_sb[r][:, start:start + cut], MULT)
-                    for acc, (t0, width) in zip(accs, spans):
-                        add_turned(acc, term, t0 - start, width, False, r == TOP - 1)
-                for acc, (t0, width) in zip(accs, spans):
-                    finish(acc, b, t0, width)
-                start += cut
+            if b < BLOCKS - 1:
+                zs.append(adapter_rows(b, f"z{b}"))
+            expert_rows(b, range(early, E // 2))
+        for b in range(BLOCKS - 1):
+            scatter(b, zs[b])
+            accs = [psum_sum.tile([P, BANK], F32, name="acc", tag="acc") for h in range(T // BANK)]
+            add_turned(accs, scat[b % 2], True, False)
+            for r in range(TOP):
+                add_expert(accs, b, r, False)
+            for h, acc in enumerate(accs):
+                held_for_z = b == BLOCKS - 2 and h == T // BANK - 1
+                total = keep.tile([P, BANK], F32, name="late", tag="late") if held_for_z else stage.tile([P, BANK], F32, name="total")
+                back = turn_back(acc, total)
+                res = stage.tile([P, BANK], F32, name="res")
+                nc.scalar.copy(res[:], back[:])
+                nc.sync.dma_start(out[P * b:P * (b + 1), h * BANK:(h + 1) * BANK], res[:])
+
+        b = BLOCKS - 1
+        accs = [psum_sum.tile([P, BANK], F32, name="acc", tag="acc") for h in range(T // BANK)]
+        z = adapter_rows(b, "late")
+        for r in range(TOP):
+            add_expert(accs, b, r, r == 0)
+        scatter(b, z)
+        backs = [turn_back(acc, stage.tile([P, BANK], F32, name="total")) for acc in accs]
+        for t0 in range(0, T, LAST_STORE):
+            res = ring.tile([P, LAST_STORE], F32, name="last")
+            part = backs[t0 // BANK][:, t0 % BANK:t0 % BANK + LAST_STORE]
+            nc.vector.tensor_tensor(res[:], part, scat[b % 2][:, t0:t0 + LAST_STORE], ADD)
+            nc.sync.dma_start(out[P * b:P * (b + 1), t0:t0 + LAST_STORE], res[:])

@@ -24,7 +24,7 @@ ASLOTS = F * D
 BLOCKS = N // P
 PIECE = 3 * C
 PIECES = SLOTS // PIECE
-LAST_STORE = 256
+LAST_STORES = (512, 256, 128, 128)
 ADD = mybir.AluOpType.add
 
 
@@ -41,7 +41,7 @@ def tile_moe_mlr_relu_kernel(
     nc = tc.nc
     with ExitStack() as ctx:
         keep = ctx.enter_context(tc.tile_pool(name="keep", bufs=1))
-        ring = ctx.enter_context(tc.tile_pool(name="ring", bufs=4))
+        shared = ctx.enter_context(tc.tile_pool(name="shared", bufs=1))
         stage = ctx.enter_context(tc.tile_pool(name="stage", bufs=3))
         psum_mm = ctx.enter_context(tc.psum_pool(name="psum_mm", bufs=4))
         psum_sum = ctx.enter_context(tc.psum_pool(name="psum_sum", bufs=2))
@@ -67,9 +67,11 @@ def tile_moe_mlr_relu_kernel(
         nc.gpsimd.memset(wa_s[:].bitcast(I32), 0)
         nc.gpsimd.memset(wb_s[:].bitcast(I32), 0)
         make_identity(nc, ident[:])
+        zero = keep.tile([P, 8], F32, name="zero")
+        nc.vector.memset(zero[:], 0.0)
         nc.vector.memset(w_s[:].bitcast(I32), 0)
-        nc.vector.memset(scat[0][:], 0.0)
-        nc.scalar.activation(scat[1][:], scat[0][:], RELU)
+        for window in scat:
+            nc.scalar.activation(window[:], zero[:, 0:1].to_broadcast([P, T]), RELU)
 
         nc.sync.dma_start(offs2_sb[:], offs2)
         x_rows = x_scales[0].rearrange("(q r) t -> r q t", r=4)
@@ -89,15 +91,26 @@ def tile_moe_mlr_relu_kernel(
             nc.sync.dma_start(pos_sb[r][:], pos)
             nc.sync.dma_start(gate_sb[r][:], gate[r])
 
-        def gather_tokens(lst, count, name, tag):
-            scales = keep.tile([P, count], U8, name=name + "_s", align_bytes=64)
+        def gather_scales(lst, scales):
             nc.vector.tensor_copy(scales[:], xs[:].indirect(lst))
-            words = keep.tile([P, count], U32, name=name + "_w", tag=tag, align_bytes=64)
-            nc.vector.tensor_copy(words[:], xw[:].bitcast(U32).indirect(lst))
-            return words, scales
+            return scales
 
-        xa_w, xa_s = gather_tokens(offs2_sb[:], ASLOTS, "xa", "xa_w")
-        h_in = keep.tile([P, ASLOTS, 4], BF16, name="h_in", tag="held", align_bytes=64)
+        def gather_words(lst, words):
+            nc.vector.tensor_copy(words[:], xw[:].bitcast(U32).indirect(lst))
+            return words
+
+        lists = [offs_sb[:, c * PIECE // 16:(c + 1) * PIECE // 16] for c in range(PIECES)]
+        xa_s = gather_scales(offs2_sb[:], keep.tile([P, ASLOTS], U8, name="xa_s", align_bytes=64))
+        xa_w = gather_words(offs2_sb[:], keep.tile([P, ASLOTS], U32, name="xa_w", align_bytes=64))
+        xg_s = [gather_scales(lists[0], keep.tile([P, PIECE], U8, name="xg_s0", align_bytes=64))]
+        xg_w = [gather_words(lists[0], keep.tile([P, PIECE], U32, name="xg_w0", align_bytes=64))]
+        for c in range(1, PIECES - 1):
+            xg_s.append(gather_scales(lists[c], keep.tile([P, PIECE], U8, name=f"xg_s{c}", align_bytes=64)))
+            xg_w.append(gather_words(lists[c], keep.tile([P, PIECE], U32, name=f"xg_w{c}", align_bytes=64)))
+
+        h_w = keep.tile([P, ASLOTS], U32, name="h_w", align_bytes=64)
+        h_s = keep.tile([P, ASLOTS], U8, name="h_s", align_bytes=64)
+        h_in = shared.tile([P, 4 * ASLOTS], BF16, name="h_in", offset=0, align_bytes=64)
         for f in range(F):
             turned = psum_sum.tile([P, 2, 2, P], F32, name="turned", tag="back")
             for half in range(2):
@@ -110,16 +123,12 @@ def tile_moe_mlr_relu_kernel(
                 pairs = h_rows[:].bitcast(F32)
                 for u in range(2):
                     nc.tensor.transpose(turned[:, half, u, :], pairs[:, u:H // 2:2], ident[:])
-            dst = h_in[:, f * D:(f + 1) * D, :].rearrange("p m j -> p (m j)").bitcast(F32)
+            dst = h_in[:, 4 * D * f:4 * D * (f + 1)].bitcast(F32)
             nc.scalar.copy(dst.rearrange("p (a m u) -> p a m u", a=2, u=2), turned[:].rearrange("p a u m -> p a m u"))
-        h_w = keep.tile([P, ASLOTS], U32, name="h_w", align_bytes=64)
-        h_s = keep.tile([P, ASLOTS], U8, name="h_s", align_bytes=64)
-        nc.vector.quantize_mx(out=h_w[:].bitcast(FP8X4), scales=h_s[:], in_=h_in[:].rearrange("p m j -> p (m j)"))
+        nc.vector.quantize_mx(out=h_w[:].bitcast(FP8X4), scales=h_s[:], in_=h_in[:])
 
-        xg = []
-        for c in range(PIECES):
-            lst = offs_sb[:, c * PIECE // 16:(c + 1) * PIECE // 16]
-            xg.append(gather_tokens(lst, PIECE, f"xg{c}", "held" if c == PIECES - 1 else f"xg{c}_w"))
+        xg_s.append(gather_scales(lists[-1], shared.tile([P, PIECE], U8, name="xg_s_last", offset=4 * PIECE, align_bytes=64)))
+        xg_w.append(gather_words(lists[-1], shared.tile([P, PIECE], U32, name="xg_w_last", offset=0, align_bytes=64)))
 
         def adapter_rows(b, tag):
             bank = psum_mm.tile([P, BANK], F32, name="bank")
@@ -140,7 +149,7 @@ def tile_moe_mlr_relu_kernel(
                 bank = psum_mm.tile([P, BANK], F32, name="bank")
                 for half in range(2):
                     e = 2 * pair + half
-                    words, scales = xg[e // 3]
+                    words, scales = xg_w[e // 3], xg_s[e // 3]
                     cols = slice((e % 3) * C, (e % 3 + 1) * C)
                     nc.tensor.matmul_mx(bank[:, half * C:(half + 1) * C],
                                         lhsT=w_w[e // 3][:, e % 3, 2 * P * b:2 * P * (b + 1)].bitcast(FP4X4),
@@ -197,8 +206,10 @@ def tile_moe_mlr_relu_kernel(
             add_expert(accs, b, r, r == 0)
         scatter(b, z)
         backs = [turn_back(acc, stage.tile([P, BANK], F32, name="total")) for acc in accs]
-        for t0 in range(0, T, LAST_STORE):
-            res = ring.tile([P, LAST_STORE], F32, name="last")
-            part = backs[t0 // BANK][:, t0 % BANK:t0 % BANK + LAST_STORE]
-            nc.vector.tensor_tensor(res[:], part, scat[b % 2][:, t0:t0 + LAST_STORE], ADD)
-            nc.sync.dma_start(out[P * b:P * (b + 1), t0:t0 + LAST_STORE], res[:])
+        t0 = 0
+        for width in LAST_STORES:
+            res = keep.tile([P, width], F32, name=f"last{t0}")
+            part = backs[t0 // BANK][:, t0 % BANK:t0 % BANK + width]
+            nc.vector.tensor_tensor(res[:], part, scat[b % 2][:, t0:t0 + width], ADD)
+            nc.sync.dma_start(out[P * b:P * (b + 1), t0:t0 + width], res[:])
+            t0 = t0 + width

@@ -15,23 +15,26 @@ U8 = mybir.dt.uint8
 FP8X4 = mybir.dt.float8_e4m3fn_x4
 FP4X4 = mybir.dt.float4_e2m1fn_x4
 MULT = mybir.AluOpType.mult
+ADD = mybir.AluOpType.add
 RELU = mybir.ActivationFunctionType.Relu
 
 P = 128
 BANK = 512
+LIST_ROWS = 16
 SLOTS = E * C
-ASLOTS = F * D
+ADAPTER_SLOTS = F * D
 BLOCKS = N // P
-PIECE = 3 * C
-PIECES = SLOTS // PIECE
-LAST_STORES = (512, 256, 128, 128)
-ADD = mybir.AluOpType.add
+HALVES = T // BANK
+PIECE_EXPERTS = 3
+PIECE = PIECE_EXPERTS * C
+PIECES = E // PIECE_EXPERTS
+LAST_STORE = 256
 
 
-def load_scale_rows(nc, plane, rows):
+def load_scale_rows(nc, tile, rows):
     by_row = rows.rearrange("g (q r) n -> r q g n", r=4)
     for r in range(4):
-        nc.sync.dma_start(plane[r:P:32, :, :].bitcast(I32), by_row[r].bitcast(I32))
+        nc.sync.dma_start(tile[r:P:32, :, :].bitcast(I32), by_row[r].bitcast(I32))
 
 
 def tile_moe_mlr_relu_kernel(
@@ -44,40 +47,40 @@ def tile_moe_mlr_relu_kernel(
         shared = ctx.enter_context(tc.tile_pool(name="shared", bufs=1))
         stage = ctx.enter_context(tc.tile_pool(name="stage", bufs=3))
         psum_mm = ctx.enter_context(tc.psum_pool(name="psum_mm", bufs=4))
-        psum_sum = ctx.enter_context(tc.psum_pool(name="psum_sum", bufs=2))
+        psum_sum = ctx.enter_context(tc.psum_pool(name="psum_sum", bufs=HALVES))
 
-        offs_sb = keep.tile([P, SLOTS // 16], U16, name="offs_sb")
-        offs2_sb = keep.tile([P, ASLOTS // 16], U16, name="offs2_sb")
-        pos_sb = [keep.tile([P, T // 16], U16, name=f"pos_sb{r}") for r in range(TOP)]
-        xw = keep.tile([P, T], I32, name="xw", align_bytes=64)
-        xs = keep.tile([P, T], U8, name="xs", align_bytes=64)
+        offs_sb = keep.tile([P, SLOTS // LIST_ROWS], U16, name="offs_sb")
+        offs2_sb = keep.tile([P, ADAPTER_SLOTS // LIST_ROWS], U16, name="offs2_sb")
+        pos_sb = [keep.tile([P, T // LIST_ROWS], U16, name=f"pos_sb{r}") for r in range(TOP)]
+        x_w = keep.tile([P, T], I32, name="x_w", align_bytes=64)
+        x_s = keep.tile([P, T], U8, name="x_s", align_bytes=64)
         wa_w = keep.tile([P, F, 2 * H], U8, name="wa_w", align_bytes=64)
         wa_s = keep.tile([P, F, H], U8, name="wa_s", align_bytes=64)
         wb_w = keep.tile([P, F, 2 * N], U8, name="wb_w", align_bytes=64)
         wb_s = keep.tile([P, F, N], U8, name="wb_s", align_bytes=64)
-        w_w = [keep.tile([P, 3, 2 * N], U8, name=f"w_w{c}", align_bytes=64) for c in range(PIECES)]
+        w_w = [keep.tile([P, PIECE_EXPERTS, 2 * N], U8, name=f"w_w{c}", align_bytes=64) for c in range(PIECES)]
         w_s = keep.tile([P, E, N], U8, name="w_s", align_bytes=64)
         gate_sb = [keep.tile([P, T], F32, name=f"gate_sb{r}") for r in range(TOP)]
-        gate2_sb = keep.tile([P, ASLOTS], F32, name="gate2_sb")
+        gate2_sb = keep.tile([P, ADAPTER_SLOTS], F32, name="gate2_sb")
         ident = keep.tile([P, P], F32, name="ident")
-        scat = [keep.tile([P, T], F32, name=f"scat{a}") for a in range(2)]
+        windows = [keep.tile([P, T], F32, name=f"window{a}") for a in range(2)]
         y = [keep.tile([P, SLOTS], F32, name=f"y{b}") for b in range(BLOCKS)]
 
-        nc.gpsimd.memset(xs[:].bitcast(I32), 0)
+        nc.gpsimd.memset(x_s[:].bitcast(I32), 0)
         nc.gpsimd.memset(wa_s[:].bitcast(I32), 0)
         nc.gpsimd.memset(wb_s[:].bitcast(I32), 0)
         make_identity(nc, ident[:])
-        zero = keep.tile([P, 8], F32, name="zero")
+        zero = keep.tile([P, 1], F32, name="zero")
         nc.vector.memset(zero[:], 0.0)
         nc.vector.memset(w_s[:].bitcast(I32), 0)
-        for window in scat:
-            nc.scalar.activation(window[:], zero[:, 0:1].to_broadcast([P, T]), RELU)
+        for window in windows:
+            nc.scalar.activation(window[:], zero[:].to_broadcast([P, T]), RELU)
 
         nc.sync.dma_start(offs2_sb[:], offs2)
-        x_rows = x_scales[0].rearrange("(q r) t -> r q t", r=4)
+        x_scale_rows = x_scales[0].rearrange("(q r) t -> r q t", r=4)
         for r in range(4):
-            nc.sync.dma_start(xs[r:P:32, :].bitcast(I32), x_rows[r].bitcast(I32))
-        nc.sync.dma_start(xw[:], x_words[0].rearrange("p t d -> p (t d)").bitcast(I32))
+            nc.sync.dma_start(x_s[r:P:32, :].bitcast(I32), x_scale_rows[r].bitcast(I32))
+        nc.sync.dma_start(x_w[:], x_words[0].rearrange("p t d -> p (t d)").bitcast(I32))
         nc.sync.dma_start(offs_sb[:], offs)
         nc.sync.dma_start(wa_w[:].bitcast(I32), wa_words[:, 0].rearrange("f p n -> p f n").bitcast(I32))
         load_scale_rows(nc, wa_s, wa_scales[:, 0])
@@ -85,131 +88,136 @@ def tile_moe_mlr_relu_kernel(
         nc.sync.dma_start(wb_w[:].bitcast(I32), wb_words[:, 0].rearrange("f p n -> p f n").bitcast(I32))
         load_scale_rows(nc, w_s, w_scales[:, 0])
         for c in range(PIECES):
-            nc.sync.dma_start(w_w[c][:].bitcast(I32), w_words[3 * c:3 * c + 3, 0].rearrange("e p n -> p e n").bitcast(I32))
+            experts = w_words[PIECE_EXPERTS * c:PIECE_EXPERTS * (c + 1), 0]
+            nc.sync.dma_start(w_w[c][:].bitcast(I32), experts.rearrange("e p n -> p e n").bitcast(I32))
         nc.sync.dma_start(gate2_sb[:], gate2)
         for r, pos in enumerate((pos1, pos2, pos3)):
             nc.sync.dma_start(pos_sb[r][:], pos)
             nc.sync.dma_start(gate_sb[r][:], gate[r])
 
-        def gather_scales(lst, scales):
-            nc.vector.tensor_copy(scales[:], xs[:].indirect(lst))
+        def gather_scales(entries, scales):
+            nc.vector.tensor_copy(scales[:], x_s[:].indirect(entries))
             return scales
 
-        def gather_words(lst, words):
-            nc.vector.tensor_copy(words[:], xw[:].bitcast(U32).indirect(lst))
+        def gather_words(entries, words):
+            nc.vector.tensor_copy(words[:], x_w[:].bitcast(U32).indirect(entries))
             return words
 
-        lists = [offs_sb[:, c * PIECE // 16:(c + 1) * PIECE // 16] for c in range(PIECES)]
-        xa_s = gather_scales(offs2_sb[:], keep.tile([P, ASLOTS], U8, name="xa_s", align_bytes=64))
-        xa_w = gather_words(offs2_sb[:], keep.tile([P, ASLOTS], U32, name="xa_w", align_bytes=64))
-        xg_s = [gather_scales(lists[0], keep.tile([P, PIECE], U8, name="xg_s0", align_bytes=64))]
-        xg_w = [gather_words(lists[0], keep.tile([P, PIECE], U32, name="xg_w0", align_bytes=64))]
-        for c in range(1, PIECES - 1):
-            xg_s.append(gather_scales(lists[c], keep.tile([P, PIECE], U8, name=f"xg_s{c}", align_bytes=64)))
-            xg_w.append(gather_words(lists[c], keep.tile([P, PIECE], U32, name=f"xg_w{c}", align_bytes=64)))
+        columns = PIECE // LIST_ROWS
+        pieces = [offs_sb[:, c * columns:(c + 1) * columns] for c in range(PIECES)]
+        xa_s = gather_scales(offs2_sb[:], keep.tile([P, ADAPTER_SLOTS], U8, name="xa_s", align_bytes=64))
+        xa_w = gather_words(offs2_sb[:], keep.tile([P, ADAPTER_SLOTS], U32, name="xa_w", align_bytes=64))
+        xe_s, xe_w = [], []
+        for c in range(PIECES - 1):
+            xe_s.append(gather_scales(pieces[c], keep.tile([P, PIECE], U8, name=f"xe_s{c}", align_bytes=64)))
+            xe_w.append(gather_words(pieces[c], keep.tile([P, PIECE], U32, name=f"xe_w{c}", align_bytes=64)))
 
-        h_w = keep.tile([P, ASLOTS], U32, name="h_w", align_bytes=64)
-        h_s = keep.tile([P, ASLOTS], U8, name="h_s", align_bytes=64)
-        h_in = shared.tile([P, 4 * ASLOTS], BF16, name="h_in", offset=0, align_bytes=64)
+        h_w = keep.tile([P, ADAPTER_SLOTS], U32, name="h_w", align_bytes=64)
+        h_s = keep.tile([P, ADAPTER_SLOTS], U8, name="h_s", align_bytes=64)
+        h_in = shared.tile([P, 4 * ADAPTER_SLOTS], BF16, name="h_in", offset=0, align_bytes=64)
         for f in range(F):
-            turned = psum_sum.tile([P, 2, 2, P], F32, name="turned", tag="back")
-            for half in range(2):
-                cols = slice(f * D + half * P, f * D + (half + 1) * P)
+            turned = psum_sum.tile([P, D // P, 2, P], F32, name="turned", tag="back")
+            for a in range(D // P):
+                slots = slice(f * D + a * P, f * D + (a + 1) * P)
                 bank = psum_mm.tile([P, BANK], F32, name="bank")
-                nc.tensor.matmul_mx(bank[:], lhsT=xa_w[:, cols].bitcast(FP8X4), lhsT_scale=xa_s[:, cols],
+                nc.tensor.matmul_mx(bank[:], lhsT=xa_w[:, slots].bitcast(FP8X4), lhsT_scale=xa_s[:, slots],
                                     rhs=wa_w[:, f, :].bitcast(FP4X4), rhs_scale=wa_s[:, f, :], start=True, stop=True)
                 h_rows = stage.tile([P, H], BF16, name="h_rows")
                 nc.scalar.activation(h_rows[:], bank[:], RELU)
                 pairs = h_rows[:].bitcast(F32)
                 for u in range(2):
-                    nc.tensor.transpose(turned[:, half, u, :], pairs[:, u:H // 2:2], ident[:])
-            dst = h_in[:, 4 * D * f:4 * D * (f + 1)].bitcast(F32)
-            nc.scalar.copy(dst.rearrange("p (a m u) -> p a m u", a=2, u=2), turned[:].rearrange("p a u m -> p a m u"))
+                    nc.tensor.transpose(turned[:, a, u, :], pairs[:, u:H // 2:2], ident[:])
+            h_pairs = h_in[:, 4 * D * f:4 * D * (f + 1)].bitcast(F32)
+            nc.scalar.copy(h_pairs.rearrange("p (a m u) -> p a m u", a=D // P, u=2),
+                           turned[:].rearrange("p a u m -> p a m u"))
         nc.vector.quantize_mx(out=h_w[:].bitcast(FP8X4), scales=h_s[:], in_=h_in[:])
 
-        xg_s.append(gather_scales(lists[-1], shared.tile([P, PIECE], U8, name="xg_s_last", offset=4 * PIECE, align_bytes=64)))
-        xg_w.append(gather_words(lists[-1], shared.tile([P, PIECE], U32, name="xg_w_last", offset=0, align_bytes=64)))
+        xe_s.append(gather_scales(pieces[-1], shared.tile([P, PIECE], U8, name="xe_s_last", offset=4 * PIECE, align_bytes=64)))
+        xe_w.append(gather_words(pieces[-1], shared.tile([P, PIECE], U32, name="xe_w_last", offset=0, align_bytes=64)))
 
         def adapter_rows(b, tag):
             bank = psum_mm.tile([P, BANK], F32, name="bank")
             for f in range(F):
-                cols = slice(f * D, (f + 1) * D)
-                nc.tensor.matmul_mx(bank[:, cols], lhsT=wb_w[:, f, 2 * P * b:2 * P * (b + 1)].bitcast(FP4X4),
+                slots = slice(f * D, (f + 1) * D)
+                nc.tensor.matmul_mx(bank[:, slots], lhsT=wb_w[:, f, 2 * P * b:2 * P * (b + 1)].bitcast(FP4X4),
                                     lhsT_scale=wb_s[:, f, P * b:P * (b + 1)],
-                                    rhs=h_w[:, cols].bitcast(FP8X4), rhs_scale=h_s[:, cols], start=True, stop=True)
-            z = keep.tile([P, ASLOTS], F32, name=f"z{b}", tag=tag)
+                                    rhs=h_w[:, slots].bitcast(FP8X4), rhs_scale=h_s[:, slots], start=True, stop=True)
+            z = keep.tile([P, ADAPTER_SLOTS], F32, name=f"z{b}", tag=tag)
             nc.scalar.copy(z[:], bank[:])
             return z
 
         def scatter(b, z):
-            nc.vector.tensor_tensor(scat[b % 2][:].indirect(offs2_sb[:]), z[:], gate2_sb[:], MULT)
+            nc.vector.tensor_tensor(windows[b % 2][:].indirect(offs2_sb[:]), z[:], gate2_sb[:], MULT)
 
-        def expert_rows(b, pairs):
-            for pair in pairs:
-                bank = psum_mm.tile([P, BANK], F32, name="bank")
-                for half in range(2):
-                    e = 2 * pair + half
-                    words, scales = xg_w[e // 3], xg_s[e // 3]
-                    cols = slice((e % 3) * C, (e % 3 + 1) * C)
-                    nc.tensor.matmul_mx(bank[:, half * C:(half + 1) * C],
-                                        lhsT=w_w[e // 3][:, e % 3, 2 * P * b:2 * P * (b + 1)].bitcast(FP4X4),
-                                        lhsT_scale=w_s[:, e, P * b:P * (b + 1)],
-                                        rhs=words[:, cols].bitcast(FP8X4), rhs_scale=scales[:, cols], start=True, stop=True)
-                nc.scalar.copy(y[b][:, pair * BANK:(pair + 1) * BANK], bank[:])
+        def expert_rows(b, expert_pair):
+            bank = psum_mm.tile([P, BANK], F32, name="bank")
+            for side in range(2):
+                e = 2 * expert_pair + side
+                c, place = divmod(e, PIECE_EXPERTS)
+                slots = slice(place * C, (place + 1) * C)
+                nc.tensor.matmul_mx(bank[:, side * C:(side + 1) * C],
+                                    lhsT=w_w[c][:, place, 2 * P * b:2 * P * (b + 1)].bitcast(FP4X4),
+                                    lhsT_scale=w_s[:, e, P * b:P * (b + 1)],
+                                    rhs=xe_w[c][:, slots].bitcast(FP8X4), rhs_scale=xe_s[c][:, slots],
+                                    start=True, stop=True)
+            nc.scalar.copy(y[b][:, expert_pair * BANK:(expert_pair + 1) * BANK], bank[:])
 
-        def add_turned(accs, term, first, last):
-            for h, acc in enumerate(accs):
+        def add_turned(sums, term, first, last):
+            for half, bank in enumerate(sums):
                 for a in range(BANK // P):
-                    t0 = h * BANK + a * P
-                    nc.tensor.matmul(acc[:, a * P:(a + 1) * P], term[:, t0:t0 + P], ident[:],
-                                     is_transpose=True, start=(first and a == 0), stop=(last and a == BANK // P - 1))
+                    t0 = half * BANK + a * P
+                    nc.tensor.matmul(bank[:, a * P:(a + 1) * P], term[:, t0:t0 + P], ident[:], is_transpose=True,
+                                     start=(first and a == 0), stop=(last and a == BANK // P - 1))
 
-        def add_expert(accs, b, r, first):
+        def add_choice(sums, b, r, first):
             term = keep.tile([P, T], F32, name=f"term{b}_{r}")
             nc.vector.tensor_tensor(term[:], y[b][:].indirect(pos_sb[r][:]), gate_sb[r][:], MULT)
-            add_turned(accs, term, first, r == TOP - 1)
+            add_turned(sums, term, first, r == TOP - 1)
 
-        def turn_back(acc, total):
-            nc.scalar.copy(total[:], acc[:])
+        def turn_back(bank, total):
+            nc.scalar.copy(total[:], bank[:])
             back = psum_sum.tile([P, BANK], F32, name="back", tag="back")
             for a in range(BANK // P):
                 nc.tensor.transpose(back[:, a * P:(a + 1) * P], total[:, a * P:(a + 1) * P], ident[:])
             return back
 
-        early = (PIECES - 1) * PIECE // BANK
-        for pair in range(early):
+        early_pairs = (PIECES - 1) * PIECE_EXPERTS // 2
+        for expert_pair in range(early_pairs):
             for b in range(BLOCKS):
-                expert_rows(b, [pair])
+                expert_rows(b, expert_pair)
+        last = BLOCKS - 1
         zs = []
         for b in range(BLOCKS):
-            if b < BLOCKS - 1:
+            if b < last:
                 zs.append(adapter_rows(b, f"z{b}"))
-            expert_rows(b, range(early, E // 2))
-        for b in range(BLOCKS - 1):
-            scatter(b, zs[b])
-            accs = [psum_sum.tile([P, BANK], F32, name="acc", tag="acc") for h in range(T // BANK)]
-            add_turned(accs, scat[b % 2], True, False)
-            for r in range(TOP):
-                add_expert(accs, b, r, False)
-            for h, acc in enumerate(accs):
-                held_for_z = b == BLOCKS - 2 and h == T // BANK - 1
-                total = keep.tile([P, BANK], F32, name="late", tag="late") if held_for_z else stage.tile([P, BANK], F32, name="total")
-                back = turn_back(acc, total)
-                res = stage.tile([P, BANK], F32, name="res")
-                nc.scalar.copy(res[:], back[:])
-                nc.sync.dma_start(out[P * b:P * (b + 1), h * BANK:(h + 1) * BANK], res[:])
+            for expert_pair in range(early_pairs, E // 2):
+                expert_rows(b, expert_pair)
 
-        b = BLOCKS - 1
-        accs = [psum_sum.tile([P, BANK], F32, name="acc", tag="acc") for h in range(T // BANK)]
-        z = adapter_rows(b, "late")
+        for b in range(last):
+            scatter(b, zs[b])
+            sums = [psum_sum.tile([P, BANK], F32, name="sums", tag="sums") for half in range(HALVES)]
+            add_turned(sums, windows[b % 2], True, False)
+            for r in range(TOP):
+                add_choice(sums, b, r, False)
+            for half, bank in enumerate(sums):
+                if b == last - 1 and half == HALVES - 1:
+                    total = keep.tile([P, BANK], F32, name="lent", tag="lent")
+                else:
+                    total = stage.tile([P, BANK], F32, name="total")
+                back = turn_back(bank, total)
+                result = stage.tile([P, BANK], F32, name="result")
+                nc.scalar.copy(result[:], back[:])
+                nc.sync.dma_start(out[P * b:P * (b + 1), half * BANK:(half + 1) * BANK], result[:])
+
+        sums = [psum_sum.tile([P, BANK], F32, name="sums", tag="sums") for half in range(HALVES)]
+        z_last = adapter_rows(last, "lent")
         for r in range(TOP):
-            add_expert(accs, b, r, r == 0)
-        scatter(b, z)
-        backs = [turn_back(acc, stage.tile([P, BANK], F32, name="total")) for acc in accs]
-        t0 = 0
-        for width in LAST_STORES:
-            res = keep.tile([P, width], F32, name=f"last{t0}")
-            part = backs[t0 // BANK][:, t0 % BANK:t0 % BANK + width]
-            nc.vector.tensor_tensor(res[:], part, scat[b % 2][:, t0:t0 + width], ADD)
-            nc.sync.dma_start(out[P * b:P * (b + 1), t0:t0 + width], res[:])
-            t0 = t0 + width
+            add_choice(sums, last, r, r == 0)
+        scatter(last, z_last)
+        backs = [turn_back(bank, stage.tile([P, BANK], F32, name="total")) for bank in sums]
+        for t0 in range(0, T, LAST_STORE):
+            finished = keep.tile([P, LAST_STORE], F32, name=f"finished{t0}")
+            half, c0 = divmod(t0, BANK)
+            nc.vector.tensor_tensor(finished[:], backs[half][:, c0:c0 + LAST_STORE],
+                                    windows[last % 2][:, t0:t0 + LAST_STORE], ADD)
+            nc.sync.dma_start(out[P * last:P * (last + 1), t0:t0 + LAST_STORE], finished[:])

@@ -29,6 +29,7 @@ PIECE_EXPERTS = 3
 PIECE = PIECE_EXPERTS * C
 PIECES = E // PIECE_EXPERTS
 LAST_STORE = 256
+SECOND = 8 * ADAPTER_SLOTS
 
 
 def load_scale_rows(nc, tile, rows):
@@ -53,7 +54,7 @@ def tile_moe_mlr_relu_kernel(
         offs2_sb = keep.tile([P, ADAPTER_SLOTS // LIST_ROWS], U16, name="offs2_sb")
         pos_sb = [keep.tile([P, T // LIST_ROWS], U16, name=f"pos_sb{r}") for r in range(TOP)]
         x_w = keep.tile([P, T], I32, name="x_w", align_bytes=64)
-        x_s = keep.tile([P, T], U8, name="x_s", align_bytes=64)
+        x_s = keep.tile([P, 2 * T], U8, name="x_s", align_bytes=64)
         wa_w = keep.tile([P, F, 2 * H], U8, name="wa_w", align_bytes=64)
         wa_s = keep.tile([P, F, H], U8, name="wa_s", align_bytes=64)
         wb_w = keep.tile([P, F, 2 * N], U8, name="wb_w", align_bytes=64)
@@ -66,30 +67,27 @@ def tile_moe_mlr_relu_kernel(
         windows = [keep.tile([P, T], F32, name=f"window{a}") for a in range(2)]
         y = [keep.tile([P, SLOTS], F32, name=f"y{b}") for b in range(BLOCKS)]
 
-        nc.gpsimd.memset(x_s[:].bitcast(I32), 0)
-        nc.gpsimd.memset(wa_s[:].bitcast(I32), 0)
-        nc.gpsimd.memset(wb_s[:].bitcast(I32), 0)
+        for scales in (x_s[:, :T], x_s[:, T:], wa_s[:], w_s[:], wb_s[:]):
+            nc.vector.memset(scales.bitcast(I32), 0)
         make_identity(nc, ident[:])
-        zero = keep.tile([P, 1], F32, name="zero")
-        nc.vector.memset(zero[:], 0.0)
-        nc.vector.memset(w_s[:].bitcast(I32), 0)
         for window in windows:
-            nc.scalar.activation(window[:], zero[:].to_broadcast([P, T]), RELU)
+            nc.scalar.activation(window[:], ident[:, 0:1].to_broadcast([P, T]), RELU, scale=0.0)
 
         nc.sync.dma_start(offs2_sb[:], offs2)
         x_scale_rows = x_scales[0].rearrange("(q r) t -> r q t", r=4)
         for r in range(4):
-            nc.sync.dma_start(x_s[r:P:32, :].bitcast(I32), x_scale_rows[r].bitcast(I32))
-        nc.sync.dma_start(x_w[:], x_words[0].rearrange("p t d -> p (t d)").bitcast(I32))
+            queue = nc.sync if r < 2 else nc.scalar
+            queue.dma_start(x_s[r:P:32, :T].bitcast(I32), x_scale_rows[r].bitcast(I32))
         nc.sync.dma_start(offs_sb[:], offs)
+        nc.sync.dma_start(x_w[:], x_words[0].rearrange("p t d -> p (t d)").bitcast(I32))
         nc.sync.dma_start(wa_w[:].bitcast(I32), wa_words[:, 0].rearrange("f p n -> p f n").bitcast(I32))
         load_scale_rows(nc, wa_s, wa_scales[:, 0])
         load_scale_rows(nc, wb_s, wb_scales[:, 0])
-        nc.sync.dma_start(wb_w[:].bitcast(I32), wb_words[:, 0].rearrange("f p n -> p f n").bitcast(I32))
         load_scale_rows(nc, w_s, w_scales[:, 0])
         for c in range(PIECES):
             experts = w_words[PIECE_EXPERTS * c:PIECE_EXPERTS * (c + 1), 0]
             nc.sync.dma_start(w_w[c][:].bitcast(I32), experts.rearrange("e p n -> p e n").bitcast(I32))
+        nc.sync.dma_start(wb_w[:].bitcast(I32), wb_words[:, 0].rearrange("f p n -> p f n").bitcast(I32))
         nc.sync.dma_start(gate2_sb[:], gate2)
         for r, pos in enumerate((pos1, pos2, pos3)):
             nc.sync.dma_start(pos_sb[r][:], pos)
@@ -105,11 +103,12 @@ def tile_moe_mlr_relu_kernel(
 
         columns = PIECE // LIST_ROWS
         pieces = [offs_sb[:, c * columns:(c + 1) * columns] for c in range(PIECES)]
-        xa_s = gather_scales(offs2_sb[:], keep.tile([P, ADAPTER_SLOTS], U8, name="xa_s", align_bytes=64))
+        halves = [offs_sb[:, u * 2 * columns:(u + 1) * 2 * columns] for u in range(2)]
+        xa_s = gather_scales(offs2_sb[:], shared.tile([P, ADAPTER_SLOTS], U8, name="xa_s", offset=SECOND, align_bytes=64))
+        xe_s = [gather_scales(halves[0], keep.tile([P, SLOTS // 2], U8, name="xe_s0", align_bytes=64))]
+        xe_w = []
         xa_w = gather_words(offs2_sb[:], keep.tile([P, ADAPTER_SLOTS], U32, name="xa_w", align_bytes=64))
-        xe_s, xe_w = [], []
         for c in range(PIECES - 1):
-            xe_s.append(gather_scales(pieces[c], keep.tile([P, PIECE], U8, name=f"xe_s{c}", align_bytes=64)))
             xe_w.append(gather_words(pieces[c], keep.tile([P, PIECE], U32, name=f"xe_w{c}", align_bytes=64)))
 
         h_w = keep.tile([P, ADAPTER_SLOTS], U32, name="h_w", align_bytes=64)
@@ -130,9 +129,9 @@ def tile_moe_mlr_relu_kernel(
             h_pairs = h_in[:, 4 * D * f:4 * D * (f + 1)].bitcast(F32)
             nc.scalar.copy(h_pairs.rearrange("p (a m u) -> p a m u", a=D // P, u=2),
                            turned[:].rearrange("p a u m -> p a m u"))
+        xe_s.append(gather_scales(halves[1], shared.tile([P, SLOTS // 2], U8, name="xe_s1", offset=SECOND, align_bytes=64)))
         nc.vector.quantize_mx(out=h_w[:].bitcast(FP8X4), scales=h_s[:], in_=h_in[:])
 
-        xe_s.append(gather_scales(pieces[-1], shared.tile([P, PIECE], U8, name="xe_s_last", offset=4 * PIECE, align_bytes=64)))
         xe_w.append(gather_words(pieces[-1], shared.tile([P, PIECE], U32, name="xe_w_last", offset=0, align_bytes=64)))
 
         def adapter_rows(b, tag):
@@ -158,7 +157,7 @@ def tile_moe_mlr_relu_kernel(
                 nc.tensor.matmul_mx(bank[:, side * C:(side + 1) * C],
                                     lhsT=w_w[c][:, place, 2 * P * b:2 * P * (b + 1)].bitcast(FP4X4),
                                     lhsT_scale=w_s[:, e, P * b:P * (b + 1)],
-                                    rhs=xe_w[c][:, slots].bitcast(FP8X4), rhs_scale=xe_s[c][:, slots],
+                                    rhs=xe_w[c][:, slots].bitcast(FP8X4), rhs_scale=xe_s[e // (E // 2)][:, (e % (E // 2)) * C:(e % (E // 2) + 1) * C],
                                     start=True, stop=True)
             nc.scalar.copy(y[b][:, expert_pair * BANK:(expert_pair + 1) * BANK], bank[:])
 
@@ -182,12 +181,11 @@ def tile_moe_mlr_relu_kernel(
             return back
 
         early_pairs = (PIECES - 1) * PIECE_EXPERTS // 2
-        for expert_pair in range(early_pairs):
-            for b in range(BLOCKS):
-                expert_rows(b, expert_pair)
         last = BLOCKS - 1
         zs = []
         for b in range(BLOCKS):
+            for expert_pair in range(early_pairs):
+                expert_rows(b, expert_pair)
             if b < last:
                 zs.append(adapter_rows(b, f"z{b}"))
             for expert_pair in range(early_pairs, E // 2):

@@ -29,6 +29,9 @@ PIECE_EXPERTS = 3
 PIECE = PIECE_EXPERTS * C
 PIECES = E // PIECE_EXPERTS
 LAST_STORE = 256
+PRODUCT_BANKS = ("mm0", "mm1", "mm2", "mm3")
+SUM_BANKS = ("sum0", "sum1")
+BACK_BANKS = ("back0", "back1")
 SECOND = 8 * ADAPTER_SLOTS
 
 
@@ -47,8 +50,21 @@ def tile_moe_mlr_relu_kernel(
         keep = ctx.enter_context(tc.tile_pool(name="keep", bufs=1))
         shared = ctx.enter_context(tc.tile_pool(name="shared", bufs=1))
         stage = ctx.enter_context(tc.tile_pool(name="stage", bufs=3))
-        psum_mm = ctx.enter_context(tc.psum_pool(name="psum_mm", bufs=4))
-        psum_sum = ctx.enter_context(tc.psum_pool(name="psum_sum", bufs=HALVES))
+        psum = ctx.enter_context(tc.psum_pool(name="psum", bufs=1))
+        taken = []
+
+        def bank_of(tag):
+            taken.append(psum.tile([P, BANK], F32, name=f"bank{len(taken)}", tag=tag))
+            return taken[-1]
+
+        turns = []
+
+        def product_bank(ring):
+            turns.append(ring[len(turns) % len(ring)])
+            return bank_of(turns[-1])
+
+        def ring(b):
+            return PRODUCT_BANKS + SUM_BANKS if b < 2 else PRODUCT_BANKS
 
         offs_sb = keep.tile([P, SLOTS // LIST_ROWS], U16, name="offs_sb")
         offs2_sb = keep.tile([P, ADAPTER_SLOTS // LIST_ROWS], U16, name="offs2_sb")
@@ -83,7 +99,6 @@ def tile_moe_mlr_relu_kernel(
         nc.sync.dma_start(wa_w[:].bitcast(I32), wa_words[:, 0].rearrange("f p n -> p f n").bitcast(I32))
         load_scale_rows(nc, wa_s, wa_scales[:, 0])
         load_scale_rows(nc, wb_s, wb_scales[:, 0])
-        load_scale_rows(nc, w_s, w_scales[:, 0])
         for c in range(PIECES):
             experts = w_words[PIECE_EXPERTS * c:PIECE_EXPERTS * (c + 1), 0]
             nc.sync.dma_start(w_w[c][:].bitcast(I32), experts.rearrange("e p n -> p e n").bitcast(I32))
@@ -92,6 +107,8 @@ def tile_moe_mlr_relu_kernel(
         for r, pos in enumerate((pos1, pos2, pos3)):
             nc.sync.dma_start(pos_sb[r][:], pos)
             nc.sync.dma_start(gate_sb[r][:], gate[r])
+            if r == 0:
+                load_scale_rows(nc, w_s, w_scales[:, 0])
 
         def gather_scales(entries, scales):
             nc.vector.tensor_copy(scales[:], x_s[:].indirect(entries))
@@ -115,27 +132,28 @@ def tile_moe_mlr_relu_kernel(
         h_s = keep.tile([P, ADAPTER_SLOTS], U8, name="h_s", align_bytes=64)
         h_in = shared.tile([P, 4 * ADAPTER_SLOTS], BF16, name="h_in", offset=0, align_bytes=64)
         for f in range(F):
-            turned = psum_sum.tile([P, D // P, 2, P], F32, name="turned", tag="back")
+            turned = bank_of(BACK_BANKS[f])[:].rearrange("p (a u m) -> p a u m", a=D // P, u=2)
             for a in range(D // P):
                 slots = slice(f * D + a * P, f * D + (a + 1) * P)
-                bank = psum_mm.tile([P, BANK], F32, name="bank")
+                bank = product_bank(ring(0))
                 nc.tensor.matmul_mx(bank[:], lhsT=xa_w[:, slots].bitcast(FP8X4), lhsT_scale=xa_s[:, slots],
                                     rhs=wa_w[:, f, :].bitcast(FP4X4), rhs_scale=wa_s[:, f, :], start=True, stop=True)
                 h_rows = stage.tile([P, H], BF16, name="h_rows")
-                nc.scalar.activation(h_rows[:], bank[:], RELU)
+                nc.scalar.activation(h_rows[:].rearrange("m (u p e) -> m u p e", u=2, e=2),
+                                     bank[:].rearrange("m (p u e) -> m u p e", u=2, e=2), RELU)
                 pairs = h_rows[:].bitcast(F32)
                 for u in range(2):
-                    nc.tensor.transpose(turned[:, a, u, :], pairs[:, u:H // 2:2], ident[:])
+                    nc.tensor.transpose(turned[:, a, u, :], pairs[:, u * P:(u + 1) * P], ident[:])
             h_pairs = h_in[:, 4 * D * f:4 * D * (f + 1)].bitcast(F32)
             nc.scalar.copy(h_pairs.rearrange("p (a m u) -> p a m u", a=D // P, u=2),
-                           turned[:].rearrange("p a u m -> p a m u"))
+                           turned.rearrange("p a u m -> p a m u"))
         xe_s.append(gather_scales(halves[1], shared.tile([P, SLOTS // 2], U8, name="xe_s1", offset=SECOND, align_bytes=64)))
         nc.vector.quantize_mx(out=h_w[:].bitcast(FP8X4), scales=h_s[:], in_=h_in[:])
 
         xe_w.append(gather_words(pieces[-1], shared.tile([P, PIECE], U32, name="xe_w_last", offset=0, align_bytes=64)))
 
         def adapter_rows(b, tag):
-            bank = psum_mm.tile([P, BANK], F32, name="bank")
+            bank = product_bank(ring(b))
             for f in range(F):
                 slots = slice(f * D, (f + 1) * D)
                 nc.tensor.matmul_mx(bank[:, slots], lhsT=wb_w[:, f, 2 * P * b:2 * P * (b + 1)].bitcast(FP4X4),
@@ -149,7 +167,7 @@ def tile_moe_mlr_relu_kernel(
             nc.vector.tensor_tensor(windows[b % 2][:].indirect(offs2_sb[:]), z[:], gate2_sb[:], MULT)
 
         def expert_rows(b, expert_pair):
-            bank = psum_mm.tile([P, BANK], F32, name="bank")
+            bank = product_bank(ring(b))
             for side in range(2):
                 e = 2 * expert_pair + side
                 c, place = divmod(e, PIECE_EXPERTS)
@@ -173,9 +191,9 @@ def tile_moe_mlr_relu_kernel(
             nc.vector.tensor_tensor(term[:], y[b][:].indirect(pos_sb[r][:]), gate_sb[r][:], MULT)
             add_turned(sums, term, first, r == TOP - 1)
 
-        def turn_back(bank, total):
+        def turn_back(half, bank, total):
             nc.scalar.copy(total[:], bank[:])
-            back = psum_sum.tile([P, BANK], F32, name="back", tag="back")
+            back = bank_of(BACK_BANKS[half])
             for a in range(BANK // P):
                 nc.tensor.transpose(back[:, a * P:(a + 1) * P], total[:, a * P:(a + 1) * P], ident[:])
             return back
@@ -193,7 +211,7 @@ def tile_moe_mlr_relu_kernel(
 
         for b in range(last):
             scatter(b, zs[b])
-            sums = [psum_sum.tile([P, BANK], F32, name="sums", tag="sums") for half in range(HALVES)]
+            sums = [bank_of(tag) for tag in SUM_BANKS]
             add_turned(sums, windows[b % 2], True, False)
             for r in range(TOP):
                 add_choice(sums, b, r, False)
@@ -202,17 +220,17 @@ def tile_moe_mlr_relu_kernel(
                     total = keep.tile([P, BANK], F32, name="lent", tag="lent")
                 else:
                     total = stage.tile([P, BANK], F32, name="total")
-                back = turn_back(bank, total)
+                back = turn_back(half, bank, total)
                 result = stage.tile([P, BANK], F32, name="result")
                 nc.scalar.copy(result[:], back[:])
                 nc.sync.dma_start(out[P * b:P * (b + 1), half * BANK:(half + 1) * BANK], result[:])
 
-        sums = [psum_sum.tile([P, BANK], F32, name="sums", tag="sums") for half in range(HALVES)]
+        sums = [bank_of(tag) for tag in SUM_BANKS]
         z_last = adapter_rows(last, "lent")
         for r in range(TOP):
             add_choice(sums, last, r, r == 0)
         scatter(last, z_last)
-        backs = [turn_back(bank, stage.tile([P, BANK], F32, name="total")) for bank in sums]
+        backs = [turn_back(half, bank, stage.tile([P, BANK], F32, name="total")) for half, bank in enumerate(sums)]
         for t0 in range(0, T, LAST_STORE):
             finished = keep.tile([P, LAST_STORE], F32, name=f"finished{t0}")
             half, c0 = divmod(t0, BANK)

@@ -83,7 +83,8 @@ def tile_moe_mlr_relu_kernel(
         windows = [keep.tile([P, T], F32, name=f"window{a}") for a in range(2)]
         y = [keep.tile([P, SLOTS], F32, name=f"y{b}") for b in range(BLOCKS)]
 
-        for scales in (x_s[:, :T], x_s[:, T:], wa_s[:], w_s[:], wb_s[:]):
+        nc.gpsimd.memset(x_s[:, :T].bitcast(I32), 0)
+        for scales in (x_s[:, T:], wa_s[:], wb_s[:], w_s[:]):
             nc.vector.memset(scales.bitcast(I32), 0)
         make_identity(nc, ident[:])
         for window in windows:

@@ -121,9 +121,8 @@ def tile_moe_mlr_relu_kernel(
 
         columns = PIECE // LIST_ROWS
         pieces = [offs_sb[:, c * columns:(c + 1) * columns] for c in range(PIECES)]
-        halves = [offs_sb[:, u * 2 * columns:(u + 1) * 2 * columns] for u in range(2)]
         xa_s = gather_scales(offs2_sb[:], shared.tile([P, ADAPTER_SLOTS], U8, name="xa_s", offset=SECOND, align_bytes=64))
-        xe_s = [gather_scales(halves[0], keep.tile([P, SLOTS // 2], U8, name="xe_s0", align_bytes=64))]
+        first_s = gather_scales(pieces[0], keep.tile([P, PIECE], U8, name="first_s", align_bytes=64))
         xe_w = []
         xa_w = gather_words(offs2_sb[:], keep.tile([P, ADAPTER_SLOTS], U32, name="xa_w", align_bytes=64))
         for c in range(PIECES - 1):
@@ -148,9 +147,12 @@ def tile_moe_mlr_relu_kernel(
             h_pairs = h_in[:, 4 * D * f:4 * D * (f + 1)].bitcast(F32)
             nc.scalar.copy(h_pairs.rearrange("p (a m u) -> p a m u", a=D // P, u=2),
                            turned.rearrange("p a u m -> p a m u"))
-        xe_s.append(gather_scales(halves[1], shared.tile([P, SLOTS // 2], U8, name="xe_s1", offset=SECOND, align_bytes=64)))
+        middle_s = gather_scales(offs_sb[:, columns:3 * columns],
+                                 shared.tile([P, 2 * PIECE], U8, name="middle_s", offset=SECOND, align_bytes=64))
         nc.vector.quantize_mx(out=h_w[:].bitcast(FP8X4), scales=h_s[:], in_=h_in[:])
 
+        last_s = gather_scales(pieces[-1], shared.tile([P, PIECE], U8, name="last_s", offset=4 * PIECE, align_bytes=64))
+        xe_s = [first_s[:], middle_s[:, :PIECE], middle_s[:, PIECE:], last_s[:]]
         xe_w.append(gather_words(pieces[-1], shared.tile([P, PIECE], U32, name="xe_w_last", offset=0, align_bytes=64)))
 
         def adapter_rows(b, tag):
@@ -176,7 +178,7 @@ def tile_moe_mlr_relu_kernel(
                 nc.tensor.matmul_mx(bank[:, side * C:(side + 1) * C],
                                     lhsT=w_w[c][:, place, 2 * P * b:2 * P * (b + 1)].bitcast(FP4X4),
                                     lhsT_scale=w_s[:, e, P * b:P * (b + 1)],
-                                    rhs=xe_w[c][:, slots].bitcast(FP8X4), rhs_scale=xe_s[e // (E // 2)][:, (e % (E // 2)) * C:(e % (E // 2) + 1) * C],
+                                    rhs=xe_w[c][:, slots].bitcast(FP8X4), rhs_scale=xe_s[c][:, slots],
                                     start=True, stop=True)
             nc.scalar.copy(y[b][:, expert_pair * BANK:(expert_pair + 1) * BANK], bank[:])
 

@@ -83,7 +83,6 @@ def tile_moe_mlr_relu_kernel(
         windows = [keep.tile([P, T], F32, name=f"window{a}") for a in range(2)]
         y = [keep.tile([P, SLOTS], F32, name=f"y{b}") for b in range(BLOCKS)]
 
-        nc.gpsimd.memset(x_s[:, :T].bitcast(I32), 0)
         for scales in (x_s[:, T:], wa_s[:], wb_s[:], w_s[:]):
             nc.vector.memset(scales.bitcast(I32), 0)
         make_identity(nc, ident[:])
@@ -91,10 +90,11 @@ def tile_moe_mlr_relu_kernel(
             nc.scalar.activation(window[:], ident[:, 0:1].to_broadcast([P, T]), RELU, scale=0.0)
 
         nc.sync.dma_start(offs2_sb[:], offs2)
-        x_scale_rows = x_scales[0].rearrange("(q r) t -> r q t", r=4)
-        for r in range(4):
-            queue = nc.sync if r < 2 else nc.scalar
-            queue.dma_start(x_s[r:P:32, :T].bitcast(I32), x_scale_rows[r].bitcast(I32))
+        x_scale_rows = x_scales[0].rearrange("(q r) t -> q r t", r=4)
+        for q in range(4):
+            queue = nc.sync if q < 2 else nc.scalar
+            queue.dma_start(x_s[32 * q:32 * (q + 1), :T].bitcast(I32),
+                            x_scale_rows[q].bitcast(I32).partition_broadcast(8))
         nc.sync.dma_start(offs_sb[:], offs)
         nc.sync.dma_start(x_w[:], x_words[0].rearrange("p t d -> p (t d)").bitcast(I32))
         nc.sync.dma_start(wa_w[:].bitcast(I32), wa_words[:, 0].rearrange("f p n -> p f n").bitcast(I32))

@@ -28,7 +28,8 @@ HALVES = T // BANK
 PIECE_EXPERTS = 3
 PIECE = PIECE_EXPERTS * C
 PIECES = E // PIECE_EXPERTS
-LAST_STORE = 256
+EARLY = 384
+STEP = 256
 PRODUCT_BANKS = ("mm0", "mm1", "mm2", "mm3")
 SUM_BANKS = ("sum0", "sum1")
 BACK_BANKS = ("back0", "back1")
@@ -80,7 +81,7 @@ def tile_moe_mlr_relu_kernel(
         gate_sb = [keep.tile([P, T], F32, name=f"gate_sb{r}") for r in range(TOP)]
         gate2_sb = keep.tile([P, ADAPTER_SLOTS], F32, name="gate2_sb")
         ident = keep.tile([P, P], F32, name="ident")
-        windows = [keep.tile([P, T], F32, name=f"window{a}") for a in range(2)]
+        windows = [keep.tile([P, T], F32, name=f"window{a}") for a in range(3)]
         y = [keep.tile([P, SLOTS], F32, name=f"y{b}") for b in range(BLOCKS)]
 
         for scales in (x_s[:, T:], wa_s[:], wb_s[:], w_s[:]):
@@ -167,7 +168,7 @@ def tile_moe_mlr_relu_kernel(
             return z
 
         def scatter(b, z):
-            nc.vector.tensor_tensor(windows[b % 2][:].indirect(offs2_sb[:]), z[:], gate2_sb[:], MULT)
+            nc.vector.tensor_tensor(windows[b % 2 if b < BLOCKS - 1 else 2][:].indirect(offs2_sb[:]), z[:], gate2_sb[:], MULT)
 
         def expert_rows(b, expert_pair):
             bank = product_bank(ring(b))
@@ -207,8 +208,7 @@ def tile_moe_mlr_relu_kernel(
         for b in range(BLOCKS):
             for expert_pair in range(early_pairs):
                 expert_rows(b, expert_pair)
-            if b < last:
-                zs.append(adapter_rows(b, f"z{b}"))
+            zs.append(adapter_rows(b, f"z{b}"))
             for expert_pair in range(early_pairs, E // 2):
                 expert_rows(b, expert_pair)
 
@@ -219,24 +219,66 @@ def tile_moe_mlr_relu_kernel(
             for r in range(TOP):
                 add_choice(sums, b, r, False)
             for half, bank in enumerate(sums):
-                if b == last - 1 and half == HALVES - 1:
-                    total = keep.tile([P, BANK], F32, name="lent", tag="lent")
-                else:
-                    total = stage.tile([P, BANK], F32, name="total")
+                total = stage.tile([P, BANK], F32, name="total")
                 back = turn_back(half, bank, total)
                 result = stage.tile([P, BANK], F32, name="result")
                 nc.scalar.copy(result[:], back[:])
                 nc.sync.dma_start(out[P * b:P * (b + 1), half * BANK:(half + 1) * BANK], result[:])
 
-        sums = [bank_of(tag) for tag in SUM_BANKS]
-        z_last = adapter_rows(last, "lent")
-        for r in range(TOP):
-            add_choice(sums, last, r, r == 0)
-        scatter(last, z_last)
-        backs = [turn_back(half, bank, stage.tile([P, BANK], F32, name="total")) for half, bank in enumerate(sums)]
-        for t0 in range(0, T, LAST_STORE):
-            finished = keep.tile([P, LAST_STORE], F32, name=f"finished{t0}")
-            half, c0 = divmod(t0, BANK)
-            nc.vector.tensor_tensor(finished[:], backs[half][:, c0:c0 + LAST_STORE],
-                                    windows[last % 2][:, t0:t0 + LAST_STORE], ADD)
-            nc.sync.dma_start(out[P * last:P * (last + 1), t0:t0 + LAST_STORE], finished[:])
+        rows = slice(P * last, P * (last + 1))
+        window = windows[2]
+
+        def fetch(r, t0, t1, term):
+            entries = pos_sb[r][:, t0 // LIST_ROWS:t1 // LIST_ROWS]
+            nc.vector.tensor_tensor(term[:], y[last][:].indirect(entries), gate_sb[r][:, t0:t1], MULT)
+            return term
+
+        def new_term(r, t0, t1):
+            return keep.tile([P, t1 - t0], F32, name=f"last_term{r}_{t0}")
+
+        def add_range(bank, term, first, final):
+            count = term.shape[1] // P
+            for a in range(count):
+                nc.tensor.matmul(bank[:, a * P:(a + 1) * P], term[:, a * P:(a + 1) * P], ident[:], is_transpose=True,
+                                 start=(first and a == 0), stop=(final and a == count - 1))
+
+        def back_range(bank, width, tag, total):
+            nc.scalar.copy(total[:, :width], bank[:, :width])
+            back = bank_of(tag)
+            for a in range(width // P):
+                nc.tensor.transpose(back[:, a * P:(a + 1) * P], total[:, a * P:(a + 1) * P], ident[:])
+            return back
+
+        ranges = ((0, EARLY), (EARLY, EARLY + STEP), (EARLY + STEP, T))
+        scatter(last, zs[last])
+        sums = [bank_of(tag) for tag in SUM_BANKS + BACK_BANKS[:1]]
+        first_choice = fetch(0, 0, T, new_term(0, 0, T))
+        for bank, (t0, t1) in zip(sums, ranges):
+            add_range(bank, window[:, t0:t1], True, False)
+        for bank, (t0, t1) in zip(sums, ranges):
+            add_range(bank, first_choice[:, t0:t1], False, False)
+        for r in (1, 2):
+            add_range(sums[0], fetch(r, 0, EARLY, new_term(r, 0, EARLY))[:], False, r == 2)
+        back = back_range(sums[0], EARLY, BACK_BANKS[1], stage.tile([P, BANK], F32, name="total"))
+        result = stage.tile([P, BANK], F32, name="result")
+        nc.scalar.copy(result[:, :EARLY], back[:, :EARLY])
+        nc.sync.dma_start(out[rows, :EARLY], result[:, :EARLY])
+        backs = []
+        for bank, (t0, t1), tag in zip(sums[1:], ranges[1:], PRODUCT_BANKS):
+            add_range(bank, fetch(1, t0, t1, new_term(1, t0, t1))[:], False, True)
+            total = keep.tile([P, t1 - t0], F32, name=f"late_total{t0}", tag=f"late_total{t0}")
+            backs.append(back_range(bank, t1 - t0, tag, total))
+
+        def finish(back, c0, term, t0):
+            width = term.shape[1]
+            finished = keep.tile([P, width], F32, name=f"finished{t0}")
+            nc.vector.tensor_tensor(finished[:], back[:, c0:c0 + width], term[:], ADD)
+            nc.sync.dma_start(out[rows, t0:t0 + width], finished[:])
+
+        t1, t2, t3 = EARLY, EARLY + STEP, EARLY + 2 * STEP
+        term1 = fetch(2, t1, t2, new_term(2, t1, t2))
+        term2 = fetch(2, t2, t3, new_term(2, t2, t3))
+        finish(backs[0], 0, term1, t1)
+        term3 = fetch(2, t3, T, keep.tile([P, T - t3], F32, name="term3", tag=f"late_total{t1}"))
+        finish(backs[1], 0, term2, t2)
+        finish(backs[1], STEP, term3, t3)

@@ -28,7 +28,7 @@ HALVES = T // BANK
 PIECE_EXPERTS = 3
 PIECE = PIECE_EXPERTS * C
 PIECES = E // PIECE_EXPERTS
-EARLY = 384
+EARLY = 256
 STEP = 256
 PRODUCT_BANKS = ("mm0", "mm1", "mm2", "mm3")
 SUM_BANKS = ("sum0", "sum1")
@@ -84,6 +84,7 @@ def tile_moe_mlr_relu_kernel(
         windows = [keep.tile([P, T], F32, name=f"window{a}") for a in range(3)]
         y = [keep.tile([P, SLOTS], F32, name=f"y{b}") for b in range(BLOCKS)]
 
+        nc.gpsimd.memset(x_s[:, :T].bitcast(I32), 0)
         for scales in (x_s[:, T:], wa_s[:], wb_s[:], w_s[:]):
             nc.vector.memset(scales.bitcast(I32), 0)
         make_identity(nc, ident[:])
@@ -91,11 +92,10 @@ def tile_moe_mlr_relu_kernel(
             nc.scalar.activation(window[:], ident[:, 0:1].to_broadcast([P, T]), RELU, scale=0.0)
 
         nc.sync.dma_start(offs2_sb[:], offs2)
-        x_scale_rows = x_scales[0].rearrange("(q r) t -> q r t", r=4)
-        for q in range(4):
-            queue = nc.sync if q < 2 else nc.scalar
-            queue.dma_start(x_s[32 * q:32 * (q + 1), :T].bitcast(I32),
-                            x_scale_rows[q].bitcast(I32).partition_broadcast(8))
+        x_scale_rows = x_scales[0].rearrange("(q r) t -> r q t", r=4)
+        for r in range(4):
+            queue = nc.sync if r < 2 else nc.scalar
+            queue.dma_start(x_s[r:P:32, :T].bitcast(I32), x_scale_rows[r].bitcast(I32))
         nc.sync.dma_start(offs_sb[:], offs)
         nc.sync.dma_start(x_w[:], x_words[0].rearrange("p t d -> p (t d)").bitcast(I32))
         nc.sync.dma_start(wa_w[:].bitcast(I32), wa_words[:, 0].rearrange("f p n -> p f n").bitcast(I32))
@@ -242,43 +242,47 @@ def tile_moe_mlr_relu_kernel(
                 nc.tensor.matmul(bank[:, a * P:(a + 1) * P], term[:, a * P:(a + 1) * P], ident[:], is_transpose=True,
                                  start=(first and a == 0), stop=(final and a == count - 1))
 
-        def back_range(bank, width, tag, total):
-            nc.scalar.copy(total[:, :width], bank[:, :width])
+        def finish(back, term, t0):
+            width = term.shape[1]
+            finished = keep.tile([P, width], F32, name=f"finished{t0}")
+            nc.vector.tensor_tensor(finished[:], back[:, :width], term[:], ADD)
+            nc.sync.dma_start(out[rows, t0:t0 + width], finished[:])
+
+        def copy_out(bank, width, name):
+            total = keep.tile([P, width], F32, name=name, tag=name)
+            nc.scalar.copy(total[:], bank[:, :width])
+            return total
+
+        def turn(total, tag):
             back = bank_of(tag)
-            for a in range(width // P):
+            for a in range(total.shape[1] // P):
                 nc.tensor.transpose(back[:, a * P:(a + 1) * P], total[:, a * P:(a + 1) * P], ident[:])
             return back
 
-        ranges = ((0, EARLY), (EARLY, EARLY + STEP), (EARLY + STEP, T))
-        scatter(last, zs[last])
-        sums = [bank_of(tag) for tag in SUM_BANKS + BACK_BANKS[:1]]
-        first_choice = fetch(0, 0, T, new_term(0, 0, T))
-        for bank, (t0, t1) in zip(sums, ranges):
-            add_range(bank, window[:, t0:t1], True, False)
-        for bank, (t0, t1) in zip(sums, ranges):
-            add_range(bank, first_choice[:, t0:t1], False, False)
-        for r in (1, 2):
-            add_range(sums[0], fetch(r, 0, EARLY, new_term(r, 0, EARLY))[:], False, r == 2)
-        back = back_range(sums[0], EARLY, BACK_BANKS[1], stage.tile([P, BANK], F32, name="total"))
-        result = stage.tile([P, BANK], F32, name="result")
-        nc.scalar.copy(result[:, :EARLY], back[:, :EARLY])
-        nc.sync.dma_start(out[rows, :EARLY], result[:, :EARLY])
-        backs = []
-        for bank, (t0, t1), tag in zip(sums[1:], ranges[1:], PRODUCT_BANKS):
-            add_range(bank, fetch(1, t0, t1, new_term(1, t0, t1))[:], False, True)
-            total = keep.tile([P, t1 - t0], F32, name=f"late_total{t0}", tag=f"late_total{t0}")
-            backs.append(back_range(bank, t1 - t0, tag, total))
-
-        def finish(back, c0, term, t0):
-            width = term.shape[1]
-            finished = keep.tile([P, width], F32, name=f"finished{t0}")
-            nc.vector.tensor_tensor(finished[:], back[:, c0:c0 + width], term[:], ADD)
-            nc.sync.dma_start(out[rows, t0:t0 + width], finished[:])
-
         t1, t2, t3 = EARLY, EARLY + STEP, EARLY + 2 * STEP
+        ranges = ((t1, t2), (t2, T), (0, t1))
+        scatter(last, zs[last])
+        sums = [bank_of(tag) for tag in (SUM_BANKS[0], SUM_BANKS[1], BACK_BANKS[0])]
+        first_choice = fetch(0, 0, T, new_term(0, 0, T))
+        for bank, (t0, end) in zip(sums, ranges):
+            add_range(bank, window[:, t0:end], True, False)
+        for bank, (t0, end) in zip(sums, ranges):
+            add_range(bank, first_choice[:, t0:end], False, False)
+        second_late = fetch(1, t1, T, new_term(1, t1, T))
+        add_range(sums[0], second_late[:, :STEP], False, True)
+        add_range(sums[1], second_late[:, STEP:], False, True)
+        back1 = turn(copy_out(sums[0], STEP, "total1")[:], PRODUCT_BANKS[0])
+        for r in (1, 2):
+            add_range(sums[2], fetch(r, 0, t1, new_term(r, 0, t1))[:], False, r == 2)
+        total23 = copy_out(sums[1], T - t2, "total23")
+        back2 = turn(total23[:, :STEP], PRODUCT_BANKS[1])
+        back0 = turn(copy_out(sums[2], t1, "total0")[:], BACK_BANKS[1])
+        nc.scalar.dma_start(out[rows, :t1], copy_out(back0, t1, "result0")[:])
+        back3 = turn(total23[:, STEP:], BACK_BANKS[0])
+
         term1 = fetch(2, t1, t2, new_term(2, t1, t2))
         term2 = fetch(2, t2, t3, new_term(2, t2, t3))
-        finish(backs[0], 0, term1, t1)
-        term3 = fetch(2, t3, T, keep.tile([P, T - t3], F32, name="term3", tag=f"late_total{t1}"))
-        finish(backs[1], 0, term2, t2)
-        finish(backs[1], STEP, term3, t3)
+        finish(back1, term1, t1)
+        term3 = fetch(2, t3, T, keep.tile([P, T - t3], F32, name="term3", tag="total1"))
+        finish(back2, term2, t2)
+        finish(back3, term3, t3)

@@ -259,30 +259,25 @@ def tile_moe_mlr_relu_kernel(
                 nc.tensor.transpose(back[:, a * P:(a + 1) * P], total[:, a * P:(a + 1) * P], ident[:])
             return back
 
-        t1, t2, t3 = EARLY, EARLY + STEP, EARLY + 2 * STEP
-        ranges = ((t1, t2), (t2, T), (0, t1))
+        steps = [(t0, t0 + STEP) for t0 in range(EARLY, T, STEP)]
         scatter(last, zs[last])
-        sums = [bank_of(tag) for tag in (SUM_BANKS[0], SUM_BANKS[1], BACK_BANKS[0])]
-        first_choice = fetch(0, 0, T, new_term(0, 0, T))
-        for bank, (t0, end) in zip(sums, ranges):
-            add_range(bank, window[:, t0:end], True, False)
-        for bank, (t0, end) in zip(sums, ranges):
-            add_range(bank, first_choice[:, t0:end], False, False)
-        second_late = fetch(1, t1, T, new_term(1, t1, T))
-        add_range(sums[0], second_late[:, :STEP], False, True)
-        add_range(sums[1], second_late[:, STEP:], False, True)
-        back1 = turn(copy_out(sums[0], STEP, "total1")[:], PRODUCT_BANKS[0])
-        for r in (1, 2):
-            add_range(sums[2], fetch(r, 0, t1, new_term(r, 0, t1))[:], False, r == 2)
-        total23 = copy_out(sums[1], T - t2, "total23")
-        back2 = turn(total23[:, :STEP], PRODUCT_BANKS[1])
-        back0 = turn(copy_out(sums[2], t1, "total0")[:], BACK_BANKS[1])
-        nc.scalar.dma_start(out[rows, :t1], copy_out(back0, t1, "result0")[:])
-        back3 = turn(total23[:, STEP:], BACK_BANKS[0])
+        sums = [bank_of(tag) for tag in SUM_BANKS + BACK_BANKS]
+        for bank, (t0, t1) in zip(sums, [(0, EARLY)] + steps):
+            add_range(bank, window[:, t0:t1], True, False)
+        for r in range(TOP):
+            add_range(sums[0], fetch(r, 0, EARLY, new_term(r, 0, EARLY))[:], False, r == TOP - 1)
+        back = turn(copy_out(sums[0], EARLY, "early_total")[:], PRODUCT_BANKS[0])
+        nc.sync.dma_start(out[rows, :EARLY], copy_out(back, EARLY, "early_result")[:])
+        first_late = fetch(0, EARLY, T, new_term(0, EARLY, T))
+        for bank, (t0, t1) in zip(sums[1:], steps):
+            add_range(bank, first_late[:, t0 - EARLY:t1 - EARLY], False, False)
+        backs = []
+        for bank, (t0, t1), tag in zip(sums[1:], steps, PRODUCT_BANKS[1:]):
+            add_range(bank, fetch(1, t0, t1, new_term(1, t0, t1))[:], False, True)
+            backs.append(turn(copy_out(bank, STEP, f"total{t0}")[:], tag))
 
-        term1 = fetch(2, t1, t2, new_term(2, t1, t2))
-        term2 = fetch(2, t2, t3, new_term(2, t2, t3))
-        finish(back1, term1, t1)
-        term3 = fetch(2, t3, T, keep.tile([P, T - t3], F32, name="term3", tag="total1"))
-        finish(back2, term2, t2)
-        finish(back3, term3, t3)
+        terms = [fetch(2, t0, t1, new_term(2, t0, t1)) for t0, t1 in steps[:2]]
+        finish(backs[0], terms[0], steps[0][0])
+        terms.append(fetch(2, *steps[2], keep.tile([P, STEP], F32, name="last_step", tag=f"total{EARLY}")))
+        for a in (1, 2):
+            finish(backs[a], terms[a], steps[a][0])

@@ -33,7 +33,8 @@ STEP = 256
 PRODUCT_BANKS = ("mm0", "mm1", "mm2", "mm3")
 SUM_BANKS = ("sum0", "sum1")
 BACK_BANKS = ("back0", "back1")
-SECOND = 8 * ADAPTER_SLOTS
+HALF_H = 8 * F * P
+SECOND = HALF_H + 4 * PIECE
 
 
 def load_scale_rows(nc, tile, rows):
@@ -85,7 +86,7 @@ def tile_moe_mlr_relu_kernel(
         y = [keep.tile([P, SLOTS], F32, name=f"y{b}") for b in range(BLOCKS)]
 
         nc.gpsimd.memset(x_s[:, :T].bitcast(I32), 0)
-        for scales in (x_s[:, T:], wa_s[:], wb_s[:], w_s[:]):
+        for scales in (x_s[:, T:], wa_s[:], wb_s[:]):
             nc.vector.memset(scales.bitcast(I32), 0)
         make_identity(nc, ident[:])
         for window in windows:
@@ -110,7 +111,10 @@ def tile_moe_mlr_relu_kernel(
             nc.sync.dma_start(pos_sb[r][:], pos)
             nc.sync.dma_start(gate_sb[r][:], gate[r])
             if r == 0:
-                load_scale_rows(nc, w_s, w_scales[:, 0])
+                for row in range(16):
+                    q, place = divmod(row, 4)
+                    nc.sync.dma_start(w_s[32 * q + place:32 * (q + 1):4, :, :].bitcast(I32),
+                                      w_scales[:, 0, row, :].bitcast(I32).partition_broadcast(8))
 
         def gather_scales(entries, scales):
             nc.vector.tensor_copy(scales[:], x_s[:].indirect(entries))
@@ -129,9 +133,10 @@ def tile_moe_mlr_relu_kernel(
         for c in range(PIECES - 1):
             xe_w.append(gather_words(pieces[c], keep.tile([P, PIECE], U32, name=f"xe_w{c}", align_bytes=64)))
 
-        h_w = keep.tile([P, ADAPTER_SLOTS], U32, name="h_w", align_bytes=64)
-        h_s = keep.tile([P, ADAPTER_SLOTS], U8, name="h_s", align_bytes=64)
-        h_in = shared.tile([P, 4 * ADAPTER_SLOTS], BF16, name="h_in", offset=0, align_bytes=64)
+        h_w = [keep.tile([P, F * P], U32, name=f"h_w{a}", align_bytes=64) for a in range(D // P)]
+        h_s = [keep.tile([P, F * P], U8, name=f"h_s{a}", align_bytes=64) for a in range(D // P)]
+        h_in = [shared.tile([P, 4 * F * P], BF16, name=f"h_in{a}", offset=HALF_H * a, align_bytes=64)
+                for a in range(D // P)]
         for f in range(F):
             turned = bank_of(BACK_BANKS[f])[:].rearrange("p (a u m) -> p a u m", a=D // P, u=2)
             for a in range(D // P):
@@ -145,24 +150,27 @@ def tile_moe_mlr_relu_kernel(
                 pairs = h_rows[:].bitcast(F32)
                 for u in range(2):
                     nc.tensor.transpose(turned[:, a, u, :], pairs[:, u * P:(u + 1) * P], ident[:])
-            h_pairs = h_in[:, 4 * D * f:4 * D * (f + 1)].bitcast(F32)
-            nc.scalar.copy(h_pairs.rearrange("p (a m u) -> p a m u", a=D // P, u=2),
-                           turned.rearrange("p a u m -> p a m u"))
+            for a in range(D // P):
+                h_pairs = h_in[a][:, 4 * P * f:4 * P * (f + 1)].bitcast(F32)
+                nc.scalar.copy(h_pairs.rearrange("p (m u) -> p m u", u=2), turned[:, a].rearrange("p u m -> p m u"))
         middle_s = gather_scales(offs_sb[:, columns:3 * columns],
                                  shared.tile([P, 2 * PIECE], U8, name="middle_s", offset=SECOND, align_bytes=64))
-        nc.vector.quantize_mx(out=h_w[:].bitcast(FP8X4), scales=h_s[:], in_=h_in[:])
+        for a in range(D // P):
+            nc.vector.quantize_mx(out=h_w[a][:].bitcast(FP8X4), scales=h_s[a][:], in_=h_in[a][:])
 
-        last_s = gather_scales(pieces[-1], shared.tile([P, PIECE], U8, name="last_s", offset=4 * PIECE, align_bytes=64))
+        last_s = gather_scales(pieces[-1], shared.tile([P, PIECE], U8, name="last_s", offset=0, align_bytes=64))
         xe_s = [first_s[:], middle_s[:, :PIECE], middle_s[:, PIECE:], last_s[:]]
-        xe_w.append(gather_words(pieces[-1], shared.tile([P, PIECE], U32, name="xe_w_last", offset=0, align_bytes=64)))
+        xe_w.append(gather_words(pieces[-1], shared.tile([P, PIECE], U32, name="xe_w_last", offset=HALF_H, align_bytes=64)))
 
         def adapter_rows(b, tag):
             bank = product_bank(ring(b))
             for f in range(F):
-                slots = slice(f * D, (f + 1) * D)
-                nc.tensor.matmul_mx(bank[:, slots], lhsT=wb_w[:, f, 2 * P * b:2 * P * (b + 1)].bitcast(FP4X4),
-                                    lhsT_scale=wb_s[:, f, P * b:P * (b + 1)],
-                                    rhs=h_w[:, slots].bitcast(FP8X4), rhs_scale=h_s[:, slots], start=True, stop=True)
+                for a in range(D // P):
+                    slots = slice(f * P, (f + 1) * P)
+                    nc.tensor.matmul_mx(bank[:, f * D + a * P:f * D + (a + 1) * P],
+                                        lhsT=wb_w[:, f, 2 * P * b:2 * P * (b + 1)].bitcast(FP4X4),
+                                        lhsT_scale=wb_s[:, f, P * b:P * (b + 1)], rhs=h_w[a][:, slots].bitcast(FP8X4),
+                                        rhs_scale=h_s[a][:, slots], start=True, stop=True)
             z = keep.tile([P, ADAPTER_SLOTS], F32, name=f"z{b}", tag=tag)
             nc.scalar.copy(z[:], bank[:])
             return z

@@ -30,6 +30,8 @@ PIECE = PIECE_EXPERTS * C
 PIECES = E // PIECE_EXPERTS
 EARLY = 256
 STEP = 256
+SCATTER_CUTS = (0, 160, 320, 512)
+LAST_SCATTER_CUTS = (0, 0, 192, 512)
 PRODUCT_BANKS = ("mm0", "mm1", "mm2", "mm3")
 SUM_BANKS = ("sum0", "sum1")
 BACK_BANKS = ("back0", "back1")
@@ -82,7 +84,7 @@ def tile_moe_mlr_relu_kernel(
         gate_sb = [keep.tile([P, T], F32, name=f"gate_sb{r}") for r in range(TOP)]
         gate2_sb = keep.tile([P, ADAPTER_SLOTS], F32, name="gate2_sb")
         ident = keep.tile([P, P], F32, name="ident")
-        windows = [keep.tile([P, T], F32, name=f"window{a}") for a in range(3)]
+        windows = [keep.tile([P, T], F32, name=f"window{a}") for a in range(BLOCKS)]
         y = [keep.tile([P, SLOTS], F32, name=f"y{b}") for b in range(BLOCKS)]
 
         nc.gpsimd.memset(x_s[:, :T].bitcast(I32), 0)
@@ -175,8 +177,9 @@ def tile_moe_mlr_relu_kernel(
             nc.scalar.copy(z[:], bank[:])
             return z
 
-        def scatter(b, z):
-            nc.vector.tensor_tensor(windows[b % 2 if b < BLOCKS - 1 else 2][:].indirect(offs2_sb[:]), z[:], gate2_sb[:], MULT)
+        def scatter(b, m0, m1):
+            entries = offs2_sb[:, m0 // LIST_ROWS:m1 // LIST_ROWS]
+            nc.vector.tensor_tensor(windows[b][:].indirect(entries), zs[b][:, m0:m1], gate2_sb[:, m0:m1], MULT)
 
         def expert_rows(b, expert_pair):
             bank = product_bank(ring(b))
@@ -214,18 +217,24 @@ def tile_moe_mlr_relu_kernel(
         last = BLOCKS - 1
         zs = []
         for b in range(BLOCKS):
+            if b > 0:
+                zs.append(adapter_rows(b, f"z{b}"))
             for expert_pair in range(early_pairs):
                 expert_rows(b, expert_pair)
-            zs.append(adapter_rows(b, f"z{b}"))
+            if b == 0:
+                zs.append(adapter_rows(b, f"z{b}"))
             for expert_pair in range(early_pairs, E // 2):
                 expert_rows(b, expert_pair)
 
+        scatter(0, 0, ADAPTER_SLOTS)
         for b in range(last):
-            scatter(b, zs[b])
             sums = [bank_of(tag) for tag in SUM_BANKS]
-            add_turned(sums, windows[b % 2], True, False)
+            add_turned(sums, windows[b], True, False)
             for r in range(TOP):
                 add_choice(sums, b, r, False)
+                cuts = SCATTER_CUTS if b + 1 < last else LAST_SCATTER_CUTS
+                if cuts[r] < cuts[r + 1]:
+                    scatter(b + 1, cuts[r], cuts[r + 1])
             for half, bank in enumerate(sums):
                 total = stage.tile([P, BANK], F32, name="total")
                 back = turn_back(half, bank, total)
@@ -234,7 +243,7 @@ def tile_moe_mlr_relu_kernel(
                 nc.sync.dma_start(out[P * b:P * (b + 1), half * BANK:(half + 1) * BANK], result[:])
 
         rows = slice(P * last, P * (last + 1))
-        window = windows[2]
+        window = windows[last]
 
         def fetch(r, t0, t1, term):
             entries = pos_sb[r][:, t0 // LIST_ROWS:t1 // LIST_ROWS]
@@ -268,7 +277,6 @@ def tile_moe_mlr_relu_kernel(
             return back
 
         steps = [(t0, t0 + STEP) for t0 in range(EARLY, T, STEP)]
-        scatter(last, zs[last])
         sums = [bank_of(tag) for tag in SUM_BANKS + BACK_BANKS]
         for bank, (t0, t1) in zip(sums, [(0, EARLY)] + steps):
             add_range(bank, window[:, t0:t1], True, False)

@@ -31,7 +31,7 @@ PIECES = E // PIECE_EXPERTS
 EARLY = 256
 STEP = 256
 SCATTER_CUTS = (0, 160, 320, 512)
-LAST_SCATTER_CUTS = (0, 0, 192, 512)
+LAST_SCATTER_CUTS = (0, 0, 0, 512)
 PRODUCT_BANKS = ("mm0", "mm1", "mm2", "mm3")
 SUM_BANKS = ("sum0", "sum1")
 BACK_BANKS = ("back0", "back1")

@@ -24,19 +24,19 @@ LIST_ROWS = 16
 SLOTS = E * C
 ADAPTER_SLOTS = F * D
 BLOCKS = N // P
-HALVES = T // BANK
+LAST = BLOCKS - 1
 PIECE_EXPERTS = 3
 PIECE = PIECE_EXPERTS * C
 PIECES = E // PIECE_EXPERTS
+PARTS = ADAPTER_SLOTS // P
 EARLY = 256
 STEP = 256
-SCATTER_CUTS = (0, 160, 320, 512)
-LAST_SCATTER_CUTS = (0, 0, 0, 512)
 PRODUCT_BANKS = ("mm0", "mm1", "mm2", "mm3")
 SUM_BANKS = ("sum0", "sum1")
 BACK_BANKS = ("back0", "back1")
 HALF_H = 8 * F * P
 SECOND = HALF_H + 4 * PIECE
+THIRD = SECOND + 2 * PIECE
 
 
 def load_scale_rows(nc, tile, rows):
@@ -63,12 +63,10 @@ def tile_moe_mlr_relu_kernel(
 
         turns = []
 
-        def product_bank(ring):
+        def product_bank(b):
+            ring = PRODUCT_BANKS + SUM_BANKS if b < 2 else PRODUCT_BANKS
             turns.append(ring[len(turns) % len(ring)])
             return bank_of(turns[-1])
-
-        def ring(b):
-            return PRODUCT_BANKS + SUM_BANKS if b < 2 else PRODUCT_BANKS
 
         offs_sb = keep.tile([P, SLOTS // LIST_ROWS], U16, name="offs_sb")
         offs2_sb = keep.tile([P, ADAPTER_SLOTS // LIST_ROWS], U16, name="offs2_sb")
@@ -77,14 +75,15 @@ def tile_moe_mlr_relu_kernel(
         x_s = keep.tile([P, 2 * T], U8, name="x_s", align_bytes=64)
         wa_w = keep.tile([P, F, 2 * H], U8, name="wa_w", align_bytes=64)
         wa_s = keep.tile([P, F, H], U8, name="wa_s", align_bytes=64)
-        wb_w = keep.tile([P, F, 2 * N], U8, name="wb_w", align_bytes=64)
+        wb_first_w = shared.tile([P, F, 2 * P], U8, name="wb_first_w", offset=THIRD, align_bytes=64)
+        wb_w = keep.tile([P, F, 2 * (N - P)], U8, name="wb_w", align_bytes=64)
         wb_s = keep.tile([P, F, N], U8, name="wb_s", align_bytes=64)
         w_w = [keep.tile([P, PIECE_EXPERTS, 2 * N], U8, name=f"w_w{c}", align_bytes=64) for c in range(PIECES)]
         w_s = keep.tile([P, E, N], U8, name="w_s", align_bytes=64)
         gate_sb = [keep.tile([P, T], F32, name=f"gate_sb{r}") for r in range(TOP)]
         gate2_sb = keep.tile([P, ADAPTER_SLOTS], F32, name="gate2_sb")
         ident = keep.tile([P, P], F32, name="ident")
-        windows = [keep.tile([P, T], F32, name=f"window{a}") for a in range(BLOCKS)]
+        windows = [keep.tile([P, T], F32, name=f"window{b}") for b in range(BLOCKS)]
         y = [keep.tile([P, SLOTS], F32, name=f"y{b}") for b in range(BLOCKS)]
 
         nc.gpsimd.memset(x_s[:, :T].bitcast(I32), 0)
@@ -107,7 +106,9 @@ def tile_moe_mlr_relu_kernel(
         for c in range(PIECES):
             experts = w_words[PIECE_EXPERTS * c:PIECE_EXPERTS * (c + 1), 0]
             nc.sync.dma_start(w_w[c][:].bitcast(I32), experts.rearrange("e p n -> p e n").bitcast(I32))
-        nc.sync.dma_start(wb_w[:].bitcast(I32), wb_words[:, 0].rearrange("f p n -> p f n").bitcast(I32))
+        wb_rows = wb_words[:, 0].rearrange("f p n -> p f n")
+        nc.sync.dma_start(wb_first_w[:].bitcast(I32), wb_rows[:, :, :2 * P].bitcast(I32))
+        nc.sync.dma_start(wb_w[:].bitcast(I32), wb_rows[:, :, 2 * P:].bitcast(I32))
         nc.sync.dma_start(gate2_sb[:], gate2)
         for r, pos in enumerate((pos1, pos2, pos3)):
             nc.sync.dma_start(pos_sb[r][:], pos)
@@ -126,14 +127,17 @@ def tile_moe_mlr_relu_kernel(
             nc.vector.tensor_copy(words[:], x_w[:].bitcast(U32).indirect(entries))
             return words
 
-        columns = PIECE // LIST_ROWS
-        pieces = [offs_sb[:, c * columns:(c + 1) * columns] for c in range(PIECES)]
+        def slots_of(first, end):
+            return offs_sb[:, first * C // LIST_ROWS:end * C // LIST_ROWS]
+
         xa_s = gather_scales(offs2_sb[:], shared.tile([P, ADAPTER_SLOTS], U8, name="xa_s", offset=SECOND, align_bytes=64))
-        first_s = gather_scales(pieces[0], keep.tile([P, PIECE], U8, name="first_s", align_bytes=64))
-        xe_w = []
+        first_s = gather_scales(slots_of(0, PIECE_EXPERTS), keep.tile([P, PIECE], U8, name="first_s", align_bytes=64))
         xa_w = gather_words(offs2_sb[:], keep.tile([P, ADAPTER_SLOTS], U32, name="xa_w", align_bytes=64))
+        expert_w = []
         for c in range(PIECES - 1):
-            xe_w.append(gather_words(pieces[c], keep.tile([P, PIECE], U32, name=f"xe_w{c}", align_bytes=64)))
+            words = gather_words(slots_of(PIECE_EXPERTS * c, PIECE_EXPERTS * (c + 1)),
+                                 keep.tile([P, PIECE], U32, name=f"xe_w{c}", align_bytes=64))
+            expert_w.extend(words[:, place * C:(place + 1) * C] for place in range(PIECE_EXPERTS))
 
         h_w = [keep.tile([P, F * P], U32, name=f"h_w{a}", align_bytes=64) for a in range(D // P)]
         h_s = [keep.tile([P, F * P], U8, name=f"h_s{a}", align_bytes=64) for a in range(D // P)]
@@ -143,7 +147,7 @@ def tile_moe_mlr_relu_kernel(
             turned = bank_of(BACK_BANKS[f])[:].rearrange("p (a u m) -> p a u m", a=D // P, u=2)
             for a in range(D // P):
                 slots = slice(f * D + a * P, f * D + (a + 1) * P)
-                bank = product_bank(ring(0))
+                bank = product_bank(0)
                 nc.tensor.matmul_mx(bank[:], lhsT=xa_w[:, slots].bitcast(FP8X4), lhsT_scale=xa_s[:, slots],
                                     rhs=wa_w[:, f, :].bitcast(FP4X4), rhs_scale=wa_s[:, f, :], start=True, stop=True)
                 h_rows = stage.tile([P, H], BF16, name="h_rows")
@@ -155,145 +159,138 @@ def tile_moe_mlr_relu_kernel(
             for a in range(D // P):
                 h_pairs = h_in[a][:, 4 * P * f:4 * P * (f + 1)].bitcast(F32)
                 nc.scalar.copy(h_pairs.rearrange("p (m u) -> p m u", u=2), turned[:, a].rearrange("p u m -> p m u"))
-        middle_s = gather_scales(offs_sb[:, columns:3 * columns],
+        middle_s = gather_scales(slots_of(PIECE_EXPERTS, 3 * PIECE_EXPERTS),
                                  shared.tile([P, 2 * PIECE], U8, name="middle_s", offset=SECOND, align_bytes=64))
         for a in range(D // P):
             nc.vector.quantize_mx(out=h_w[a][:].bitcast(FP8X4), scales=h_s[a][:], in_=h_in[a][:])
 
-        last_s = gather_scales(pieces[-1], shared.tile([P, PIECE], U8, name="last_s", offset=0, align_bytes=64))
-        xe_s = [first_s[:], middle_s[:, :PIECE], middle_s[:, PIECE:], last_s[:]]
-        xe_w.append(gather_words(pieces[-1], shared.tile([P, PIECE], U32, name="xe_w_last", offset=HALF_H, align_bytes=64)))
+        last_s = gather_scales(slots_of(E - PIECE_EXPERTS, E),
+                               shared.tile([P, PIECE], U8, name="last_s", offset=0, align_bytes=64))
+        piece_s = [first_s[:], middle_s[:, :PIECE], middle_s[:, PIECE:], last_s[:]]
+        words = gather_words(slots_of(E - PIECE_EXPERTS, E - 1),
+                             shared.tile([P, PIECE - C], U32, name="xe_w_last", offset=HALF_H, align_bytes=64))
+        expert_w.extend(words[:, place * C:(place + 1) * C] for place in range(PIECE_EXPERTS - 1))
 
-        def adapter_rows(b, tag):
-            bank = product_bank(ring(b))
-            for f in range(F):
-                for a in range(D // P):
-                    slots = slice(f * P, (f + 1) * P)
-                    nc.tensor.matmul_mx(bank[:, f * D + a * P:f * D + (a + 1) * P],
-                                        lhsT=wb_w[:, f, 2 * P * b:2 * P * (b + 1)].bitcast(FP4X4),
-                                        lhsT_scale=wb_s[:, f, P * b:P * (b + 1)], rhs=h_w[a][:, slots].bitcast(FP8X4),
-                                        rhs_scale=h_s[a][:, slots], start=True, stop=True)
-            z = keep.tile([P, ADAPTER_SLOTS], F32, name=f"z{b}", tag=tag)
-            nc.scalar.copy(z[:], bank[:])
-            return z
+        z = [keep.tile([P, ADAPTER_SLOTS], F32, name=f"z{b}") for b in range(BLOCKS)]
 
-        def scatter(b, m0, m1):
+        def adapter_rows(b, first, end, bank):
+            for part in range(first, end):
+                f, a = divmod(part, D // P)
+                columns = wb_w[:, f, 2 * P * (b - 1):2 * P * b] if b > 0 else wb_first_w[:, f, :]
+                nc.tensor.matmul_mx(bank[:, part * P:(part + 1) * P], lhsT=columns.bitcast(FP4X4),
+                                    lhsT_scale=wb_s[:, f, P * b:P * (b + 1)],
+                                    rhs=h_w[a][:, f * P:(f + 1) * P].bitcast(FP8X4),
+                                    rhs_scale=h_s[a][:, f * P:(f + 1) * P], start=True, stop=True)
+            nc.scalar.copy(z[b][:, first * P:end * P], bank[:, first * P:end * P])
+
+        def scatter(b, first, end):
+            m0, m1 = first * P, end * P
             entries = offs2_sb[:, m0 // LIST_ROWS:m1 // LIST_ROWS]
-            nc.vector.tensor_tensor(windows[b][:].indirect(entries), zs[b][:, m0:m1], gate2_sb[:, m0:m1], MULT)
+            nc.vector.tensor_tensor(windows[b][:].indirect(entries), z[b][:, m0:m1], gate2_sb[:, m0:m1], MULT)
 
         def expert_rows(b, expert_pair):
-            bank = product_bank(ring(b))
+            bank = product_bank(b)
             for side in range(2):
                 e = 2 * expert_pair + side
                 c, place = divmod(e, PIECE_EXPERTS)
-                slots = slice(place * C, (place + 1) * C)
                 nc.tensor.matmul_mx(bank[:, side * C:(side + 1) * C],
                                     lhsT=w_w[c][:, place, 2 * P * b:2 * P * (b + 1)].bitcast(FP4X4),
-                                    lhsT_scale=w_s[:, e, P * b:P * (b + 1)],
-                                    rhs=xe_w[c][:, slots].bitcast(FP8X4), rhs_scale=xe_s[c][:, slots],
-                                    start=True, stop=True)
+                                    lhsT_scale=w_s[:, e, P * b:P * (b + 1)], rhs=expert_w[e].bitcast(FP8X4),
+                                    rhs_scale=piece_s[c][:, place * C:(place + 1) * C], start=True, stop=True)
             nc.scalar.copy(y[b][:, expert_pair * BANK:(expert_pair + 1) * BANK], bank[:])
 
-        def add_turned(sums, term, first, last):
-            for half, bank in enumerate(sums):
-                for a in range(BANK // P):
-                    t0 = half * BANK + a * P
-                    nc.tensor.matmul(bank[:, a * P:(a + 1) * P], term[:, t0:t0 + P], ident[:], is_transpose=True,
-                                     start=(first and a == 0), stop=(last and a == BANK // P - 1))
-
-        def add_choice(sums, b, r, first):
-            term = keep.tile([P, T], F32, name=f"term{b}_{r}")
-            nc.vector.tensor_tensor(term[:], y[b][:].indirect(pos_sb[r][:]), gate_sb[r][:], MULT)
-            add_turned(sums, term, first, r == TOP - 1)
-
-        def turn_back(half, bank, total):
-            nc.scalar.copy(total[:], bank[:])
-            back = bank_of(BACK_BANKS[half])
-            for a in range(BANK // P):
-                nc.tensor.transpose(back[:, a * P:(a + 1) * P], total[:, a * P:(a + 1) * P], ident[:])
-            return back
-
-        early_pairs = (PIECES - 1) * PIECE_EXPERTS // 2
-        last = BLOCKS - 1
-        zs = []
-        for b in range(BLOCKS):
-            if b > 0:
-                zs.append(adapter_rows(b, f"z{b}"))
-            for expert_pair in range(early_pairs):
-                expert_rows(b, expert_pair)
-            if b == 0:
-                zs.append(adapter_rows(b, f"z{b}"))
-            for expert_pair in range(early_pairs, E // 2):
-                expert_rows(b, expert_pair)
-
-        scatter(0, 0, ADAPTER_SLOTS)
-        for b in range(last):
-            sums = [bank_of(tag) for tag in SUM_BANKS]
-            add_turned(sums, windows[b], True, False)
-            for r in range(TOP):
-                add_choice(sums, b, r, False)
-                cuts = SCATTER_CUTS if b + 1 < last else LAST_SCATTER_CUTS
-                if cuts[r] < cuts[r + 1]:
-                    scatter(b + 1, cuts[r], cuts[r + 1])
-            for half, bank in enumerate(sums):
-                total = stage.tile([P, BANK], F32, name="total")
-                back = turn_back(half, bank, total)
-                result = stage.tile([P, BANK], F32, name="result")
-                nc.scalar.copy(result[:], back[:])
-                nc.sync.dma_start(out[P * b:P * (b + 1), half * BANK:(half + 1) * BANK], result[:])
-
-        rows = slice(P * last, P * (last + 1))
-        window = windows[last]
-
-        def fetch(r, t0, t1, term):
+        def fetch(b, r, t0, t1, tag=None):
+            name = f"term{b}_{r}_{t0}"
+            term = keep.tile([P, t1 - t0], F32, name=name, tag=tag or name)
             entries = pos_sb[r][:, t0 // LIST_ROWS:t1 // LIST_ROWS]
-            nc.vector.tensor_tensor(term[:], y[last][:].indirect(entries), gate_sb[r][:, t0:t1], MULT)
+            nc.vector.tensor_tensor(term[:], y[b][:].indirect(entries), gate_sb[r][:, t0:t1], MULT)
             return term
 
-        def new_term(r, t0, t1):
-            return keep.tile([P, t1 - t0], F32, name=f"last_term{r}_{t0}")
-
-        def add_range(bank, term, first, final):
+        def add_turned(bank, term, opens, closes):
             count = term.shape[1] // P
             for a in range(count):
                 nc.tensor.matmul(bank[:, a * P:(a + 1) * P], term[:, a * P:(a + 1) * P], ident[:], is_transpose=True,
-                                 start=(first and a == 0), stop=(final and a == count - 1))
+                                 start=(opens and a == 0), stop=(closes and a == count - 1))
 
-        def finish(back, term, t0):
-            width = term.shape[1]
-            finished = keep.tile([P, width], F32, name=f"finished{t0}")
-            nc.vector.tensor_tensor(finished[:], back[:, :width], term[:], ADD)
-            nc.sync.dma_start(out[rows, t0:t0 + width], finished[:])
+        def copy_out(bank, tile):
+            nc.scalar.copy(tile[:], bank[:, :tile.shape[1]])
+            return tile
 
-        def copy_out(bank, width, name):
-            total = keep.tile([P, width], F32, name=name, tag=name)
-            nc.scalar.copy(total[:], bank[:, :width])
-            return total
-
-        def turn(total, tag):
+        def turn_back(total, tag):
             back = bank_of(tag)
             for a in range(total.shape[1] // P):
                 nc.tensor.transpose(back[:, a * P:(a + 1) * P], total[:, a * P:(a + 1) * P], ident[:])
             return back
 
-        steps = [(t0, t0 + STEP) for t0 in range(EARLY, T, STEP)]
-        sums = [bank_of(tag) for tag in SUM_BANKS + BACK_BANKS]
-        for bank, (t0, t1) in zip(sums, [(0, EARLY)] + steps):
-            add_range(bank, window[:, t0:t1], True, False)
-        for r in range(TOP):
-            add_range(sums[0], fetch(r, 0, EARLY, new_term(r, 0, EARLY))[:], False, r == TOP - 1)
-        back = turn(copy_out(sums[0], EARLY, "early_total")[:], PRODUCT_BANKS[0])
-        nc.sync.dma_start(out[rows, :EARLY], copy_out(back, EARLY, "early_result")[:])
-        first_late = fetch(0, EARLY, T, new_term(0, EARLY, T))
-        for bank, (t0, t1) in zip(sums[1:], steps):
-            add_range(bank, first_late[:, t0 - EARLY:t1 - EARLY], False, False)
-        backs = []
-        for bank, (t0, t1), tag in zip(sums[1:], steps, PRODUCT_BANKS[1:]):
-            add_range(bank, fetch(1, t0, t1, new_term(1, t0, t1))[:], False, True)
-            backs.append(turn(copy_out(bank, STEP, f"total{t0}")[:], tag))
+        early_pairs = (E - PIECE_EXPERTS) // 2
+        for expert_pair in range(early_pairs):
+            expert_rows(0, expert_pair)
+        adapter_rows(0, 0, 1, product_bank(0))
+        scatter(0, 0, 1)
+        adapter_rows(0, 1, PARTS, bank_of(turns[-1]))
+        expert_w.append(gather_words(slots_of(E - 1, E),
+                                     shared.tile([P, C], U32, name="final_w", offset=THIRD, align_bytes=64))[:])
+        for expert_pair in range(early_pairs, E // 2):
+            expert_rows(0, expert_pair)
+        for b in range(1, BLOCKS):
+            adapter_rows(b, 0, PARTS if b < LAST else PARTS - 1, product_bank(b))
+            for expert_pair in range(E // 2):
+                expert_rows(b, expert_pair)
+        adapter_rows(LAST, PARTS - 1, PARTS, product_bank(LAST))
 
-        terms = [fetch(2, t0, t1, new_term(2, t0, t1)) for t0, t1 in steps[:2]]
+        scatter(0, 1, PARTS)
+
+        for b in range(LAST):
+            before_last = b == LAST - 1
+            halved = TOP - 1 if before_last else 1
+            sums = [bank_of(tag) for tag in SUM_BANKS]
+            for half, bank in enumerate(sums):
+                add_turned(bank, windows[b][:, half * BANK:(half + 1) * BANK], True, False)
+            part = 0
+            for r in range(TOP):
+                width = BANK if r == halved else T
+                for t0 in range(0, T, width):
+                    term = fetch(b, r, t0, t0 + width)
+                    for c0 in range(0, width, BANK):
+                        add_turned(sums[(t0 + c0) // BANK], term[:, c0:c0 + BANK], False, r == TOP - 1)
+                    if r > 0 or not before_last:
+                        scatter(b + 1, part, part + 1)
+                        part = part + 1
+            for half, bank in enumerate(sums):
+                total = copy_out(bank, stage.tile([P, BANK], F32, name="total"))
+                back = turn_back(total, BACK_BANKS[half])
+                result = copy_out(back, stage.tile([P, BANK], F32, name="result"))
+                nc.sync.dma_start(out[P * b:P * (b + 1), half * BANK:(half + 1) * BANK], result[:])
+
+        last_rows = slice(P * LAST, P * (LAST + 1))
+        steps = [(t0, t0 + STEP) for t0 in range(EARLY, T, STEP)]
+        early_sum, *step_sums = [bank_of(tag) for tag in SUM_BANKS + BACK_BANKS]
+        for r in range(TOP - 1):
+            add_turned(early_sum, fetch(LAST, r, 0, EARLY)[:], r == 0, False)
+        scatter(LAST, PARTS - 1, PARTS)
+        add_turned(early_sum, windows[LAST][:, :EARLY], False, False)
+        add_turned(early_sum, fetch(LAST, TOP - 1, 0, EARLY)[:], False, True)
+        for bank, (t0, t1) in zip(step_sums, steps):
+            add_turned(bank, windows[LAST][:, t0:t1], True, False)
+        back = turn_back(copy_out(early_sum, keep.tile([P, EARLY], F32, name="early_total")), PRODUCT_BANKS[0])
+        nc.sync.dma_start(out[last_rows, :EARLY], copy_out(back, keep.tile([P, EARLY], F32, name="early_result"))[:])
+
+        first_choice = fetch(LAST, 0, EARLY, T)
+        for bank, (t0, t1) in zip(step_sums, steps):
+            add_turned(bank, first_choice[:, t0 - EARLY:t1 - EARLY], False, False)
+        backs = []
+        for bank, (t0, t1), tag in zip(step_sums, steps, PRODUCT_BANKS[1:]):
+            add_turned(bank, fetch(LAST, 1, t0, t1)[:], False, True)
+            total = keep.tile([P, STEP], F32, name=f"total{t0}", tag=f"total{t0}")
+            backs.append(turn_back(copy_out(bank, total), tag))
+
+        def finish(back, term, t0):
+            finished = keep.tile([P, STEP], F32, name=f"finished{t0}")
+            nc.vector.tensor_tensor(finished[:], back[:, :STEP], term[:], ADD)
+            nc.sync.dma_start(out[last_rows, t0:t0 + STEP], finished[:])
+
+        terms = [fetch(LAST, TOP - 1, t0, t1) for t0, t1 in steps[:-1]]
         finish(backs[0], terms[0], steps[0][0])
-        terms.append(fetch(2, *steps[2], keep.tile([P, STEP], F32, name="last_step", tag=f"total{EARLY}")))
-        for a in (1, 2):
-            finish(backs[a], terms[a], steps[a][0])
+        terms.append(fetch(LAST, TOP - 1, *steps[-1], tag=f"total{EARLY}"))
+        for back, term, (t0, t1) in list(zip(backs, terms, steps))[1:]:
+            finish(back, term, t0)

@@ -17,6 +17,7 @@ FP4X4 = mybir.dt.float4_e2m1fn_x4
 MULT = mybir.AluOpType.mult
 ADD = mybir.AluOpType.add
 RELU = mybir.ActivationFunctionType.Relu
+COPY = mybir.ActivationFunctionType.Copy
 
 P = 128
 BANK = 512
@@ -31,12 +32,23 @@ PIECES = E // PIECE_EXPERTS
 PARTS = ADAPTER_SLOTS // P
 EARLY = 256
 STEP = 256
-PRODUCT_BANKS = ("mm0", "mm1", "mm2", "mm3")
-SUM_BANKS = ("sum0", "sum1")
-BACK_BANKS = ("back0", "back1")
-HALF_H = 8 * F * P
-SECOND = HALF_H + 4 * PIECE
-THIRD = SECOND + 2 * PIECE
+RING = ("mm0", "mm1", "mm2", "mm3")
+HELD = ("q0", "q1", "q2", "q3")
+SUM_BANKS = (HELD[2:], RING[:2])
+BACK_BANKS = HELD[:2]
+AT_H = (0, 4 * PIECE)
+AT_XA_S = AT_H[1] + 4 * PIECE
+AT_XA_W = AT_XA_S + 2 * PIECE
+AT_ZERO = AT_XA_W + 4 * PIECE
+AT_TIES = AT_ZERO + 2 * H
+TERM = 4 * T
+EDGE = TERM // 8
+AT_TOTAL = AT_TIES
+AT_SECOND = AT_TOTAL + TERM
+AT_THIRD = AT_SECOND + 2 * TERM
+AT_TERMS = ((None, AT_SECOND, AT_THIRD),
+            (AT_SECOND, AT_THIRD - TERM + EDGE, AT_THIRD + TERM - EDGE),
+            (AT_TOTAL, AT_THIRD, AT_THIRD + 2 * TERM - 2 * EDGE))
 
 
 def load_scale_rows(nc, tile, rows):
@@ -61,13 +73,6 @@ def tile_moe_mlr_relu_kernel(
             taken.append(psum.tile([P, BANK], F32, name=f"bank{len(taken)}", tag=tag))
             return taken[-1]
 
-        turns = []
-
-        def product_bank(b):
-            ring = PRODUCT_BANKS + SUM_BANKS if b < 2 else PRODUCT_BANKS
-            turns.append(ring[len(turns) % len(ring)])
-            return bank_of(turns[-1])
-
         offs_sb = keep.tile([P, SLOTS // LIST_ROWS], U16, name="offs_sb")
         offs2_sb = keep.tile([P, ADAPTER_SLOTS // LIST_ROWS], U16, name="offs2_sb")
         pos_sb = [keep.tile([P, T // LIST_ROWS], U16, name=f"pos_sb{r}") for r in range(TOP)]
@@ -75,8 +80,7 @@ def tile_moe_mlr_relu_kernel(
         x_s = keep.tile([P, 2 * T], U8, name="x_s", align_bytes=64)
         wa_w = keep.tile([P, F, 2 * H], U8, name="wa_w", align_bytes=64)
         wa_s = keep.tile([P, F, H], U8, name="wa_s", align_bytes=64)
-        wb_first_w = shared.tile([P, F, 2 * P], U8, name="wb_first_w", offset=THIRD, align_bytes=64)
-        wb_w = keep.tile([P, F, 2 * (N - P)], U8, name="wb_w", align_bytes=64)
+        wb_w = keep.tile([P, F, 2 * N], U8, name="wb_w", align_bytes=64)
         wb_s = keep.tile([P, F, N], U8, name="wb_s", align_bytes=64)
         w_w = [keep.tile([P, PIECE_EXPERTS, 2 * N], U8, name=f"w_w{c}", align_bytes=64) for c in range(PIECES)]
         w_s = keep.tile([P, E, N], U8, name="w_s", align_bytes=64)
@@ -87,11 +91,11 @@ def tile_moe_mlr_relu_kernel(
         y = [keep.tile([P, SLOTS], F32, name=f"y{b}") for b in range(BLOCKS)]
 
         nc.gpsimd.memset(x_s[:, :T].bitcast(I32), 0)
-        for scales in (x_s[:, T:], wa_s[:], wb_s[:]):
+        for scales in (x_s[:, T:], wa_s[:], w_s[:], wb_s[:]):
             nc.vector.memset(scales.bitcast(I32), 0)
         make_identity(nc, ident[:])
-        for window in windows:
-            nc.scalar.activation(window[:], ident[:, 0:1].to_broadcast([P, T]), RELU, scale=0.0)
+        zero = shared.tile([P, 1], F32, name="zero", offset=AT_ZERO, align_bytes=64)
+        nc.gpsimd.memset(zero[:], 0.0)
 
         nc.sync.dma_start(offs2_sb[:], offs2)
         x_scale_rows = x_scales[0].rearrange("(q r) t -> r q t", r=4)
@@ -99,25 +103,21 @@ def tile_moe_mlr_relu_kernel(
             queue = nc.sync if r < 2 else nc.scalar
             queue.dma_start(x_s[r:P:32, :T].bitcast(I32), x_scale_rows[r].bitcast(I32))
         nc.sync.dma_start(offs_sb[:], offs)
+        for window in windows:
+            nc.scalar.activation(window[:], zero[:].to_broadcast([P, T]), RELU)
         nc.sync.dma_start(x_w[:], x_words[0].rearrange("p t d -> p (t d)").bitcast(I32))
         nc.sync.dma_start(wa_w[:].bitcast(I32), wa_words[:, 0].rearrange("f p n -> p f n").bitcast(I32))
         load_scale_rows(nc, wa_s, wa_scales[:, 0])
-        load_scale_rows(nc, wb_s, wb_scales[:, 0])
+        load_scale_rows(nc, w_s, w_scales[:, 0])
         for c in range(PIECES):
             experts = w_words[PIECE_EXPERTS * c:PIECE_EXPERTS * (c + 1), 0]
             nc.sync.dma_start(w_w[c][:].bitcast(I32), experts.rearrange("e p n -> p e n").bitcast(I32))
-        wb_rows = wb_words[:, 0].rearrange("f p n -> p f n")
-        nc.sync.dma_start(wb_first_w[:].bitcast(I32), wb_rows[:, :, :2 * P].bitcast(I32))
-        nc.sync.dma_start(wb_w[:].bitcast(I32), wb_rows[:, :, 2 * P:].bitcast(I32))
+        load_scale_rows(nc, wb_s, wb_scales[:, 0])
+        nc.sync.dma_start(wb_w[:].bitcast(I32), wb_words[:, 0].rearrange("f p n -> p f n").bitcast(I32))
         nc.sync.dma_start(gate2_sb[:], gate2)
         for r, pos in enumerate((pos1, pos2, pos3)):
             nc.sync.dma_start(pos_sb[r][:], pos)
             nc.sync.dma_start(gate_sb[r][:], gate[r])
-            if r == 0:
-                for row in range(16):
-                    q, place = divmod(row, 4)
-                    nc.sync.dma_start(w_s[32 * q + place:32 * (q + 1):4, :, :].bitcast(I32),
-                                      w_scales[:, 0, row, :].bitcast(I32).partition_broadcast(8))
 
         def gather_scales(entries, scales):
             nc.vector.tensor_copy(scales[:], x_s[:].indirect(entries))
@@ -128,80 +128,97 @@ def tile_moe_mlr_relu_kernel(
             return words
 
         def slots_of(first, end):
-            return offs_sb[:, first * C // LIST_ROWS:end * C // LIST_ROWS]
+            return offs_sb[:, first * PIECE // LIST_ROWS:end * PIECE // LIST_ROWS]
 
-        xa_s = gather_scales(offs2_sb[:], shared.tile([P, ADAPTER_SLOTS], U8, name="xa_s", offset=SECOND, align_bytes=64))
-        first_s = gather_scales(slots_of(0, PIECE_EXPERTS), keep.tile([P, PIECE], U8, name="first_s", align_bytes=64))
-        xa_w = gather_words(offs2_sb[:], keep.tile([P, ADAPTER_SLOTS], U32, name="xa_w", align_bytes=64))
-        expert_w = []
-        for c in range(PIECES - 1):
-            words = gather_words(slots_of(PIECE_EXPERTS * c, PIECE_EXPERTS * (c + 1)),
-                                 keep.tile([P, PIECE], U32, name=f"xe_w{c}", align_bytes=64))
-            expert_w.extend(words[:, place * C:(place + 1) * C] for place in range(PIECE_EXPERTS))
+        xa_s = gather_scales(offs2_sb[:], shared.tile([P, ADAPTER_SLOTS], U8, name="xa_s", offset=AT_XA_S, align_bytes=64))
+        first_s = gather_scales(slots_of(0, 1), keep.tile([P, PIECE], U8, name="first_s", align_bytes=64))
+        xa_w = gather_words(offs2_sb[:], shared.tile([P, ADAPTER_SLOTS], U32, name="xa_w", offset=AT_XA_W, align_bytes=64))
+        piece_w = [gather_words(slots_of(c, c + 1), keep.tile([P, PIECE], U32, name=f"xe_w{c}", align_bytes=64))
+                   for c in range(2)]
 
-        h_w = [keep.tile([P, F * P], U32, name=f"h_w{a}", align_bytes=64) for a in range(D // P)]
-        h_s = [keep.tile([P, F * P], U8, name=f"h_s{a}", align_bytes=64) for a in range(D // P)]
-        h_in = [shared.tile([P, 4 * F * P], BF16, name=f"h_in{a}", offset=HALF_H * a, align_bytes=64)
-                for a in range(D // P)]
+        h_w = [keep.tile([P, D], U32, name=f"h_w{f}", align_bytes=64) for f in range(F)]
+        h_s = [keep.tile([P, D], U8, name=f"h_s{f}", align_bytes=64) for f in range(F)]
+        h_in = [shared.tile([P, 4 * D], BF16, name=f"h_in{f}", offset=AT_H[f], align_bytes=64) for f in range(F)]
         for f in range(F):
-            turned = bank_of(BACK_BANKS[f])[:].rearrange("p (a u m) -> p a u m", a=D // P, u=2)
+            turned = bank_of(HELD[f])[:].rearrange("p (a u m) -> p a u m", a=D // P, u=2)
             for a in range(D // P):
                 slots = slice(f * D + a * P, f * D + (a + 1) * P)
-                bank = product_bank(0)
+                bank = bank_of(RING[2 * f + a])
                 nc.tensor.matmul_mx(bank[:], lhsT=xa_w[:, slots].bitcast(FP8X4), lhsT_scale=xa_s[:, slots],
                                     rhs=wa_w[:, f, :].bitcast(FP4X4), rhs_scale=wa_s[:, f, :], start=True, stop=True)
-                h_rows = stage.tile([P, H], BF16, name="h_rows")
+                if f == 0 and a == 0:
+                    h_rows = shared.tile([P, H], BF16, name="first_h_rows", offset=AT_ZERO, align_bytes=64)
+                else:
+                    h_rows = stage.tile([P, H], BF16, name="h_rows")
                 nc.scalar.activation(h_rows[:].rearrange("m (u p e) -> m u p e", u=2, e=2),
                                      bank[:].rearrange("m (p u e) -> m u p e", u=2, e=2), RELU)
                 pairs = h_rows[:].bitcast(F32)
                 for u in range(2):
                     nc.tensor.transpose(turned[:, a, u, :], pairs[:, u * P:(u + 1) * P], ident[:])
-            for a in range(D // P):
-                h_pairs = h_in[a][:, 4 * P * f:4 * P * (f + 1)].bitcast(F32)
-                nc.scalar.copy(h_pairs.rearrange("p (m u) -> p m u", u=2), turned[:, a].rearrange("p u m -> p m u"))
-        middle_s = gather_scales(slots_of(PIECE_EXPERTS, 3 * PIECE_EXPERTS),
-                                 shared.tile([P, 2 * PIECE], U8, name="middle_s", offset=SECOND, align_bytes=64))
-        for a in range(D // P):
-            nc.vector.quantize_mx(out=h_w[a][:].bitcast(FP8X4), scales=h_s[a][:], in_=h_in[a][:])
-
-        last_s = gather_scales(slots_of(E - PIECE_EXPERTS, E),
-                               shared.tile([P, PIECE], U8, name="last_s", offset=0, align_bytes=64))
+            nc.scalar.copy(h_in[f][:].bitcast(F32).rearrange("p (a m u) -> p a m u", a=D // P, u=2),
+                           turned.rearrange("p a u m -> p a m u"))
+        middle_s = gather_scales(slots_of(1, 3),
+                                 shared.tile([P, 2 * PIECE], U8, name="middle_s", offset=AT_XA_S, align_bytes=64))
+        piece_w.append(gather_words(slots_of(2, 3),
+                                    shared.tile([P, PIECE], U32, name="xe_w2", offset=AT_XA_W, align_bytes=64)))
+        for f in range(F):
+            nc.vector.quantize_mx(out=h_w[f][:].bitcast(FP8X4), scales=h_s[f][:], in_=h_in[f][:])
+        last_s = gather_scales(slots_of(3, 4), shared.tile([P, PIECE], U8, name="last_s", offset=AT_H[0], align_bytes=64))
+        expert_w = [words[:, place * C:(place + 1) * C] for words in piece_w for place in range(PIECE_EXPERTS)]
+        pair = gather_words(offs_sb[:, (E - 3) * C // LIST_ROWS:(E - 1) * C // LIST_ROWS],
+                            shared.tile([P, 2 * C], U32, name="xe_w3", offset=AT_H[1] + 4 * C, align_bytes=64))
+        single = gather_words(offs_sb[:, (E - 1) * C // LIST_ROWS:],
+                              shared.tile([P, C], U32, name="xe_w4", offset=AT_H[1], align_bytes=64))
+        expert_w.extend((pair[:, :C], pair[:, C:], single[:]))
         piece_s = [first_s[:], middle_s[:, :PIECE], middle_s[:, PIECE:], last_s[:]]
-        words = gather_words(slots_of(E - PIECE_EXPERTS, E - 1),
-                             shared.tile([P, PIECE - C], U32, name="xe_w_last", offset=HALF_H, align_bytes=64))
-        expert_w.extend(words[:, place * C:(place + 1) * C] for place in range(PIECE_EXPERTS - 1))
 
-        z = [keep.tile([P, ADAPTER_SLOTS], F32, name=f"z{b}") for b in range(BLOCKS)]
-
-        def adapter_rows(b, first, end, bank):
-            for part in range(first, end):
-                f, a = divmod(part, D // P)
-                columns = wb_w[:, f, 2 * P * (b - 1):2 * P * b] if b > 0 else wb_first_w[:, f, :]
-                nc.tensor.matmul_mx(bank[:, part * P:(part + 1) * P], lhsT=columns.bitcast(FP4X4),
-                                    lhsT_scale=wb_s[:, f, P * b:P * (b + 1)],
-                                    rhs=h_w[a][:, f * P:(f + 1) * P].bitcast(FP8X4),
-                                    rhs_scale=h_s[a][:, f * P:(f + 1) * P], start=True, stop=True)
-            nc.scalar.copy(z[b][:, first * P:end * P], bank[:, first * P:end * P])
-
-        def scatter(b, first, end):
-            m0, m1 = first * P, end * P
-            entries = offs2_sb[:, m0 // LIST_ROWS:m1 // LIST_ROWS]
-            nc.vector.tensor_tensor(windows[b][:].indirect(entries), z[b][:, m0:m1], gate2_sb[:, m0:m1], MULT)
-
-        def expert_rows(b, expert_pair):
-            bank = product_bank(b)
-            for side in range(2):
-                e = 2 * expert_pair + side
+        def expert_rows(b, first, count, tag):
+            bank = bank_of(tag)
+            for side in range(count):
+                e = first + side
                 c, place = divmod(e, PIECE_EXPERTS)
                 nc.tensor.matmul_mx(bank[:, side * C:(side + 1) * C],
                                     lhsT=w_w[c][:, place, 2 * P * b:2 * P * (b + 1)].bitcast(FP4X4),
                                     lhsT_scale=w_s[:, e, P * b:P * (b + 1)], rhs=expert_w[e].bitcast(FP8X4),
                                     rhs_scale=piece_s[c][:, place * C:(place + 1) * C], start=True, stop=True)
-            nc.scalar.copy(y[b][:, expert_pair * BANK:(expert_pair + 1) * BANK], bank[:])
+            nc.scalar.copy(y[b][:, first * C:(first + count) * C], bank[:, :count * C])
 
-        def fetch(b, r, t0, t1, tag=None):
+        def piece_rows(b, c, tags):
+            expert_rows(b, PIECE_EXPERTS * c, 2, tags[0])
+            expert_rows(b, PIECE_EXPERTS * c + 2, 1, tags[1])
+
+        def adapter_rows(b, tag):
+            bank = bank_of(tag)
+            for f in range(F):
+                nc.tensor.matmul_mx(bank[:, f * D:(f + 1) * D],
+                                    lhsT=wb_w[:, f, 2 * P * b:2 * P * (b + 1)].bitcast(FP4X4),
+                                    lhsT_scale=wb_s[:, f, P * b:P * (b + 1)],
+                                    rhs=h_w[f][:].bitcast(FP8X4), rhs_scale=h_s[f][:], start=True, stop=True)
+            return bank
+
+        z = {}
+
+        def gate_rows(b, bank, first, end, at=None):
+            shape, name = [P, (end - first) * P], f"z{b}_{first}"
+            if at is None:
+                tile = keep.tile(shape, F32, name=name)
+            else:
+                tile = shared.tile(shape, F32, name=name, offset=at, align_bytes=64)
+            nc.vector.tensor_tensor(tile[:], bank[:, first * P:end * P], gate2_sb[:, first * P:end * P], MULT)
+            for part in range(first, end):
+                z[b, part] = tile[:, (part - first) * P:(part - first + 1) * P]
+
+        def scatter(b, part):
+            m0, m1 = part * P, (part + 1) * P
+            entries = offs2_sb[:, m0 // LIST_ROWS:m1 // LIST_ROWS]
+            nc.scalar.activation(windows[b][:].indirect(entries), z[b, part], COPY)
+
+        def fetch(b, r, t0, t1, tag=None, at=None):
             name = f"term{b}_{r}_{t0}"
-            term = keep.tile([P, t1 - t0], F32, name=name, tag=tag or name)
+            if at is None:
+                term = keep.tile([P, t1 - t0], F32, name=name, tag=tag or name)
+            else:
+                term = shared.tile([P, t1 - t0], F32, name=name, offset=at, align_bytes=64)
             entries = pos_sb[r][:, t0 // LIST_ROWS:t1 // LIST_ROWS]
             nc.vector.tensor_tensor(term[:], y[b][:].indirect(entries), gate_sb[r][:, t0:t1], MULT)
             return term
@@ -222,65 +239,80 @@ def tile_moe_mlr_relu_kernel(
                 nc.tensor.transpose(back[:, a * P:(a + 1) * P], total[:, a * P:(a + 1) * P], ident[:])
             return back
 
-        early_pairs = (E - PIECE_EXPERTS) // 2
-        for expert_pair in range(early_pairs):
-            expert_rows(0, expert_pair)
-        adapter_rows(0, 0, 1, product_bank(0))
-        scatter(0, 0, 1)
-        adapter_rows(0, 1, PARTS, bank_of(turns[-1]))
-        expert_w.append(gather_words(slots_of(E - 1, E),
-                                     shared.tile([P, C], U32, name="final_w", offset=THIRD, align_bytes=64))[:])
-        for expert_pair in range(early_pairs, E // 2):
-            expert_rows(0, expert_pair)
-        for b in range(1, BLOCKS):
-            adapter_rows(b, 0, PARTS if b < LAST else PARTS - 1, product_bank(b))
-            for expert_pair in range(E // 2):
-                expert_rows(b, expert_pair)
-        adapter_rows(LAST, PARTS - 1, PARTS, product_bank(LAST))
+        wide = RING + HELD[:2]
+        early_banks = wide + wide + RING[:2] + HELD[:2]
+        for c in range(2):
+            for b in range(BLOCKS):
+                turn = 2 * (BLOCKS * c + b)
+                piece_rows(b, c, early_banks[turn:turn + 2])
+        z_banks = [adapter_rows(b, HELD[b]) for b in range(2)]
+        gate_rows(0, z_banks[0], 0, PARTS)
+        gate_rows(1, z_banks[1], 0, 2)
+        for c in range(2, PIECES):
+            piece_rows(0, c, RING[2:])
+            piece_rows(1, c, RING[:2])
+        late_banks = HELD[:1] + RING[2:] + RING[:2] + HELD[:1]
+        for b in range(2, BLOCKS):
+            for pair in range(PIECE_EXPERTS):
+                expert_rows(b, E // 2 + 2 * pair, 2, late_banks[PIECE_EXPERTS * (b - 2) + pair])
+        z_banks.extend(adapter_rows(b, RING[b]) for b in range(2, BLOCKS))
+        for b, part in list(z):
+            scatter(b, part)
+        later = [[(1, 2, 4), (2, 0, 2)], [(2, 2, 4), (3, 0, 4)], []]
 
-        scatter(0, 1, PARTS)
-
-        for b in range(LAST):
-            before_last = b == LAST - 1
-            halved = TOP - 1 if before_last else 1
-            sums = [bank_of(tag) for tag in SUM_BANKS]
+        def second_stage(b, sums):
+            totals = []
             for half, bank in enumerate(sums):
-                add_turned(bank, windows[b][:, half * BANK:(half + 1) * BANK], True, False)
-            part = 0
-            for r in range(TOP):
-                width = BANK if r == halved else T
-                for t0 in range(0, T, width):
-                    term = fetch(b, r, t0, t0 + width)
-                    for c0 in range(0, width, BANK):
-                        add_turned(sums[(t0 + c0) // BANK], term[:, c0:c0 + BANK], False, r == TOP - 1)
-                    if r > 0 or not before_last:
-                        scatter(b + 1, part, part + 1)
-                        part = part + 1
-            for half, bank in enumerate(sums):
-                total = copy_out(bank, stage.tile([P, BANK], F32, name="total"))
-                back = turn_back(total, BACK_BANKS[half])
+                if b == 0 and half == 0:
+                    total = shared.tile([P, BANK], F32, name="first_total", offset=AT_TOTAL, align_bytes=64)
+                else:
+                    total = stage.tile([P, BANK], F32, name="total")
+                totals.append(copy_out(bank, total))
+            backs = [turn_back(total, tag) for total, tag in zip(totals, BACK_BANKS)]
+            at = AT_TERMS[b][2] + EDGE
+            pieces = []
+            for block, first, end in later[b]:
+                gate_rows(block, z_banks[block], first, end, at)
+                at = at + 4 * P * (end - first)
+                pieces.extend((block, part) for part in range(first, end))
+            for piece in pieces[:1]:
+                scatter(*piece)
+            for half, back in enumerate(backs):
                 result = copy_out(back, stage.tile([P, BANK], F32, name="result"))
                 nc.sync.dma_start(out[P * b:P * (b + 1), half * BANK:(half + 1) * BANK], result[:])
+            for piece in pieces[1:]:
+                scatter(*piece)
+
+        for b in range(LAST):
+            sums = [bank_of(tag) for tag in SUM_BANKS[b % 2]]
+            for r in range(TOP):
+                term = fetch(b, r, 0, T, at=AT_TERMS[b][r])
+                for half, bank in enumerate(sums):
+                    add_turned(bank, term[:, half * BANK:(half + 1) * BANK], r == 0, r == TOP - 1 and b > 0)
+                if r == (1 if b > 0 else 2):
+                    for half, bank in enumerate(sums):
+                        add_turned(bank, windows[b][:, half * BANK:(half + 1) * BANK], False, b == 0)
+            second_stage(b, sums)
 
         last_rows = slice(P * LAST, P * (LAST + 1))
         steps = [(t0, t0 + STEP) for t0 in range(EARLY, T, STEP)]
-        early_sum, *step_sums = [bank_of(tag) for tag in SUM_BANKS + BACK_BANKS]
+        odd, even = AT_TERMS[LAST - 1][1:]
+        width = 4 * STEP
+        early_sum, *step_sums = [bank_of(tag) for tag in RING]
         for r in range(TOP - 1):
-            add_turned(early_sum, fetch(LAST, r, 0, EARLY)[:], r == 0, False)
-        scatter(LAST, PARTS - 1, PARTS)
+            add_turned(early_sum, fetch(LAST, r, 0, EARLY, at=odd + width * r)[:], r == 0, False)
         add_turned(early_sum, windows[LAST][:, :EARLY], False, False)
-        add_turned(early_sum, fetch(LAST, TOP - 1, 0, EARLY)[:], False, True)
-        for bank, (t0, t1) in zip(step_sums, steps):
-            add_turned(bank, windows[LAST][:, t0:t1], True, False)
-        back = turn_back(copy_out(early_sum, keep.tile([P, EARLY], F32, name="early_total")), PRODUCT_BANKS[0])
+        add_turned(early_sum, fetch(LAST, TOP - 1, 0, EARLY, at=odd + width * 3)[:], False, True)
+        back = turn_back(copy_out(early_sum, keep.tile([P, EARLY], F32, name="early_total")), HELD[2])
         nc.sync.dma_start(out[last_rows, :EARLY], copy_out(back, keep.tile([P, EARLY], F32, name="early_result"))[:])
 
-        first_choice = fetch(LAST, 0, EARLY, T)
+        first_choice = fetch(LAST, 0, EARLY, T, at=even)
         for bank, (t0, t1) in zip(step_sums, steps):
-            add_turned(bank, first_choice[:, t0 - EARLY:t1 - EARLY], False, False)
+            add_turned(bank, first_choice[:, t0 - EARLY:t1 - EARLY], True, False)
+            add_turned(bank, windows[LAST][:, t0:t1], False, False)
         backs = []
-        for bank, (t0, t1), tag in zip(step_sums, steps, PRODUCT_BANKS[1:]):
-            add_turned(bank, fetch(LAST, 1, t0, t1)[:], False, True)
+        for bank, (t0, t1), tag, at in zip(step_sums, steps, HELD[3:] + HELD[:2], (odd, odd + width, odd + 5 * width // 2)):
+            add_turned(bank, fetch(LAST, 1, t0, t1, at=at)[:], False, True)
             total = keep.tile([P, STEP], F32, name=f"total{t0}", tag=f"total{t0}")
             backs.append(turn_back(copy_out(bank, total), tag))
 
@@ -289,7 +321,8 @@ def tile_moe_mlr_relu_kernel(
             nc.vector.tensor_tensor(finished[:], back[:, :STEP], term[:], ADD)
             nc.sync.dma_start(out[last_rows, t0:t0 + STEP], finished[:])
 
-        terms = [fetch(LAST, TOP - 1, t0, t1) for t0, t1 in steps[:-1]]
+        terms = [fetch(LAST, TOP - 1, t0, t1, at=at)
+                 for (t0, t1), at in zip(steps[:-1], (odd + 7 * width // 2, even + 3 * width))]
         finish(backs[0], terms[0], steps[0][0])
         terms.append(fetch(LAST, TOP - 1, *steps[-1], tag=f"total{EARLY}"))
         for back, term, (t0, t1) in list(zip(backs, terms, steps))[1:]:

@@ -213,15 +213,18 @@ def tile_moe_mlr_relu_kernel(
             entries = offs2_sb[:, m0 // LIST_ROWS:m1 // LIST_ROWS]
             nc.scalar.activation(windows[b][:].indirect(entries), z[b, part], COPY)
 
-        def fetch(b, r, t0, t1, tag=None, at=None):
-            name = f"term{b}_{r}_{t0}"
+        def term_tile(name, width, tag=None, at=None):
             if at is None:
-                term = keep.tile([P, t1 - t0], F32, name=name, tag=tag or name)
-            else:
-                term = shared.tile([P, t1 - t0], F32, name=name, offset=at, align_bytes=64)
+                return keep.tile([P, width], F32, name=name, tag=tag or name)
+            return shared.tile([P, width], F32, name=name, offset=at, align_bytes=64)
+
+        def fetch_into(term, b, r, t0, t1):
             entries = pos_sb[r][:, t0 // LIST_ROWS:t1 // LIST_ROWS]
-            nc.vector.tensor_tensor(term[:], y[b][:].indirect(entries), gate_sb[r][:, t0:t1], MULT)
+            nc.vector.tensor_tensor(term, y[b][:].indirect(entries), gate_sb[r][:, t0:t1], MULT)
             return term
+
+        def fetch(b, r, t0, t1, tag=None, at=None):
+            return fetch_into(term_tile(f"term{b}_{r}_{t0}", t1 - t0, tag, at)[:], b, r, t0, t1)
 
         def add_turned(bank, term, opens, closes):
             count = term.shape[1] // P
@@ -258,7 +261,7 @@ def tile_moe_mlr_relu_kernel(
         z_banks.extend(adapter_rows(b, RING[b]) for b in range(2, BLOCKS))
         for b, part in list(z):
             scatter(b, part)
-        later = [[(1, 2, 4), (2, 0, 2)], [(2, 2, 4), (3, 0, 4)], []]
+        later = [[(1, 2, 4), (2, 0, 4)], [(3, 0, 4)], []]
 
         def second_stage(b, sums):
             totals = []
@@ -285,13 +288,16 @@ def tile_moe_mlr_relu_kernel(
 
         for b in range(LAST):
             sums = [bank_of(tag) for tag in SUM_BANKS[b % 2]]
-            for r in range(TOP):
-                term = fetch(b, r, 0, T, at=AT_TERMS[b][r])
-                for half, bank in enumerate(sums):
-                    add_turned(bank, term[:, half * BANK:(half + 1) * BANK], r == 0, r == TOP - 1 and b > 0)
+            terms = [term_tile(f"term{b}_{r}", T, at=AT_TERMS[b][r]) for r in range(TOP)]
+            whole = [(r, 0, T) for r in range(TOP)]
+            halves = [(r, t0, t0 + BANK) for t0 in range(0, T, BANK) for r in range(1, TOP)]
+            for r, t0, t1 in whole if b < LAST - 1 else whole[:1] + halves:
+                term = fetch_into(terms[r][:, t0:t1], b, r, t0, t1)
+                for c0 in range(t0, t1, BANK):
+                    add_turned(sums[c0 // BANK], term[:, c0 - t0:c0 - t0 + BANK], r == 0, r == TOP - 1 and b > 0)
                 if r == (1 if b > 0 else 2):
-                    for half, bank in enumerate(sums):
-                        add_turned(bank, windows[b][:, half * BANK:(half + 1) * BANK], False, b == 0)
+                    for c0 in range(t0, t1, BANK):
+                        add_turned(sums[c0 // BANK], windows[b][:, c0:c0 + BANK], False, b == 0)
             second_stage(b, sums)
 
         last_rows = slice(P * LAST, P * (LAST + 1))
@@ -299,17 +305,18 @@ def tile_moe_mlr_relu_kernel(
         odd, even = AT_TERMS[LAST - 1][1:]
         width = 4 * STEP
         early_sum, *step_sums = [bank_of(tag) for tag in RING]
+        add_turned(early_sum, windows[LAST][:, :EARLY], True, False)
+        for bank, (t0, t1) in zip(step_sums, steps):
+            add_turned(bank, windows[LAST][:, t0:t1], True, False)
         for r in range(TOP - 1):
-            add_turned(early_sum, fetch(LAST, r, 0, EARLY, at=odd + width * r)[:], r == 0, False)
-        add_turned(early_sum, windows[LAST][:, :EARLY], False, False)
+            add_turned(early_sum, fetch(LAST, r, 0, EARLY, at=odd + width * r)[:], False, False)
         add_turned(early_sum, fetch(LAST, TOP - 1, 0, EARLY, at=odd + width * 3)[:], False, True)
         back = turn_back(copy_out(early_sum, keep.tile([P, EARLY], F32, name="early_total")), HELD[2])
         nc.sync.dma_start(out[last_rows, :EARLY], copy_out(back, keep.tile([P, EARLY], F32, name="early_result"))[:])
 
         first_choice = fetch(LAST, 0, EARLY, T, at=even)
         for bank, (t0, t1) in zip(step_sums, steps):
-            add_turned(bank, first_choice[:, t0 - EARLY:t1 - EARLY], True, False)
-            add_turned(bank, windows[LAST][:, t0:t1], False, False)
+            add_turned(bank, first_choice[:, t0 - EARLY:t1 - EARLY], False, False)
         backs = []
         for bank, (t0, t1), tag, at in zip(step_sums, steps, HELD[3:] + HELD[:2], (odd, odd + width, odd + 5 * width // 2)):
             add_turned(bank, fetch(LAST, 1, t0, t1, at=at)[:], False, True)

@@ -26,20 +26,18 @@ SLOTS = E * C
 ADAPTER_SLOTS = F * D
 BLOCKS = N // P
 LAST = BLOCKS - 1
-PIECE_EXPERTS = 3
-PIECE = PIECE_EXPERTS * C
-PIECES = E // PIECE_EXPERTS
+PAIRS = E // 2
+WEIGHT_LOADS = ((0, 2), (2, 6), (6, E))
 PARTS = ADAPTER_SLOTS // P
 EARLY = 256
 STEP = 256
 RING = ("mm0", "mm1", "mm2", "mm3")
 HELD = ("q0", "q1", "q2", "q3")
 SUM_BANKS = (HELD[2:], RING[:2])
-BACK_BANKS = HELD[:2]
-AT_H = (0, 4 * PIECE)
-AT_XA_S = AT_H[1] + 4 * PIECE
-AT_XA_W = AT_XA_S + 2 * PIECE
-AT_ZERO = AT_XA_W + 4 * PIECE
+BACK_BANKS = RING[2:]
+AT_H = (0, 16 * C)
+AT_XA_S = AT_H[1] + 18 * C + 2 * C
+AT_ZERO = AT_XA_S + 4 * C
 AT_TIES = AT_ZERO + 2 * H
 TERM = 4 * T
 EDGE = TERM // 8
@@ -82,12 +80,12 @@ def tile_moe_mlr_relu_kernel(
         wa_s = keep.tile([P, F, H], U8, name="wa_s", align_bytes=64)
         wb_w = keep.tile([P, F, 2 * N], U8, name="wb_w", align_bytes=64)
         wb_s = keep.tile([P, F, N], U8, name="wb_s", align_bytes=64)
-        w_w = [keep.tile([P, PIECE_EXPERTS, 2 * N], U8, name=f"w_w{c}", align_bytes=64) for c in range(PIECES)]
+        w_w = [keep.tile([P, end - first, 2 * N], U8, name=f"w_w{first}", align_bytes=64) for first, end in WEIGHT_LOADS]
         w_s = keep.tile([P, E, N], U8, name="w_s", align_bytes=64)
         gate_sb = [keep.tile([P, T], F32, name=f"gate_sb{r}") for r in range(TOP)]
         gate2_sb = keep.tile([P, ADAPTER_SLOTS], F32, name="gate2_sb")
         ident = keep.tile([P, P], F32, name="ident")
-        windows = [keep.tile([P, T], F32, name=f"window{b}") for b in range(BLOCKS)]
+        windows = [keep.tile([P, T], F32, name=f"window{b}") for b in range(2)]
         y = [keep.tile([P, SLOTS], F32, name=f"y{b}") for b in range(BLOCKS)]
 
         nc.gpsimd.memset(x_s[:, :T].bitcast(I32), 0)
@@ -109,9 +107,9 @@ def tile_moe_mlr_relu_kernel(
         nc.sync.dma_start(wa_w[:].bitcast(I32), wa_words[:, 0].rearrange("f p n -> p f n").bitcast(I32))
         load_scale_rows(nc, wa_s, wa_scales[:, 0])
         load_scale_rows(nc, w_s, w_scales[:, 0])
-        for c in range(PIECES):
-            experts = w_words[PIECE_EXPERTS * c:PIECE_EXPERTS * (c + 1), 0]
-            nc.sync.dma_start(w_w[c][:].bitcast(I32), experts.rearrange("e p n -> p e n").bitcast(I32))
+        for tile, (first, end) in zip(w_w, WEIGHT_LOADS):
+            nc.sync.dma_start(tile[:].bitcast(I32), w_words[first:end, 0].rearrange("e p n -> p e n").bitcast(I32))
+        weights = [tile[:, place, :] for tile in w_w for place in range(tile.shape[1])]
         load_scale_rows(nc, wb_s, wb_scales[:, 0])
         nc.sync.dma_start(wb_w[:].bitcast(I32), wb_words[:, 0].rearrange("f p n -> p f n").bitcast(I32))
         nc.sync.dma_start(gate2_sb[:], gate2)
@@ -127,14 +125,22 @@ def tile_moe_mlr_relu_kernel(
             nc.vector.tensor_copy(words[:], x_w[:].bitcast(U32).indirect(entries))
             return words
 
-        def slots_of(first, end):
-            return offs_sb[:, first * PIECE // LIST_ROWS:end * PIECE // LIST_ROWS]
+        expert_w, expert_s = [], []
+
+        def experts(first, end, gather, dtype, into, at=None):
+            shape, name = [P, (end - first) * C], f"xe{len(expert_w)}_{len(expert_s)}"
+            if at is None:
+                tile = keep.tile(shape, dtype, name=name, align_bytes=64)
+            else:
+                tile = shared.tile(shape, dtype, name=name, offset=at, align_bytes=64)
+            gather(offs_sb[:, first * C // LIST_ROWS:end * C // LIST_ROWS], tile)
+            into.extend(tile[:, place * C:(place + 1) * C] for place in range(end - first))
 
         xa_s = gather_scales(offs2_sb[:], shared.tile([P, ADAPTER_SLOTS], U8, name="xa_s", offset=AT_XA_S, align_bytes=64))
-        first_s = gather_scales(slots_of(0, 1), keep.tile([P, PIECE], U8, name="first_s", align_bytes=64))
-        xa_w = gather_words(offs2_sb[:], shared.tile([P, ADAPTER_SLOTS], U32, name="xa_w", offset=AT_XA_W, align_bytes=64))
-        piece_w = [gather_words(slots_of(c, c + 1), keep.tile([P, PIECE], U32, name=f"xe_w{c}", align_bytes=64))
-                   for c in range(2)]
+        experts(0, 2, gather_scales, U8, expert_s)
+        xa_w = gather_words(offs2_sb[:], keep.tile([P, ADAPTER_SLOTS], U32, name="xa_w", align_bytes=64))
+        for first, end in ((0, 2), (2, 5), (5, 8)):
+            experts(first, end, gather_words, U32, expert_w)
 
         h_w = [keep.tile([P, D], U32, name=f"h_w{f}", align_bytes=64) for f in range(F)]
         h_s = [keep.tile([P, D], U8, name=f"h_s{f}", align_bytes=64) for f in range(F)]
@@ -157,35 +163,23 @@ def tile_moe_mlr_relu_kernel(
                     nc.tensor.transpose(turned[:, a, u, :], pairs[:, u * P:(u + 1) * P], ident[:])
             nc.scalar.copy(h_in[f][:].bitcast(F32).rearrange("p (a m u) -> p a m u", a=D // P, u=2),
                            turned.rearrange("p a u m -> p a m u"))
-        middle_s = gather_scales(slots_of(1, 3),
-                                 shared.tile([P, 2 * PIECE], U8, name="middle_s", offset=AT_XA_S, align_bytes=64))
-        piece_w.append(gather_words(slots_of(2, 3),
-                                    shared.tile([P, PIECE], U32, name="xe_w2", offset=AT_XA_W, align_bytes=64)))
+        experts(2, 5, gather_scales, U8, expert_s, AT_XA_S - 2 * C)
+        experts(5, 8, gather_scales, U8, expert_s, AT_XA_S + C)
         for f in range(F):
             nc.vector.quantize_mx(out=h_w[f][:].bitcast(FP8X4), scales=h_s[f][:], in_=h_in[f][:])
-        last_s = gather_scales(slots_of(3, 4), shared.tile([P, PIECE], U8, name="last_s", offset=AT_H[0], align_bytes=64))
-        expert_w = [words[:, place * C:(place + 1) * C] for words in piece_w for place in range(PIECE_EXPERTS)]
-        pair = gather_words(offs_sb[:, (E - 3) * C // LIST_ROWS:(E - 1) * C // LIST_ROWS],
-                            shared.tile([P, 2 * C], U32, name="xe_w3", offset=AT_H[1] + 4 * C, align_bytes=64))
-        single = gather_words(offs_sb[:, (E - 1) * C // LIST_ROWS:],
-                              shared.tile([P, C], U32, name="xe_w4", offset=AT_H[1], align_bytes=64))
-        expert_w.extend((pair[:, :C], pair[:, C:], single[:]))
-        piece_s = [first_s[:], middle_s[:, :PIECE], middle_s[:, PIECE:], last_s[:]]
+        experts(8, E, gather_scales, U8, expert_s, AT_H[1] + 2 * C)
+        experts(8, E - 1, gather_words, U32, expert_w, AT_H[1] + 6 * C)
+        experts(E - 1, E, gather_words, U32, expert_w, AT_H[1] - 2 * C)
 
-        def expert_rows(b, first, count, tag):
+        def expert_rows(b, pair, tag):
             bank = bank_of(tag)
-            for side in range(count):
-                e = first + side
-                c, place = divmod(e, PIECE_EXPERTS)
+            for side in range(2):
+                e = 2 * pair + side
                 nc.tensor.matmul_mx(bank[:, side * C:(side + 1) * C],
-                                    lhsT=w_w[c][:, place, 2 * P * b:2 * P * (b + 1)].bitcast(FP4X4),
+                                    lhsT=weights[e][:, 2 * P * b:2 * P * (b + 1)].bitcast(FP4X4),
                                     lhsT_scale=w_s[:, e, P * b:P * (b + 1)], rhs=expert_w[e].bitcast(FP8X4),
-                                    rhs_scale=piece_s[c][:, place * C:(place + 1) * C], start=True, stop=True)
-            nc.scalar.copy(y[b][:, first * C:(first + count) * C], bank[:, :count * C])
-
-        def piece_rows(b, c, tags):
-            expert_rows(b, PIECE_EXPERTS * c, 2, tags[0])
-            expert_rows(b, PIECE_EXPERTS * c + 2, 1, tags[1])
+                                    rhs_scale=expert_s[e], start=True, stop=True)
+            nc.scalar.copy(y[b][:, pair * BANK:(pair + 1) * BANK], bank[:])
 
         def adapter_rows(b, tag):
             bank = bank_of(tag)
@@ -211,7 +205,7 @@ def tile_moe_mlr_relu_kernel(
         def scatter(b, part):
             m0, m1 = part * P, (part + 1) * P
             entries = offs2_sb[:, m0 // LIST_ROWS:m1 // LIST_ROWS]
-            nc.scalar.activation(windows[b][:].indirect(entries), z[b, part], COPY)
+            nc.scalar.activation(windows[b % 2][:].indirect(entries), z[b, part], COPY)
 
         def term_tile(name, width, tag=None, at=None):
             if at is None:
@@ -242,26 +236,24 @@ def tile_moe_mlr_relu_kernel(
                 nc.tensor.transpose(back[:, a * P:(a + 1) * P], total[:, a * P:(a + 1) * P], ident[:])
             return back
 
-        wide = RING + HELD[:2]
-        early_banks = wide + wide + RING[:2] + HELD[:2]
-        for c in range(2):
+        for pair, tags in enumerate((RING, HELD[2:] + HELD[:2], RING)):
             for b in range(BLOCKS):
-                turn = 2 * (BLOCKS * c + b)
-                piece_rows(b, c, early_banks[turn:turn + 2])
+                expert_rows(b, pair, tags[b])
         z_banks = [adapter_rows(b, HELD[b]) for b in range(2)]
         gate_rows(0, z_banks[0], 0, PARTS)
-        gate_rows(1, z_banks[1], 0, 2)
-        for c in range(2, PIECES):
-            piece_rows(0, c, RING[2:])
-            piece_rows(1, c, RING[:2])
-        late_banks = HELD[:1] + RING[2:] + RING[:2] + HELD[:1]
-        for b in range(2, BLOCKS):
-            for pair in range(PIECE_EXPERTS):
-                expert_rows(b, E // 2 + 2 * pair, 2, late_banks[PIECE_EXPERTS * (b - 2) + pair])
-        z_banks.extend(adapter_rows(b, RING[b]) for b in range(2, BLOCKS))
-        for b, part in list(z):
-            scatter(b, part)
-        later = [[(1, 2, 4), (2, 0, 4)], [(3, 0, 4)], []]
+        gate_rows(1, z_banks[1], 0, PARTS - 1)
+        for b, tag in enumerate(HELD[2:] + RING[:2]):
+            expert_rows(b, 3, tag)
+        for b, tags in enumerate((RING[2:], HELD[2:], RING[:2], RING[2:])):
+            for side in range(2):
+                expert_rows(b, PAIRS - 2 + side, tags[side])
+            if b == 1:
+                for part in range(PARTS):
+                    scatter(0, part)
+        z_banks.append(adapter_rows(2, HELD[0]))
+        for part in range(PARTS - 1):
+            scatter(1, part)
+        later = [[(1, PARTS - 1, PARTS), (2, 0, PARTS)], [(3, 0, PARTS)], []]
 
         def second_stage(b, sums):
             totals = []
@@ -278,6 +270,8 @@ def tile_moe_mlr_relu_kernel(
                 gate_rows(block, z_banks[block], first, end, at)
                 at = at + 4 * P * (end - first)
                 pieces.extend((block, part) for part in range(first, end))
+            if b == 0:
+                z_banks.append(adapter_rows(LAST, HELD[1]))
             for piece in pieces[:1]:
                 scatter(*piece)
             for half, back in enumerate(backs):
@@ -294,20 +288,20 @@ def tile_moe_mlr_relu_kernel(
             for r, t0, t1 in whole if b < LAST - 1 else whole[:1] + halves:
                 term = fetch_into(terms[r][:, t0:t1], b, r, t0, t1)
                 for c0 in range(t0, t1, BANK):
-                    add_turned(sums[c0 // BANK], term[:, c0 - t0:c0 - t0 + BANK], r == 0, r == TOP - 1 and b > 0)
-                if r == (1 if b > 0 else 2):
+                    add_turned(sums[c0 // BANK], term[:, c0 - t0:c0 - t0 + BANK], r == 0, r == TOP - 1)
+                if r == 1:
                     for c0 in range(t0, t1, BANK):
-                        add_turned(sums[c0 // BANK], windows[b][:, c0:c0 + BANK], False, b == 0)
+                        add_turned(sums[c0 // BANK], windows[b % 2][:, c0:c0 + BANK], False, False)
             second_stage(b, sums)
 
         last_rows = slice(P * LAST, P * (LAST + 1))
         steps = [(t0, t0 + STEP) for t0 in range(EARLY, T, STEP)]
         odd, even = AT_TERMS[LAST - 1][1:]
         width = 4 * STEP
-        early_sum, *step_sums = [bank_of(tag) for tag in RING]
-        add_turned(early_sum, windows[LAST][:, :EARLY], True, False)
+        early_sum, *step_sums = [bank_of(tag) for tag in HELD[:1] + RING[:2] + HELD[1:2]]
+        add_turned(early_sum, windows[LAST % 2][:, :EARLY], True, False)
         for bank, (t0, t1) in zip(step_sums, steps):
-            add_turned(bank, windows[LAST][:, t0:t1], True, False)
+            add_turned(bank, windows[LAST % 2][:, t0:t1], True, False)
         for r in range(TOP - 1):
             add_turned(early_sum, fetch(LAST, r, 0, EARLY, at=odd + width * r)[:], False, False)
         add_turned(early_sum, fetch(LAST, TOP - 1, 0, EARLY, at=odd + width * 3)[:], False, True)
@@ -318,7 +312,7 @@ def tile_moe_mlr_relu_kernel(
         for bank, (t0, t1) in zip(step_sums, steps):
             add_turned(bank, first_choice[:, t0 - EARLY:t1 - EARLY], False, False)
         backs = []
-        for bank, (t0, t1), tag, at in zip(step_sums, steps, HELD[3:] + HELD[:2], (odd, odd + width, odd + 5 * width // 2)):
+        for bank, (t0, t1), tag, at in zip(step_sums, steps, HELD[3:] + BACK_BANKS, (odd, odd + width, odd + 5 * width // 2)):
             add_turned(bank, fetch(LAST, 1, t0, t1, at=at)[:], False, True)
             total = keep.tile([P, STEP], F32, name=f"total{t0}", tag=f"total{t0}")
             backs.append(turn_back(copy_out(bank, total), tag))

@@ -29,20 +29,20 @@ LAST = BLOCKS - 1
 PAIRS = E // 2
 WEIGHT_LOADS = ((0, 2), (2, 6), (6, E))
 PARTS = ADAPTER_SLOTS // P
-EARLY = 256
 STEP = 256
 RING = ("mm0", "mm1", "mm2", "mm3")
 HELD = ("q0", "q1", "q2", "q3")
-SUM_BANKS = (HELD[2:], RING[:2])
-BACK_BANKS = RING[2:]
+SUM_BANKS = (HELD[2:], HELD[:2])
+BACK_BANKS = RING[:2]
 AT_H = (0, 16 * C)
 AT_XA_S = AT_H[1] + 18 * C + 2 * C
-AT_ZERO = AT_XA_S + 4 * C
+AT_XA_W = AT_XA_S + 2 * C
+AT_ZERO = AT_XA_W + 8 * C
 AT_TIES = AT_ZERO + 2 * H
 TERM = 4 * T
 EDGE = TERM // 8
-AT_TOTAL = AT_TIES
-AT_SECOND = AT_TOTAL + TERM
+AT_TOTAL = AT_TIES + TERM
+AT_SECOND = AT_TOTAL + 2 * TERM
 AT_THIRD = AT_SECOND + 2 * TERM
 AT_TERMS = ((None, AT_SECOND, AT_THIRD),
             (AT_SECOND, AT_THIRD - TERM + EDGE, AT_THIRD + TERM - EDGE),
@@ -137,8 +137,8 @@ def tile_moe_mlr_relu_kernel(
             into.extend(tile[:, place * C:(place + 1) * C] for place in range(end - first))
 
         xa_s = gather_scales(offs2_sb[:], shared.tile([P, ADAPTER_SLOTS], U8, name="xa_s", offset=AT_XA_S, align_bytes=64))
-        experts(0, 2, gather_scales, U8, expert_s)
-        xa_w = gather_words(offs2_sb[:], keep.tile([P, ADAPTER_SLOTS], U32, name="xa_w", align_bytes=64))
+        experts(0, 3, gather_scales, U8, expert_s)
+        xa_w = gather_words(offs2_sb[:], shared.tile([P, ADAPTER_SLOTS], U32, name="xa_w", offset=AT_XA_W, align_bytes=64))
         for first, end in ((0, 2), (2, 5), (5, 8)):
             experts(first, end, gather_words, U32, expert_w)
 
@@ -163,11 +163,11 @@ def tile_moe_mlr_relu_kernel(
                     nc.tensor.transpose(turned[:, a, u, :], pairs[:, u * P:(u + 1) * P], ident[:])
             nc.scalar.copy(h_in[f][:].bitcast(F32).rearrange("p (a m u) -> p a m u", a=D // P, u=2),
                            turned.rearrange("p a u m -> p a m u"))
-        experts(2, 5, gather_scales, U8, expert_s, AT_XA_S - 2 * C)
-        experts(5, 8, gather_scales, U8, expert_s, AT_XA_S + C)
+        experts(3, 5, gather_scales, U8, expert_s, AT_XA_S)
+        experts(5, 8, gather_scales, U8, expert_s, AT_XA_W)
+        experts(8, E, gather_scales, U8, expert_s, AT_XA_W + 4 * C)
         for f in range(F):
             nc.vector.quantize_mx(out=h_w[f][:].bitcast(FP8X4), scales=h_s[f][:], in_=h_in[f][:])
-        experts(8, E, gather_scales, U8, expert_s, AT_H[1] + 2 * C)
         experts(8, E - 1, gather_words, U32, expert_w, AT_H[1] + 6 * C)
         experts(E - 1, E, gather_words, U32, expert_w, AT_H[1] - 2 * C)
 
@@ -200,16 +200,15 @@ def tile_moe_mlr_relu_kernel(
                 tile = shared.tile(shape, F32, name=name, offset=at, align_bytes=64)
             nc.vector.tensor_tensor(tile[:], bank[:, first * P:end * P], gate2_sb[:, first * P:end * P], MULT)
             for part in range(first, end):
-                z[b, part] = tile[:, (part - first) * P:(part - first + 1) * P]
+                z[b, part] = tile[:, (part - first) * P:]
 
-        def scatter(b, part):
-            m0, m1 = part * P, (part + 1) * P
-            entries = offs2_sb[:, m0 // LIST_ROWS:m1 // LIST_ROWS]
-            nc.scalar.activation(windows[b % 2][:].indirect(entries), z[b, part], COPY)
+        def scatter(b, first, end):
+            entries = offs2_sb[:, first * P // LIST_ROWS:end * P // LIST_ROWS]
+            nc.scalar.activation(windows[b % 2][:].indirect(entries), z[b, first][:, :(end - first) * P], COPY)
 
-        def term_tile(name, width, tag=None, at=None):
+        def term_tile(name, width, at=None):
             if at is None:
-                return keep.tile([P, width], F32, name=name, tag=tag or name)
+                return keep.tile([P, width], F32, name=name)
             return shared.tile([P, width], F32, name=name, offset=at, align_bytes=64)
 
         def fetch_into(term, b, r, t0, t1):
@@ -217,8 +216,8 @@ def tile_moe_mlr_relu_kernel(
             nc.vector.tensor_tensor(term, y[b][:].indirect(entries), gate_sb[r][:, t0:t1], MULT)
             return term
 
-        def fetch(b, r, t0, t1, tag=None, at=None):
-            return fetch_into(term_tile(f"term{b}_{r}_{t0}", t1 - t0, tag, at)[:], b, r, t0, t1)
+        def fetch(b, r, t0, t1, at):
+            return fetch_into(term_tile(f"term{b}_{r}_{t0}", t1 - t0, at)[:], b, r, t0, t1)
 
         def add_turned(bank, term, opens, closes):
             count = term.shape[1] // P
@@ -236,23 +235,22 @@ def tile_moe_mlr_relu_kernel(
                 nc.tensor.transpose(back[:, a * P:(a + 1) * P], total[:, a * P:(a + 1) * P], ident[:])
             return back
 
-        for pair, tags in enumerate((RING, HELD[2:] + HELD[:2], RING)):
-            for b in range(BLOCKS):
-                expert_rows(b, pair, tags[b])
-        z_banks = [adapter_rows(b, HELD[b]) for b in range(2)]
-        gate_rows(0, z_banks[0], 0, PARTS)
-        gate_rows(1, z_banks[1], 0, PARTS - 1)
-        for b, tag in enumerate(HELD[2:] + RING[:2]):
-            expert_rows(b, 3, tag)
-        for b, tags in enumerate((RING[2:], HELD[2:], RING[:2], RING[2:])):
-            for side in range(2):
-                expert_rows(b, PAIRS - 2 + side, tags[side])
-            if b == 1:
-                for part in range(PARTS):
-                    scatter(0, part)
-        z_banks.append(adapter_rows(2, HELD[0]))
-        for part in range(PARTS - 1):
-            scatter(1, part)
+        for pair in range(4):
+            for b, tag in enumerate(RING if pair % 2 == 0 else HELD[2:] + HELD[:2]):
+                expert_rows(b, pair, tag)
+            if pair == 2:
+                z_banks = [adapter_rows(b, RING[b]) for b in range(2)]
+                gate_rows(0, z_banks[0], 0, PARTS)
+                gate_rows(1, z_banks[1], 0, PARTS - 1)
+        late = [(b, pair) for b in range(BLOCKS) for pair in range(4, PAIRS)]
+        late_banks = RING[2:] + HELD[2:] + HELD[:2] + HELD[:1] + RING[:1]
+        for turn, ((b, pair), tag) in enumerate(zip(late, late_banks)):
+            expert_rows(b, pair, tag)
+            if turn == 4:
+                z_banks.extend(adapter_rows(block, RING[block]) for block in range(2, BLOCKS))
+                scatter(0, 0, PARTS - 1)
+                scatter(0, PARTS - 1, PARTS)
+        scatter(1, 0, PARTS - 1)
         later = [[(1, PARTS - 1, PARTS), (2, 0, PARTS)], [(3, 0, PARTS)], []]
 
         def second_stage(b, sums):
@@ -265,13 +263,10 @@ def tile_moe_mlr_relu_kernel(
                 totals.append(copy_out(bank, total))
             backs = [turn_back(total, tag) for total, tag in zip(totals, BACK_BANKS)]
             at = AT_TERMS[b][2] + EDGE
-            pieces = []
             for block, first, end in later[b]:
                 gate_rows(block, z_banks[block], first, end, at)
                 at = at + 4 * P * (end - first)
-                pieces.extend((block, part) for part in range(first, end))
-            if b == 0:
-                z_banks.append(adapter_rows(LAST, HELD[1]))
+            pieces = ([(1, PARTS - 1, PARTS), (2, 0, PARTS - 1), (2, PARTS - 1, PARTS)], [(3, 0, 1), (3, 1, PARTS)], [])[b]
             for piece in pieces[:1]:
                 scatter(*piece)
             for half, back in enumerate(backs):
@@ -295,36 +290,21 @@ def tile_moe_mlr_relu_kernel(
             second_stage(b, sums)
 
         last_rows = slice(P * LAST, P * (LAST + 1))
-        steps = [(t0, t0 + STEP) for t0 in range(EARLY, T, STEP)]
-        odd, even = AT_TERMS[LAST - 1][1:]
-        width = 4 * STEP
-        early_sum, *step_sums = [bank_of(tag) for tag in HELD[:1] + RING[:2] + HELD[1:2]]
-        add_turned(early_sum, windows[LAST % 2][:, :EARLY], True, False)
-        for bank, (t0, t1) in zip(step_sums, steps):
-            add_turned(bank, windows[LAST % 2][:, t0:t1], True, False)
-        for r in range(TOP - 1):
-            add_turned(early_sum, fetch(LAST, r, 0, EARLY, at=odd + width * r)[:], False, False)
-        add_turned(early_sum, fetch(LAST, TOP - 1, 0, EARLY, at=odd + width * 3)[:], False, True)
-        back = turn_back(copy_out(early_sum, keep.tile([P, EARLY], F32, name="early_total")), HELD[2])
-        nc.sync.dma_start(out[last_rows, :EARLY], copy_out(back, keep.tile([P, EARLY], F32, name="early_result"))[:])
-
-        first_choice = fetch(LAST, 0, EARLY, T, at=even)
-        for bank, (t0, t1) in zip(step_sums, steps):
-            add_turned(bank, first_choice[:, t0 - EARLY:t1 - EARLY], False, False)
+        steps = range(0, T, STEP)
+        step_sums = [bank_of(tag) for tag in RING[2:3] + HELD[:2] + RING[3:]]
+        for bank, t0 in zip(step_sums, steps):
+            add_turned(bank, windows[LAST % 2][:, t0:t0 + STEP], True, False)
+        first_choice = fetch(LAST, 0, 0, T, at=AT_TOTAL - TERM + EDGE)
+        for bank, t0 in zip(step_sums, steps):
+            add_turned(bank, first_choice[:, t0:t0 + STEP], False, False)
+        second_choice = term_tile("last_second", T, at=AT_TOTAL + TERM - EDGE)
         backs = []
-        for bank, (t0, t1), tag, at in zip(step_sums, steps, HELD[3:] + BACK_BANKS, (odd, odd + width, odd + 5 * width // 2)):
-            add_turned(bank, fetch(LAST, 1, t0, t1, at=at)[:], False, True)
-            total = keep.tile([P, STEP], F32, name=f"total{t0}", tag=f"total{t0}")
-            backs.append(turn_back(copy_out(bank, total), tag))
-
-        def finish(back, term, t0):
+        for bank, t0, tag in zip(step_sums, steps, HELD[2:] + BACK_BANKS):
+            add_turned(bank, fetch_into(second_choice[:, t0:t0 + STEP], LAST, 1, t0, t0 + STEP), False, True)
+            backs.append(turn_back(copy_out(bank, keep.tile([P, STEP], F32, name=f"total{t0}")), tag))
+        third_choice = term_tile("last_third", T, at=AT_TERMS[LAST - 1][1])
+        fetch_into(third_choice[:], LAST, TOP - 1, 0, T)
+        for back, t0 in zip(backs, steps):
             finished = keep.tile([P, STEP], F32, name=f"finished{t0}")
-            nc.vector.tensor_tensor(finished[:], back[:, :STEP], term[:], ADD)
+            nc.vector.tensor_tensor(finished[:], back[:, :STEP], third_choice[:, t0:t0 + STEP], ADD)
             nc.sync.dma_start(out[last_rows, t0:t0 + STEP], finished[:])
-
-        terms = [fetch(LAST, TOP - 1, t0, t1, at=at)
-                 for (t0, t1), at in zip(steps[:-1], (odd + 7 * width // 2, even + 3 * width))]
-        finish(backs[0], terms[0], steps[0][0])
-        terms.append(fetch(LAST, TOP - 1, *steps[-1], tag=f"total{EARLY}"))
-        for back, term, (t0, t1) in list(zip(backs, terms, steps))[1:]:
-            finish(back, term, t0)

@@ -229,11 +229,13 @@ def tile_moe_mlr_relu_kernel(
             nc.scalar.copy(tile[:], bank[:, :tile.shape[1]])
             return tile
 
-        def turn_back(total, tag):
-            back = bank_of(tag)
+        def turn_into(total, back):
             for a in range(total.shape[1] // P):
                 nc.tensor.transpose(back[:, a * P:(a + 1) * P], total[:, a * P:(a + 1) * P], ident[:])
             return back
+
+        def turn_back(total, tag):
+            return turn_into(total, bank_of(tag)[:])
 
         for pair in range(4):
             for b, tag in enumerate(RING if pair % 2 == 0 else HELD[2:] + HELD[:2]):
@@ -251,9 +253,8 @@ def tile_moe_mlr_relu_kernel(
                 scatter(0, 0, PARTS - 1)
                 scatter(0, PARTS - 1, PARTS)
         scatter(1, 0, PARTS - 1)
-        later = [[(1, PARTS - 1, PARTS), (2, 0, PARTS)], [(3, 0, PARTS)], []]
 
-        def second_stage(b, sums):
+        def totals_of(b, sums):
             totals = []
             for half, bank in enumerate(sums):
                 if b == 0 and half == 0:
@@ -261,50 +262,76 @@ def tile_moe_mlr_relu_kernel(
                 else:
                     total = stage.tile([P, BANK], F32, name="total")
                 totals.append(copy_out(bank, total))
-            backs = [turn_back(total, tag) for total, tag in zip(totals, BACK_BANKS)]
-            at = AT_TERMS[b][2] + EDGE
-            for block, first, end in later[b]:
-                gate_rows(block, z_banks[block], first, end, at)
-                at = at + 4 * P * (end - first)
-            pieces = ([(1, PARTS - 1, PARTS), (2, 0, PARTS - 1), (2, PARTS - 1, PARTS)], [(3, 0, 1), (3, 1, PARTS)], [])[b]
-            for piece in pieces[:1]:
-                scatter(*piece)
+            return [turn_back(total, tag) for total, tag in zip(totals, BACK_BANKS)]
+
+        def store_results(b, backs):
             for half, back in enumerate(backs):
                 result = copy_out(back, stage.tile([P, BANK], F32, name="result"))
                 nc.sync.dma_start(out[P * b:P * (b + 1), half * BANK:(half + 1) * BANK], result[:])
-            for piece in pieces[1:]:
-                scatter(*piece)
 
-        for b in range(LAST):
+        def fetch_plain(term, b, r, t0, t1):
+            entries = pos_sb[r][:, t0 // LIST_ROWS:t1 // LIST_ROWS]
+            nc.scalar.activation(term, y[b][:].indirect(entries), COPY)
+
+        def finish(b, back, term, t0, t1):
+            finished = keep.tile([P, t1 - t0], F32, name=f"finished{b}_{t0}")
+            nc.vector.tensor_tensor(finished[:], back[:, :t1 - t0], term, ADD)
+            nc.sync.dma_start(out[P * b:P * (b + 1), t0:t1], finished[:])
+
+        def sums_of(b, choices):
             sums = [bank_of(tag) for tag in SUM_BANKS[b % 2]]
-            terms = [term_tile(f"term{b}_{r}", T, at=AT_TERMS[b][r]) for r in range(TOP)]
-            whole = [(r, 0, T) for r in range(TOP)]
-            halves = [(r, t0, t0 + BANK) for t0 in range(0, T, BANK) for r in range(1, TOP)]
-            for r, t0, t1 in whole if b < LAST - 1 else whole[:1] + halves:
-                term = fetch_into(terms[r][:, t0:t1], b, r, t0, t1)
-                for c0 in range(t0, t1, BANK):
-                    add_turned(sums[c0 // BANK], term[:, c0 - t0:c0 - t0 + BANK], r == 0, r == TOP - 1)
-                if r == 1:
-                    for c0 in range(t0, t1, BANK):
-                        add_turned(sums[c0 // BANK], windows[b % 2][:, c0:c0 + BANK], False, False)
-            second_stage(b, sums)
+            for r in range(choices):
+                term = fetch(b, r, 0, T, AT_TERMS[b][r])
+                window_next = r == choices - 2
+                for half, bank in enumerate(sums):
+                    add_turned(bank, term[:, half * BANK:(half + 1) * BANK], r == 0, r == choices - 1)
+                if window_next:
+                    for half, bank in enumerate(sums):
+                        add_turned(bank, windows[b % 2][:, half * BANK:(half + 1) * BANK], False, False)
+            return sums
 
-        last_rows = slice(P * LAST, P * (LAST + 1))
+        backs = totals_of(0, sums_of(0, TOP))
+        gate_rows(1, z_banks[1], PARTS - 1, PARTS, AT_TERMS[0][2] + EDGE)
+        gate_rows(2, z_banks[2], 0, PARTS, AT_TERMS[0][2] + EDGE + 4 * P)
+        scatter(1, PARTS - 1, PARTS)
+        store_results(0, backs)
+        scatter(2, 0, PARTS - 1)
+        scatter(2, PARTS - 1, PARTS)
+
+        backs = totals_of(1, sums_of(1, TOP))
+        gate_rows(LAST, z_banks[LAST], 0, PARTS, AT_TERMS[1][2] + EDGE)
+        plain = [term_tile("plain0", BANK, AT_TERMS[2][2])]
+        scatter(LAST, 0, 1)
+        store_results(1, backs)
+        scatter(LAST, 1, 3)
+        fetch_plain(plain[0][:, :STEP], 2, TOP - 1, 0, STEP)
+        scatter(LAST, 3, PARTS)
+        fetch_plain(plain[0][:, STEP:], 2, TOP - 1, STEP, BANK)
+
+        held_backs = totals_of(2, sums_of(2, TOP - 1))
+        plain.append(term_tile("plain1", BANK, AT_THIRD + EDGE))
+        fetch_plain(plain[1][:], 2, TOP - 1, BANK, T)
+
         steps = range(0, T, STEP)
         step_sums = [bank_of(tag) for tag in RING[2:3] + HELD[:2] + RING[3:]]
-        for bank, t0 in zip(step_sums, steps):
-            add_turned(bank, windows[LAST % 2][:, t0:t0 + STEP], True, False)
         first_choice = fetch(LAST, 0, 0, T, at=AT_TOTAL - TERM + EDGE)
         for bank, t0 in zip(step_sums, steps):
-            add_turned(bank, first_choice[:, t0:t0 + STEP], False, False)
+            add_turned(bank, first_choice[:, t0:t0 + STEP], True, False)
+        for bank, t0 in zip(step_sums, steps):
+            add_turned(bank, windows[LAST % 2][:, t0:t0 + STEP], False, False)
         second_choice = term_tile("last_second", T, at=AT_TOTAL + TERM - EDGE)
-        backs = []
-        for bank, t0, tag in zip(step_sums, steps, HELD[2:] + BACK_BANKS):
+        for bank, t0 in zip(step_sums, steps):
             add_turned(bank, fetch_into(second_choice[:, t0:t0 + STEP], LAST, 1, t0, t0 + STEP), False, True)
-            backs.append(turn_back(copy_out(bank, keep.tile([P, STEP], F32, name=f"total{t0}")), tag))
-        third_choice = term_tile("last_third", T, at=AT_TERMS[LAST - 1][1])
-        fetch_into(third_choice[:], LAST, TOP - 1, 0, T)
+        back_banks = [bank_of(tag) for tag in HELD[2:]]
+        backs = []
+        for step, (bank, t0) in enumerate(zip(step_sums, steps)):
+            total = copy_out(bank, keep.tile([P, STEP], F32, name=f"total{t0}"))
+            backs.append(turn_into(total, back_banks[step // 2][:, step % 2 * STEP:(step % 2 + 1) * STEP]))
+        third_choice = fetch(LAST, TOP - 1, 0, T, AT_THIRD + TERM - 2 * EDGE)
+        gated = [term_tile("gated0", BANK, AT_THIRD + EDGE - 4 * BANK), term_tile("gated1", BANK)]
+        for half in range(2):
+            nc.vector.tensor_tensor(gated[half][:], plain[half][:], gate_sb[TOP - 1][:, half * BANK:(half + 1) * BANK], MULT)
+        for half, back in enumerate(held_backs):
+            finish(2, back, gated[half][:], half * BANK, (half + 1) * BANK)
         for back, t0 in zip(backs, steps):
-            finished = keep.tile([P, STEP], F32, name=f"finished{t0}")
-            nc.vector.tensor_tensor(finished[:], back[:, :STEP], third_choice[:, t0:t0 + STEP], ADD)
-            nc.sync.dma_start(out[last_rows, t0:t0 + STEP], finished[:])
+            finish(LAST, back, third_choice[:, t0:t0 + STEP], t0, t0 + STEP)

@@ -43,7 +43,8 @@ TERM = 4 * T
 EDGE = TERM // 8
 AT_TOTAL = AT_TIES + TERM
 AT_SECOND = AT_TOTAL + 2 * TERM
-AT_THIRD = AT_SECOND + 2 * TERM
+AT_PLAIN = AT_SECOND + TERM
+AT_THIRD = AT_PLAIN + 3 * TERM // 2
 AT_TERMS = ((None, AT_SECOND, AT_THIRD),
             (AT_SECOND, AT_THIRD - TERM + EDGE, AT_THIRD + TERM - EDGE),
             (AT_TOTAL, AT_THIRD, AT_THIRD + 2 * TERM - 2 * EDGE))
@@ -238,7 +239,7 @@ def tile_moe_mlr_relu_kernel(
             return turn_into(total, bank_of(tag)[:])
 
         for pair in range(4):
-            for b, tag in enumerate(RING if pair % 2 == 0 else HELD[2:] + HELD[:2]):
+            for b, tag in enumerate(RING if pair % 2 == 0 else HELD[2:] + HELD[:2] if pair == 1 else HELD[2:] + HELD[:1]):
                 expert_rows(b, pair, tag)
             if pair == 2:
                 z_banks = [adapter_rows(b, RING[b]) for b in range(2)]
@@ -248,6 +249,8 @@ def tile_moe_mlr_relu_kernel(
         late_banks = RING[2:] + HELD[2:] + HELD[:2] + HELD[:1] + RING[:1]
         for turn, ((b, pair), tag) in enumerate(zip(late, late_banks)):
             expert_rows(b, pair, tag)
+            if turn == 1:
+                expert_rows(LAST, 3, HELD[1])
             if turn == 4:
                 z_banks.extend(adapter_rows(block, RING[block]) for block in range(2, BLOCKS))
                 scatter(0, 0, PARTS - 1)
@@ -257,8 +260,9 @@ def tile_moe_mlr_relu_kernel(
         def totals_of(b, sums):
             totals = []
             for half, bank in enumerate(sums):
-                if b == 0 and half == 0:
-                    total = shared.tile([P, BANK], F32, name="first_total", offset=AT_TOTAL, align_bytes=64)
+                if b == 0:
+                    total = shared.tile([P, BANK], F32, name=f"first_total{half}", offset=(AT_TOTAL, AT_PLAIN)[half],
+                                        align_bytes=64)
                 else:
                     total = stage.tile([P, BANK], F32, name="total")
                 totals.append(copy_out(bank, total))
@@ -295,18 +299,17 @@ def tile_moe_mlr_relu_kernel(
         gate_rows(2, z_banks[2], 0, PARTS, AT_TERMS[0][2] + EDGE + 4 * P)
         scatter(1, PARTS - 1, PARTS)
         store_results(0, backs)
+        plain = [term_tile("plain0", BANK, AT_PLAIN)]
         scatter(2, 0, PARTS - 1)
+        fetch_plain(plain[0][:, :STEP], 2, TOP - 1, 0, STEP)
         scatter(2, PARTS - 1, PARTS)
+        fetch_plain(plain[0][:, STEP:], 2, TOP - 1, STEP, BANK)
 
         backs = totals_of(1, sums_of(1, TOP))
         gate_rows(LAST, z_banks[LAST], 0, PARTS, AT_TERMS[1][2] + EDGE)
-        plain = [term_tile("plain0", BANK, AT_TERMS[2][2])]
         scatter(LAST, 0, 1)
         store_results(1, backs)
-        scatter(LAST, 1, 3)
-        fetch_plain(plain[0][:, :STEP], 2, TOP - 1, 0, STEP)
-        scatter(LAST, 3, PARTS)
-        fetch_plain(plain[0][:, STEP:], 2, TOP - 1, STEP, BANK)
+        scatter(LAST, 1, PARTS)
 
         held_backs = totals_of(2, sums_of(2, TOP - 1))
         plain.append(term_tile("plain1", BANK, AT_THIRD + EDGE))
@@ -314,24 +317,30 @@ def tile_moe_mlr_relu_kernel(
 
         steps = range(0, T, STEP)
         step_sums = [bank_of(tag) for tag in RING[2:3] + HELD[:2] + RING[3:]]
+        for bank, t0 in zip(step_sums, steps):
+            add_turned(bank, windows[LAST % 2][:, t0:t0 + STEP], True, False)
         first_choice = fetch(LAST, 0, 0, T, at=AT_TOTAL - TERM + EDGE)
         for bank, t0 in zip(step_sums, steps):
-            add_turned(bank, first_choice[:, t0:t0 + STEP], True, False)
-        for bank, t0 in zip(step_sums, steps):
-            add_turned(bank, windows[LAST % 2][:, t0:t0 + STEP], False, False)
+            add_turned(bank, first_choice[:, t0:t0 + STEP], False, False)
         second_choice = term_tile("last_second", T, at=AT_TOTAL + TERM - EDGE)
         for bank, t0 in zip(step_sums, steps):
             add_turned(bank, fetch_into(second_choice[:, t0:t0 + STEP], LAST, 1, t0, t0 + STEP), False, True)
+        last_plain = term_tile("last_plain", T, AT_THIRD + TERM - 2 * EDGE)
         back_banks = [bank_of(tag) for tag in HELD[2:]]
         backs = []
         for step, (bank, t0) in enumerate(zip(step_sums, steps)):
+            fetch_plain(last_plain[:, t0:t0 + STEP], LAST, TOP - 1, t0, t0 + STEP)
             total = copy_out(bank, keep.tile([P, STEP], F32, name=f"total{t0}"))
             backs.append(turn_into(total, back_banks[step // 2][:, step % 2 * STEP:(step % 2 + 1) * STEP]))
-        third_choice = fetch(LAST, TOP - 1, 0, T, AT_THIRD + TERM - 2 * EDGE)
-        gated = [term_tile("gated0", BANK, AT_THIRD + EDGE - 4 * BANK), term_tile("gated1", BANK)]
-        for half in range(2):
-            nc.vector.tensor_tensor(gated[half][:], plain[half][:], gate_sb[TOP - 1][:, half * BANK:(half + 1) * BANK], MULT)
+
+        def gated(b, term, t0, at=None):
+            product = term_tile(f"gated{b}_{t0}", BANK, at)
+            nc.vector.tensor_tensor(product[:], term, gate_sb[TOP - 1][:, t0:t0 + BANK], MULT)
+            return product
+
+        terms = [gated(2, plain[0][:], 0, AT_THIRD + EDGE - 4 * BANK), gated(2, plain[1][:], BANK)]
         for half, back in enumerate(held_backs):
-            finish(2, back, gated[half][:], half * BANK, (half + 1) * BANK)
-        for back, t0 in zip(backs, steps):
-            finish(LAST, back, third_choice[:, t0:t0 + STEP], t0, t0 + STEP)
+            finish(2, back, terms[half][:], half * BANK, (half + 1) * BANK)
+        terms = [gated(LAST, last_plain[:, t0:t0 + BANK], t0) for t0 in range(0, T, BANK)]
+        for step, (back, t0) in enumerate(zip(backs, steps)):
+            finish(LAST, back, terms[step // 2][:, step % 2 * STEP:(step % 2 + 1) * STEP], t0, t0 + STEP)

@@ -30,24 +30,19 @@ PAIRS = E // 2
 WEIGHT_LOADS = ((0, 2), (2, 6), (6, E))
 PARTS = ADAPTER_SLOTS // P
 STEP = 256
+LAG = 2
 RING = ("mm0", "mm1", "mm2", "mm3")
 HELD = ("q0", "q1", "q2", "q3")
-SUM_BANKS = (HELD[2:], HELD[:2])
-BACK_BANKS = RING[:2]
+SUM_BANKS = (HELD[2:], RING[2:], HELD[:2], RING[:2])
+SQUARED = 2
+SQUARE = 32
+RUNS = P // SQUARE
 AT_H = (0, 16 * C)
 AT_XA_S = AT_H[1] + 18 * C + 2 * C
 AT_XA_W = AT_XA_S + 2 * C
 AT_ZERO = AT_XA_W + 8 * C
 AT_TIES = AT_ZERO + 2 * H
 TERM = 4 * T
-EDGE = TERM // 8
-AT_TOTAL = AT_TIES + TERM
-AT_SECOND = AT_TOTAL + 2 * TERM
-AT_PLAIN = AT_SECOND + TERM
-AT_THIRD = AT_PLAIN + 3 * TERM // 2
-AT_TERMS = ((None, AT_SECOND, AT_THIRD),
-            (AT_SECOND, AT_THIRD - TERM + EDGE, AT_THIRD + TERM - EDGE),
-            (AT_TOTAL, AT_THIRD, AT_THIRD + 2 * TERM - 2 * EDGE))
 
 
 def load_scale_rows(nc, tile, rows):
@@ -83,7 +78,7 @@ def tile_moe_mlr_relu_kernel(
         wb_s = keep.tile([P, F, N], U8, name="wb_s", align_bytes=64)
         w_w = [keep.tile([P, end - first, 2 * N], U8, name=f"w_w{first}", align_bytes=64) for first, end in WEIGHT_LOADS]
         w_s = keep.tile([P, E, N], U8, name="w_s", align_bytes=64)
-        gate_sb = [keep.tile([P, T], F32, name=f"gate_sb{r}") for r in range(TOP)]
+        gate_sb = keep.tile([P, TOP, T], F32, name="gate_sb")
         gate2_sb = keep.tile([P, ADAPTER_SLOTS], F32, name="gate2_sb")
         ident = keep.tile([P, P], F32, name="ident")
         windows = [keep.tile([P, T], F32, name=f"window{b}") for b in range(2)]
@@ -116,7 +111,7 @@ def tile_moe_mlr_relu_kernel(
         nc.sync.dma_start(gate2_sb[:], gate2)
         for r, pos in enumerate((pos1, pos2, pos3)):
             nc.sync.dma_start(pos_sb[r][:], pos)
-            nc.sync.dma_start(gate_sb[r][:], gate[r])
+        nc.sync.dma_start(gate_sb[:], gate.rearrange("r p t -> p r t"))
 
         def gather_scales(entries, scales):
             nc.vector.tensor_copy(scales[:], x_s[:].indirect(entries))
@@ -191,156 +186,145 @@ def tile_moe_mlr_relu_kernel(
                                     rhs=h_w[f][:].bitcast(FP8X4), rhs_scale=h_s[f][:], start=True, stop=True)
             return bank
 
-        z = {}
+        lanes = keep.tile([P, (BLOCKS * PARTS + LAG) * STEP], F32, name="lanes", align_bytes=64)
+        z = [lanes[:, b * T:(b + 1) * T] for b in range(BLOCKS)]
+        plain = [lanes[:, b * T + LAG * STEP:(b + 1) * T + LAG * STEP] for b in range(BLOCKS)]
 
-        def gate_rows(b, bank, first, end, at=None):
-            shape, name = [P, (end - first) * P], f"z{b}_{first}"
-            if at is None:
-                tile = keep.tile(shape, F32, name=name)
-            else:
-                tile = shared.tile(shape, F32, name=name, offset=at, align_bytes=64)
-            nc.vector.tensor_tensor(tile[:], bank[:, first * P:end * P], gate2_sb[:, first * P:end * P], MULT)
-            for part in range(first, end):
-                z[b, part] = tile[:, (part - first) * P:]
+        def gate_rows(b, bank):
+            nc.vector.tensor_tensor(z[b].rearrange("n (k s) -> n k s", s=STEP)[:, :, :P],
+                                    bank[:].rearrange("n (k m) -> n k m", m=P),
+                                    gate2_sb[:].rearrange("n (k m) -> n k m", m=P), MULT)
 
-        def scatter(b, first, end):
-            entries = offs2_sb[:, first * P // LIST_ROWS:end * P // LIST_ROWS]
-            nc.scalar.activation(windows[b % 2][:].indirect(entries), z[b, first][:, :(end - first) * P], COPY)
+        def scatter(turn):
+            b, part = divmod(turn, PARTS)
+            entries = offs2_sb[:, part * P // LIST_ROWS:(part + 1) * P // LIST_ROWS]
+            nc.scalar.activation(windows[b % 2][:].indirect(entries), z[b][:, part * STEP:part * STEP + P], COPY)
 
         def term_tile(name, width, at=None):
             if at is None:
-                return keep.tile([P, width], F32, name=name)
+                return keep.tile([P, width], F32, name=name, align_bytes=64)
             return shared.tile([P, width], F32, name=name, offset=at, align_bytes=64)
 
-        def fetch_into(term, b, r, t0, t1):
-            entries = pos_sb[r][:, t0 // LIST_ROWS:t1 // LIST_ROWS]
-            nc.vector.tensor_tensor(term, y[b][:].indirect(entries), gate_sb[r][:, t0:t1], MULT)
-            return term
+        sums = {}
+        terms = {}
 
-        def fetch(b, r, t0, t1, at):
-            return fetch_into(term_tile(f"term{b}_{r}_{t0}", t1 - t0, at)[:], b, r, t0, t1)
+        def add_turned(b, half, term, opens=False, closes=False):
+            for c in range(BANK // P):
+                t0 = half * BANK + c * P
+                nc.tensor.matmul(sums[b][half][:, c * P:(c + 1) * P], term[:, t0:t0 + P], ident[:], is_transpose=True,
+                                 start=(opens and c == 0), stop=(closes and c == BANK // P - 1))
 
-        def add_turned(bank, term, opens, closes):
-            count = term.shape[1] // P
-            for a in range(count):
-                nc.tensor.matmul(bank[:, a * P:(a + 1) * P], term[:, a * P:(a + 1) * P], ident[:], is_transpose=True,
-                                 start=(opens and a == 0), stop=(closes and a == count - 1))
+        def fetch(b, r, place=None, closes=False):
+            term = term_tile(f"term{b}_{r}", T)[:] if place is None else place
+            terms[b, r] = term
+            nc.vector.tensor_tensor(term, y[b][:].indirect(pos_sb[r][:]), gate_sb[:, r, :], MULT)
+            if r == 0:
+                sums[b] = [bank_of(tag) for tag in SUM_BANKS[b]]
+            for half in range(2):
+                add_turned(b, half, term, opens=(r == 0), closes=closes)
 
-        def copy_out(bank, tile):
-            nc.scalar.copy(tile[:], bank[:, :tile.shape[1]])
-            return tile
+        def add_window(b, closes=False):
+            for half in range(2):
+                add_turned(b, half, windows[b % 2], closes=closes)
 
-        def turn_into(total, back):
-            for a in range(total.shape[1] // P):
-                nc.tensor.transpose(back[:, a * P:(a + 1) * P], total[:, a * P:(a + 1) * P], ident[:])
-            return back
+        def fetch_plain(turn):
+            b, part = divmod(turn, PARTS)
+            entries = pos_sb[TOP - 1][:, part * STEP // LIST_ROWS:(part + 1) * STEP // LIST_ROWS]
+            nc.scalar.activation(plain[b][:, part * STEP:(part + 1) * STEP], y[b][:].indirect(entries), COPY)
 
-        def turn_back(total, tag):
-            return turn_into(total, bank_of(tag)[:])
+        def weave(first, end):
+            for turn in range(first, end):
+                scatter(turn)
+                fetch_plain(turn - LAG - 1)
+
+        gated = {}
+
+        def gate_plain(b, place, halves=range(2)):
+            gated[b] = place
+            for half in halves:
+                tokens = slice(half * BANK, (half + 1) * BANK)
+                nc.vector.tensor_tensor(place[:, tokens], plain[b][:, tokens], gate_sb[:, TOP - 1, tokens], MULT)
+                if b < SQUARED:
+                    add_turned(b, half, place, closes=True)
+
+        def finish_squared(b):
+            result = totals[b] = term_tile(f"result{b}", T)
+            for half in range(2):
+                nc.vector.transpose(result[:, half * BANK:(half + 1) * BANK], sums[b][half][:])
+            rows = out[P * b:P * (b + 1), :].rearrange("(j a) (c i u) -> i j a c u", a=SQUARE, i=RUNS, u=SQUARE)
+            for i in range(RUNS):
+                held = result[i * SQUARE:(i + 1) * SQUARE, :].rearrange("a (c j u) -> a j c u", j=RUNS, u=SQUARE)
+                for j in range(RUNS):
+                    nc.sync.dma_start(rows[i, j], held[:, j])
+
+        backs = {}
+        totals = {}
+
+        def turn_back(b):
+            backs[b] = []
+            for half, tag in enumerate(SUM_BANKS[LAST - b]):
+                total = totals[b, half] = plain[LAST][:, STEP:STEP + BANK] if (b, half) == (2, 0) else term_tile(f"total{b}_{half}", BANK)[:]
+                nc.scalar.copy(total, sums[b][half][:])
+                back = bank_of(tag)
+                for c in range(BANK // P):
+                    nc.tensor.transpose(back[:, c * P:(c + 1) * P], total[:, c * P:(c + 1) * P], ident[:])
+                backs[b].append(back)
+
+        def finish(b, first, end, width):
+            for t0 in range(first, end, width):
+                finished = term_tile(f"finished{b}_{t0}", width)
+                back = backs[b][t0 // BANK][:, t0 % BANK:t0 % BANK + width]
+                nc.vector.tensor_tensor(finished[:], back, gated[b][:, t0:t0 + width], ADD)
+                nc.sync.dma_start(out[P * b:P * (b + 1), t0:t0 + width], finished[:])
 
         for pair in range(4):
             for b, tag in enumerate(RING if pair % 2 == 0 else HELD[2:] + HELD[:2] if pair == 1 else HELD[2:] + HELD[:1]):
                 expert_rows(b, pair, tag)
             if pair == 2:
                 z_banks = [adapter_rows(b, RING[b]) for b in range(2)]
-                gate_rows(0, z_banks[0], 0, PARTS)
-                gate_rows(1, z_banks[1], 0, PARTS - 1)
-        late = [(b, pair) for b in range(BLOCKS) for pair in range(4, PAIRS)]
-        late_banks = RING[2:] + HELD[2:] + HELD[:2] + HELD[:1] + RING[:1]
-        for turn, ((b, pair), tag) in enumerate(zip(late, late_banks)):
-            expert_rows(b, pair, tag)
-            if turn == 1:
-                expert_rows(LAST, 3, HELD[1])
-            if turn == 4:
-                z_banks.extend(adapter_rows(block, RING[block]) for block in range(2, BLOCKS))
-                scatter(0, 0, PARTS - 1)
-                scatter(0, PARTS - 1, PARTS)
-        scatter(1, 0, PARTS - 1)
+                gate_rows(0, z_banks[0])
+                gate_rows(1, z_banks[1])
 
-        def totals_of(b, sums):
-            totals = []
-            for half, bank in enumerate(sums):
-                if b == 0:
-                    total = shared.tile([P, BANK], F32, name=f"first_total{half}", offset=(AT_TOTAL, AT_PLAIN)[half],
-                                        align_bytes=64)
-                else:
-                    total = stage.tile([P, BANK], F32, name="total")
-                totals.append(copy_out(bank, total))
-            return [turn_back(total, tag) for total, tag in zip(totals, BACK_BANKS)]
+        for pair in range(4, PAIRS):
+            expert_rows(0, pair, RING[pair - 2])
+        expert_rows(LAST, 3, HELD[1])
+        late_banks = HELD[2:] + HELD[:1] + RING[2:3]
+        for turn, tag in enumerate(late_banks):
+            expert_rows(1 + turn // 2, 4 + turn % 2, tag)
+            if turn <= LAG:
+                scatter(turn)
+        z_banks.extend(adapter_rows(block, tag) for block, tag in ((2, RING[3]), (LAST, HELD[1])))
+        weave(LAG + 1, 2 * PARTS)
+        for pair in range(4, PAIRS):
+            expert_rows(LAST, pair, RING[pair - 4])
 
-        def store_results(b, backs):
-            for half, back in enumerate(backs):
-                result = copy_out(back, stage.tile([P, BANK], F32, name="result"))
-                nc.sync.dma_start(out[P * b:P * (b + 1), half * BANK:(half + 1) * BANK], result[:])
-
-        def fetch_plain(term, b, r, t0, t1):
-            entries = pos_sb[r][:, t0 // LIST_ROWS:t1 // LIST_ROWS]
-            nc.scalar.activation(term, y[b][:].indirect(entries), COPY)
-
-        def finish(b, back, term, t0, t1):
-            finished = keep.tile([P, t1 - t0], F32, name=f"finished{b}_{t0}")
-            nc.vector.tensor_tensor(finished[:], back[:, :t1 - t0], term, ADD)
-            nc.sync.dma_start(out[P * b:P * (b + 1), t0:t1], finished[:])
-
-        def sums_of(b, choices):
-            sums = [bank_of(tag) for tag in SUM_BANKS[b % 2]]
-            for r in range(choices):
-                term = fetch(b, r, 0, T, AT_TERMS[b][r])
-                window_next = r == choices - 2
-                for half, bank in enumerate(sums):
-                    add_turned(bank, term[:, half * BANK:(half + 1) * BANK], r == 0, r == choices - 1)
-                if window_next:
-                    for half, bank in enumerate(sums):
-                        add_turned(bank, windows[b % 2][:, half * BANK:(half + 1) * BANK], False, False)
-            return sums
-
-        backs = totals_of(0, sums_of(0, TOP))
-        gate_rows(1, z_banks[1], PARTS - 1, PARTS, AT_TERMS[0][2] + EDGE)
-        gate_rows(2, z_banks[2], 0, PARTS, AT_TERMS[0][2] + EDGE + 4 * P)
-        scatter(1, PARTS - 1, PARTS)
-        store_results(0, backs)
-        plain = [term_tile("plain0", BANK, AT_PLAIN)]
-        scatter(2, 0, PARTS - 1)
-        fetch_plain(plain[0][:, :STEP], 2, TOP - 1, 0, STEP)
-        scatter(2, PARTS - 1, PARTS)
-        fetch_plain(plain[0][:, STEP:], 2, TOP - 1, STEP, BANK)
-
-        backs = totals_of(1, sums_of(1, TOP))
-        gate_rows(LAST, z_banks[LAST], 0, PARTS, AT_TERMS[1][2] + EDGE)
-        scatter(LAST, 0, 1)
-        store_results(1, backs)
-        scatter(LAST, 1, PARTS)
-
-        held_backs = totals_of(2, sums_of(2, TOP - 1))
-        plain.append(term_tile("plain1", BANK, AT_THIRD + EDGE))
-        fetch_plain(plain[1][:], 2, TOP - 1, BANK, T)
-
-        steps = range(0, T, STEP)
-        step_sums = [bank_of(tag) for tag in RING[2:3] + HELD[:2] + RING[3:]]
-        for bank, t0 in zip(step_sums, steps):
-            add_turned(bank, windows[LAST % 2][:, t0:t0 + STEP], True, False)
-        first_choice = fetch(LAST, 0, 0, T, at=AT_TOTAL - TERM + EDGE)
-        for bank, t0 in zip(step_sums, steps):
-            add_turned(bank, first_choice[:, t0:t0 + STEP], False, False)
-        second_choice = term_tile("last_second", T, at=AT_TOTAL + TERM - EDGE)
-        for bank, t0 in zip(step_sums, steps):
-            add_turned(bank, fetch_into(second_choice[:, t0:t0 + STEP], LAST, 1, t0, t0 + STEP), False, True)
-        last_plain = term_tile("last_plain", T, AT_THIRD + TERM - 2 * EDGE)
-        back_banks = [bank_of(tag) for tag in HELD[2:]]
-        backs = []
-        for step, (bank, t0) in enumerate(zip(step_sums, steps)):
-            fetch_plain(last_plain[:, t0:t0 + STEP], LAST, TOP - 1, t0, t0 + STEP)
-            total = copy_out(bank, keep.tile([P, STEP], F32, name=f"total{t0}"))
-            backs.append(turn_into(total, back_banks[step // 2][:, step % 2 * STEP:(step % 2 + 1) * STEP]))
-
-        def gated(b, term, t0, at=None):
-            product = term_tile(f"gated{b}_{t0}", BANK, at)
-            nc.vector.tensor_tensor(product[:], term, gate_sb[TOP - 1][:, t0:t0 + BANK], MULT)
-            return product
-
-        terms = [gated(2, plain[0][:], 0, AT_THIRD + EDGE - 4 * BANK), gated(2, plain[1][:], BANK)]
-        for half, back in enumerate(held_backs):
-            finish(2, back, terms[half][:], half * BANK, (half + 1) * BANK)
-        terms = [gated(LAST, last_plain[:, t0:t0 + BANK], t0) for t0 in range(0, T, BANK)]
-        for step, (back, t0) in enumerate(zip(backs, steps)):
-            finish(LAST, back, terms[step // 2][:, step % 2 * STEP:(step % 2 + 1) * STEP], t0, t0 + STEP)
+        fetch(0, 0, z[2])
+        fetch(0, 1, z[LAST])
+        add_window(0)
+        for b in range(2, BLOCKS):
+            gate_rows(b, z_banks[b])
+        weave(2 * PARTS, 3 * PARTS)
+        fetch(1, 0)
+        fetch(1, 1)
+        add_window(1)
+        weave(3 * PARTS, BLOCKS * PARTS)
+        fetch_plain(BLOCKS * PARTS - 1)
+        fetch(2, 0)
+        gate_plain(0, plain[0])
+        fetch(2, 1)
+        add_window(2, closes=True)
+        finish_squared(0)
+        gate_plain(1, plain[0])
+        fetch(LAST, 0, terms[2, 1])
+        add_window(LAST)
+        finish_squared(1)
+        turn_back(2)
+        fetch_plain(BLOCKS * PARTS - 3)
+        fetch_plain(BLOCKS * PARTS - 2)
+        fetch(LAST, 1, plain[0], closes=True)
+        turn_back(LAST)
+        gate_plain(2, terms[LAST, 0])
+        for half in range(2):
+            gate_plain(LAST, plain[LAST], [half])
+            finish(2, half * BANK, (half + 1) * BANK, BANK)
+        finish(LAST, 0, T, STEP)

@@ -33,16 +33,16 @@ STEP = 256
 LAG = 2
 RING = ("mm0", "mm1", "mm2", "mm3")
 HELD = ("q0", "q1", "q2", "q3")
-SUM_BANKS = (HELD[2:], RING[2:], HELD[:2], RING[:2])
-SQUARED = 2
+SUM_BANKS = (HELD[2:], HELD[:2], RING[:2], RING[2:])
+SQUARED = 1
 SQUARE = 32
 RUNS = P // SQUARE
 AT_H = (0, 16 * C)
-AT_XA_S = AT_H[1] + 18 * C + 2 * C
-AT_XA_W = AT_XA_S + 2 * C
-AT_ZERO = AT_XA_W + 8 * C
-AT_TIES = AT_ZERO + 2 * H
-TERM = 4 * T
+AT_XA_S = AT_H[1] + 19 * C
+AT_XA_W = (AT_XA_S + 2 * C, AT_XA_S + 16 * C)
+AT_ZERO = AT_XA_W[1] + 4 * C
+AT_WINDOW = AT_ZERO + 2 * H
+WINDOW_OF = (0, 1, 2, 1)
 
 
 def load_scale_rows(nc, tile, rows):
@@ -82,6 +82,7 @@ def tile_moe_mlr_relu_kernel(
         gate2_sb = keep.tile([P, ADAPTER_SLOTS], F32, name="gate2_sb")
         ident = keep.tile([P, P], F32, name="ident")
         windows = [keep.tile([P, T], F32, name=f"window{b}") for b in range(2)]
+        windows.append(shared.tile([P, T], F32, name="window2", offset=AT_WINDOW, align_bytes=64))
         y = [keep.tile([P, SLOTS], F32, name=f"y{b}") for b in range(BLOCKS)]
 
         nc.gpsimd.memset(x_s[:, :T].bitcast(I32), 0)
@@ -134,8 +135,10 @@ def tile_moe_mlr_relu_kernel(
 
         xa_s = gather_scales(offs2_sb[:], shared.tile([P, ADAPTER_SLOTS], U8, name="xa_s", offset=AT_XA_S, align_bytes=64))
         experts(0, 3, gather_scales, U8, expert_s)
-        xa_w = gather_words(offs2_sb[:], shared.tile([P, ADAPTER_SLOTS], U32, name="xa_w", offset=AT_XA_W, align_bytes=64))
-        for first, end in ((0, 2), (2, 5), (5, 8)):
+        xa_w = [gather_words(offs2_sb[:, f * D // LIST_ROWS:(f + 1) * D // LIST_ROWS],
+                             shared.tile([P, D], U32, name=f"xa_w{f}", offset=AT_XA_W[f], align_bytes=64))
+                for f in range(F)]
+        for first, end in ((0, 2), (2, 5)):
             experts(first, end, gather_words, U32, expert_w)
 
         h_w = [keep.tile([P, D], U32, name=f"h_w{f}", align_bytes=64) for f in range(F)]
@@ -146,7 +149,7 @@ def tile_moe_mlr_relu_kernel(
             for a in range(D // P):
                 slots = slice(f * D + a * P, f * D + (a + 1) * P)
                 bank = bank_of(RING[2 * f + a])
-                nc.tensor.matmul_mx(bank[:], lhsT=xa_w[:, slots].bitcast(FP8X4), lhsT_scale=xa_s[:, slots],
+                nc.tensor.matmul_mx(bank[:], lhsT=xa_w[f][:, a * P:(a + 1) * P].bitcast(FP8X4), lhsT_scale=xa_s[:, slots],
                                     rhs=wa_w[:, f, :].bitcast(FP4X4), rhs_scale=wa_s[:, f, :], start=True, stop=True)
                 if f == 0 and a == 0:
                     h_rows = shared.tile([P, H], BF16, name="first_h_rows", offset=AT_ZERO, align_bytes=64)
@@ -159,9 +162,10 @@ def tile_moe_mlr_relu_kernel(
                     nc.tensor.transpose(turned[:, a, u, :], pairs[:, u * P:(u + 1) * P], ident[:])
             nc.scalar.copy(h_in[f][:].bitcast(F32).rearrange("p (a m u) -> p a m u", a=D // P, u=2),
                            turned.rearrange("p a u m -> p a m u"))
-        experts(3, 5, gather_scales, U8, expert_s, AT_XA_S)
-        experts(5, 8, gather_scales, U8, expert_s, AT_XA_W)
-        experts(8, E, gather_scales, U8, expert_s, AT_XA_W + 4 * C)
+        experts(3, 5, gather_scales, U8, expert_s, AT_XA_W[0])
+        experts(5, 8, gather_words, U32, expert_w, AT_XA_W[0] + 2 * C)
+        experts(5, 8, gather_scales, U8, expert_s, AT_XA_S - C)
+        experts(8, E, gather_scales, U8, expert_s, AT_XA_W[1])
         for f in range(F):
             nc.vector.quantize_mx(out=h_w[f][:].bitcast(FP8X4), scales=h_s[f][:], in_=h_in[f][:])
         experts(8, E - 1, gather_words, U32, expert_w, AT_H[1] + 6 * C)
@@ -186,9 +190,13 @@ def tile_moe_mlr_relu_kernel(
                                     rhs=h_w[f][:].bitcast(FP8X4), rhs_scale=h_s[f][:], start=True, stop=True)
             return bank
 
-        lanes = keep.tile([P, (BLOCKS * PARTS + LAG) * STEP], F32, name="lanes", align_bytes=64)
-        z = [lanes[:, b * T:(b + 1) * T] for b in range(BLOCKS)]
-        plain = [lanes[:, b * T + LAG * STEP:(b + 1) * T + LAG * STEP] for b in range(BLOCKS)]
+        lanes = keep.tile([P, (BLOCKS * PARTS + 1) * STEP], F32, name="lanes", align_bytes=64)
+
+        def lane(step, steps=PARTS):
+            return lanes[:, step * STEP:(step + steps) * STEP]
+
+        z = [lane(1 + b * PARTS) for b in range(BLOCKS)]
+        plain = [lane(1 + b * PARTS + LAG) for b in range(LAST)]
 
         def gate_rows(b, bank):
             nc.vector.tensor_tensor(z[b].rearrange("n (k s) -> n k s", s=STEP)[:, :, :P],
@@ -198,7 +206,7 @@ def tile_moe_mlr_relu_kernel(
         def scatter(turn):
             b, part = divmod(turn, PARTS)
             entries = offs2_sb[:, part * P // LIST_ROWS:(part + 1) * P // LIST_ROWS]
-            nc.scalar.activation(windows[b % 2][:].indirect(entries), z[b][:, part * STEP:part * STEP + P], COPY)
+            nc.scalar.activation(windows[WINDOW_OF[b]][:].indirect(entries), z[b][:, part * STEP:part * STEP + P], COPY)
 
         def term_tile(name, width, at=None):
             if at is None:
@@ -225,17 +233,16 @@ def tile_moe_mlr_relu_kernel(
 
         def add_window(b, closes=False):
             for half in range(2):
-                add_turned(b, half, windows[b % 2], closes=closes)
+                add_turned(b, half, windows[WINDOW_OF[b]], closes=closes)
 
-        def fetch_plain(turn):
-            b, part = divmod(turn, PARTS)
+        def fetch_plain(b, part):
             entries = pos_sb[TOP - 1][:, part * STEP // LIST_ROWS:(part + 1) * STEP // LIST_ROWS]
             nc.scalar.activation(plain[b][:, part * STEP:(part + 1) * STEP], y[b][:].indirect(entries), COPY)
 
         def weave(first, end):
             for turn in range(first, end):
                 scatter(turn)
-                fetch_plain(turn - LAG - 1)
+                fetch_plain(*divmod(turn - LAG - 1, PARTS))
 
         gated = {}
 
@@ -260,71 +267,74 @@ def tile_moe_mlr_relu_kernel(
         backs = {}
         totals = {}
 
-        def turn_back(b):
-            backs[b] = []
-            for half, tag in enumerate(SUM_BANKS[LAST - b]):
-                total = totals[b, half] = plain[LAST][:, STEP:STEP + BANK] if (b, half) == (2, 0) else term_tile(f"total{b}_{half}", BANK)[:]
+        def turn_back(b, halves=range(2)):
+            for half in halves:
+                total = totals[b, half] = term_tile(f"total{b}_{half}", BANK)[:]
                 nc.scalar.copy(total, sums[b][half][:])
-                back = bank_of(tag)
+                backs[b, half] = bank_of(SUM_BANKS[b - 1][half])
                 for c in range(BANK // P):
-                    nc.tensor.transpose(back[:, c * P:(c + 1) * P], total[:, c * P:(c + 1) * P], ident[:])
-                backs[b].append(back)
+                    nc.tensor.transpose(backs[b, half][:, c * P:(c + 1) * P], total[:, c * P:(c + 1) * P], ident[:])
 
-        def finish(b, first, end, width):
-            for t0 in range(first, end, width):
-                finished = term_tile(f"finished{b}_{t0}", width)
-                back = backs[b][t0 // BANK][:, t0 % BANK:t0 % BANK + width]
-                nc.vector.tensor_tensor(finished[:], back, gated[b][:, t0:t0 + width], ADD)
-                nc.sync.dma_start(out[P * b:P * (b + 1), t0:t0 + width], finished[:])
+        def finish(b, t0, term):
+            width = term.shape[1]
+            finished = term_tile(f"finished{b}_{t0}", width)
+            back = backs[b, t0 // BANK][:, t0 % BANK:t0 % BANK + width]
+            nc.vector.tensor_tensor(finished[:], back, term, ADD)
+            nc.sync.dma_start(out[P * b:P * (b + 1), t0:t0 + width], finished[:])
 
         for pair in range(4):
-            for b, tag in enumerate(RING if pair % 2 == 0 else HELD[2:] + HELD[:2] if pair == 1 else HELD[2:] + HELD[:1]):
+            for b, tag in enumerate(RING if pair % 2 == 0 else HELD[2:] + HELD[:2]):
                 expert_rows(b, pair, tag)
             if pair == 2:
                 z_banks = [adapter_rows(b, RING[b]) for b in range(2)]
                 gate_rows(0, z_banks[0])
                 gate_rows(1, z_banks[1])
 
-        for pair in range(4, PAIRS):
-            expert_rows(0, pair, RING[pair - 2])
-        expert_rows(LAST, 3, HELD[1])
-        late_banks = HELD[2:] + HELD[:1] + RING[2:3]
-        for turn, tag in enumerate(late_banks):
-            expert_rows(1 + turn // 2, 4 + turn % 2, tag)
-            if turn <= LAG:
-                scatter(turn)
-        z_banks.extend(adapter_rows(block, tag) for block, tag in ((2, RING[3]), (LAST, HELD[1])))
-        weave(LAG + 1, 2 * PARTS)
-        for pair in range(4, PAIRS):
-            expert_rows(LAST, pair, RING[pair - 4])
+        def late_rows(b, tags, scatters=()):
+            for turn, tag in enumerate(tags):
+                expert_rows(b, 4 + turn, tag)
+                if turn < len(scatters):
+                    scatter(scatters[turn])
 
-        fetch(0, 0, z[2])
-        fetch(0, 1, z[LAST])
-        add_window(0)
+        late_rows(0, RING[2:])
         for b in range(2, BLOCKS):
-            gate_rows(b, z_banks[b])
-        weave(2 * PARTS, 3 * PARTS)
-        fetch(1, 0)
-        fetch(1, 1)
-        add_window(1)
-        weave(3 * PARTS, BLOCKS * PARTS)
-        fetch_plain(BLOCKS * PARTS - 1)
+            gate_rows(b, adapter_rows(b, HELD[b]))
+        late_rows(1, HELD[:2], (0, 1))
+        late_rows(2, RING[:2], (2,))
+        weave(LAG + 1, 2 * PARTS)
+        late_rows(LAST, RING[2:])
+        weave(2 * PARTS, LAST * PARTS)
+        fetch_plain(2, 1)
+
+        for b in range(2):
+            fetch(b, 0)
+            fetch(b, 1)
+            add_window(b, closes=(b >= SQUARED))
         fetch(2, 0)
-        gate_plain(0, plain[0])
+        gate_plain(0, plain[0], (1, 0))
         fetch(2, 1)
         add_window(2, closes=True)
         finish_squared(0)
-        gate_plain(1, plain[0])
-        fetch(LAST, 0, terms[2, 1])
-        add_window(LAST)
-        finish_squared(1)
+        scatter(LAST * PARTS)
+        turn_back(1)
+        weave(LAST * PARTS + 1, BLOCKS * PARTS - 1)
+        scatter(BLOCKS * PARTS - 1)
+        plain.append(term_tile("last_plain", T, AT_WINDOW)[:])
+        fetch_plain(LAST, 2)
+        fetch(LAST, 0, lane(1))
+        gate_plain(1, terms[2, 1])
+        fetch(LAST, 1, lane(1 + PARTS))
+        add_window(LAST, closes=True)
         turn_back(2)
-        fetch_plain(BLOCKS * PARTS - 3)
-        fetch_plain(BLOCKS * PARTS - 2)
-        fetch(LAST, 1, plain[0], closes=True)
+        fetch_plain(LAST, 3)
         turn_back(LAST)
-        gate_plain(2, terms[LAST, 0])
-        for half in range(2):
-            gate_plain(LAST, plain[LAST], [half])
-            finish(2, half * BANK, (half + 1) * BANK, BANK)
-        finish(LAST, 0, T, STEP)
+        for t0 in range(0, T, BANK):
+            finish(1, t0, gated[1][:, t0:t0 + BANK])
+        nc.vector.tensor_tensor(gated[1][:, :BANK], y[LAST][:].indirect(pos_sb[TOP - 1][:, :BANK // LIST_ROWS]),
+                                gate_sb[:, TOP - 1, :BANK], MULT)
+        gate_plain(2, terms[LAST, 1])
+        for t0 in range(0, T, BANK):
+            finish(2, t0, gated[2][:, t0:t0 + BANK])
+        nc.vector.tensor_tensor(gated[2][:, :BANK], plain[LAST][:, BANK:], gate_sb[:, TOP - 1, BANK:], MULT)
+        for t0 in range(0, T, STEP):
+            finish(LAST, t0, gated[1 + t0 // BANK][:, t0 % BANK:t0 % BANK + STEP])

@@ -30,7 +30,7 @@ PAIRS = E // 2
 WEIGHT_LOADS = ((0, 2), (2, 6), (6, E))
 PARTS = ADAPTER_SLOTS // P
 STEP = 256
-LAG = 2
+LAG = 1
 RING = ("mm0", "mm1", "mm2", "mm3")
 HELD = ("q0", "q1", "q2", "q3")
 SUM_BANKS = (HELD[2:], HELD[:2], RING[:2], RING[2:])
@@ -41,7 +41,6 @@ AT_H = (0, 16 * C)
 AT_XA_S = AT_H[1] + 19 * C
 AT_XA_W = (AT_XA_S + 2 * C, AT_XA_S + 16 * C)
 AT_ZERO = AT_XA_W[1] + 4 * C
-AT_WINDOW = AT_ZERO + 2 * H
 WINDOW_OF = (0, 1, 2, 1)
 
 
@@ -81,8 +80,7 @@ def tile_moe_mlr_relu_kernel(
         gate_sb = keep.tile([P, TOP, T], F32, name="gate_sb")
         gate2_sb = keep.tile([P, ADAPTER_SLOTS], F32, name="gate2_sb")
         ident = keep.tile([P, P], F32, name="ident")
-        windows = [keep.tile([P, T], F32, name=f"window{b}") for b in range(2)]
-        windows.append(shared.tile([P, T], F32, name="window2", offset=AT_WINDOW, align_bytes=64))
+        windows = [keep.tile([P, T], F32, name=f"window{b}") for b in range(LAST)]
         y = [keep.tile([P, SLOTS], F32, name=f"y{b}") for b in range(BLOCKS)]
 
         nc.gpsimd.memset(x_s[:, :T].bitcast(I32), 0)
@@ -190,13 +188,11 @@ def tile_moe_mlr_relu_kernel(
                                     rhs=h_w[f][:].bitcast(FP8X4), rhs_scale=h_s[f][:], start=True, stop=True)
             return bank
 
-        lanes = keep.tile([P, (BLOCKS * PARTS + 1) * STEP], F32, name="lanes", align_bytes=64)
-
-        def lane(step, steps=PARTS):
-            return lanes[:, step * STEP:(step + steps) * STEP]
-
-        z = [lane(1 + b * PARTS) for b in range(BLOCKS)]
-        plain = [lane(1 + b * PARTS + LAG) for b in range(LAST)]
+        lanes = keep.tile([P, BLOCKS * T], F32, name="lanes", align_bytes=64)
+        z = [lanes[:, b * T:(b + 1) * T] for b in range(LAST)]
+        z.append(lanes[:, LAST * T - P:BLOCKS * T - P])
+        plain = [lanes[:, b * T + LAG * STEP:(b + 1) * T + LAG * STEP] for b in range(LAST)]
+        last_plain = lanes[:, LAST * T + LAG * STEP:LAST * T + (LAG + 1) * STEP]
 
         def gate_rows(b, bank):
             nc.vector.tensor_tensor(z[b].rearrange("n (k s) -> n k s", s=STEP)[:, :, :P],
@@ -235,24 +231,19 @@ def tile_moe_mlr_relu_kernel(
             for half in range(2):
                 add_turned(b, half, windows[WINDOW_OF[b]], closes=closes)
 
-        def fetch_plain(b, part):
-            entries = pos_sb[TOP - 1][:, part * STEP // LIST_ROWS:(part + 1) * STEP // LIST_ROWS]
-            nc.scalar.activation(plain[b][:, part * STEP:(part + 1) * STEP], y[b][:].indirect(entries), COPY)
+        def fetch_plain(into, b, t0):
+            entries = pos_sb[TOP - 1][:, t0 // LIST_ROWS:(t0 + STEP) // LIST_ROWS]
+            nc.scalar.activation(into, y[b][:].indirect(entries), COPY)
 
-        def weave(first, end):
+        def weave(first, end, lag):
             for turn in range(first, end):
                 scatter(turn)
-                fetch_plain(*divmod(turn - LAG - 1, PARTS))
+                b, part = divmod(turn - lag - 1, PARTS)
+                fetch_plain(plain[b][:, part * STEP:(part + 1) * STEP], b, part * STEP)
 
-        gated = {}
-
-        def gate_plain(b, place, halves=range(2)):
-            gated[b] = place
-            for half in halves:
-                tokens = slice(half * BANK, (half + 1) * BANK)
-                nc.vector.tensor_tensor(place[:, tokens], plain[b][:, tokens], gate_sb[:, TOP - 1, tokens], MULT)
-                if b < SQUARED:
-                    add_turned(b, half, place, closes=True)
+        def gate_third(engine, place, source, t0):
+            engine.tensor_tensor(place, source, gate_sb[:, TOP - 1, t0:t0 + place.shape[1]], MULT)
+            return place
 
         def finish_squared(b):
             result = totals[b] = term_tile(f"result{b}", T)
@@ -300,41 +291,48 @@ def tile_moe_mlr_relu_kernel(
         for b in range(2, BLOCKS):
             gate_rows(b, adapter_rows(b, HELD[b]))
         late_rows(1, HELD[:2], (0, 1))
-        late_rows(2, RING[:2], (2,))
-        weave(LAG + 1, 2 * PARTS)
+        late_rows(2, RING[:2])
+        weave(LAG + 1, 2 * PARTS, LAG)
         late_rows(LAST, RING[2:])
-        weave(2 * PARTS, LAST * PARTS)
-        fetch_plain(2, 1)
+        weave(2 * PARTS, LAST * PARTS, LAG)
 
         for b in range(2):
             fetch(b, 0)
             fetch(b, 1)
             add_window(b, closes=(b >= SQUARED))
         fetch(2, 0)
-        gate_plain(0, plain[0], (1, 0))
-        fetch(2, 1)
+        first_gated = term_tile("first_gated", T)[:]
+        for half in (1, 0):
+            tokens = slice(half * BANK, (half + 1) * BANK)
+            gate_third(nc.vector, first_gated[:, tokens], plain[0][:, tokens], half * BANK)
+            add_turned(0, half, first_gated, closes=True)
+        middle = term_tile("middle", T + 3 * STEP)
+        fetch(2, 1, middle[:, 3 * STEP:])
+        gated = {(1, 0): gate_third(nc.gpsimd, plain[0][:, :BANK], plain[1][:, :BANK], 0)}
         add_window(2, closes=True)
         finish_squared(0)
         scatter(LAST * PARTS)
         turn_back(1)
-        weave(LAST * PARTS + 1, BLOCKS * PARTS - 1)
+        weave(LAST * PARTS + 1, BLOCKS * PARTS - 1, LAG + 1)
         scatter(BLOCKS * PARTS - 1)
-        plain.append(term_tile("last_plain", T, AT_WINDOW)[:])
-        fetch_plain(LAST, 2)
-        fetch(LAST, 0, lane(1))
-        gate_plain(1, terms[2, 1])
-        fetch(LAST, 1, lane(1 + PARTS))
+        fused = T - STEP
+        fetch_plain(last_plain, LAST, fused)
+        fetch(LAST, 0, first_gated)
+        gated[1, 1] = gate_third(nc.vector, middle[:, T:T + BANK], plain[1][:, BANK:], BANK)
+        fetch(LAST, 1, middle[:, :T])
+        gated[2, 0] = gate_third(nc.gpsimd, plain[1][:, BANK:], plain[2][:, :BANK], 0)
         add_window(LAST, closes=True)
         turn_back(2)
-        fetch_plain(LAST, 3)
         turn_back(LAST)
-        for t0 in range(0, T, BANK):
-            finish(1, t0, gated[1][:, t0:t0 + BANK])
-        nc.vector.tensor_tensor(gated[1][:, :BANK], y[LAST][:].indirect(pos_sb[TOP - 1][:, :BANK // LIST_ROWS]),
-                                gate_sb[:, TOP - 1, :BANK], MULT)
-        gate_plain(2, terms[LAST, 1])
-        for t0 in range(0, T, BANK):
-            finish(2, t0, gated[2][:, t0:t0 + BANK])
-        nc.vector.tensor_tensor(gated[2][:, :BANK], plain[LAST][:, BANK:], gate_sb[:, TOP - 1, BANK:], MULT)
-        for t0 in range(0, T, STEP):
-            finish(LAST, t0, gated[1 + t0 // BANK][:, t0 % BANK:t0 % BANK + STEP])
+        for half in range(2):
+            finish(1, half * BANK, gated[1, half])
+        gated[2, 1] = gate_third(nc.vector, gated[1, 0], plain[2][:, BANK:], BANK)
+        last_gated = middle[:, T:]
+        nc.vector.tensor_tensor(last_gated, y[LAST][:].indirect(pos_sb[TOP - 1][:, :fused // LIST_ROWS]),
+                                gate_sb[:, TOP - 1, :fused], MULT)
+        last_part = gate_third(nc.gpsimd, plain[2][:, BANK:BANK + STEP], last_plain, fused)
+        for half in range(2):
+            finish(2, half * BANK, gated[2, half])
+        for t0 in range(0, fused, STEP):
+            finish(LAST, t0, last_gated[:, t0:t0 + STEP])
+        finish(LAST, fused, last_part)

@@ -27,21 +27,11 @@ ADAPTER_SLOTS = F * D
 BLOCKS = N // P
 LAST = BLOCKS - 1
 PAIRS = E // 2
-WEIGHT_LOADS = ((0, 2), (2, 6), (6, E))
 PARTS = ADAPTER_SLOTS // P
 STEP = 256
-LAG = 1
-RING = ("mm0", "mm1", "mm2", "mm3")
-HELD = ("q0", "q1", "q2", "q3")
-SUM_BANKS = (HELD[2:], HELD[:2], RING[:2], RING[2:])
-SQUARED = 1
 SQUARE = 32
 RUNS = P // SQUARE
-AT_H = (0, 16 * C)
-AT_XA_S = AT_H[1] + 19 * C
-AT_XA_W = (AT_XA_S + 2 * C, AT_XA_S + 16 * C)
-AT_ZERO = AT_XA_W[1] + 4 * C
-WINDOW_OF = (0, 1, 2, 1)
+WEIGHT_LOADS = ((0, 2), (2, 6), (6, E))
 
 
 def load_scale_rows(nc, tile, rows):
@@ -57,50 +47,52 @@ def tile_moe_mlr_relu_kernel(
     nc = tc.nc
     with ExitStack() as ctx:
         keep = ctx.enter_context(tc.tile_pool(name="keep", bufs=1))
-        shared = ctx.enter_context(tc.tile_pool(name="shared", bufs=1))
-        stage = ctx.enter_context(tc.tile_pool(name="stage", bufs=3))
+        ring = ctx.enter_context(tc.tile_pool(name="ring", bufs=3))
         psum = ctx.enter_context(tc.psum_pool(name="psum", bufs=1))
         taken = []
 
-        def bank_of(tag):
-            taken.append(psum.tile([P, BANK], F32, name=f"bank{len(taken)}", tag=tag))
+        def bank_of(number):
+            taken.append(psum.tile([P, BANK], F32, name=f"bank{len(taken)}", tag=f"b{number}"))
             return taken[-1]
+
+        def floats(name, width):
+            return keep.tile([P, width], F32, name=name, align_bytes=64)
 
         offs_sb = keep.tile([P, SLOTS // LIST_ROWS], U16, name="offs_sb")
         offs2_sb = keep.tile([P, ADAPTER_SLOTS // LIST_ROWS], U16, name="offs2_sb")
         pos_sb = [keep.tile([P, T // LIST_ROWS], U16, name=f"pos_sb{r}") for r in range(TOP)]
         x_w = keep.tile([P, T], I32, name="x_w", align_bytes=64)
-        x_s = keep.tile([P, 2 * T], U8, name="x_s", align_bytes=64)
+        x_s = keep.tile([P, T], U8, name="x_s", align_bytes=64)
         wa_w = keep.tile([P, F, 2 * H], U8, name="wa_w", align_bytes=64)
         wa_s = keep.tile([P, F, H], U8, name="wa_s", align_bytes=64)
         wb_w = keep.tile([P, F, 2 * N], U8, name="wb_w", align_bytes=64)
         wb_s = keep.tile([P, F, N], U8, name="wb_s", align_bytes=64)
         w_w = [keep.tile([P, end - first, 2 * N], U8, name=f"w_w{first}", align_bytes=64) for first, end in WEIGHT_LOADS]
         w_s = keep.tile([P, E, N], U8, name="w_s", align_bytes=64)
-        gate_sb = keep.tile([P, TOP, T], F32, name="gate_sb")
-        gate2_sb = keep.tile([P, ADAPTER_SLOTS], F32, name="gate2_sb")
-        ident = keep.tile([P, P], F32, name="ident")
-        windows = [keep.tile([P, T], F32, name=f"window{b}") for b in range(LAST)]
-        y = [keep.tile([P, SLOTS], F32, name=f"y{b}") for b in range(BLOCKS)]
+        gate_sb = [floats(f"gate_sb{r}", T) for r in range(TOP)]
+        gate2_sb = floats("gate2_sb", ADAPTER_SLOTS)
+        ident = floats("ident", P)
+        windows = [floats(f"window{b}", T) for b in range(LAST)]
+        y = [floats(f"y{b}", SLOTS) for b in range(BLOCKS)]
 
-        nc.gpsimd.memset(x_s[:, :T].bitcast(I32), 0)
-        for scales in (x_s[:, T:], wa_s[:], w_s[:], wb_s[:]):
+        nc.gpsimd.memset(x_s[:].bitcast(I32), 0)
+        zero = floats("zero", 1)
+        nc.gpsimd.memset(zero[:], 0.0)
+        for scales in (wa_s[:], w_s[:], wb_s[:]):
             nc.vector.memset(scales.bitcast(I32), 0)
         make_identity(nc, ident[:])
-        zero = shared.tile([P, 1], F32, name="zero", offset=AT_ZERO, align_bytes=64)
-        nc.gpsimd.memset(zero[:], 0.0)
 
         nc.sync.dma_start(offs2_sb[:], offs2)
         x_scale_rows = x_scales[0].rearrange("(q r) t -> r q t", r=4)
         for r in range(4):
             queue = nc.sync if r < 2 else nc.scalar
-            queue.dma_start(x_s[r:P:32, :T].bitcast(I32), x_scale_rows[r].bitcast(I32))
-        nc.sync.dma_start(offs_sb[:], offs)
+            queue.dma_start(x_s[r:P:32, :].bitcast(I32), x_scale_rows[r].bitcast(I32))
         for window in windows:
             nc.scalar.activation(window[:], zero[:].to_broadcast([P, T]), RELU)
         nc.sync.dma_start(x_w[:], x_words[0].rearrange("p t d -> p (t d)").bitcast(I32))
         nc.sync.dma_start(wa_w[:].bitcast(I32), wa_words[:, 0].rearrange("f p n -> p f n").bitcast(I32))
         load_scale_rows(nc, wa_s, wa_scales[:, 0])
+        nc.sync.dma_start(offs_sb[:], offs)
         load_scale_rows(nc, w_s, w_scales[:, 0])
         for tile, (first, end) in zip(w_w, WEIGHT_LOADS):
             nc.sync.dma_start(tile[:].bitcast(I32), w_words[first:end, 0].rearrange("e p n -> p e n").bitcast(I32))
@@ -110,49 +102,35 @@ def tile_moe_mlr_relu_kernel(
         nc.sync.dma_start(gate2_sb[:], gate2)
         for r, pos in enumerate((pos1, pos2, pos3)):
             nc.sync.dma_start(pos_sb[r][:], pos)
-        nc.sync.dma_start(gate_sb[:], gate.rearrange("r p t -> p r t"))
+        for r in range(TOP):
+            nc.sync.dma_start(gate_sb[r][:], gate[r])
 
-        def gather_scales(entries, scales):
-            nc.vector.tensor_copy(scales[:], x_s[:].indirect(entries))
+        def entries(tile, first, count):
+            return tile[:, first // LIST_ROWS:(first + count) // LIST_ROWS]
+
+        def gather_scales(picked, scales):
+            nc.vector.tensor_copy(scales[:], x_s[:].indirect(picked))
             return scales
 
-        def gather_words(entries, words):
-            nc.vector.tensor_copy(words[:], x_w[:].bitcast(U32).indirect(entries))
+        def gather_words(picked, words):
+            nc.vector.tensor_copy(words[:], x_w[:].bitcast(U32).indirect(picked))
             return words
 
-        expert_w, expert_s = [], []
-
-        def experts(first, end, gather, dtype, into, at=None):
-            shape, name = [P, (end - first) * C], f"xe{len(expert_w)}_{len(expert_s)}"
-            if at is None:
-                tile = keep.tile(shape, dtype, name=name, align_bytes=64)
-            else:
-                tile = shared.tile(shape, dtype, name=name, offset=at, align_bytes=64)
-            gather(offs_sb[:, first * C // LIST_ROWS:end * C // LIST_ROWS], tile)
-            into.extend(tile[:, place * C:(place + 1) * C] for place in range(end - first))
-
-        xa_s = gather_scales(offs2_sb[:], shared.tile([P, ADAPTER_SLOTS], U8, name="xa_s", offset=AT_XA_S, align_bytes=64))
-        experts(0, 3, gather_scales, U8, expert_s)
-        xa_w = [gather_words(offs2_sb[:, f * D // LIST_ROWS:(f + 1) * D // LIST_ROWS],
-                             shared.tile([P, D], U32, name=f"xa_w{f}", offset=AT_XA_W[f], align_bytes=64))
+        xa_s = gather_scales(offs2_sb[:], keep.tile([P, ADAPTER_SLOTS], U8, name="xa_s", align_bytes=64))
+        xa_w = [gather_words(entries(offs2_sb, f * D, D), keep.tile([P, D], U32, name=f"xa_w{f}", align_bytes=64))
                 for f in range(F)]
-        for first, end in ((0, 2), (2, 5)):
-            experts(first, end, gather_words, U32, expert_w)
 
         h_w = [keep.tile([P, D], U32, name=f"h_w{f}", align_bytes=64) for f in range(F)]
         h_s = [keep.tile([P, D], U8, name=f"h_s{f}", align_bytes=64) for f in range(F)]
-        h_in = [shared.tile([P, 4 * D], BF16, name=f"h_in{f}", offset=AT_H[f], align_bytes=64) for f in range(F)]
+        h_in = [keep.tile([P, 4 * D], BF16, name=f"h_in{f}", align_bytes=64) for f in range(F)]
         for f in range(F):
-            turned = bank_of(HELD[f])[:].rearrange("p (a u m) -> p a u m", a=D // P, u=2)
+            turned = bank_of(4 + f)[:].rearrange("p (a u m) -> p a u m", a=D // P, u=2)
             for a in range(D // P):
                 slots = slice(f * D + a * P, f * D + (a + 1) * P)
-                bank = bank_of(RING[2 * f + a])
+                bank = bank_of(2 * f + a)
                 nc.tensor.matmul_mx(bank[:], lhsT=xa_w[f][:, a * P:(a + 1) * P].bitcast(FP8X4), lhsT_scale=xa_s[:, slots],
                                     rhs=wa_w[:, f, :].bitcast(FP4X4), rhs_scale=wa_s[:, f, :], start=True, stop=True)
-                if f == 0 and a == 0:
-                    h_rows = shared.tile([P, H], BF16, name="first_h_rows", offset=AT_ZERO, align_bytes=64)
-                else:
-                    h_rows = stage.tile([P, H], BF16, name="h_rows")
+                h_rows = keep.tile([P, H], BF16, name=f"h_rows{f}_{a}")
                 nc.scalar.activation(h_rows[:].rearrange("m (u p e) -> m u p e", u=2, e=2),
                                      bank[:].rearrange("m (p u e) -> m u p e", u=2, e=2), RELU)
                 pairs = h_rows[:].bitcast(F32)
@@ -160,27 +138,31 @@ def tile_moe_mlr_relu_kernel(
                     nc.tensor.transpose(turned[:, a, u, :], pairs[:, u * P:(u + 1) * P], ident[:])
             nc.scalar.copy(h_in[f][:].bitcast(F32).rearrange("p (a m u) -> p a m u", a=D // P, u=2),
                            turned.rearrange("p a u m -> p a m u"))
-        experts(3, 5, gather_scales, U8, expert_s, AT_XA_W[0])
-        experts(5, 8, gather_words, U32, expert_w, AT_XA_W[0] + 2 * C)
-        experts(5, 8, gather_scales, U8, expert_s, AT_XA_S - C)
-        experts(8, E, gather_scales, U8, expert_s, AT_XA_W[1])
-        for f in range(F):
-            nc.vector.quantize_mx(out=h_w[f][:].bitcast(FP8X4), scales=h_s[f][:], in_=h_in[f][:])
-        experts(8, E - 1, gather_words, U32, expert_w, AT_H[1] + 6 * C)
-        experts(E - 1, E, gather_words, U32, expert_w, AT_H[1] - 2 * C)
 
-        def expert_rows(b, pair, tag):
-            bank = bank_of(tag)
+        tokens = {}
+
+        def gather_pair(pair):
+            picked = entries(offs_sb, pair * BANK, BANK)
+            scales = gather_scales(picked, ring.tile([P, BANK], U8, name=f"pair_s{pair}", tag="pair_s", align_bytes=64))
+            words = gather_words(picked, ring.tile([P, BANK], U32, name=f"pair_w{pair}", tag="pair_w", align_bytes=64))
+            tokens[pair] = words, scales
+
+        def expert_products(b, pair, number):
+            bank = bank_of(number)
+            words, scales = tokens[pair]
             for side in range(2):
                 e = 2 * pair + side
-                nc.tensor.matmul_mx(bank[:, side * C:(side + 1) * C],
-                                    lhsT=weights[e][:, 2 * P * b:2 * P * (b + 1)].bitcast(FP4X4),
-                                    lhsT_scale=w_s[:, e, P * b:P * (b + 1)], rhs=expert_w[e].bitcast(FP8X4),
-                                    rhs_scale=expert_s[e], start=True, stop=True)
+                slots = slice(side * C, (side + 1) * C)
+                nc.tensor.matmul_mx(bank[:, slots], lhsT=weights[e][:, 2 * P * b:2 * P * (b + 1)].bitcast(FP4X4),
+                                    lhsT_scale=w_s[:, e, P * b:P * (b + 1)], rhs=words[:, slots].bitcast(FP8X4),
+                                    rhs_scale=scales[:, slots], start=True, stop=True)
+            return bank
+
+        def copy_rows(b, pair, bank):
             nc.scalar.copy(y[b][:, pair * BANK:(pair + 1) * BANK], bank[:])
 
-        def adapter_rows(b, tag):
-            bank = bank_of(tag)
+        def adapter_products(b, number):
+            bank = bank_of(number)
             for f in range(F):
                 nc.tensor.matmul_mx(bank[:, f * D:(f + 1) * D],
                                     lhsT=wb_w[:, f, 2 * P * b:2 * P * (b + 1)].bitcast(FP4X4),
@@ -188,65 +170,65 @@ def tile_moe_mlr_relu_kernel(
                                     rhs=h_w[f][:].bitcast(FP8X4), rhs_scale=h_s[f][:], start=True, stop=True)
             return bank
 
-        lanes = keep.tile([P, BLOCKS * T], F32, name="lanes", align_bytes=64)
-        z = [lanes[:, b * T:(b + 1) * T] for b in range(LAST)]
-        z.append(lanes[:, LAST * T - P:BLOCKS * T - P])
-        plain = [lanes[:, b * T + LAG * STEP:(b + 1) * T + LAG * STEP] for b in range(LAST)]
-        last_plain = lanes[:, LAST * T + LAG * STEP:LAST * T + (LAG + 1) * STEP]
+        lane = floats("lane", 3 * BANK - P)
+        z = [lane[:, BANK - P:2 * BANK - P], floats("z1", BANK)[:], lane[:, :BANK], lane[:, 2 * BANK - 2 * P:3 * BANK - 2 * P]]
 
         def gate_rows(b, bank):
-            nc.vector.tensor_tensor(z[b].rearrange("n (k s) -> n k s", s=STEP)[:, :, :P],
-                                    bank[:].rearrange("n (k m) -> n k m", m=P),
-                                    gate2_sb[:].rearrange("n (k m) -> n k m", m=P), MULT)
+            nc.vector.tensor_tensor(z[b], bank[:], gate2_sb[:], MULT)
 
-        def scatter(turn):
-            b, part = divmod(turn, PARTS)
-            entries = offs2_sb[:, part * P // LIST_ROWS:(part + 1) * P // LIST_ROWS]
-            nc.scalar.activation(windows[WINDOW_OF[b]][:].indirect(entries), z[b][:, part * STEP:part * STEP + P], COPY)
+        PAIR_BANKS = ((6, 7, 0, 1), (2, 3, 4, 5), (6, 7, 0, 1), (2, 3, 4, 5), (0, 1, 2, 3), (4, 5, 0, 1))
+        z_banks = {}
+        for pair in range(PAIRS - 1):
+            gather_pair(pair)
+            if pair == 3:
+                for f in range(F):
+                    nc.vector.quantize_mx(out=h_w[f][:].bitcast(FP8X4), scales=h_s[f][:], in_=h_in[f][:])
+            if pair == 4:
+                for b in range(2):
+                    z_banks[b] = adapter_products(b, 6 + b)
+            for b in range(BLOCKS):
+                copy_rows(b, pair, expert_products(b, pair, PAIR_BANKS[pair][b]))
+        gather_pair(PAIRS - 1)
+        for b in range(2):
+            gate_rows(b, z_banks[b])
+        late = [expert_products(b, PAIRS - 1, PAIR_BANKS[PAIRS - 1][b]) for b in range(BLOCKS)]
+        for b in range(2, BLOCKS):
+            z_banks[b] = adapter_products(b, b)
+        copy_rows(0, PAIRS - 1, late[0])
 
-        def term_tile(name, width, at=None):
-            if at is None:
-                return keep.tile([P, width], F32, name=name, align_bytes=64)
-            return shared.tile([P, width], F32, name=name, offset=at, align_bytes=64)
+        window_of = windows + windows[:1]
+        PART_ORDER = (0, PARTS - 1, 1, 2)
+
+        def scatter(b, turn):
+            part = PART_ORDER[turn]
+            nc.scalar.activation(window_of[b][:].indirect(entries(offs2_sb, part * P, P)), z[b][:, part * P:(part + 1) * P], COPY)
+
+        def fetch_plain(into, b, r, t0):
+            nc.scalar.activation(into, y[b][:].indirect(entries(pos_sb[r], t0, into.shape[1])), COPY)
+
+        def fetch_woven(into, b, r, t0):
+            nc.scalar.activation(into, y[b][:].indirect(entries(pos_sb[r], t0, into.shape[1])), COPY)
+
+        def fetch_gated(into, b, r, t0=0):
+            width = into.shape[1]
+            nc.vector.tensor_tensor(into, y[b][:].indirect(entries(pos_sb[r], t0, width)), gate_sb[r][:, t0:t0 + width], MULT)
+
+        def times_gate(engine, into, source, r, t0):
+            engine.tensor_tensor(into, source, gate_sb[r][:, t0:t0 + into.shape[1]], MULT)
 
         sums = {}
-        terms = {}
 
         def add_turned(b, half, term, opens=False, closes=False):
             for c in range(BANK // P):
-                t0 = half * BANK + c * P
-                nc.tensor.matmul(sums[b][half][:, c * P:(c + 1) * P], term[:, t0:t0 + P], ident[:], is_transpose=True,
+                nc.tensor.matmul(sums[b][half][:, c * P:(c + 1) * P], term[:, c * P:(c + 1) * P], ident[:], is_transpose=True,
                                  start=(opens and c == 0), stop=(closes and c == BANK // P - 1))
 
-        def fetch(b, r, place=None, closes=False):
-            term = term_tile(f"term{b}_{r}", T)[:] if place is None else place
-            terms[b, r] = term
-            nc.vector.tensor_tensor(term, y[b][:].indirect(pos_sb[r][:]), gate_sb[:, r, :], MULT)
-            if r == 0:
-                sums[b] = [bank_of(tag) for tag in SUM_BANKS[b]]
+        def add_both(b, term, opens=False):
             for half in range(2):
-                add_turned(b, half, term, opens=(r == 0), closes=closes)
-
-        def add_window(b, closes=False):
-            for half in range(2):
-                add_turned(b, half, windows[WINDOW_OF[b]], closes=closes)
-
-        def fetch_plain(into, b, t0):
-            entries = pos_sb[TOP - 1][:, t0 // LIST_ROWS:(t0 + STEP) // LIST_ROWS]
-            nc.scalar.activation(into, y[b][:].indirect(entries), COPY)
-
-        def weave(first, end, lag):
-            for turn in range(first, end):
-                scatter(turn)
-                b, part = divmod(turn - lag - 1, PARTS)
-                fetch_plain(plain[b][:, part * STEP:(part + 1) * STEP], b, part * STEP)
-
-        def gate_third(engine, place, source, t0):
-            engine.tensor_tensor(place, source, gate_sb[:, TOP - 1, t0:t0 + place.shape[1]], MULT)
-            return place
+                add_turned(b, half, term[:, half * BANK:(half + 1) * BANK], opens=opens)
 
         def finish_squared(b):
-            result = totals[b] = term_tile(f"result{b}", T)
+            result = floats(f"result{b}", T)
             for half in range(2):
                 nc.vector.transpose(result[:, half * BANK:(half + 1) * BANK], sums[b][half][:])
             rows = out[P * b:P * (b + 1), :].rearrange("(j a) (c i u) -> i j a c u", a=SQUARE, i=RUNS, u=SQUARE)
@@ -254,85 +236,122 @@ def tile_moe_mlr_relu_kernel(
                 held = result[i * SQUARE:(i + 1) * SQUARE, :].rearrange("a (c j u) -> a j c u", j=RUNS, u=SQUARE)
                 for j in range(RUNS):
                     nc.sync.dma_start(rows[i, j], held[:, j])
+            return result
 
-        backs = {}
-        totals = {}
+        lo, hi = slice(0, BANK), slice(BANK, T)
+        EDGE = P // 2
+        term_b, term_c = (floats(f"term_{name}", T) for name in "bc")
+        wide_a = floats("wide_a", BANK + T)
+        term_a = wide_a[:, BANK:]
+        term_d = floats("term_d", T + BANK - EDGE)
+        wide30 = floats("wide30", STEP + T)
+        wide21 = wide30[:, STEP:]
+        wide22 = floats("wide22", BANK)
+        plain = {key: floats(f"plain{key[0]}_{key[1]}", T)[:] for key in ((0, 2), (1, 2), (3, 0))}
+        plain[2, 1], plain[2, 2] = wide21[:, :T], wide22[:]
+        term31 = term_a
 
-        def turn_back(b, halves=range(2)):
-            for half in halves:
-                total = totals[b, half] = term_tile(f"total{b}_{half}", BANK)[:]
-                nc.scalar.copy(total, sums[b][half][:])
-                backs[b, half] = bank_of(SUM_BANKS[b - 1][half])
-                for c in range(BANK // P):
-                    nc.tensor.transpose(backs[b, half][:, c * P:(c + 1) * P], total[:, c * P:(c + 1) * P], ident[:])
+        def astride(tile):
+            return tile[:, BANK - EDGE:T - EDGE], tile[:, T - EDGE:]
 
-        def finish(b, t0, term):
-            width = term.shape[1]
-            finished = term_tile(f"finished{b}_{t0}", width)
-            back = backs[b, t0 // BANK][:, t0 % BANK:t0 % BANK + width]
-            nc.vector.tensor_tensor(finished[:], back, term, ADD)
-            nc.sync.dma_start(out[P * b:P * (b + 1), t0:t0 + width], finished[:])
+        def weave(b, r, turns):
+            for turn in turns:
+                scatter(b, turn)
+                fetch_woven(plain[b, r][:, turn * STEP:(turn + 1) * STEP], b, r, turn * STEP)
 
-        for pair in range(4):
-            for b, tag in enumerate(RING if pair % 2 == 0 else HELD[2:] + HELD[:2]):
-                expert_rows(b, pair, tag)
-            if pair == 2:
-                z_banks = [adapter_rows(b, RING[b]) for b in range(2)]
-                gate_rows(0, z_banks[0])
-                gate_rows(1, z_banks[1])
-
-        def late_rows(b, tags, scatters=()):
-            for turn, tag in enumerate(tags):
-                expert_rows(b, 4 + turn, tag)
-                if turn < len(scatters):
-                    scatter(scatters[turn])
-
-        late_rows(0, RING[2:])
+        sums[0] = [bank_of(4), bank_of(6)]
+        fetch_gated(term_a, 0, 0)
+        add_both(0, term_a, opens=True)
+        weave(0, 2, (0,))
+        copy_rows(1, PAIRS - 1, late[1])
+        weave(0, 2, (1, 2, 3))
+        fetch_gated(term_b[:], 0, 1)
+        add_both(0, term_b)
+        add_both(0, window_of[0])
         for b in range(2, BLOCKS):
-            gate_rows(b, adapter_rows(b, HELD[b]))
-        late_rows(1, HELD[:2], (0, 1))
-        late_rows(2, RING[:2])
-        weave(LAG + 1, 2 * PARTS, LAG)
-        late_rows(LAST, RING[2:])
-        weave(2 * PARTS, LAST * PARTS, LAG)
+            gate_rows(b, z_banks[b])
+        times_gate(nc.gpsimd, term_d[:, lo], plain[0, 2][:, lo], 2, 0)
+        add_turned(0, 0, term_d[:, lo], closes=True)
+        times_gate(nc.vector, term_d[:, hi], plain[0, 2][:, hi], 2, BANK)
+        add_turned(0, 1, term_d[:, hi], closes=True)
 
-        for b in range(2):
-            fetch(b, 0)
-            fetch(b, 1)
-            add_window(b, closes=(b >= SQUARED))
-        fetch(2, 0)
-        first_gated = term_tile("first_gated", T)[:]
-        for half in (1, 0):
-            tokens = slice(half * BANK, (half + 1) * BANK)
-            gate_third(nc.vector, first_gated[:, tokens], plain[0][:, tokens], half * BANK)
-            add_turned(0, half, first_gated, closes=True)
-        middle = term_tile("middle", T + 3 * STEP)
-        fetch(2, 1, middle[:, 3 * STEP:])
-        gated = {(1, 0): gate_third(nc.gpsimd, plain[0][:, :BANK], plain[1][:, :BANK], 0)}
-        add_window(2, closes=True)
-        finish_squared(0)
-        scatter(LAST * PARTS)
-        turn_back(1)
-        weave(LAST * PARTS + 1, BLOCKS * PARTS - 1, LAG + 1)
-        scatter(BLOCKS * PARTS - 1)
-        fused = T - STEP
-        fetch_plain(last_plain, LAST, fused)
-        fetch(LAST, 0, first_gated)
-        gated[1, 1] = gate_third(nc.vector, middle[:, T:T + BANK], plain[1][:, BANK:], BANK)
-        fetch(LAST, 1, middle[:, :T])
-        gated[2, 0] = gate_third(nc.gpsimd, plain[1][:, BANK:], plain[2][:, :BANK], 0)
-        add_window(LAST, closes=True)
-        turn_back(2)
-        turn_back(LAST)
+        sums[1] = [bank_of(5), bank_of(7)]
+        weave(1, 2, range(PARTS))
+        copy_rows(2, PAIRS - 1, late[2])
+        fetch_gated(term_a, 1, 0)
+        add_both(1, term_a, opens=True)
+        add_both(1, window_of[1])
+        fetch_gated(term_b[:], 1, 1)
+        add_both(1, term_b)
+        result0 = finish_squared(0)
+        times_gate(nc.gpsimd, term_a[:, lo], plain[1, 2][:, lo], 2, 0)
+        add_turned(1, 0, term_a[:, lo], closes=True)
+        times_gate(nc.vector, term_d[:, hi], plain[1, 2][:, hi], 2, BANK)
+        add_turned(1, 1, term_d[:, hi], closes=True)
+
+        sums[2] = [bank_of(2), bank_of(3)]
         for half in range(2):
-            finish(1, half * BANK, gated[1, half])
-        gated[2, 1] = gate_third(nc.vector, gated[1, 0], plain[2][:, BANK:], BANK)
-        last_gated = middle[:, T:]
-        nc.vector.tensor_tensor(last_gated, y[LAST][:].indirect(pos_sb[TOP - 1][:, :fused // LIST_ROWS]),
-                                gate_sb[:, TOP - 1, :fused], MULT)
-        last_part = gate_third(nc.gpsimd, plain[2][:, BANK:BANK + STEP], last_plain, fused)
-        for half in range(2):
-            finish(2, half * BANK, gated[2, half])
-        for t0 in range(0, fused, STEP):
-            finish(LAST, t0, last_gated[:, t0:t0 + STEP])
-        finish(LAST, fused, last_part)
+            scatter(2, half)
+            into = plain[2, 1][:, half * BANK:(half + 1) * BANK]
+            fetch_woven(into[:, :STEP], 2, 1, half * BANK)
+            fetch_plain(into[:, STEP:], 2, 1, half * BANK + STEP)
+        copy_rows(LAST, PAIRS - 1, late[LAST])
+        for step in range(2):
+            scatter(2, 2 + step)
+            fetch_woven(plain[2, 2][:, step * STEP:(step + 1) * STEP], 2, 2, step * STEP)
+        fetch_gated(term_c[:], 2, 0)
+        add_both(2, term_c, opens=True)
+        result1 = finish_squared(1)
+        times_gate(nc.gpsimd, term_a[:, lo], plain[2, 1][:, lo], 1, 0)
+        add_turned(2, 0, term_a[:, lo])
+        gated21, gated22 = astride(term_d)
+        times_gate(nc.vector, gated21, plain[2, 1][:, hi], 1, BANK)
+        add_turned(2, 1, gated21)
+        add_both(2, window_of[2])
+        times_gate(nc.vector, gated22, plain[2, 2][:, lo], 2, 0)
+        add_turned(2, 0, gated22, closes=True)
+        fetch_gated(wide21[:, hi], 2, 2, BANK)
+        add_turned(2, 1, wide21[:, hi], closes=True)
+
+        sums[LAST] = [bank_of(0)]
+        weave(LAST, 0, range(PARTS))
+        fetch_gated(term31, LAST, 1)
+        add_turned(LAST, 0, term31[:, lo], opens=True)
+        add_turned(LAST, 0, window_of[LAST][:, lo])
+        result2 = finish_squared(2)
+        gated30 = wide30[:, STEP:STEP + BANK]
+        times_gate(nc.gpsimd, gated30, plain[LAST, 0][:, lo], 0, 0)
+        add_turned(LAST, 0, gated30, closes=True)
+        plain32 = lane[:, 2 * BANK - P:]
+        fetch_plain(plain32, LAST, 2, 0)
+        early_plain = lane[:, 2 * BANK - 3 * P:2 * BANK - P]
+        fetch_plain(early_plain, LAST, 2, BANK)
+        total = floats("total", BANK)
+        nc.scalar.copy(total[:], sums[LAST][0][:])
+        back = bank_of(1)
+        for c in range(BANK // P):
+            nc.tensor.transpose(back[:, c * P:(c + 1) * P], total[:, c * P:(c + 1) * P], ident[:])
+        middle = STEP + BANK - EDGE
+        last_plain = [early_plain, wide30[:, middle:middle + STEP]]
+        fetch_plain(last_plain[1], LAST, 2, T - STEP)
+        runs = wide_a[:, :T].rearrange("n (c s u) -> n s c u", s=2, u=P)
+        first_sum, gated30b = runs[:, 0], runs[:, 1]
+
+        def in_runs(span):
+            return span.rearrange("n (c u) -> n c u", u=P)
+
+        partial = floats("partial", BANK)
+        finished = floats("finished", T)
+        last_gated = [plain32[:, :STEP], total[:, STEP:]]
+        nc.vector.tensor_tensor(first_sum, in_runs(window_of[LAST][:, hi]), in_runs(term31[:, hi]), ADD)
+        nc.vector.tensor_tensor(gated30b, in_runs(plain[LAST, 0][:, hi]), in_runs(gate_sb[0][:, hi]), MULT)
+        times_gate(nc.vector, term31[:, hi], plain32, 2, 0)
+        nc.vector.tensor_tensor(in_runs(partial[:]), first_sum, gated30b, ADD)
+        times_gate(nc.vector, last_gated[0], last_plain[0], 2, BANK)
+        nc.vector.tensor_tensor(finished[:, lo], back[:], term31[:, hi], ADD)
+        nc.sync.dma_start(out[P * LAST:, lo], finished[:, lo])
+        times_gate(nc.vector, last_gated[1], last_plain[1], 2, T - STEP)
+        for step in range(2):
+            span = slice(BANK + step * STEP, BANK + (step + 1) * STEP)
+            nc.vector.tensor_tensor(finished[:, span], partial[:, step * STEP:(step + 1) * STEP], last_gated[step], ADD)
+            nc.sync.dma_start(out[P * LAST:, span], finished[:, span])

@@ -170,7 +170,7 @@ def tile_moe_mlr_relu_kernel(
                                     rhs=h_w[f][:].bitcast(FP8X4), rhs_scale=h_s[f][:], start=True, stop=True)
             return bank
 
-        lane = floats("lane", 3 * BANK - P)
+        lane = floats("lane", 3 * BANK - 2 * P)
         z = [lane[:, BANK - P:2 * BANK - P], floats("z1", BANK)[:], lane[:, :BANK], lane[:, 2 * BANK - 2 * P:3 * BANK - 2 * P]]
 
         def gate_rows(b, bank):
@@ -243,13 +243,10 @@ def tile_moe_mlr_relu_kernel(
         term_b, term_c = (floats(f"term_{name}", T) for name in "bc")
         wide_a = floats("wide_a", BANK + T)
         term_a = wide_a[:, BANK:]
-        term_d = floats("term_d", T + BANK - EDGE)
-        wide30 = floats("wide30", STEP + T)
-        wide21 = wide30[:, STEP:]
-        wide22 = floats("wide22", BANK)
-        plain = {key: floats(f"plain{key[0]}_{key[1]}", T)[:] for key in ((0, 2), (1, 2), (3, 0))}
-        plain[2, 1], plain[2, 2] = wide21[:, :T], wide22[:]
-        term31 = term_a
+        term_d = floats("term_d", 2 * T - EDGE)
+        wide21 = floats("wide21", T)[:]
+        plain = {key: floats(f"plain{key[0]}_{key[1]}", T)[:] for key in ((0, 2), (1, 2))}
+        plain[2, 1] = wide21
 
         def astride(tile):
             return tile[:, BANK - EDGE:T - EDGE], tile[:, T - EDGE:]
@@ -290,68 +287,57 @@ def tile_moe_mlr_relu_kernel(
         add_turned(1, 1, term_d[:, hi], closes=True)
 
         sums[2] = [bank_of(2), bank_of(3)]
-        for half in range(2):
-            scatter(2, half)
-            into = plain[2, 1][:, half * BANK:(half + 1) * BANK]
-            fetch_woven(into[:, :STEP], 2, 1, half * BANK)
-            fetch_plain(into[:, STEP:], 2, 1, half * BANK + STEP)
+        weave(2, 1, (0, 1))
         copy_rows(LAST, PAIRS - 1, late[LAST])
-        for step in range(2):
-            scatter(2, 2 + step)
-            fetch_woven(plain[2, 2][:, step * STEP:(step + 1) * STEP], 2, 2, step * STEP)
+        weave(2, 1, (2, 3))
         fetch_gated(term_c[:], 2, 0)
         add_both(2, term_c, opens=True)
         result1 = finish_squared(1)
         times_gate(nc.gpsimd, term_a[:, lo], plain[2, 1][:, lo], 1, 0)
         add_turned(2, 0, term_a[:, lo])
-        gated21, gated22 = astride(term_d)
+        gated21, term22 = astride(term_d)
+        add_both(2, window_of[2])
+        fetch_gated(term22, 2, 2)
+        add_turned(2, 0, term22[:, lo], closes=True)
         times_gate(nc.vector, gated21, plain[2, 1][:, hi], 1, BANK)
         add_turned(2, 1, gated21)
-        add_both(2, window_of[2])
-        times_gate(nc.vector, gated22, plain[2, 2][:, lo], 2, 0)
-        add_turned(2, 0, gated22, closes=True)
-        fetch_gated(wide21[:, hi], 2, 2, BANK)
-        add_turned(2, 1, wide21[:, hi], closes=True)
+        add_turned(2, 1, term22[:, hi], closes=True)
 
         sums[LAST] = [bank_of(0)]
-        weave(LAST, 0, range(PARTS))
-        fetch_gated(term31, LAST, 1)
-        add_turned(LAST, 0, term31[:, lo], opens=True)
-        add_turned(LAST, 0, window_of[LAST][:, lo])
+        plain_hi = [floats(f"plain_hi{r}", BANK) for r in range(2)]
+        for turn in range(PARTS):
+            r, step = divmod(turn, 2)
+            scatter(LAST, turn)
+            fetch_woven(plain_hi[r][:, step * STEP:(step + 1) * STEP], LAST, r, BANK + step * STEP)
+        fetch_gated(term_a[:, lo], LAST, 1)
+        add_turned(LAST, 0, term_a[:, lo], opens=True)
+        fetch_gated(gated21, LAST, 0)
+        add_turned(LAST, 0, gated21)
+        add_turned(LAST, 0, window_of[LAST][:, lo], closes=True)
         result2 = finish_squared(2)
-        gated30 = wide30[:, STEP:STEP + BANK]
-        times_gate(nc.gpsimd, gated30, plain[LAST, 0][:, lo], 0, 0)
-        add_turned(LAST, 0, gated30, closes=True)
-        plain32 = lane[:, 2 * BANK - P:]
-        fetch_plain(plain32, LAST, 2, 0)
-        early_plain = lane[:, 2 * BANK - 3 * P:2 * BANK - P]
-        fetch_plain(early_plain, LAST, 2, BANK)
+        gated30, term32 = wide_a[:, STEP:STEP + BANK], wide_a[:, STEP + BANK:STEP + T]
+        times_gate(nc.gpsimd, gated30, plain_hi[0][:], 0, BANK)
+        plain32 = z[LAST]
+        fetch_plain(plain32[:, STEP:], LAST, 2, 0)
         total = floats("total", BANK)
         nc.scalar.copy(total[:], sums[LAST][0][:])
         back = bank_of(1)
         for c in range(BANK // P):
             nc.tensor.transpose(back[:, c * P:(c + 1) * P], total[:, c * P:(c + 1) * P], ident[:])
-        middle = STEP + BANK - EDGE
-        last_plain = [early_plain, wide30[:, middle:middle + STEP]]
-        fetch_plain(last_plain[1], LAST, 2, T - STEP)
-        runs = wide_a[:, :T].rearrange("n (c s u) -> n s c u", s=2, u=P)
-        first_sum, gated30b = runs[:, 0], runs[:, 1]
-
-        def in_runs(span):
-            return span.rearrange("n (c u) -> n c u", u=P)
-
-        partial = floats("partial", BANK)
+        last_plain = gated21[:, STEP:]
+        fetch_plain(last_plain, LAST, 2, STEP)
+        sum_a, sum_b = (floats(name, BANK) for name in ("sum_a", "sum_b"))
         finished = floats("finished", T)
-        last_gated = [plain32[:, :STEP], total[:, STEP:]]
-        nc.vector.tensor_tensor(first_sum, in_runs(window_of[LAST][:, hi]), in_runs(term31[:, hi]), ADD)
-        nc.vector.tensor_tensor(gated30b, in_runs(plain[LAST, 0][:, hi]), in_runs(gate_sb[0][:, hi]), MULT)
-        times_gate(nc.vector, term31[:, hi], plain32, 2, 0)
-        nc.vector.tensor_tensor(in_runs(partial[:]), first_sum, gated30b, ADD)
-        times_gate(nc.vector, last_gated[0], last_plain[0], 2, BANK)
-        nc.vector.tensor_tensor(finished[:, lo], back[:], term31[:, hi], ADD)
-        nc.sync.dma_start(out[P * LAST:, lo], finished[:, lo])
-        times_gate(nc.vector, last_gated[1], last_plain[1], 2, T - STEP)
-        for step in range(2):
-            span = slice(BANK + step * STEP, BANK + (step + 1) * STEP)
-            nc.vector.tensor_tensor(finished[:, span], partial[:, step * STEP:(step + 1) * STEP], last_gated[step], ADD)
+        fetch_gated(term32, LAST, 2, BANK)
+        nc.vector.tensor_tensor(sum_a[:], gated30, window_of[LAST][:, hi], ADD)
+        times_gate(nc.vector, plain_hi[0][:], plain_hi[1][:], 1, BANK)
+        nc.vector.tensor_tensor(sum_b[:], sum_a[:], term32, ADD)
+        gated32 = gated30
+        times_gate(nc.vector, gated32[:, :STEP], plain32[:, STEP:], 2, 0)
+        nc.vector.tensor_tensor(finished[:, hi], sum_b[:], plain_hi[0][:], ADD)
+        nc.sync.dma_start(out[P * LAST:, hi], finished[:, hi])
+        times_gate(nc.vector, gated32[:, STEP:], last_plain, 2, STEP)
+        for t0 in range(0, BANK, STEP):
+            span = slice(t0, t0 + STEP)
+            nc.vector.tensor_tensor(finished[:, span], back[:, span], gated32[:, span], ADD)
             nc.sync.dma_start(out[P * LAST:, span], finished[:, span])

@@ -31,6 +31,9 @@ PARTS = ADAPTER_SLOTS // P
 STEP = 256
 SQUARE = 32
 RUNS = P // SQUARE
+LEAD = 1
+AT_PAIR_S = (0, 2 * BANK, 0, 2 * BANK, 0, 2 * BANK - STEP)
+AT_LANE = 2 * BANK + STEP
 WEIGHT_LOADS = ((0, 2), (2, 6), (6, E))
 
 
@@ -47,7 +50,8 @@ def tile_moe_mlr_relu_kernel(
     nc = tc.nc
     with ExitStack() as ctx:
         keep = ctx.enter_context(tc.tile_pool(name="keep", bufs=1))
-        ring = ctx.enter_context(tc.tile_pool(name="ring", bufs=3))
+        ring = ctx.enter_context(tc.tile_pool(name="ring", bufs=2))
+        shared = ctx.enter_context(tc.tile_pool(name="shared", bufs=1))
         psum = ctx.enter_context(tc.psum_pool(name="psum", bufs=1))
         taken = []
 
@@ -75,7 +79,6 @@ def tile_moe_mlr_relu_kernel(
         windows = [floats(f"window{b}", T) for b in range(LAST)]
         y = [floats(f"y{b}", SLOTS) for b in range(BLOCKS)]
 
-        nc.gpsimd.memset(x_s[:].bitcast(I32), 0)
         zero = floats("zero", 1)
         nc.gpsimd.memset(zero[:], 0.0)
         for scales in (wa_s[:], w_s[:], wb_s[:]):
@@ -83,23 +86,24 @@ def tile_moe_mlr_relu_kernel(
         make_identity(nc, ident[:])
 
         nc.sync.dma_start(offs2_sb[:], offs2)
-        x_scale_rows = x_scales[0].rearrange("(q r) t -> r q t", r=4)
-        for r in range(4):
-            queue = nc.sync if r < 2 else nc.scalar
-            queue.dma_start(x_s[r:P:32, :].bitcast(I32), x_scale_rows[r].bitcast(I32))
+        for q in range(4):
+            queue = nc.sync if q < 2 else nc.scalar
+            queue.dma_start(x_s[32 * q:32 * (q + 1), :].bitcast(I32),
+                            x_scales[0, 4 * q:4 * (q + 1), :].bitcast(I32).partition_broadcast(8))
+        nc.sync.dma_start(offs_sb[:], offs)
         for window in windows:
             nc.scalar.activation(window[:], zero[:].to_broadcast([P, T]), RELU)
         nc.sync.dma_start(x_w[:], x_words[0].rearrange("p t d -> p (t d)").bitcast(I32))
         nc.sync.dma_start(wa_w[:].bitcast(I32), wa_words[:, 0].rearrange("f p n -> p f n").bitcast(I32))
         load_scale_rows(nc, wa_s, wa_scales[:, 0])
-        nc.sync.dma_start(offs_sb[:], offs)
         load_scale_rows(nc, w_s, w_scales[:, 0])
         for tile, (first, end) in zip(w_w, WEIGHT_LOADS):
+            if end == E:
+                load_scale_rows(nc, wb_s, wb_scales[:, 0])
+                nc.sync.dma_start(wb_w[:].bitcast(I32), wb_words[:, 0].rearrange("f p n -> p f n").bitcast(I32))
+                nc.sync.dma_start(gate2_sb[:], gate2)
             nc.sync.dma_start(tile[:].bitcast(I32), w_words[first:end, 0].rearrange("e p n -> p e n").bitcast(I32))
         weights = [tile[:, place, :] for tile in w_w for place in range(tile.shape[1])]
-        load_scale_rows(nc, wb_s, wb_scales[:, 0])
-        nc.sync.dma_start(wb_w[:].bitcast(I32), wb_words[:, 0].rearrange("f p n -> p f n").bitcast(I32))
-        nc.sync.dma_start(gate2_sb[:], gate2)
         for r, pos in enumerate((pos1, pos2, pos3)):
             nc.sync.dma_start(pos_sb[r][:], pos)
         for r in range(TOP):
@@ -116,7 +120,14 @@ def tile_moe_mlr_relu_kernel(
             nc.vector.tensor_copy(words[:], x_w[:].bitcast(U32).indirect(picked))
             return words
 
-        xa_s = gather_scales(offs2_sb[:], keep.tile([P, ADAPTER_SLOTS], U8, name="xa_s", align_bytes=64))
+        xa_s = gather_scales(offs2_sb[:], shared.tile([P, ADAPTER_SLOTS], U8, name="xa_s", offset=AT_PAIR_S[1], align_bytes=64))
+        pair_scales = {}
+
+        def gather_pair_scales(pair):
+            tile = shared.tile([P, BANK], U8, name=f"pair_s{pair}", offset=AT_PAIR_S[pair], align_bytes=64)
+            pair_scales[pair] = gather_scales(entries(offs_sb, pair * BANK, BANK), tile)
+
+        gather_pair_scales(0)
         xa_w = [gather_words(entries(offs2_sb, f * D, D), keep.tile([P, D], U32, name=f"xa_w{f}", align_bytes=64))
                 for f in range(F)]
 
@@ -141,11 +152,14 @@ def tile_moe_mlr_relu_kernel(
 
         tokens = {}
 
-        def gather_pair(pair):
-            picked = entries(offs_sb, pair * BANK, BANK)
-            scales = gather_scales(picked, ring.tile([P, BANK], U8, name=f"pair_s{pair}", tag="pair_s", align_bytes=64))
-            words = gather_words(picked, ring.tile([P, BANK], U32, name=f"pair_w{pair}", tag="pair_w", align_bytes=64))
-            tokens[pair] = words, scales
+        def gather_pair(pair, cuts=1):
+            if pair > 0:
+                gather_pair_scales(pair)
+            words = ring.tile([P, BANK], U32, name=f"pair_w{pair}", tag="pair_w", align_bytes=64)
+            width = BANK // cuts
+            for cut in range(cuts):
+                gather_words(entries(offs_sb, pair * BANK + cut * width, width), words[:, cut * width:(cut + 1) * width])
+            tokens[pair] = words, pair_scales[pair]
 
         def expert_products(b, pair, number):
             bank = bank_of(number)
@@ -170,38 +184,50 @@ def tile_moe_mlr_relu_kernel(
                                     rhs=h_w[f][:].bitcast(FP8X4), rhs_scale=h_s[f][:], start=True, stop=True)
             return bank
 
-        lane = floats("lane", 3 * BANK - 2 * P)
-        z = [lane[:, BANK - P:2 * BANK - P], floats("z1", BANK)[:], lane[:, :BANK], lane[:, 2 * BANK - 2 * P:3 * BANK - 2 * P]]
+        z = []
 
         def gate_rows(b, bank):
-            nc.vector.tensor_tensor(z[b], bank[:], gate2_sb[:], MULT)
-
-        PAIR_BANKS = ((6, 7, 0, 1), (2, 3, 4, 5), (6, 7, 0, 1), (2, 3, 4, 5), (0, 1, 2, 3), (4, 5, 0, 1))
-        z_banks = {}
-        for pair in range(PAIRS - 1):
-            gather_pair(pair)
-            if pair == 3:
-                for f in range(F):
-                    nc.vector.quantize_mx(out=h_w[f][:].bitcast(FP8X4), scales=h_s[f][:], in_=h_in[f][:])
-            if pair == 4:
-                for b in range(2):
-                    z_banks[b] = adapter_products(b, 6 + b)
-            for b in range(BLOCKS):
-                copy_rows(b, pair, expert_products(b, pair, PAIR_BANKS[pair][b]))
-        gather_pair(PAIRS - 1)
-        for b in range(2):
-            gate_rows(b, z_banks[b])
-        late = [expert_products(b, PAIRS - 1, PAIR_BANKS[PAIRS - 1][b]) for b in range(BLOCKS)]
-        for b in range(2, BLOCKS):
-            z_banks[b] = adapter_products(b, b)
-        copy_rows(0, PAIRS - 1, late[0])
+            nc.vector.tensor_tensor(z[b], bank[:].rearrange("n (k m) -> n k m", m=P),
+                                    gate2_sb[:].rearrange("n (k m) -> n k m", m=P), MULT)
 
         window_of = windows + windows[:1]
-        PART_ORDER = (0, PARTS - 1, 1, 2)
+        PART_ORDER = (1, 2, 0, PARTS - 1)
 
-        def scatter(b, turn):
-            part = PART_ORDER[turn]
-            nc.scalar.activation(window_of[b][:].indirect(entries(offs2_sb, part * P, P)), z[b][:, part * P:(part + 1) * P], COPY)
+        def scatter(turn):
+            b, part = turn // PARTS, PART_ORDER[turn % PARTS]
+            nc.scalar.activation(window_of[b][:].indirect(entries(offs2_sb, part * P, P)), z[b][:, part], COPY)
+
+        PAIR_BANKS = ((6, 7, 0, 1), (2, 3, 4, 5), (6, 7, 0, 1), (3, 4, 5, 6))
+        z_banks = {}
+        for pair in range(PAIRS - 2):
+            gather_pair(pair)
+            if pair == 2:
+                for f in range(F):
+                    nc.vector.quantize_mx(out=h_w[f][:].bitcast(FP8X4), scales=h_s[f][:], in_=h_in[f][:])
+            if pair == 3:
+                z_banks[0] = adapter_products(0, 2)
+            for b in range(BLOCKS):
+                copy_rows(b, pair, expert_products(b, pair, PAIR_BANKS[pair][b]))
+        gather_pair(PAIRS - 2)
+        lane = shared.tile([P, 28, P], F32, name="lane", offset=AT_LANE, align_bytes=64)
+        z.extend([lane[:, 3:7], lane[:, 4::6], lane[:, :4], lane[:, 6:10]])
+        gate_rows(0, z_banks[0])
+        for b, number in ((1, 7), (2, 0), (3, 1)):
+            z_banks[b] = adapter_products(b, number)
+        for b in range(2):
+            copy_rows(b, PAIRS - 2, expert_products(b, PAIRS - 2, 3 + b))
+        for turn in range(LEAD):
+            scatter(turn)
+        gather_pair(PAIRS - 1, cuts=2)
+        gate_rows(1, z_banks[1])
+        late = {(b, PAIRS - 2): expert_products(b, PAIRS - 2, number) for b, number in ((2, 5), (LAST, 2))}
+        for b, number in enumerate((6, 3, 4)):
+            late[b, PAIRS - 1] = expert_products(b, PAIRS - 1, number)
+        for side in range(2):
+            nc.scalar.copy(y[0][:, SLOTS - BANK + side * C:SLOTS - BANK + (side + 1) * C],
+                           late[0, PAIRS - 1][:, side * C:(side + 1) * C])
+        copy_rows(1, PAIRS - 1, late[1, PAIRS - 1])
+        late[LAST, PAIRS - 1] = expert_products(LAST, PAIRS - 1, 3)
 
         def fetch_plain(into, b, r, t0):
             nc.scalar.activation(into, y[b][:].indirect(entries(pos_sb[r], t0, into.shape[1])), COPY)
@@ -218,10 +244,13 @@ def tile_moe_mlr_relu_kernel(
 
         sums = {}
 
-        def add_turned(b, half, term, opens=False, closes=False):
-            for c in range(BANK // P):
+        def add_turned(b, half, term, opens=False, closes=False, backwards=False):
+            order = list(range(BANK // P))
+            if backwards:
+                order = order[::-1]
+            for c in order:
                 nc.tensor.matmul(sums[b][half][:, c * P:(c + 1) * P], term[:, c * P:(c + 1) * P], ident[:], is_transpose=True,
-                                 start=(opens and c == 0), stop=(closes and c == BANK // P - 1))
+                                 start=(opens and c == order[0]), stop=(closes and c == order[-1]))
 
         def add_both(b, term, opens=False):
             for half in range(2):
@@ -240,88 +269,89 @@ def tile_moe_mlr_relu_kernel(
 
         lo, hi = slice(0, BANK), slice(BANK, T)
         EDGE = P // 2
-        term_b, term_c = (floats(f"term_{name}", T) for name in "bc")
-        wide_a = floats("wide_a", BANK + T)
-        term_a = wide_a[:, BANK:]
-        term_d = floats("term_d", 2 * T - EDGE)
-        wide21 = floats("wide21", T)[:]
+        term_b = floats("term_b", T)
+        strip = floats("strip", 4 * (T - EDGE) + BANK)
+        terms = [strip[:, BANK - EDGE + n * (T - EDGE):BANK - EDGE + n * (T - EDGE) + T] for n in range(4)]
+        ahead_of = [strip[:, n * (T - EDGE):n * (T - EDGE) + BANK] for n in range(2)]
+        wide21 = floats("wide21", BANK)[:]
         plain = {key: floats(f"plain{key[0]}_{key[1]}", T)[:] for key in ((0, 2), (1, 2))}
         plain[2, 1] = wide21
 
-        def astride(tile):
-            return tile[:, BANK - EDGE:T - EDGE], tile[:, T - EDGE:]
-
         def weave(b, r, turns):
             for turn in turns:
-                scatter(b, turn)
+                scatter(b * PARTS + turn + LEAD)
                 fetch_woven(plain[b, r][:, turn * STEP:(turn + 1) * STEP], b, r, turn * STEP)
 
-        sums[0] = [bank_of(4), bank_of(6)]
-        fetch_gated(term_a, 0, 0)
-        add_both(0, term_a, opens=True)
-        weave(0, 2, (0,))
-        copy_rows(1, PAIRS - 1, late[1])
-        weave(0, 2, (1, 2, 3))
+        sums[0] = [bank_of(6), bank_of(7)]
+        fetch_gated(terms[0], 0, 0)
+        add_both(0, terms[0], opens=True)
+        weave(0, 2, range(PARTS))
+        add_both(0, window_of[0])
         fetch_gated(term_b[:], 0, 1)
         add_both(0, term_b)
-        add_both(0, window_of[0])
         for b in range(2, BLOCKS):
             gate_rows(b, z_banks[b])
-        times_gate(nc.gpsimd, term_d[:, lo], plain[0, 2][:, lo], 2, 0)
-        add_turned(0, 0, term_d[:, lo], closes=True)
-        times_gate(nc.vector, term_d[:, hi], plain[0, 2][:, hi], 2, BANK)
-        add_turned(0, 1, term_d[:, hi], closes=True)
+        times_gate(nc.gpsimd, ahead_of[0], plain[0, 2][:, lo], 2, 0)
+        add_turned(0, 0, ahead_of[0], closes=True)
+        gated02 = floats("gated02", BANK)
+        times_gate(nc.vector, gated02[:], plain[0, 2][:, hi], 2, BANK)
+        add_turned(0, 1, gated02, closes=True)
 
-        sums[1] = [bank_of(5), bank_of(7)]
+        sums[1] = [bank_of(0), bank_of(1)]
         weave(1, 2, range(PARTS))
-        copy_rows(2, PAIRS - 1, late[2])
-        fetch_gated(term_a, 1, 0)
-        add_both(1, term_a, opens=True)
+        for pair in range(PAIRS - 2, PAIRS):
+            copy_rows(2, pair, late[2, pair])
+        fetch_gated(terms[1], 1, 0)
+        add_both(1, terms[1], opens=True)
         add_both(1, window_of[1])
         fetch_gated(term_b[:], 1, 1)
         add_both(1, term_b)
         result0 = finish_squared(0)
-        times_gate(nc.gpsimd, term_a[:, lo], plain[1, 2][:, lo], 2, 0)
-        add_turned(1, 0, term_a[:, lo], closes=True)
-        times_gate(nc.vector, term_d[:, hi], plain[1, 2][:, hi], 2, BANK)
-        add_turned(1, 1, term_d[:, hi], closes=True)
+        times_gate(nc.gpsimd, ahead_of[1], plain[1, 2][:, lo], 2, 0)
+        add_turned(1, 0, ahead_of[1], closes=True)
+        gated12 = terms[1][:, P:P + BANK]
+        times_gate(nc.vector, gated12, plain[1, 2][:, hi], 2, BANK)
+        add_turned(1, 1, gated12, closes=True)
 
-        sums[2] = [bank_of(2), bank_of(3)]
+        sums[2] = [bank_of(4), bank_of(5)]
         weave(2, 1, (0, 1))
-        copy_rows(LAST, PAIRS - 1, late[LAST])
-        weave(2, 1, (2, 3))
-        fetch_gated(term_c[:], 2, 0)
-        add_both(2, term_c, opens=True)
-        result1 = finish_squared(1)
-        times_gate(nc.gpsimd, term_a[:, lo], plain[2, 1][:, lo], 1, 0)
-        add_turned(2, 0, term_a[:, lo])
-        gated21, term22 = astride(term_d)
+        scatter(LAST * PARTS - 1)
+        for pair in range(PAIRS - 2, PAIRS):
+            copy_rows(LAST, pair, late[LAST, pair])
+        fetch_gated(terms[2], 2, 0)
+        for half, span in ((1, hi), (0, lo)):
+            add_turned(2, half, terms[2][:, span], opens=True, backwards=True)
         add_both(2, window_of[2])
+        result1 = finish_squared(1)
+        times_gate(nc.gpsimd, ahead_of[1], plain[2, 1][:, lo], 1, 0)
+        add_turned(2, 0, ahead_of[1])
+        gated21, term22 = terms[2][:, STEP:STEP + BANK], terms[3]
         fetch_gated(term22, 2, 2)
         add_turned(2, 0, term22[:, lo], closes=True)
-        times_gate(nc.vector, gated21, plain[2, 1][:, hi], 1, BANK)
+        fetch_gated(gated21, 2, 1, BANK)
         add_turned(2, 1, gated21)
         add_turned(2, 1, term22[:, hi], closes=True)
 
-        sums[LAST] = [bank_of(0)]
+        sums[LAST] = [bank_of(2)]
         plain_hi = [floats(f"plain_hi{r}", BANK) for r in range(2)]
         for turn in range(PARTS):
             r, step = divmod(turn, 2)
-            scatter(LAST, turn)
-            fetch_woven(plain_hi[r][:, step * STEP:(step + 1) * STEP], LAST, r, BANK + step * STEP)
-        fetch_gated(term_a[:, lo], LAST, 1)
-        add_turned(LAST, 0, term_a[:, lo], opens=True)
+            scatter(LAST * PARTS + turn)
+            fetch_plain(plain_hi[r][:, step * STEP:(step + 1) * STEP], LAST, r, BANK + step * STEP)
+        fetch_gated(ahead_of[1], LAST, 1)
+        add_turned(LAST, 0, ahead_of[1], opens=True)
         fetch_gated(gated21, LAST, 0)
-        add_turned(LAST, 0, gated21)
-        add_turned(LAST, 0, window_of[LAST][:, lo], closes=True)
+        add_turned(LAST, 0, window_of[LAST][:, lo])
+        add_turned(LAST, 0, gated21, closes=True)
         result2 = finish_squared(2)
-        gated30, term32 = wide_a[:, STEP:STEP + BANK], wide_a[:, STEP + BANK:STEP + T]
+        middle = T - EDGE + STEP
+        gated30, term32 = strip[:, middle - BANK:middle], strip[:, middle:middle + BANK]
         times_gate(nc.gpsimd, gated30, plain_hi[0][:], 0, BANK)
-        plain32 = z[LAST]
+        plain32 = z[LAST].rearrange("n k m -> n (k m)")
         fetch_plain(plain32[:, STEP:], LAST, 2, 0)
         total = floats("total", BANK)
         nc.scalar.copy(total[:], sums[LAST][0][:])
-        back = bank_of(1)
+        back = bank_of(3)
         for c in range(BANK // P):
             nc.tensor.transpose(back[:, c * P:(c + 1) * P], total[:, c * P:(c + 1) * P], ident[:])
         last_plain = gated21[:, STEP:]

@@ -244,8 +244,8 @@ def tile_moe_mlr_relu_kernel(
 
         sums = {}
 
-        def add_turned(b, half, term, opens=False, closes=False, backwards=False):
-            order = list(range(BANK // P))
+        def add_turned(b, half, term, opens=False, closes=False, backwards=False, chunks=range(BANK // P)):
+            order = list(chunks)
             if backwards:
                 order = order[::-1]
             for c in order:
@@ -269,13 +269,15 @@ def tile_moe_mlr_relu_kernel(
 
         lo, hi = slice(0, BANK), slice(BANK, T)
         EDGE = P // 2
-        term_b = floats("term_b", T)
-        strip = floats("strip", 4 * (T - EDGE) + BANK)
-        terms = [strip[:, BANK - EDGE + n * (T - EDGE):BANK - EDGE + n * (T - EDGE) + T] for n in range(4)]
-        ahead_of = [strip[:, n * (T - EDGE):n * (T - EDGE) + BANK] for n in range(2)]
-        wide21 = floats("wide21", BANK)[:]
-        plain = {key: floats(f"plain{key[0]}_{key[1]}", T)[:] for key in ((0, 2), (1, 2))}
-        plain[2, 1] = wide21
+        strip = floats("strip", 4288)
+
+        def place(first, width):
+            return strip[:, first:first + width]
+
+        by_pool = place(448, BANK)
+        term00, term10, term11, term20 = (place(first, T) for first in (896, 1856, 960, 2816))
+        term01 = floats("term01", T)
+        plain = {(0, 2): floats("plain0", T)[:], (1, 2): floats("plain1", BANK)[:], (2, 1): floats("plain2", BANK)[:]}
 
         def weave(b, r, turns):
             for turn in turns:
@@ -283,90 +285,110 @@ def tile_moe_mlr_relu_kernel(
                 fetch_woven(plain[b, r][:, turn * STEP:(turn + 1) * STEP], b, r, turn * STEP)
 
         sums[0] = [bank_of(6), bank_of(7)]
-        fetch_gated(terms[0], 0, 0)
-        add_both(0, terms[0], opens=True)
+        fetch_gated(term00, 0, 0)
+        add_both(0, term00, opens=True)
         weave(0, 2, range(PARTS))
         add_both(0, window_of[0])
-        fetch_gated(term_b[:], 0, 1)
-        add_both(0, term_b)
+        fetch_gated(term01[:], 0, 1)
+        add_both(0, term01)
         for b in range(2, BLOCKS):
             gate_rows(b, z_banks[b])
-        times_gate(nc.gpsimd, ahead_of[0], plain[0, 2][:, lo], 2, 0)
-        add_turned(0, 0, ahead_of[0], closes=True)
+        times_gate(nc.gpsimd, by_pool, plain[0, 2][:, lo], 2, 0)
+        add_turned(0, 0, by_pool, closes=True)
         gated02 = floats("gated02", BANK)
         times_gate(nc.vector, gated02[:], plain[0, 2][:, hi], 2, BANK)
         add_turned(0, 1, gated02, closes=True)
 
         sums[1] = [bank_of(0), bank_of(1)]
-        weave(1, 2, range(PARTS))
+        fetch_plain(plain[1, 2][:, :STEP], 1, 2, 0)
+        scatter(PARTS + 1)
+        fetch_plain(plain[1, 2][:, STEP:], 1, 2, STEP)
+        for turn in range(PARTS + 2, 2 * PARTS):
+            scatter(turn)
         for pair in range(PAIRS - 2, PAIRS):
             copy_rows(2, pair, late[2, pair])
-        fetch_gated(terms[1], 1, 0)
-        add_both(1, terms[1], opens=True)
+        fetch_gated(term10, 1, 0)
+        add_both(1, term10, opens=True)
         add_both(1, window_of[1])
-        fetch_gated(term_b[:], 1, 1)
-        add_both(1, term_b)
         result0 = finish_squared(0)
-        times_gate(nc.gpsimd, ahead_of[1], plain[1, 2][:, lo], 2, 0)
-        add_turned(1, 0, ahead_of[1], closes=True)
-        gated12 = terms[1][:, P:P + BANK]
-        times_gate(nc.vector, gated12, plain[1, 2][:, hi], 2, BANK)
+        times_gate(nc.gpsimd, by_pool, plain[1, 2], 2, 0)
+        add_turned(1, 0, by_pool)
+        fetch_gated(term11, 1, 1)
+        add_turned(1, 0, term11[:, lo], closes=True)
+        add_turned(1, 1, term11[:, hi])
+        gated12 = term10[:, 3 * P:3 * P + BANK]
+        fetch_gated(gated12, 1, 2, BANK)
         add_turned(1, 1, gated12, closes=True)
 
         sums[2] = [bank_of(4), bank_of(5)]
-        weave(2, 1, (0, 1))
-        scatter(LAST * PARTS - 1)
+        for step in range(2):
+            scatter(2 * PARTS + step)
+            fetch_plain(plain[2, 1][:, step * STEP:(step + 1) * STEP], 2, 1, step * STEP)
+        for turn in range(2 * PARTS + 2, LAST * PARTS):
+            scatter(turn)
         for pair in range(PAIRS - 2, PAIRS):
             copy_rows(LAST, pair, late[LAST, pair])
-        fetch_gated(terms[2], 2, 0)
+        for turn in range(LAST * PARTS, BLOCKS * PARTS):
+            scatter(turn)
+        fetch_gated(term20, 2, 0)
         for half, span in ((1, hi), (0, lo)):
-            add_turned(2, half, terms[2][:, span], opens=True, backwards=True)
-        add_both(2, window_of[2])
+            add_turned(2, half, term20[:, span], opens=True, backwards=True)
         result1 = finish_squared(1)
-        times_gate(nc.gpsimd, ahead_of[1], plain[2, 1][:, lo], 1, 0)
-        add_turned(2, 0, ahead_of[1])
-        gated21, term22 = terms[2][:, STEP:STEP + BANK], terms[3]
-        fetch_gated(term22, 2, 2)
-        add_turned(2, 0, term22[:, lo], closes=True)
-        fetch_gated(gated21, 2, 1, BANK)
-        add_turned(2, 1, gated21)
-        add_turned(2, 1, term22[:, hi], closes=True)
+        times_gate(nc.gpsimd, by_pool, plain[2, 1], 1, 0)
+        add_turned(2, 0, by_pool)
+        term21 = place(3776, BANK)
+        fetch_gated(term21, 2, 1, BANK)
+        add_turned(2, 0, window_of[2][:, lo], closes=True)
+        add_turned(2, 1, window_of[2][:, hi])
+        add_turned(2, 1, term21, closes=True)
+
+        def total_of(b, half):
+            total = floats(f"total{b}_{half}", BANK)
+            nc.scalar.copy(total[:], sums[b][half][:])
+            return total
+
+        def turn_back(total, number):
+            back = bank_of(number)
+            for c in range(BANK // P):
+                nc.tensor.transpose(back[:, c * P:(c + 1) * P], total[:, c * P:(c + 1) * P], ident[:])
+            return back
 
         sums[LAST] = [bank_of(2)]
-        plain_hi = [floats(f"plain_hi{r}", BANK) for r in range(2)]
-        for turn in range(PARTS):
-            r, step = divmod(turn, 2)
-            scatter(LAST * PARTS + turn)
-            fetch_plain(plain_hi[r][:, step * STEP:(step + 1) * STEP], LAST, r, BANK + step * STEP)
-        fetch_gated(ahead_of[1], LAST, 1)
-        add_turned(LAST, 0, ahead_of[1], opens=True)
-        fetch_gated(gated21, LAST, 0)
+        totals2 = [total_of(2, half) for half in range(2)]
+        for t0 in range(0, BANK, STEP):
+            fetch_plain(term21[:, t0:t0 + STEP], LAST, 0, BANK + t0)
+        term31, term30, term22 = place(0, BANK), place(3264, BANK), place(896, T)
+        fetch_gated(term31, LAST, 1)
+        add_turned(LAST, 0, term31, opens=True)
         add_turned(LAST, 0, window_of[LAST][:, lo])
-        add_turned(LAST, 0, gated21, closes=True)
-        result2 = finish_squared(2)
-        middle = T - EDGE + STEP
-        gated30, term32 = strip[:, middle - BANK:middle], strip[:, middle:middle + BANK]
-        times_gate(nc.gpsimd, gated30, plain_hi[0][:], 0, BANK)
-        plain32 = z[LAST].rearrange("n k m -> n (k m)")
-        fetch_plain(plain32[:, STEP:], LAST, 2, 0)
-        total = floats("total", BANK)
-        nc.scalar.copy(total[:], sums[LAST][0][:])
-        back = bank_of(3)
-        for c in range(BANK // P):
-            nc.tensor.transpose(back[:, c * P:(c + 1) * P], total[:, c * P:(c + 1) * P], ident[:])
-        last_plain = gated21[:, STEP:]
-        fetch_plain(last_plain, LAST, 2, STEP)
-        sum_a, sum_b = (floats(name, BANK) for name in ("sum_a", "sum_b"))
-        finished = floats("finished", T)
+        fetch_gated(term30, LAST, 0)
+        backs2 = [turn_back(totals2[half], 6 + half) for half in range(2)]
+        add_turned(LAST, 0, term30, closes=True)
+        term32, plain31 = totals2[0][:], totals2[1][:]
+        fetch_plain(plain31, LAST, 1, BANK)
+        total = total_of(LAST, 0)
+        back = turn_back(total, 3)
+        plain32 = [place(3712 - STEP, STEP), place(3712, STEP)]
+        fetch_gated(term22, 2, 2)
         fetch_gated(term32, LAST, 2, BANK)
-        nc.vector.tensor_tensor(sum_a[:], gated30, window_of[LAST][:, hi], ADD)
-        times_gate(nc.vector, plain_hi[0][:], plain_hi[1][:], 1, BANK)
-        nc.vector.tensor_tensor(sum_b[:], sum_a[:], term32, ADD)
-        gated32 = gated30
-        times_gate(nc.vector, gated32[:, :STEP], plain32[:, STEP:], 2, 0)
-        nc.vector.tensor_tensor(finished[:, hi], sum_b[:], plain_hi[0][:], ADD)
+        finished2 = floats("finished2", T)
+        for half, span in enumerate((lo, hi)):
+            nc.vector.tensor_tensor(finished2[:, span], backs2[half][:], term22[:, span], ADD)
+            nc.sync.dma_start(out[2 * P:LAST * P, span], finished2[:, span])
+        times_gate(nc.gpsimd, term31, term21, 0, BANK)
+        for step in range(2):
+            fetch_plain(plain32[step], LAST, 2, step * STEP)
+        sum_a, gated31 = term22[:, lo], floats("gated31", BANK)
+        sum_b = floats("sum_b", BANK)
+        finished = floats("finished", T)
+        gated32 = term32
+        nc.vector.tensor_tensor(sum_a, term32, window_of[LAST][:, hi], ADD)
+        times_gate(nc.vector, gated31[:], plain31, 1, BANK)
+        nc.vector.tensor_tensor(sum_b[:], sum_a, term31, ADD)
+        times_gate(nc.vector, gated32[:, :STEP], plain32[0], 2, 0)
+        nc.vector.tensor_tensor(finished[:, hi], sum_b[:], gated31[:], ADD)
         nc.sync.dma_start(out[P * LAST:, hi], finished[:, hi])
-        times_gate(nc.vector, gated32[:, STEP:], last_plain, 2, STEP)
+        times_gate(nc.vector, gated32[:, STEP:], plain32[1], 2, STEP)
         for t0 in range(0, BANK, STEP):
             span = slice(t0, t0 + STEP)
             nc.vector.tensor_tensor(finished[:, span], back[:, span], gated32[:, span], ADD)

@@ -31,9 +31,10 @@ PARTS = ADAPTER_SLOTS // P
 STEP = 256
 SQUARE = 32
 RUNS = P // SQUARE
-LEAD = 1
-AT_PAIR_S = (0, 2 * BANK, 0, 2 * BANK, 0, 2 * BANK - STEP)
-AT_LANE = 2 * BANK + STEP
+AT_XA_W = 0
+AT_XA_S = 4 * D
+AT_LANE = AT_XA_S + STEP
+AT_PAIR_S = (AT_LANE + 14 * 4 * P, AT_XA_S, AT_XA_W)
 WEIGHT_LOADS = ((0, 2), (2, 6), (6, E))
 
 
@@ -50,7 +51,7 @@ def tile_moe_mlr_relu_kernel(
     nc = tc.nc
     with ExitStack() as ctx:
         keep = ctx.enter_context(tc.tile_pool(name="keep", bufs=1))
-        ring = ctx.enter_context(tc.tile_pool(name="ring", bufs=2))
+        ring = ctx.enter_context(tc.tile_pool(name="ring", bufs=3))
         shared = ctx.enter_context(tc.tile_pool(name="shared", bufs=1))
         psum = ctx.enter_context(tc.psum_pool(name="psum", bufs=1))
         taken = []
@@ -76,7 +77,7 @@ def tile_moe_mlr_relu_kernel(
         gate_sb = [floats(f"gate_sb{r}", T) for r in range(TOP)]
         gate2_sb = floats("gate2_sb", ADAPTER_SLOTS)
         ident = floats("ident", P)
-        windows = [floats(f"window{b}", T) for b in range(LAST)]
+        windows = [floats(f"window{b}", T) for b in range(2)]
         y = [floats(f"y{b}", SLOTS) for b in range(BLOCKS)]
 
         zero = floats("zero", 1)
@@ -120,16 +121,18 @@ def tile_moe_mlr_relu_kernel(
             nc.vector.tensor_copy(words[:], x_w[:].bitcast(U32).indirect(picked))
             return words
 
-        xa_s = gather_scales(offs2_sb[:], shared.tile([P, ADAPTER_SLOTS], U8, name="xa_s", offset=AT_PAIR_S[1], align_bytes=64))
+        xa_s = gather_scales(offs2_sb[:], shared.tile([P, ADAPTER_SLOTS], U8, name="xa_s", offset=AT_XA_S, align_bytes=64))
         pair_scales = {}
 
         def gather_pair_scales(pair):
-            tile = shared.tile([P, BANK], U8, name=f"pair_s{pair}", offset=AT_PAIR_S[pair], align_bytes=64)
+            tile = shared.tile([P, BANK], U8, name=f"pair_s{pair}", offset=AT_PAIR_S[pair % 3], align_bytes=64)
             pair_scales[pair] = gather_scales(entries(offs_sb, pair * BANK, BANK), tile)
 
         gather_pair_scales(0)
-        xa_w = [gather_words(entries(offs2_sb, f * D, D), keep.tile([P, D], U32, name=f"xa_w{f}", align_bytes=64))
-                for f in range(F)]
+        xa_w = [shared.tile([P, D], U32, name="xa_w0", offset=AT_XA_W, align_bytes=64),
+                keep.tile([P, D], U32, name="xa_w1", align_bytes=64)]
+        for f in range(F):
+            gather_words(entries(offs2_sb, f * D, D), xa_w[f])
 
         h_w = [keep.tile([P, D], U32, name=f"h_w{f}", align_bytes=64) for f in range(F)]
         h_s = [keep.tile([P, D], U8, name=f"h_s{f}", align_bytes=64) for f in range(F)]
@@ -190,44 +193,37 @@ def tile_moe_mlr_relu_kernel(
             nc.vector.tensor_tensor(z[b], bank[:].rearrange("n (k m) -> n k m", m=P),
                                     gate2_sb[:].rearrange("n (k m) -> n k m", m=P), MULT)
 
-        window_of = windows + windows[:1]
-        PART_ORDER = (1, 2, 0, PARTS - 1)
+        window_of = windows + windows
+        PART_ORDER = (0, PARTS - 1, 1, 2)
 
         def scatter(turn):
             b, part = turn // PARTS, PART_ORDER[turn % PARTS]
             nc.scalar.activation(window_of[b][:].indirect(entries(offs2_sb, part * P, P)), z[b][:, part], COPY)
 
-        PAIR_BANKS = ((6, 7, 0, 1), (2, 3, 4, 5), (6, 7, 0, 1), (3, 4, 5, 6))
+        PAIR_BANKS = ((6, 7, 0, 1), (2, 3, 4, 5), (6, 7, 0, 1), (2, 3, 4, 5), (0, 1, 2, 3), (4, 5, 0, 1))
         z_banks = {}
-        for pair in range(PAIRS - 2):
+        for pair in range(PAIRS - 1):
             gather_pair(pair)
-            if pair == 2:
+            if pair == 3:
                 for f in range(F):
                     nc.vector.quantize_mx(out=h_w[f][:].bitcast(FP8X4), scales=h_s[f][:], in_=h_in[f][:])
-            if pair == 3:
-                z_banks[0] = adapter_products(0, 2)
+            if pair == 4:
+                for b in range(2):
+                    z_banks[b] = adapter_products(b, 6 + b)
             for b in range(BLOCKS):
                 copy_rows(b, pair, expert_products(b, pair, PAIR_BANKS[pair][b]))
-        gather_pair(PAIRS - 2)
-        lane = shared.tile([P, 28, P], F32, name="lane", offset=AT_LANE, align_bytes=64)
-        z.extend([lane[:, 3:7], lane[:, 4::6], lane[:, :4], lane[:, 6:10]])
-        gate_rows(0, z_banks[0])
-        for b, number in ((1, 7), (2, 0), (3, 1)):
-            z_banks[b] = adapter_products(b, number)
-        for b in range(2):
-            copy_rows(b, PAIRS - 2, expert_products(b, PAIRS - 2, 3 + b))
-        for turn in range(LEAD):
-            scatter(turn)
         gather_pair(PAIRS - 1, cuts=2)
-        gate_rows(1, z_banks[1])
-        late = {(b, PAIRS - 2): expert_products(b, PAIRS - 2, number) for b, number in ((2, 5), (LAST, 2))}
-        for b, number in enumerate((6, 3, 4)):
-            late[b, PAIRS - 1] = expert_products(b, PAIRS - 1, number)
+        lane = shared.tile([P, 14, P], F32, name="lane", offset=AT_LANE, align_bytes=64)
+        z.extend([lane[:, 3:7], lane[:, 10:], lane[:, :4], lane[:, 6:10]])
+        for b in range(2):
+            gate_rows(b, z_banks[b])
+        late = [expert_products(b, PAIRS - 1, PAIR_BANKS[PAIRS - 1][b]) for b in range(BLOCKS)]
+        for b in range(2, BLOCKS):
+            z_banks[b] = adapter_products(b, b)
         for side in range(2):
             nc.scalar.copy(y[0][:, SLOTS - BANK + side * C:SLOTS - BANK + (side + 1) * C],
-                           late[0, PAIRS - 1][:, side * C:(side + 1) * C])
-        copy_rows(1, PAIRS - 1, late[1, PAIRS - 1])
-        late[LAST, PAIRS - 1] = expert_products(LAST, PAIRS - 1, 3)
+                           late[0][:, side * C:(side + 1) * C])
+        copy_rows(1, PAIRS - 1, late[1])
 
         def fetch_plain(into, b, r, t0):
             nc.scalar.activation(into, y[b][:].indirect(entries(pos_sb[r], t0, into.shape[1])), COPY)
@@ -256,91 +252,24 @@ def tile_moe_mlr_relu_kernel(
             for half in range(2):
                 add_turned(b, half, term[:, half * BANK:(half + 1) * BANK], opens=opens)
 
-        def finish_squared(b):
-            result = floats(f"result{b}", T)
-            for half in range(2):
-                nc.vector.transpose(result[:, half * BANK:(half + 1) * BANK], sums[b][half][:])
-            rows = out[P * b:P * (b + 1), :].rearrange("(j a) (c i u) -> i j a c u", a=SQUARE, i=RUNS, u=SQUARE)
-            for i in range(RUNS):
-                held = result[i * SQUARE:(i + 1) * SQUARE, :].rearrange("a (c j u) -> a j c u", j=RUNS, u=SQUARE)
-                for j in range(RUNS):
-                    nc.sync.dma_start(rows[i, j], held[:, j])
-            return result
-
         lo, hi = slice(0, BANK), slice(BANK, T)
         EDGE = P // 2
-        strip = floats("strip", 4288)
+        strip = floats("strip", 4352)
+        second = floats("second", 1728)
 
-        def place(first, width):
-            return strip[:, first:first + width]
+        def place(tile, first, width):
+            return tile[:, first:first + width]
 
-        by_pool = place(448, BANK)
-        term00, term10, term11, term20 = (place(first, T) for first in (896, 1856, 960, 2816))
-        term01 = floats("term01", T)
-        plain = {(0, 2): floats("plain0", T)[:], (1, 2): floats("plain1", BANK)[:], (2, 1): floats("plain2", BANK)[:]}
+        plain = [floats(f"plain{b}", BANK) for b in range(2)]
 
-        def weave(b, r, turns):
-            for turn in turns:
-                scatter(b * PARTS + turn + LEAD)
-                fetch_woven(plain[b, r][:, turn * STEP:(turn + 1) * STEP], b, r, turn * STEP)
+        def weave(b, r, t0):
+            for step in range(2):
+                scatter(b * PARTS + step)
+                fetch_plain(plain[b][:, step * STEP:(step + 1) * STEP], b, r, t0 + step * STEP)
 
-        sums[0] = [bank_of(6), bank_of(7)]
-        fetch_gated(term00, 0, 0)
-        add_both(0, term00, opens=True)
-        weave(0, 2, range(PARTS))
-        add_both(0, window_of[0])
-        fetch_gated(term01[:], 0, 1)
-        add_both(0, term01)
-        for b in range(2, BLOCKS):
-            gate_rows(b, z_banks[b])
-        times_gate(nc.gpsimd, by_pool, plain[0, 2][:, lo], 2, 0)
-        add_turned(0, 0, by_pool, closes=True)
-        gated02 = floats("gated02", BANK)
-        times_gate(nc.vector, gated02[:], plain[0, 2][:, hi], 2, BANK)
-        add_turned(0, 1, gated02, closes=True)
-
-        sums[1] = [bank_of(0), bank_of(1)]
-        fetch_plain(plain[1, 2][:, :STEP], 1, 2, 0)
-        scatter(PARTS + 1)
-        fetch_plain(plain[1, 2][:, STEP:], 1, 2, STEP)
-        for turn in range(PARTS + 2, 2 * PARTS):
-            scatter(turn)
-        for pair in range(PAIRS - 2, PAIRS):
-            copy_rows(2, pair, late[2, pair])
-        fetch_gated(term10, 1, 0)
-        add_both(1, term10, opens=True)
-        add_both(1, window_of[1])
-        result0 = finish_squared(0)
-        times_gate(nc.gpsimd, by_pool, plain[1, 2], 2, 0)
-        add_turned(1, 0, by_pool)
-        fetch_gated(term11, 1, 1)
-        add_turned(1, 0, term11[:, lo], closes=True)
-        add_turned(1, 1, term11[:, hi])
-        gated12 = term10[:, 3 * P:3 * P + BANK]
-        fetch_gated(gated12, 1, 2, BANK)
-        add_turned(1, 1, gated12, closes=True)
-
-        sums[2] = [bank_of(4), bank_of(5)]
-        for step in range(2):
-            scatter(2 * PARTS + step)
-            fetch_plain(plain[2, 1][:, step * STEP:(step + 1) * STEP], 2, 1, step * STEP)
-        for turn in range(2 * PARTS + 2, LAST * PARTS):
-            scatter(turn)
-        for pair in range(PAIRS - 2, PAIRS):
-            copy_rows(LAST, pair, late[LAST, pair])
-        for turn in range(LAST * PARTS, BLOCKS * PARTS):
-            scatter(turn)
-        fetch_gated(term20, 2, 0)
-        for half, span in ((1, hi), (0, lo)):
-            add_turned(2, half, term20[:, span], opens=True, backwards=True)
-        result1 = finish_squared(1)
-        times_gate(nc.gpsimd, by_pool, plain[2, 1], 1, 0)
-        add_turned(2, 0, by_pool)
-        term21 = place(3776, BANK)
-        fetch_gated(term21, 2, 1, BANK)
-        add_turned(2, 0, window_of[2][:, lo], closes=True)
-        add_turned(2, 1, window_of[2][:, hi])
-        add_turned(2, 1, term21, closes=True)
+        def rest_of_scatter(b):
+            for turn in range(2, PARTS):
+                scatter(b * PARTS + turn)
 
         def total_of(b, half):
             total = floats(f"total{b}_{half}", BANK)
@@ -353,40 +282,105 @@ def tile_moe_mlr_relu_kernel(
                 nc.tensor.transpose(back[:, c * P:(c + 1) * P], total[:, c * P:(c + 1) * P], ident[:])
             return back
 
-        sums[LAST] = [bank_of(2)]
+        def finish(b, backs, thirds):
+            finished = floats(f"finished{b}", T)
+            for half, span in enumerate((lo, hi)):
+                nc.vector.tensor_tensor(finished[:, span], backs[half][:], thirds[half], ADD)
+                nc.sync.dma_start(out[b * P:(b + 1) * P, span], finished[:, span])
+            return finished
+
+        def close_with_window(b, term):
+            add_turned(b, 0, term[:, lo], closes=True)
+            add_turned(b, 1, term[:, hi])
+            add_turned(b, 1, window_of[b][:, hi], closes=True, chunks=(3,))
+
+        sums[0] = [bank_of(4), bank_of(6)]
+        term00, gated02 = place(strip, 1408, T), place(strip, 960, BANK)
+        term01, term02 = place(second, 704, T), place(second, 256, BANK)
+        fetch_gated(term00, 0, 0)
+        add_both(0, term00, opens=True)
+        weave(0, 2, 0)
+        rest_of_scatter(0)
+        fetch_gated(term01, 0, 1)
+        add_both(0, term01)
+        for half, span in enumerate((lo, hi)):
+            add_turned(0, half, window_of[0][:, span], closes=True)
+        for b in range(2, BLOCKS):
+            gate_rows(b, z_banks[b])
+        times_gate(nc.gpsimd, gated02, plain[0][:], 2, 0)
+
+        sums[1] = [bank_of(5), bank_of(7)]
+        weave(1, 2, 0)
+        totals0 = [total_of(0, half) for half in range(2)]
+        rest_of_scatter(1)
+        for b in range(2, BLOCKS):
+            copy_rows(b, PAIRS - 1, late[b])
+        term10, term11 = place(strip, 2368, T), term01
+        fetch_gated(term10, 1, 0)
+        add_both(1, term10, opens=True)
+        add_turned(1, 0, window_of[1][:, lo])
+        add_turned(1, 1, window_of[1][:, hi], chunks=(0, 1, 2))
+        fetch_gated(term11, 1, 1)
+        close_with_window(1, term11)
+        backs0 = [turn_back(totals0[half], 2 + half) for half in range(2)]
+
+        sums[2] = [bank_of(4), bank_of(6)]
+        plain.append(term10[:, P:P + BANK])
+        weave(2, 2, 0)
+        totals1 = [total_of(1, half) for half in range(2)]
+        rest_of_scatter(2)
+        term20, term21 = place(strip, 3328, T), place(strip, 0, T)
+        fetch_gated(term20, 2, 0)
+        add_both(2, term20, opens=True)
+        add_both(2, window_of[2])
+        fetch_gated(term02, 0, 2, BANK)
+        done0 = finish(0, backs0, (gated02, term02))
+        gated12 = totals0[0][:]
+        times_gate(nc.gpsimd, gated12, plain[1][:], 2, 0)
+        fetch_gated(term21, 2, 1)
+        for half, span in enumerate((lo, hi)):
+            add_turned(2, half, term21[:, span], closes=True)
+        backs1 = [turn_back(totals1[half], half) for half in range(2)]
+
+        sums[LAST] = [bank_of(5)]
+        plain.append(totals0[1])
+        weave(LAST, 0, BANK)
         totals2 = [total_of(2, half) for half in range(2)]
-        for t0 in range(0, BANK, STEP):
-            fetch_plain(term21[:, t0:t0 + STEP], LAST, 0, BANK + t0)
-        term31, term30, term22 = place(0, BANK), place(3264, BANK), place(896, T)
+        rest_of_scatter(LAST)
+        term31, term12 = place(second, 0, BANK), place(second, BANK, BANK)
+        term30 = place(strip, 1408, BANK)
         fetch_gated(term31, LAST, 1)
         add_turned(LAST, 0, term31, opens=True)
-        add_turned(LAST, 0, window_of[LAST][:, lo])
-        fetch_gated(term30, LAST, 0)
-        backs2 = [turn_back(totals2[half], 6 + half) for half in range(2)]
-        add_turned(LAST, 0, term30, closes=True)
-        term32, plain31 = totals2[0][:], totals2[1][:]
+        plain31 = term31
         fetch_plain(plain31, LAST, 1, BANK)
+        fetch_gated(term30, LAST, 0)
+        add_turned(LAST, 0, term30, chunks=(0, 1, 2))
+        add_turned(LAST, 0, window_of[LAST][:, lo])
+        add_turned(LAST, 0, term30, closes=True, chunks=(3,))
+        backs2 = [turn_back(totals2[half], 2 + half) for half in range(2)]
         total = total_of(LAST, 0)
-        back = turn_back(total, 3)
-        plain32 = [place(3712 - STEP, STEP), place(3712, STEP)]
-        fetch_gated(term22, 2, 2)
-        fetch_gated(term32, LAST, 2, BANK)
-        finished2 = floats("finished2", T)
-        for half, span in enumerate((lo, hi)):
-            nc.vector.tensor_tensor(finished2[:, span], backs2[half][:], term22[:, span], ADD)
-            nc.sync.dma_start(out[2 * P:LAST * P, span], finished2[:, span])
-        times_gate(nc.gpsimd, term31, term21, 0, BANK)
+        back = turn_back(total, 7)
+        plain32 = [place(strip, 1856 - STEP, STEP), place(strip, 1856, STEP)]
         for step in range(2):
             fetch_plain(plain32[step], LAST, 2, step * STEP)
-        sum_a, gated31 = term22[:, lo], floats("gated31", BANK)
+        fetch_gated(term12, 1, 2, BANK)
+        done1 = finish(1, backs1, (gated12, term12))
+        gated22 = totals1[0][:]
+        times_gate(nc.gpsimd, gated22, plain[2], 2, 0)
+        term22, term32 = gated12, term12
+        fetch_gated(term22, 2, 2, BANK)
+        fetch_gated(term32, LAST, 2, BANK)
+        done2 = finish(2, backs2, (gated22, term22))
+        gated30 = totals2[0][:]
+        times_gate(nc.gpsimd, gated30, plain[LAST][:], 0, BANK)
+        sum_a, gated31, gated32 = gated22, term22, term32
         sum_b = floats("sum_b", BANK)
         finished = floats("finished", T)
-        gated32 = term32
         nc.vector.tensor_tensor(sum_a, term32, window_of[LAST][:, hi], ADD)
-        times_gate(nc.vector, gated31[:], plain31, 1, BANK)
-        nc.vector.tensor_tensor(sum_b[:], sum_a, term31, ADD)
+        times_gate(nc.vector, gated31, plain31, 1, BANK)
+        nc.vector.tensor_tensor(sum_b[:], sum_a, gated30, ADD)
         times_gate(nc.vector, gated32[:, :STEP], plain32[0], 2, 0)
-        nc.vector.tensor_tensor(finished[:, hi], sum_b[:], gated31[:], ADD)
+        nc.vector.tensor_tensor(finished[:, hi], sum_b[:], gated31, ADD)
         nc.sync.dma_start(out[P * LAST:, hi], finished[:, hi])
         times_gate(nc.vector, gated32[:, STEP:], plain32[1], 2, STEP)
         for t0 in range(0, BANK, STEP):

@@ -31,10 +31,10 @@ PARTS = ADAPTER_SLOTS // P
 STEP = 256
 SQUARE = 32
 RUNS = P // SQUARE
-AT_XA_W = 0
-AT_XA_S = 4 * D
-AT_LANE = AT_XA_S + STEP
-AT_PAIR_S = (AT_LANE + 14 * 4 * P, AT_XA_S, AT_XA_W)
+AT_XA_S = 0
+AT_XA_W = ADAPTER_SLOTS
+AT_LANE = AT_XA_W + STEP
+AT_PAIR_S = (AT_LANE + 14 * 4 * P, AT_XA_W, AT_XA_S)
 WEIGHT_LOADS = ((0, 2), (2, 6), (6, E))
 
 
@@ -210,20 +210,23 @@ def tile_moe_mlr_relu_kernel(
             if pair == 4:
                 for b in range(2):
                     z_banks[b] = adapter_products(b, 6 + b)
-            for b in range(BLOCKS):
+            for b in range(BLOCKS if pair < 4 else 1):
                 copy_rows(b, pair, expert_products(b, pair, PAIR_BANKS[pair][b]))
+        held = {b: expert_products(b, PAIRS - 2, b) for b in range(1, BLOCKS)}
         gather_pair(PAIRS - 1, cuts=2)
         lane = shared.tile([P, 14, P], F32, name="lane", offset=AT_LANE, align_bytes=64)
         z.extend([lane[:, 3:7], lane[:, 10:], lane[:, :4], lane[:, 6:10]])
         for b in range(2):
             gate_rows(b, z_banks[b])
-        late = [expert_products(b, PAIRS - 1, PAIR_BANKS[PAIRS - 1][b]) for b in range(BLOCKS)]
-        for b in range(2, BLOCKS):
-            z_banks[b] = adapter_products(b, b)
+        late = [expert_products(b, PAIRS - 1, PAIR_BANKS[PAIRS - 1][b]) for b in range(LAST)]
         for side in range(2):
             nc.scalar.copy(y[0][:, SLOTS - BANK + side * C:SLOTS - BANK + (side + 1) * C],
                            late[0][:, side * C:(side + 1) * C])
+        copy_rows(1, PAIRS - 2, held[1])
         copy_rows(1, PAIRS - 1, late[1])
+        late.append(expert_products(LAST, PAIRS - 1, PAIR_BANKS[PAIRS - 1][LAST]))
+        for b in range(2, BLOCKS):
+            z_banks[b] = adapter_products(b, 2 + b)
 
         def fetch_plain(into, b, r, t0):
             nc.scalar.activation(into, y[b][:].indirect(entries(pos_sb[r], t0, into.shape[1])), COPY)
@@ -255,7 +258,7 @@ def tile_moe_mlr_relu_kernel(
         lo, hi = slice(0, BANK), slice(BANK, T)
         EDGE = P // 2
         strip = floats("strip", 4352)
-        second = floats("second", 1728)
+        second = floats("second", 3200)
 
         def place(tile, first, width):
             return tile[:, first:first + width]
@@ -282,21 +285,21 @@ def tile_moe_mlr_relu_kernel(
                 nc.tensor.transpose(back[:, c * P:(c + 1) * P], total[:, c * P:(c + 1) * P], ident[:])
             return back
 
-        def finish(b, backs, thirds):
+        def finish(b, backs, thirds, halves=(0, 1)):
             finished = floats(f"finished{b}", T)
-            for half, span in enumerate((lo, hi)):
+            for half in halves:
+                span = (lo, hi)[half]
                 nc.vector.tensor_tensor(finished[:, span], backs[half][:], thirds[half], ADD)
                 nc.sync.dma_start(out[b * P:(b + 1) * P, span], finished[:, span])
             return finished
 
-        def close_with_window(b, term):
-            add_turned(b, 0, term[:, lo], closes=True)
-            add_turned(b, 1, term[:, hi])
-            add_turned(b, 1, window_of[b][:, hi], closes=True, chunks=(3,))
+        def copy_late(b):
+            copy_rows(b, PAIRS - 2, held[b])
+            copy_rows(b, PAIRS - 1, late[b])
 
-        sums[0] = [bank_of(4), bank_of(6)]
+        sums[0] = [bank_of(6), bank_of(7)]
         term00, gated02 = place(strip, 1408, T), place(strip, 960, BANK)
-        term01, term02 = place(second, 704, T), place(second, 256, BANK)
+        term01, term02 = place(second, 1216, T), place(second, 768, BANK)
         fetch_gated(term00, 0, 0)
         add_both(0, term00, opens=True)
         weave(0, 2, 0)
@@ -309,81 +312,65 @@ def tile_moe_mlr_relu_kernel(
             gate_rows(b, z_banks[b])
         times_gate(nc.gpsimd, gated02, plain[0][:], 2, 0)
 
-        sums[1] = [bank_of(5), bank_of(7)]
+        sums[1] = [bank_of(4), bank_of(5)]
         weave(1, 2, 0)
         totals0 = [total_of(0, half) for half in range(2)]
+        copy_late(2)
         rest_of_scatter(1)
-        for b in range(2, BLOCKS):
-            copy_rows(b, PAIRS - 1, late[b])
+        copy_late(LAST)
         term10, term11 = place(strip, 2368, T), term01
         fetch_gated(term10, 1, 0)
         add_both(1, term10, opens=True)
-        add_turned(1, 0, window_of[1][:, lo])
-        add_turned(1, 1, window_of[1][:, hi], chunks=(0, 1, 2))
         fetch_gated(term11, 1, 1)
-        close_with_window(1, term11)
-        backs0 = [turn_back(totals0[half], 2 + half) for half in range(2)]
+        add_both(1, term11)
+        for half, span in enumerate((lo, hi)):
+            add_turned(1, half, window_of[1][:, span], closes=True)
+        backs0 = [turn_back(totals0[half], (2, 0)[half]) for half in range(2)]
 
-        sums[2] = [bank_of(4), bank_of(6)]
+        sums[2] = [bank_of(6), bank_of(7)]
         plain.append(term10[:, P:P + BANK])
         weave(2, 2, 0)
         totals1 = [total_of(1, half) for half in range(2)]
         rest_of_scatter(2)
-        term20, term21 = place(strip, 3328, T), place(strip, 0, T)
+        term20, term21 = place(strip, 3328, T), place(second, 2176, T)
         fetch_gated(term20, 2, 0)
         add_both(2, term20, opens=True)
-        add_both(2, window_of[2])
         fetch_gated(term02, 0, 2, BANK)
-        done0 = finish(0, backs0, (gated02, term02))
-        gated12 = totals0[0][:]
-        times_gate(nc.gpsimd, gated12, plain[1][:], 2, 0)
         fetch_gated(term21, 2, 1)
+        add_both(2, term21)
         for half, span in enumerate((lo, hi)):
-            add_turned(2, half, term21[:, span], closes=True)
-        backs1 = [turn_back(totals1[half], half) for half in range(2)]
+            add_turned(2, half, window_of[2][:, span], closes=True)
+        done0 = finish(0, backs0, (gated02, term02))
+        gated12 = y[0][:, lo]
+        times_gate(nc.gpsimd, gated12, plain[1][:], 2, 0)
+        backs1 = [turn_back(totals1[half], (3, 1)[half]) for half in range(2)]
 
-        sums[LAST] = [bank_of(5)]
+        sums[LAST] = [bank_of(4), bank_of(5)]
         plain.append(totals0[1])
-        weave(LAST, 0, BANK)
-        totals2 = [total_of(2, half) for half in range(2)]
+        weave(LAST, 2, 0)
+        totals2 = {half: total_of(2, half) for half in (1, 0)}
         rest_of_scatter(LAST)
-        term31, term12 = place(second, 0, BANK), place(second, BANK, BANK)
-        term30 = place(strip, 1408, BANK)
-        fetch_gated(term31, LAST, 1)
-        add_turned(LAST, 0, term31, opens=True)
-        plain31 = term31
-        fetch_plain(plain31, LAST, 1, BANK)
+        term30, term12 = place(second, 0, T), place(second, T, BANK)
+        term31, term22 = place(strip, 1408, T), place(strip, 512, BANK)
         fetch_gated(term30, LAST, 0)
-        add_turned(LAST, 0, term30, chunks=(0, 1, 2))
-        add_turned(LAST, 0, window_of[LAST][:, lo])
-        add_turned(LAST, 0, term30, closes=True, chunks=(3,))
-        backs2 = [turn_back(totals2[half], 2 + half) for half in range(2)]
-        total = total_of(LAST, 0)
-        back = turn_back(total, 7)
-        plain32 = [place(strip, 1856 - STEP, STEP), place(strip, 1856, STEP)]
-        for step in range(2):
-            fetch_plain(plain32[step], LAST, 2, step * STEP)
+        add_both(LAST, term30, opens=True)
+        fetch_gated(term31, LAST, 1)
+        add_both(LAST, term31)
+        for half, span in ((1, hi), (0, lo)):
+            add_turned(LAST, half, window_of[LAST][:, span], closes=True)
+        backs2 = {half: turn_back(totals2[half], (2, 0)[half]) for half in (1, 0)}
+        backs3 = {half: turn_back(total_of(LAST, half), 6 + half) for half in (1, 0)}
         fetch_gated(term12, 1, 2, BANK)
-        done1 = finish(1, backs1, (gated12, term12))
-        gated22 = totals1[0][:]
-        times_gate(nc.gpsimd, gated22, plain[2], 2, 0)
-        term22, term32 = gated12, term12
         fetch_gated(term22, 2, 2, BANK)
+        term32 = y[1][:, lo]
         fetch_gated(term32, LAST, 2, BANK)
-        done2 = finish(2, backs2, (gated22, term22))
-        gated30 = totals2[0][:]
-        times_gate(nc.gpsimd, gated30, plain[LAST][:], 0, BANK)
-        sum_a, gated31, gated32 = gated22, term22, term32
-        sum_b = floats("sum_b", BANK)
+        gated22, gated32 = y[2][:, lo], y[2][:, hi]
+        times_gate(nc.gpsimd, gated22, plain[2], 2, 0)
+        times_gate(nc.gpsimd, gated32, plain[LAST][:], 2, 0)
+        done1 = finish(1, backs1, (gated12, term12))
+        done2 = finish(2, backs2, (gated22, term22), (1, 0))
         finished = floats("finished", T)
-        nc.vector.tensor_tensor(sum_a, term32, window_of[LAST][:, hi], ADD)
-        times_gate(nc.vector, gated31, plain31, 1, BANK)
-        nc.vector.tensor_tensor(sum_b[:], sum_a, gated30, ADD)
-        times_gate(nc.vector, gated32[:, :STEP], plain32[0], 2, 0)
-        nc.vector.tensor_tensor(finished[:, hi], sum_b[:], gated31, ADD)
-        nc.sync.dma_start(out[P * LAST:, hi], finished[:, hi])
-        times_gate(nc.vector, gated32[:, STEP:], plain32[1], 2, STEP)
-        for t0 in range(0, BANK, STEP):
-            span = slice(t0, t0 + STEP)
-            nc.vector.tensor_tensor(finished[:, span], back[:, span], gated32[:, span], ADD)
+        for half, t0, width in ((1, BANK, BANK), (0, 0, STEP), (0, STEP, STEP)):
+            span, within = slice(t0, t0 + width), slice(t0 % BANK, t0 % BANK + width)
+            nc.vector.tensor_tensor(finished[:, span], backs3[half][:, within], (gated32, term32)[half][:, within], ADD)
             nc.sync.dma_start(out[P * LAST:, span], finished[:, span])

@@ -328,7 +328,7 @@ def tile_moe_mlr_relu_kernel(
         backs0 = [turn_back(totals0[half], (2, 0)[half]) for half in range(2)]
 
         sums[2] = [bank_of(6), bank_of(7)]
-        plain.append(term10[:, P:P + BANK])
+        plain.append(term10[:, 3 * P:3 * P + BANK])
         weave(2, 2, 0)
         totals1 = [total_of(1, half) for half in range(2)]
         rest_of_scatter(2)
@@ -351,26 +351,38 @@ def tile_moe_mlr_relu_kernel(
         totals2 = {half: total_of(2, half) for half in (1, 0)}
         rest_of_scatter(LAST)
         term30, term12 = place(second, 0, T), place(second, T, BANK)
-        term31, term22 = place(strip, 1408, T), place(strip, 512, BANK)
+        term31 = place(strip, 1408, T)
         fetch_gated(term30, LAST, 0)
         add_both(LAST, term30, opens=True)
-        fetch_gated(term31, LAST, 1)
-        add_both(LAST, term31)
-        for half, span in ((1, hi), (0, lo)):
-            add_turned(LAST, half, window_of[LAST][:, span], closes=True)
-        backs2 = {half: turn_back(totals2[half], (2, 0)[half]) for half in (1, 0)}
-        backs3 = {half: turn_back(total_of(LAST, half), 6 + half) for half in (1, 0)}
         fetch_gated(term12, 1, 2, BANK)
-        fetch_gated(term22, 2, 2, BANK)
-        term32 = y[1][:, lo]
-        fetch_gated(term32, LAST, 2, BANK)
-        gated22, gated32 = y[2][:, lo], y[2][:, hi]
+        fetch_gated(term31, LAST, 1)
+        add_turned(LAST, 0, term31[:, lo])
+        add_turned(LAST, 1, term31[:, hi], chunks=(0, 1, 2))
+        add_turned(LAST, 0, window_of[LAST][:, lo], closes=True)
+        add_turned(LAST, 1, window_of[LAST][:, hi])
+        add_turned(LAST, 1, term31[:, hi], closes=True, chunks=(3,))
+        backs2 = {half: turn_back(totals2[half], (2, 0)[half]) for half in (1, 0)}
+        backs3 = [turn_back(total_of(LAST, half), 6 + half) for half in range(2)]
+        last_plain = [place(strip, 2368 - STEP, STEP), place(strip, 2368, STEP)]
+        for step in range(2):
+            fetch_plain(last_plain[step], LAST, 2, BANK + step * STEP)
+        gated22, gated32 = y[1][:, lo], term12
         times_gate(nc.gpsimd, gated22, plain[2], 2, 0)
-        times_gate(nc.gpsimd, gated32, plain[LAST][:], 2, 0)
         done1 = finish(1, backs1, (gated12, term12))
+        term22 = gated12
+        fetch_gated(term22, 2, 2, BANK)
+        times_gate(nc.gpsimd, gated32, plain[LAST][:], 2, 0)
         done2 = finish(2, backs2, (gated22, term22), (1, 0))
         finished = floats("finished", T)
-        for half, t0, width in ((1, BANK, BANK), (0, 0, STEP), (0, STEP, STEP)):
+        last_gated = term22
+
+        def finish_last(t0, width, third):
             span, within = slice(t0, t0 + width), slice(t0 % BANK, t0 % BANK + width)
-            nc.vector.tensor_tensor(finished[:, span], backs3[half][:, within], (gated32, term32)[half][:, within], ADD)
+            nc.vector.tensor_tensor(finished[:, span], backs3[t0 // BANK][:, within], third[:, within], ADD)
             nc.sync.dma_start(out[P * LAST:, span], finished[:, span])
+
+        times_gate(nc.vector, last_gated[:, :STEP], last_plain[0], 2, BANK)
+        finish_last(0, BANK, gated32)
+        times_gate(nc.vector, last_gated[:, STEP:], last_plain[1], 2, T - STEP)
+        for t0 in range(BANK, T, STEP):
+            finish_last(t0, STEP, last_gated)

@@ -31,6 +31,7 @@ PARTS = ADAPTER_SLOTS // P
 STEP = 256
 SQUARE = 32
 RUNS = P // SQUARE
+AT_TERM = 16384
 AT_XA_S = 0
 AT_XA_W = ADAPTER_SLOTS
 AT_LANE = AT_XA_W + STEP
@@ -74,10 +75,11 @@ def tile_moe_mlr_relu_kernel(
         wb_s = keep.tile([P, F, N], U8, name="wb_s", align_bytes=64)
         w_w = [keep.tile([P, end - first, 2 * N], U8, name=f"w_w{first}", align_bytes=64) for first, end in WEIGHT_LOADS]
         w_s = keep.tile([P, E, N], U8, name="w_s", align_bytes=64)
-        gate_sb = [floats(f"gate_sb{r}", T) for r in range(TOP)]
+        first_gates = keep.tile([P, 2, T], F32, name="first_gates", align_bytes=64)
+        gate_sb = [first_gates[:, 0], first_gates[:, 1], floats("third_gate", T)[:]]
         gate2_sb = floats("gate2_sb", ADAPTER_SLOTS)
         ident = floats("ident", P)
-        windows = [floats(f"window{b}", T) for b in range(2)]
+        windows = [floats("window", T)]
         y = [floats(f"y{b}", SLOTS) for b in range(BLOCKS)]
 
         zero = floats("zero", 1)
@@ -107,8 +109,8 @@ def tile_moe_mlr_relu_kernel(
         weights = [tile[:, place, :] for tile in w_w for place in range(tile.shape[1])]
         for r, pos in enumerate((pos1, pos2, pos3)):
             nc.sync.dma_start(pos_sb[r][:], pos)
-        for r in range(TOP):
-            nc.sync.dma_start(gate_sb[r][:], gate[r])
+        nc.sync.dma_start(first_gates[:], gate[:2].rearrange("r p t -> p r t"))
+        nc.sync.dma_start(gate_sb[2], gate[2])
 
         def entries(tile, first, count):
             return tile[:, first // LIST_ROWS:(first + count) // LIST_ROWS]
@@ -193,12 +195,11 @@ def tile_moe_mlr_relu_kernel(
             nc.vector.tensor_tensor(z[b], bank[:].rearrange("n (k m) -> n k m", m=P),
                                     gate2_sb[:].rearrange("n (k m) -> n k m", m=P), MULT)
 
-        window_of = windows + windows
-        PART_ORDER = (0, PARTS - 1, 1, 2)
+        window_of = windows * LAST
 
-        def scatter(turn):
-            b, part = turn // PARTS, PART_ORDER[turn % PARTS]
-            nc.scalar.activation(window_of[b][:].indirect(entries(offs2_sb, part * P, P)), z[b][:, part], COPY)
+        def scatter(b, part, parts=1):
+            source = z[b][:, part:part + parts].rearrange("n k m -> n (k m)")
+            nc.scalar.activation(window_of[b][:].indirect(entries(offs2_sb, part * P, parts * P)), source, COPY)
 
         PAIR_BANKS = ((6, 7, 0, 1), (2, 3, 4, 5), (6, 7, 0, 1), (2, 3, 4, 5), (0, 1, 2, 3), (4, 5, 0, 1))
         z_banks = {}
@@ -257,22 +258,10 @@ def tile_moe_mlr_relu_kernel(
 
         lo, hi = slice(0, BANK), slice(BANK, T)
         EDGE = P // 2
-        strip = floats("strip", 4352)
-        second = floats("second", 3200)
+        plain = [floats("plain0", BANK)]
 
-        def place(tile, first, width):
-            return tile[:, first:first + width]
-
-        plain = [floats(f"plain{b}", BANK) for b in range(2)]
-
-        def weave(b, r, t0):
-            for step in range(2):
-                scatter(b * PARTS + step)
-                fetch_plain(plain[b][:, step * STEP:(step + 1) * STEP], b, r, t0 + step * STEP)
-
-        def rest_of_scatter(b):
-            for turn in range(2, PARTS):
-                scatter(b * PARTS + turn)
+        def plain_part(b, step):
+            fetch_plain(plain[b][:, step * STEP:(step + 1) * STEP], b, 2, step * STEP)
 
         def total_of(b, half):
             total = floats(f"total{b}_{half}", BANK)
@@ -285,104 +274,113 @@ def tile_moe_mlr_relu_kernel(
                 nc.tensor.transpose(back[:, c * P:(c + 1) * P], total[:, c * P:(c + 1) * P], ident[:])
             return back
 
-        def finish(b, backs, thirds, halves=(0, 1)):
-            finished = floats(f"finished{b}", T)
-            for half in halves:
-                span = (lo, hi)[half]
+        def finish(b, finished, backs, thirds):
+            for half, span in enumerate((lo, hi)):
                 nc.vector.tensor_tensor(finished[:, span], backs[half][:], thirds[half], ADD)
                 nc.sync.dma_start(out[b * P:(b + 1) * P, span], finished[:, span])
-            return finished
+
+        def close_with_window(b):
+            for half, span in enumerate((lo, hi)):
+                add_turned(b, half, window_of[b][:, span], closes=True)
 
         def copy_late(b):
             copy_rows(b, PAIRS - 2, held[b])
             copy_rows(b, PAIRS - 1, late[b])
 
+        ring_a = floats("ring_a", T)[:]
+        wide_b = floats("wide_b", BANK - EDGE + T)
+        ring_b = wide_b[:, BANK - EDGE:]
+        wide_c = floats("wide_c", T + STEP - EDGE)
+        ring_c = wide_c[:, :T]
+
         sums[0] = [bank_of(6), bank_of(7)]
-        term00, gated02 = place(strip, 1408, T), place(strip, 960, BANK)
-        term01, term02 = place(second, 1216, T), place(second, 768, BANK)
-        fetch_gated(term00, 0, 0)
-        add_both(0, term00, opens=True)
-        weave(0, 2, 0)
-        rest_of_scatter(0)
-        fetch_gated(term01, 0, 1)
-        add_both(0, term01)
-        for half, span in enumerate((lo, hi)):
-            add_turned(0, half, window_of[0][:, span], closes=True)
+        fetch_gated(ring_a, 0, 0)
+        add_both(0, ring_a, opens=True)
+        for step, part in enumerate((0, PARTS - 1)):
+            scatter(0, part)
+            plain_part(0, step)
+        scatter(0, 1, 2)
+        fetch_gated(ring_b, 0, 1)
+        add_both(0, ring_b)
+        close_with_window(0)
+        for b in range(2, BLOCKS):
+            copy_late(b)
+        totals0 = [total_of(0, half) for half in range(2)]
+
+        sums[1] = [bank_of(2), bank_of(0)]
+        fetch_gated(ring_c, 1, 0)
+        add_both(1, ring_c, opens=True)
         for b in range(2, BLOCKS):
             gate_rows(b, z_banks[b])
+        gated02 = wide_b[:, lo]
         times_gate(nc.gpsimd, gated02, plain[0][:], 2, 0)
-
-        sums[1] = [bank_of(4), bank_of(5)]
-        weave(1, 2, 0)
-        totals0 = [total_of(0, half) for half in range(2)]
-        copy_late(2)
-        rest_of_scatter(1)
-        copy_late(LAST)
-        term10, term11 = place(strip, 2368, T), term01
-        fetch_gated(term10, 1, 0)
-        add_both(1, term10, opens=True)
-        fetch_gated(term11, 1, 1)
-        add_both(1, term11)
-        for half, span in enumerate((lo, hi)):
-            add_turned(1, half, window_of[1][:, span], closes=True)
-        backs0 = [turn_back(totals0[half], (2, 0)[half]) for half in range(2)]
+        backs0 = [turn_back(totals0[half], 4 + half) for half in range(2)]
+        plain.extend(totals0)
+        scatter(1, 0, 3)
+        plain_part(1, 0)
+        scatter(1, 3)
+        plain_part(1, 1)
+        for step in range(2):
+            plain_part(2, step)
+        fetch_gated(ring_a, 1, 1)
+        add_both(1, ring_a)
+        close_with_window(1)
+        totals1 = [total_of(1, half) for half in range(2)]
 
         sums[2] = [bank_of(6), bank_of(7)]
-        plain.append(term10[:, 3 * P:3 * P + BANK])
-        weave(2, 2, 0)
-        totals1 = [total_of(1, half) for half in range(2)]
-        rest_of_scatter(2)
-        term20, term21 = place(strip, 3328, T), place(second, 2176, T)
-        fetch_gated(term20, 2, 0)
+        term20 = shared.tile([P, T], F32, name="term20", offset=AT_TERM, align_bytes=64)
+        fetch_gated(term20[:], 2, 0)
         add_both(2, term20, opens=True)
-        fetch_gated(term02, 0, 2, BANK)
-        fetch_gated(term21, 2, 1)
-        add_both(2, term21)
-        for half, span in enumerate((lo, hi)):
-            add_turned(2, half, window_of[2][:, span], closes=True)
-        done0 = finish(0, backs0, (gated02, term02))
-        gated12 = y[0][:, lo]
-        times_gate(nc.gpsimd, gated12, plain[1][:], 2, 0)
+        fetch_gated(ring_c, 2, 1)
+        add_both(2, ring_c)
         backs1 = [turn_back(totals1[half], (3, 1)[half]) for half in range(2)]
+        scatter(2, 0, 3)
+        scatter(2, 3)
 
-        sums[LAST] = [bank_of(4), bank_of(5)]
-        plain.append(totals0[1])
-        weave(LAST, 2, 0)
-        totals2 = {half: total_of(2, half) for half in (1, 0)}
-        rest_of_scatter(LAST)
-        term30, term12 = place(second, 0, T), place(second, T, BANK)
-        term31 = place(strip, 1408, T)
-        fetch_gated(term30, LAST, 0)
-        add_both(LAST, term30, opens=True)
-        fetch_gated(term12, 1, 2, BANK)
-        fetch_gated(term31, LAST, 1)
-        add_turned(LAST, 0, term31[:, lo])
-        add_turned(LAST, 1, term31[:, hi], chunks=(0, 1, 2))
+        sums[LAST] = [bank_of(2), bank_of(0)]
+        window_of.append(shared.tile([P, T], F32, name="last_window", offset=AT_TERM, align_bytes=64))
+        nc.gpsimd.memset(window_of[LAST][:], 0.0)
+        fetch_gated(ring_a, LAST, 0)
+        add_both(LAST, ring_a, opens=True)
+        close_with_window(2)
+        scatter(LAST, 0, 3)
+        scatter(LAST, 3)
+        totals2 = [total_of(2, half) for half in range(2)]
+        term02 = totals1[0][:]
+        fetch_gated(term02, 0, 2, BANK)
+        fetch_gated(ring_c, LAST, 1)
+        add_turned(LAST, 0, ring_c[:, lo])
+        add_turned(LAST, 1, ring_c[:, hi], chunks=(0, 1, 2))
         add_turned(LAST, 0, window_of[LAST][:, lo], closes=True)
         add_turned(LAST, 1, window_of[LAST][:, hi])
-        add_turned(LAST, 1, term31[:, hi], closes=True, chunks=(3,))
-        backs2 = {half: turn_back(totals2[half], (2, 0)[half]) for half in (1, 0)}
-        backs3 = [turn_back(total_of(LAST, half), 6 + half) for half in range(2)]
-        last_plain = [place(strip, 2368 - STEP, STEP), place(strip, 2368, STEP)]
+        add_turned(LAST, 1, ring_c[:, hi], closes=True, chunks=(3,))
+        backs2 = [turn_back(totals2[half], 6 + half) for half in range(2)]
+        gated12 = y[0][:, lo]
+        times_gate(nc.gpsimd, gated12, plain[1][:], 2, 0)
+        finish(0, ring_a, backs0, (gated02, term02))
+        plain.append(ring_c[:, lo])
         for step in range(2):
-            fetch_plain(last_plain[step], LAST, 2, BANK + step * STEP)
-        gated22, gated32 = y[1][:, lo], term12
-        times_gate(nc.gpsimd, gated22, plain[2], 2, 0)
-        done1 = finish(1, backs1, (gated12, term12))
-        term22 = gated12
+            plain_part(LAST, step)
+        backs3 = [turn_back(total_of(LAST, half), 4 + half) for half in range(2)]
+        last_plain = wide_c[:, T - EDGE:]
+        fetch_plain(last_plain, LAST, 2, BANK)
+        term12, gated22 = gated02, term02
+        fetch_gated(term12, 1, 2, BANK)
+        times_gate(nc.gpsimd, gated22, plain[2][:], 2, 0)
+        finish(1, floats("finished1", T), backs1, (gated12, term12))
+        term22, gated32, last_gated = gated12, y[2][:, lo], term12
         fetch_gated(term22, 2, 2, BANK)
-        times_gate(nc.gpsimd, gated32, plain[LAST][:], 2, 0)
-        done2 = finish(2, backs2, (gated22, term22), (1, 0))
+        fetch_gated(last_gated[:, STEP:], LAST, 2, T - STEP)
+        times_gate(nc.gpsimd, gated32, plain[LAST], 2, 0)
+        finish(2, floats("finished2", T), backs2, (gated22, term22))
         finished = floats("finished", T)
-        last_gated = term22
 
         def finish_last(t0, width, third):
             span, within = slice(t0, t0 + width), slice(t0 % BANK, t0 % BANK + width)
             nc.vector.tensor_tensor(finished[:, span], backs3[t0 // BANK][:, within], third[:, within], ADD)
             nc.sync.dma_start(out[P * LAST:, span], finished[:, span])
 
-        times_gate(nc.vector, last_gated[:, :STEP], last_plain[0], 2, BANK)
         finish_last(0, BANK, gated32)
-        times_gate(nc.vector, last_gated[:, STEP:], last_plain[1], 2, T - STEP)
-        for t0 in range(BANK, T, STEP):
-            finish_last(t0, STEP, last_gated)
+        times_gate(nc.vector, term22[:, :STEP], last_plain, 2, BANK)
+        finish_last(T - STEP, STEP, last_gated)
+        finish_last(BANK, STEP, term22)

@@ -79,7 +79,7 @@ def tile_moe_mlr_relu_kernel(
         gate_sb = [first_gates[:, 0], first_gates[:, 1], floats("third_gate", T)[:]]
         gate2_sb = floats("gate2_sb", ADAPTER_SLOTS)
         ident = floats("ident", P)
-        windows = [floats("window", T)]
+        windows = [floats(f"window{b}", T) for b in range(2)]
         y = [floats(f"y{b}", SLOTS) for b in range(BLOCKS)]
 
         zero = floats("zero", 1)
@@ -195,7 +195,7 @@ def tile_moe_mlr_relu_kernel(
             nc.vector.tensor_tensor(z[b], bank[:].rearrange("n (k m) -> n k m", m=P),
                                     gate2_sb[:].rearrange("n (k m) -> n k m", m=P), MULT)
 
-        window_of = windows * LAST
+        window_of = windows + windows[1:]
 
         def scatter(b, part, parts=1):
             source = z[b][:, part:part + parts].rearrange("n k m -> n (k m)")
@@ -296,36 +296,36 @@ def tile_moe_mlr_relu_kernel(
         sums[0] = [bank_of(6), bank_of(7)]
         fetch_gated(ring_a, 0, 0)
         add_both(0, ring_a, opens=True)
-        for step, part in enumerate((0, PARTS - 1)):
-            scatter(0, part)
+        scatter(0, 0, 3)
+        scatter(0, 3)
+        for step in range(2):
             plain_part(0, step)
-        scatter(0, 1, 2)
+        add_both(0, window_of[0])
         fetch_gated(ring_b, 0, 1)
-        add_both(0, ring_b)
-        close_with_window(0)
-        for b in range(2, BLOCKS):
-            copy_late(b)
+        for half, span in enumerate((lo, hi)):
+            add_turned(0, half, ring_b[:, span], closes=True)
+        scatter(1, 0, 3)
+        scatter(1, 3)
+        copy_late(2)
         totals0 = [total_of(0, half) for half in range(2)]
+        copy_late(LAST)
 
-        sums[1] = [bank_of(2), bank_of(0)]
         fetch_gated(ring_c, 1, 0)
-        add_both(1, ring_c, opens=True)
         for b in range(2, BLOCKS):
             gate_rows(b, z_banks[b])
+        sums[1] = [bank_of(4), bank_of(5)]
+        add_both(1, ring_c, opens=True)
+        add_turned(1, 0, window_of[1][:, lo])
+        add_turned(1, 1, window_of[1][:, hi], chunks=(0, 1, 2))
         gated02 = wide_b[:, lo]
         times_gate(nc.gpsimd, gated02, plain[0][:], 2, 0)
-        backs0 = [turn_back(totals0[half], 4 + half) for half in range(2)]
-        plain.extend(totals0)
-        scatter(1, 0, 3)
-        plain_part(1, 0)
-        scatter(1, 3)
-        plain_part(1, 1)
-        for step in range(2):
-            plain_part(2, step)
         fetch_gated(ring_a, 1, 1)
-        add_both(1, ring_a)
-        close_with_window(1)
+        add_turned(1, 0, ring_a[:, lo], closes=True)
+        add_turned(1, 1, ring_a[:, hi])
+        add_turned(1, 1, window_of[1][:, hi], closes=True, chunks=(3,))
+        backs0 = [turn_back(totals0[half], (2, 0)[half]) for half in range(2)]
         totals1 = [total_of(1, half) for half in range(2)]
+        plain.extend(totals0)
 
         sums[2] = [bank_of(6), bank_of(7)]
         term20 = shared.tile([P, T], F32, name="term20", offset=AT_TERM, align_bytes=64)
@@ -335,9 +335,13 @@ def tile_moe_mlr_relu_kernel(
         add_both(2, ring_c)
         backs1 = [turn_back(totals1[half], (3, 1)[half]) for half in range(2)]
         scatter(2, 0, 3)
+        plain_part(1, 0)
         scatter(2, 3)
+        plain_part(1, 1)
+        for step in range(2):
+            plain_part(2, step)
 
-        sums[LAST] = [bank_of(2), bank_of(0)]
+        sums[LAST] = [bank_of(4), bank_of(5)]
         window_of.append(shared.tile([P, T], F32, name="last_window", offset=AT_TERM, align_bytes=64))
         nc.gpsimd.memset(window_of[LAST][:], 0.0)
         fetch_gated(ring_a, LAST, 0)
@@ -345,7 +349,6 @@ def tile_moe_mlr_relu_kernel(
         close_with_window(2)
         scatter(LAST, 0, 3)
         scatter(LAST, 3)
-        totals2 = [total_of(2, half) for half in range(2)]
         term02 = totals1[0][:]
         fetch_gated(term02, 0, 2, BANK)
         fetch_gated(ring_c, LAST, 1)
@@ -354,14 +357,14 @@ def tile_moe_mlr_relu_kernel(
         add_turned(LAST, 0, window_of[LAST][:, lo], closes=True)
         add_turned(LAST, 1, window_of[LAST][:, hi])
         add_turned(LAST, 1, ring_c[:, hi], closes=True, chunks=(3,))
-        backs2 = [turn_back(totals2[half], 6 + half) for half in range(2)]
-        gated12 = y[0][:, lo]
-        times_gate(nc.gpsimd, gated12, plain[1][:], 2, 0)
-        finish(0, ring_a, backs0, (gated02, term02))
         plain.append(ring_c[:, lo])
         for step in range(2):
             plain_part(LAST, step)
-        backs3 = [turn_back(total_of(LAST, half), 4 + half) for half in range(2)]
+        backs2 = [turn_back(total_of(2, half), 6 + half) for half in range(2)]
+        gated12 = y[0][:, lo]
+        times_gate(nc.gpsimd, gated12, plain[1][:], 2, 0)
+        finish(0, ring_a, backs0, (gated02, term02))
+        backs3 = [turn_back(total_of(LAST, half), (2, 0)[half]) for half in range(2)]
         last_plain = wide_c[:, T - EDGE:]
         fetch_plain(last_plain, LAST, 2, BANK)
         term12, gated22 = gated02, term02

@@ -157,21 +157,20 @@ def tile_moe_mlr_relu_kernel(
 
         tokens = {}
 
-        def gather_pair(pair, cuts=1):
+        def gather_pair(pair, cuts=(0, BANK)):
             if pair > 0:
                 gather_pair_scales(pair)
             words = ring.tile([P, BANK], U32, name=f"pair_w{pair}", tag="pair_w", align_bytes=64)
-            width = BANK // cuts
-            for cut in range(cuts):
-                gather_words(entries(offs_sb, pair * BANK + cut * width, width), words[:, cut * width:(cut + 1) * width])
+            for first, end in zip(cuts, cuts[1:]):
+                gather_words(entries(offs_sb, pair * BANK + first, end - first), words[:, first:end])
             tokens[pair] = words, pair_scales[pair]
 
-        def expert_products(b, pair, number):
+        def expert_products(b, pair, number, cuts=(0, C, BANK)):
             bank = bank_of(number)
             words, scales = tokens[pair]
-            for side in range(2):
-                e = 2 * pair + side
-                slots = slice(side * C, (side + 1) * C)
+            for first, end in zip(cuts, cuts[1:]):
+                e = 2 * pair + first // C
+                slots = slice(first, end)
                 nc.tensor.matmul_mx(bank[:, slots], lhsT=weights[e][:, 2 * P * b:2 * P * (b + 1)].bitcast(FP4X4),
                                     lhsT_scale=w_s[:, e, P * b:P * (b + 1)], rhs=words[:, slots].bitcast(FP8X4),
                                     rhs_scale=scales[:, slots], start=True, stop=True)
@@ -214,18 +213,19 @@ def tile_moe_mlr_relu_kernel(
             for b in range(BLOCKS if pair < 4 else 1):
                 copy_rows(b, pair, expert_products(b, pair, PAIR_BANKS[pair][b]))
         held = {b: expert_products(b, PAIRS - 2, b) for b in range(1, BLOCKS)}
-        gather_pair(PAIRS - 1, cuts=2)
+        gather_pair(PAIRS - 1, (0, BANK - P, BANK))
         lane = shared.tile([P, 14, P], F32, name="lane", offset=AT_LANE, align_bytes=64)
         z.extend([lane[:, 3:7], lane[:, 10:], lane[:, :4], lane[:, 6:10]])
         for b in range(2):
             gate_rows(b, z_banks[b])
-        late = [expert_products(b, PAIRS - 1, PAIR_BANKS[PAIRS - 1][b]) for b in range(LAST)]
-        for side in range(2):
-            nc.scalar.copy(y[0][:, SLOTS - BANK + side * C:SLOTS - BANK + (side + 1) * C],
-                           late[0][:, side * C:(side + 1) * C])
+        late = [expert_products(0, PAIRS - 1, PAIR_BANKS[PAIRS - 1][0], (0, C, BANK - P))]
+        closing = expert_products(0, PAIRS - 1, 5, (BANK - P, BANK))
+        nc.scalar.copy(y[0][:, SLOTS - BANK:SLOTS - P], late[0][:, :BANK - P])
+        nc.scalar.copy(y[0][:, SLOTS - P:], closing[:, BANK - P:])
         copy_rows(1, PAIRS - 2, held[1])
+        late.append(expert_products(1, PAIRS - 1, 0))
         copy_rows(1, PAIRS - 1, late[1])
-        late.append(expert_products(LAST, PAIRS - 1, PAIR_BANKS[PAIRS - 1][LAST]))
+        late.extend(expert_products(b, PAIRS - 1, b - 2) for b in range(2, BLOCKS))
         for b in range(2, BLOCKS):
             z_banks[b] = adapter_products(b, 2 + b)
 
@@ -334,12 +334,9 @@ def tile_moe_mlr_relu_kernel(
         fetch_gated(ring_c, 2, 1)
         add_both(2, ring_c)
         backs1 = [turn_back(totals1[half], (3, 1)[half]) for half in range(2)]
-        scatter(2, 0, 3)
-        plain_part(1, 0)
-        scatter(2, 3)
-        plain_part(1, 1)
-        for step in range(2):
-            plain_part(2, step)
+        for part in range(PARTS):
+            scatter(2, part)
+            plain_part(1 + part // 2, part % 2)
 
         sums[LAST] = [bank_of(4), bank_of(5)]
         window_of.append(shared.tile([P, T], F32, name="last_window", offset=AT_TERM, align_bytes=64))
@@ -365,15 +362,16 @@ def tile_moe_mlr_relu_kernel(
         times_gate(nc.gpsimd, gated12, plain[1][:], 2, 0)
         finish(0, ring_a, backs0, (gated02, term02))
         backs3 = [turn_back(total_of(LAST, half), (2, 0)[half]) for half in range(2)]
-        last_plain = wide_c[:, T - EDGE:]
-        fetch_plain(last_plain, LAST, 2, BANK)
+        last_plain = [wide_c[:, T - EDGE - STEP:T - EDGE], wide_c[:, T - EDGE:]]
+        for step in range(2):
+            fetch_plain(last_plain[step], LAST, 2, BANK + step * STEP)
         term12, gated22 = gated02, term02
         fetch_gated(term12, 1, 2, BANK)
         times_gate(nc.gpsimd, gated22, plain[2][:], 2, 0)
-        finish(1, floats("finished1", T), backs1, (gated12, term12))
-        term22, gated32, last_gated = gated12, y[2][:, lo], term12
+        finished1 = floats("finished1", T)
+        finish(1, finished1, backs1, (gated12, term12))
+        term22, gated32 = gated12, term12
         fetch_gated(term22, 2, 2, BANK)
-        fetch_gated(last_gated[:, STEP:], LAST, 2, T - STEP)
         times_gate(nc.gpsimd, gated32, plain[LAST], 2, 0)
         finish(2, floats("finished2", T), backs2, (gated22, term22))
         finished = floats("finished", T)
@@ -383,7 +381,9 @@ def tile_moe_mlr_relu_kernel(
             nc.vector.tensor_tensor(finished[:, span], backs3[t0 // BANK][:, within], third[:, within], ADD)
             nc.sync.dma_start(out[P * LAST:, span], finished[:, span])
 
+        last_gated = gated22
+        times_gate(nc.gpsimd, last_gated[:, :STEP], last_plain[0], 2, BANK)
         finish_last(0, BANK, gated32)
-        times_gate(nc.vector, term22[:, :STEP], last_plain, 2, BANK)
-        finish_last(T - STEP, STEP, last_gated)
-        finish_last(BANK, STEP, term22)
+        times_gate(nc.vector, term22[:, STEP:], last_plain[1], 2, T - STEP)
+        finish_last(BANK, STEP, last_gated)
+        finish_last(T - STEP, STEP, term22)

@@ -31,7 +31,9 @@ PARTS = ADAPTER_SLOTS // P
 STEP = 256
 SQUARE = 32
 RUNS = P // SQUARE
+SCALE_CUTS = (0, 1, 4, 6, 8, 10, E)
 AT_TERM = 16384
+AT_PAIR_W = tuple(AT_TERM + 4 * T + 4 * BANK * slot for slot in range(3))
 AT_XA_S = 0
 AT_XA_W = ADAPTER_SLOTS
 AT_LANE = AT_XA_W + STEP
@@ -52,7 +54,6 @@ def tile_moe_mlr_relu_kernel(
     nc = tc.nc
     with ExitStack() as ctx:
         keep = ctx.enter_context(tc.tile_pool(name="keep", bufs=1))
-        ring = ctx.enter_context(tc.tile_pool(name="ring", bufs=3))
         shared = ctx.enter_context(tc.tile_pool(name="shared", bufs=1))
         psum = ctx.enter_context(tc.psum_pool(name="psum", bufs=1))
         taken = []
@@ -124,15 +125,17 @@ def tile_moe_mlr_relu_kernel(
             return words
 
         xa_s = gather_scales(offs2_sb[:], shared.tile([P, ADAPTER_SLOTS], U8, name="xa_s", offset=AT_XA_S, align_bytes=64))
-        pair_scales = {}
+        expert_scales = []
 
-        def gather_pair_scales(pair):
-            tile = shared.tile([P, BANK], U8, name=f"pair_s{pair}", offset=AT_PAIR_S[pair % 3], align_bytes=64)
-            pair_scales[pair] = gather_scales(entries(offs_sb, pair * BANK, BANK), tile)
+        def gather_expert_scales(turn):
+            first, end = SCALE_CUTS[turn] * C, SCALE_CUTS[turn + 1] * C
+            tile = shared.tile([P, end - first], U8, name=f"scales{turn}", offset=AT_PAIR_S[turn % 3], align_bytes=64)
+            gather_scales(entries(offs_sb, first, end - first), tile)
+            expert_scales.extend(tile[:, at:at + C] for at in range(0, end - first, C))
 
-        gather_pair_scales(0)
+        gather_expert_scales(0)
         xa_w = [shared.tile([P, D], U32, name="xa_w0", offset=AT_XA_W, align_bytes=64),
-                keep.tile([P, D], U32, name="xa_w1", align_bytes=64)]
+                shared.tile([P, D], U32, name="xa_w1", offset=AT_PAIR_W[2] - 2 * D, align_bytes=64)]
         for f in range(F):
             gather_words(entries(offs2_sb, f * D, D), xa_w[f])
 
@@ -158,22 +161,23 @@ def tile_moe_mlr_relu_kernel(
         tokens = {}
 
         def gather_pair(pair, cuts=(0, BANK)):
-            if pair > 0:
-                gather_pair_scales(pair)
-            words = ring.tile([P, BANK], U32, name=f"pair_w{pair}", tag="pair_w", align_bytes=64)
+            if pair > 1:
+                gather_expert_scales(pair)
+            words = shared.tile([P, BANK], U32, name=f"pair_w{pair}", offset=AT_PAIR_W[pair % 3], align_bytes=64)
             for first, end in zip(cuts, cuts[1:]):
                 gather_words(entries(offs_sb, pair * BANK + first, end - first), words[:, first:end])
-            tokens[pair] = words, pair_scales[pair]
+            if pair == 0:
+                gather_expert_scales(1)
+            tokens[pair] = words
 
         def expert_products(b, pair, number, cuts=(0, C, BANK)):
             bank = bank_of(number)
-            words, scales = tokens[pair]
             for first, end in zip(cuts, cuts[1:]):
                 e = 2 * pair + first // C
                 slots = slice(first, end)
                 nc.tensor.matmul_mx(bank[:, slots], lhsT=weights[e][:, 2 * P * b:2 * P * (b + 1)].bitcast(FP4X4),
-                                    lhsT_scale=w_s[:, e, P * b:P * (b + 1)], rhs=words[:, slots].bitcast(FP8X4),
-                                    rhs_scale=scales[:, slots], start=True, stop=True)
+                                    lhsT_scale=w_s[:, e, P * b:P * (b + 1)], rhs=tokens[pair][:, slots].bitcast(FP8X4),
+                                    rhs_scale=expert_scales[e][:, first % C:first % C + end - first], start=True, stop=True)
             return bank
 
         def copy_rows(b, pair, bank):
@@ -210,9 +214,9 @@ def tile_moe_mlr_relu_kernel(
             if pair == 4:
                 for b in range(2):
                     z_banks[b] = adapter_products(b, 6 + b)
-            for b in range(BLOCKS if pair < 4 else 1):
+            for b in range(BLOCKS if pair < 4 else 2):
                 copy_rows(b, pair, expert_products(b, pair, PAIR_BANKS[pair][b]))
-        held = {b: expert_products(b, PAIRS - 2, b) for b in range(1, BLOCKS)}
+        held = {b: expert_products(b, PAIRS - 2, b) for b in range(2, BLOCKS)}
         gather_pair(PAIRS - 1, (0, BANK - P, BANK))
         lane = shared.tile([P, 14, P], F32, name="lane", offset=AT_LANE, align_bytes=64)
         z.extend([lane[:, 3:7], lane[:, 10:], lane[:, :4], lane[:, 6:10]])
@@ -222,7 +226,6 @@ def tile_moe_mlr_relu_kernel(
         closing = expert_products(0, PAIRS - 1, 5, (BANK - P, BANK))
         nc.scalar.copy(y[0][:, SLOTS - BANK:SLOTS - P], late[0][:, :BANK - P])
         nc.scalar.copy(y[0][:, SLOTS - P:], closing[:, BANK - P:])
-        copy_rows(1, PAIRS - 2, held[1])
         late.append(expert_products(1, PAIRS - 1, 0))
         copy_rows(1, PAIRS - 1, late[1])
         late.extend(expert_products(b, PAIRS - 1, b - 2) for b in range(2, BLOCKS))

from contextlib import ExitStack

import concourse.mybir as mybir
from concourse.masks import make_identity

K, T, E, C, F, D, H, N, TOP = 512, 1024, 12, 256, 2, 256, 512, 512, 3
FLOPS = 2 * K * N * E * C + 2 * K * H * F * D + 2 * H * N * F * D

F32 = mybir.dt.float32
BF16 = mybir.dt.bfloat16
I32 = mybir.dt.int32
U32 = mybir.dt.uint32
U16 = mybir.dt.uint16
U8 = mybir.dt.uint8
FP8X4 = mybir.dt.float8_e4m3fn_x4
FP4X4 = mybir.dt.float4_e2m1fn_x4
MULT = mybir.AluOpType.mult
ADD = mybir.AluOpType.add
RELU = mybir.ActivationFunctionType.Relu
COPY = mybir.ActivationFunctionType.Copy

P = 128
BANK = 512
LIST_ROWS = 16
SLOTS = E * C
ADAPTER_SLOTS = F * D
BLOCKS = N // P
LAST = BLOCKS - 1
PAIRS = E // 2
PARTS = ADAPTER_SLOTS // P
STEP = 256
SQUARE = 32
RUNS = P // SQUARE
SCALE_CUTS = (0, 1, 4, 6, 8, 10, E)
AT_TERM = 16384
AT_PAIR_W = tuple(AT_TERM + 4 * T + 4 * BANK * slot for slot in range(3))
AT_XA_S = 0
AT_XA_W = ADAPTER_SLOTS
AT_LANE = AT_XA_W + STEP
AT_PAIR_S = (AT_LANE + 14 * 4 * P, AT_XA_W, AT_XA_S)
WEIGHT_LOADS = ((0, 2), (2, 6), (6, E))


def load_scale_rows(nc, tile, rows):
    by_row = rows.rearrange("g (q r) n -> r q g n", r=4)
    for r in range(4):
        nc.sync.dma_start(tile[r:P:32, :, :].bitcast(I32), by_row[r].bitcast(I32))


def tile_moe_mlr_relu_kernel(
    tc, x_words, x_scales, w_words, w_scales, wa_words, wa_scales, wb_words, wb_scales,
    gate, gate2, offs, pos1, pos2, pos3, offs2, out,
):
    nc = tc.nc
    with ExitStack() as ctx:
        keep = ctx.enter_context(tc.tile_pool(name="keep", bufs=1))
        shared = ctx.enter_context(tc.tile_pool(name="shared", bufs=1))
        psum = ctx.enter_context(tc.psum_pool(name="psum", bufs=1))
        taken = []

        def bank_of(number):
            taken.append(psum.tile([P, BANK], F32, name=f"bank{len(taken)}", tag=f"b{number}"))
            return taken[-1]

        def floats(name, width):
            return keep.tile([P, width], F32, name=name, align_bytes=64)

        offs_sb = keep.tile([P, SLOTS // LIST_ROWS], U16, name="offs_sb")
        offs2_sb = keep.tile([P, ADAPTER_SLOTS // LIST_ROWS], U16, name="offs2_sb")
        pos_sb = [keep.tile([P, T // LIST_ROWS], U16, name=f"pos_sb{r}") for r in range(TOP)]
        x_w = keep.tile([P, T], I32, name="x_w", align_bytes=64)
        x_s = keep.tile([P, T], U8, name="x_s", align_bytes=64)
        wa_w = keep.tile([P, F, 2 * H], U8, name="wa_w", align_bytes=64)
        wa_s = keep.tile([P, F, H], U8, name="wa_s", align_bytes=64)
        wb_w = keep.tile([P, F, 2 * N], U8, name="wb_w", align_bytes=64)
        wb_s = keep.tile([P, F, N], U8, name="wb_s", align_bytes=64)
        w_w = [keep.tile([P, end - first, 2 * N], U8, name=f"w_w{first}", align_bytes=64) for first, end in WEIGHT_LOADS]
        w_s = keep.tile([P, E, N], U8, name="w_s", align_bytes=64)
        first_gates = keep.tile([P, 2, T], F32, name="first_gates", align_bytes=64)
        gate_sb = [first_gates[:, 0], first_gates[:, 1], floats("third_gate", T)[:]]
        gate2_sb = floats("gate2_sb", ADAPTER_SLOTS)
        ident = floats("ident", P)
        windows = [floats(f"window{b}", T) for b in range(2)]
        y = [floats(f"y{b}", SLOTS) for b in range(BLOCKS)]

        zero = floats("zero", 1)
        nc.gpsimd.memset(zero[:], 0.0)
        for scales in (wa_s[:], w_s[:], wb_s[:]):
            nc.vector.memset(scales.bitcast(I32), 0)
        make_identity(nc, ident[:])

        nc.sync.dma_start(offs2_sb[:], offs2)
        for q in range(4):
            queue = nc.sync if q < 2 else nc.scalar
            queue.dma_start(x_s[32 * q:32 * (q + 1), :].bitcast(I32),
                            x_scales[0, 4 * q:4 * (q + 1), :].bitcast(I32).partition_broadcast(8))
        nc.sync.dma_start(offs_sb[:], offs)
        for window in windows:
            nc.scalar.activation(window[:], zero[:].to_broadcast([P, T]), RELU)
        nc.sync.dma_start(x_w[:], x_words[0].rearrange("p t d -> p (t d)").bitcast(I32))
        nc.sync.dma_start(wa_w[:].bitcast(I32), wa_words[:, 0].rearrange("f p n -> p f n").bitcast(I32))
        load_scale_rows(nc, wa_s, wa_scales[:, 0])
        load_scale_rows(nc, w_s, w_scales[:, 0])
        for tile, (first, end) in zip(w_w, WEIGHT_LOADS):
            if end == E:
                load_scale_rows(nc, wb_s, wb_scales[:, 0])
                nc.sync.dma_start(wb_w[:].bitcast(I32), wb_words[:, 0].rearrange("f p n -> p f n").bitcast(I32))
                nc.sync.dma_start(gate2_sb[:], gate2)
            nc.sync.dma_start(tile[:].bitcast(I32), w_words[first:end, 0].rearrange("e p n -> p e n").bitcast(I32))
        weights = [tile[:, place, :] for tile in w_w for place in range(tile.shape[1])]
        for r, pos in enumerate((pos1, pos2, pos3)):
            nc.sync.dma_start(pos_sb[r][:], pos)
        nc.sync.dma_start(first_gates[:], gate[:2].rearrange("r p t -> p r t"))
        nc.sync.dma_start(gate_sb[2], gate[2])

        def entries(tile, first, count):
            return tile[:, first // LIST_ROWS:(first + count) // LIST_ROWS]

        def gather_scales(picked, scales):
            nc.vector.tensor_copy(scales[:], x_s[:].indirect(picked))
            return scales

        def gather_words(picked, words):
            nc.vector.tensor_copy(words[:], x_w[:].bitcast(U32).indirect(picked))
            return words

        xa_s = gather_scales(offs2_sb[:], shared.tile([P, ADAPTER_SLOTS], U8, name="xa_s", offset=AT_XA_S, align_bytes=64))
        expert_scales = []

        def gather_expert_scales(turn):
            first, end = SCALE_CUTS[turn] * C, SCALE_CUTS[turn + 1] * C
            tile = shared.tile([P, end - first], U8, name=f"scales{turn}", offset=AT_PAIR_S[turn % 3], align_bytes=64)
            gather_scales(entries(offs_sb, first, end - first), tile)
            expert_scales.extend(tile[:, at:at + C] for at in range(0, end - first, C))

        gather_expert_scales(0)
        xa_w = [shared.tile([P, D], U32, name="xa_w0", offset=AT_XA_W, align_bytes=64),
                shared.tile([P, D], U32, name="xa_w1", offset=AT_PAIR_W[2] - 2 * D, align_bytes=64)]
        for f in range(F):
            gather_words(entries(offs2_sb, f * D, D), xa_w[f])

        h_w = [keep.tile([P, D], U32, name=f"h_w{f}", align_bytes=64) for f in range(F)]
        h_s = [keep.tile([P, D], U8, name=f"h_s{f}", align_bytes=64) for f in range(F)]
        h_in = [keep.tile([P, 4 * D], BF16, name=f"h_in{f}", align_bytes=64) for f in range(F)]
        for f in range(F):
            turned = bank_of(4 + f)[:].rearrange("p (a u m) -> p a u m", a=D // P, u=2)
            for a in range(D // P):
                slots = slice(f * D + a * P, f * D + (a + 1) * P)
                bank = bank_of(2 * f + a)
                nc.tensor.matmul_mx(bank[:], lhsT=xa_w[f][:, a * P:(a + 1) * P].bitcast(FP8X4), lhsT_scale=xa_s[:, slots],
                                    rhs=wa_w[:, f, :].bitcast(FP4X4), rhs_scale=wa_s[:, f, :], start=True, stop=True)
                h_rows = keep.tile([P, H], BF16, name=f"h_rows{f}_{a}")
                nc.scalar.activation(h_rows[:].rearrange("m (u p e) -> m u p e", u=2, e=2),
                                     bank[:].rearrange("m (p u e) -> m u p e", u=2, e=2), RELU)
                pairs = h_rows[:].bitcast(F32)
                for u in range(2):
                    nc.tensor.transpose(turned[:, a, u, :], pairs[:, u * P:(u + 1) * P], ident[:])
            nc.scalar.copy(h_in[f][:].bitcast(F32).rearrange("p (a m u) -> p a m u", a=D // P, u=2),
                           turned.rearrange("p a u m -> p a m u"))

        tokens = {}

        def gather_pair(pair, cuts=(0, BANK)):
            if pair > 1:
                gather_expert_scales(pair)
            words = shared.tile([P, BANK], U32, name=f"pair_w{pair}", offset=AT_PAIR_W[pair % 3], align_bytes=64)
            for first, end in zip(cuts, cuts[1:]):
                gather_words(entries(offs_sb, pair * BANK + first, end - first), words[:, first:end])
            if pair == 0:
                gather_expert_scales(1)
            tokens[pair] = words

        def expert_products(b, pair, number, cuts=(0, C, BANK)):
            bank = bank_of(number)
            for first, end in zip(cuts, cuts[1:]):
                e = 2 * pair + first // C
                slots = slice(first, end)
                nc.tensor.matmul_mx(bank[:, slots], lhsT=weights[e][:, 2 * P * b:2 * P * (b + 1)].bitcast(FP4X4),
                                    lhsT_scale=w_s[:, e, P * b:P * (b + 1)], rhs=tokens[pair][:, slots].bitcast(FP8X4),
                                    rhs_scale=expert_scales[e][:, first % C:first % C + end - first], start=True, stop=True)
            return bank

        def copy_rows(b, pair, bank):
            nc.scalar.copy(y[b][:, pair * BANK:(pair + 1) * BANK], bank[:])

        def adapter_products(b, number):
            bank = bank_of(number)
            for f in range(F):
                nc.tensor.matmul_mx(bank[:, f * D:(f + 1) * D],
                                    lhsT=wb_w[:, f, 2 * P * b:2 * P * (b + 1)].bitcast(FP4X4),
                                    lhsT_scale=wb_s[:, f, P * b:P * (b + 1)],
                                    rhs=h_w[f][:].bitcast(FP8X4), rhs_scale=h_s[f][:], start=True, stop=True)
            return bank

        z = []

        def gate_rows(b, bank):
            nc.vector.tensor_tensor(z[b], bank[:].rearrange("n (k m) -> n k m", m=P),
                                    gate2_sb[:].rearrange("n (k m) -> n k m", m=P), MULT)

        window_of = windows + windows[1:]

        def scatter(b, part, parts=1):
            source = z[b][:, part:part + parts].rearrange("n k m -> n (k m)")
            nc.scalar.activation(window_of[b][:].indirect(entries(offs2_sb, part * P, parts * P)), source, COPY)

        PAIR_BANKS = ((6, 7, 0, 1), (2, 3, 4, 5), (6, 7, 0, 1), (2, 3, 4, 5), (0, 1, 2, 3), (4, 5, 0, 1))
        z_banks = {}
        for pair in range(PAIRS - 1):
            gather_pair(pair)
            if pair == 3:
                for f in range(F):
                    nc.vector.quantize_mx(out=h_w[f][:].bitcast(FP8X4), scales=h_s[f][:], in_=h_in[f][:])
            if pair == 4:
                for b in range(2):
                    z_banks[b] = adapter_products(b, 6 + b)
            for b in range(BLOCKS if pair < 4 else 2):
                copy_rows(b, pair, expert_products(b, pair, PAIR_BANKS[pair][b]))
        held = {b: expert_products(b, PAIRS - 2, b) for b in range(2, BLOCKS)}
        gather_pair(PAIRS - 1, (0, BANK - P, BANK))
        lane = shared.tile([P, 14, P], F32, name="lane", offset=AT_LANE, align_bytes=64)
        z.extend([lane[:, 3:7], lane[:, 10:], lane[:, :4], lane[:, 6:10]])
        for b in range(2):
            gate_rows(b, z_banks[b])
        late = [expert_products(0, PAIRS - 1, PAIR_BANKS[PAIRS - 1][0], (0, C, BANK - P))]
        closing = expert_products(0, PAIRS - 1, 5, (BANK - P, BANK))
        nc.scalar.copy(y[0][:, SLOTS - BANK:SLOTS - P], late[0][:, :BANK - P])
        nc.scalar.copy(y[0][:, SLOTS - P:], closing[:, BANK - P:])
        late.append(expert_products(1, PAIRS - 1, 0))
        copy_rows(1, PAIRS - 1, late[1])
        late.extend(expert_products(b, PAIRS - 1, b - 2) for b in range(2, BLOCKS))
        for b in range(2, BLOCKS):
            z_banks[b] = adapter_products(b, 2 + b)

        def fetch_plain(into, b, r, t0):
            nc.scalar.activation(into, y[b][:].indirect(entries(pos_sb[r], t0, into.shape[1])), COPY)

        def fetch_woven(into, b, r, t0):
            nc.scalar.activation(into, y[b][:].indirect(entries(pos_sb[r], t0, into.shape[1])), COPY)

        def fetch_gated(into, b, r, t0=0):
            width = into.shape[1]
            nc.vector.tensor_tensor(into, y[b][:].indirect(entries(pos_sb[r], t0, width)), gate_sb[r][:, t0:t0 + width], MULT)

        def times_gate(engine, into, source, r, t0):
            engine.tensor_tensor(into, source, gate_sb[r][:, t0:t0 + into.shape[1]], MULT)

        sums = {}

        def add_turned(b, half, term, opens=False, closes=False, backwards=False, chunks=range(BANK // P)):
            order = list(chunks)
            if backwards:
                order = order[::-1]
            for c in order:
                nc.tensor.matmul(sums[b][half][:, c * P:(c + 1) * P], term[:, c * P:(c + 1) * P], ident[:], is_transpose=True,
                                 start=(opens and c == order[0]), stop=(closes and c == order[-1]))

        def add_both(b, term, opens=False):
            for half in range(2):
                add_turned(b, half, term[:, half * BANK:(half + 1) * BANK], opens=opens)

        lo, hi = slice(0, BANK), slice(BANK, T)
        EDGE = P // 2
        plain = [floats("plain0", BANK)]

        def plain_part(b, step):
            fetch_plain(plain[b][:, step * STEP:(step + 1) * STEP], b, 2, step * STEP)

        def total_of(b, half):
            total = floats(f"total{b}_{half}", BANK)
            nc.scalar.copy(total[:], sums[b][half][:])
            return total

        def turn_back(total, number):
            back = bank_of(number)
            for c in range(BANK // P):
                nc.tensor.transpose(back[:, c * P:(c + 1) * P], total[:, c * P:(c + 1) * P], ident[:])
            return back

        def finish(b, finished, backs, thirds):
            for half, span in enumerate((lo, hi)):
                nc.vector.tensor_tensor(finished[:, span], backs[half][:], thirds[half], ADD)
                nc.sync.dma_start(out[b * P:(b + 1) * P, span], finished[:, span])

        def close_with_window(b):
            for half, span in enumerate((lo, hi)):
                add_turned(b, half, window_of[b][:, span], closes=True)

        def copy_late(b):
            copy_rows(b, PAIRS - 2, held[b])
            copy_rows(b, PAIRS - 1, late[b])

        ring_a = floats("ring_a", T)[:]
        wide_b = floats("wide_b", BANK - EDGE + T)
        ring_b = wide_b[:, BANK - EDGE:]
        wide_c = floats("wide_c", T + STEP - EDGE)
        ring_c = wide_c[:, :T]

        sums[0] = [bank_of(6), bank_of(7)]
        fetch_gated(ring_a, 0, 0)
        add_both(0, ring_a, opens=True)
        scatter(0, 0, 3)
        scatter(0, 3)
        for step in range(2):
            plain_part(0, step)
        add_both(0, window_of[0])
        fetch_gated(ring_b, 0, 1)
        for half, span in enumerate((lo, hi)):
            add_turned(0, half, ring_b[:, span], closes=True)
        scatter(1, 0, 3)
        scatter(1, 3)
        copy_late(2)
        totals0 = [total_of(0, half) for half in range(2)]
        copy_late(LAST)

        fetch_gated(ring_c, 1, 0)
        for b in range(2, BLOCKS):
            gate_rows(b, z_banks[b])
        sums[1] = [bank_of(4), bank_of(5)]
        add_both(1, ring_c, opens=True)
        add_turned(1, 0, window_of[1][:, lo])
        add_turned(1, 1, window_of[1][:, hi], chunks=(0, 1, 2))
        gated02 = wide_b[:, lo]
        times_gate(nc.gpsimd, gated02, plain[0][:], 2, 0)
        fetch_gated(ring_a, 1, 1)
        add_turned(1, 0, ring_a[:, lo], closes=True)
        add_turned(1, 1, ring_a[:, hi])
        add_turned(1, 1, window_of[1][:, hi], closes=True, chunks=(3,))
        backs0 = [turn_back(totals0[half], (2, 0)[half]) for half in range(2)]
        totals1 = [total_of(1, half) for half in range(2)]
        plain.extend(totals0)

        sums[2] = [bank_of(6), bank_of(7)]
        term20 = shared.tile([P, T], F32, name="term20", offset=AT_TERM, align_bytes=64)
        fetch_gated(term20[:], 2, 0)
        add_both(2, term20, opens=True)
        fetch_gated(ring_c, 2, 1)
        add_both(2, ring_c)
        backs1 = [turn_back(totals1[half], (3, 1)[half]) for half in range(2)]
        for part in range(PARTS):
            scatter(2, part)
            plain_part(1 + part // 2, part % 2)

        sums[LAST] = [bank_of(4), bank_of(5)]
        window_of.append(shared.tile([P, T], F32, name="last_window", offset=AT_TERM, align_bytes=64))
        nc.gpsimd.memset(window_of[LAST][:], 0.0)
        fetch_gated(ring_a, LAST, 0)
        add_both(LAST, ring_a, opens=True)
        close_with_window(2)
        scatter(LAST, 0, 3)
        scatter(LAST, 3)
        term02 = totals1[0][:]
        fetch_gated(term02, 0, 2, BANK)
        fetch_gated(ring_c, LAST, 1)
        add_turned(LAST, 0, ring_c[:, lo])
        add_turned(LAST, 1, ring_c[:, hi], chunks=(0, 1, 2))
        add_turned(LAST, 0, window_of[LAST][:, lo], closes=True)
        add_turned(LAST, 1, window_of[LAST][:, hi])
        add_turned(LAST, 1, ring_c[:, hi], closes=True, chunks=(3,))
        plain.append(ring_c[:, lo])
        for step in range(2):
            plain_part(LAST, step)
        backs2 = [turn_back(total_of(2, half), 6 + half) for half in range(2)]
        gated12 = y[0][:, lo]
        times_gate(nc.gpsimd, gated12, plain[1][:], 2, 0)
        finish(0, ring_a, backs0, (gated02, term02))
        backs3 = [turn_back(total_of(LAST, half), (2, 0)[half]) for half in range(2)]
        last_plain = [wide_c[:, T - EDGE - STEP:T - EDGE], wide_c[:, T - EDGE:]]
        for step in range(2):
            fetch_plain(last_plain[step], LAST, 2, BANK + step * STEP)
        term12, gated22 = gated02, term02
        fetch_gated(term12, 1, 2, BANK)
        times_gate(nc.gpsimd, gated22, plain[2][:], 2, 0)
        finished1 = floats("finished1", T)
        finish(1, finished1, backs1, (gated12, term12))
        term22, gated32 = gated12, term12
        fetch_gated(term22, 2, 2, BANK)
        times_gate(nc.gpsimd, gated32, plain[LAST], 2, 0)
        finish(2, floats("finished2", T), backs2, (gated22, term22))
        finished = floats("finished", T)

        def finish_last(t0, width, third):
            span, within = slice(t0, t0 + width), slice(t0 % BANK, t0 % BANK + width)
            nc.vector.tensor_tensor(finished[:, span], backs3[t0 // BANK][:, within], third[:, within], ADD)
            nc.sync.dma_start(out[P * LAST:, span], finished[:, span])

        last_gated = gated22
        times_gate(nc.gpsimd, last_gated[:, :STEP], last_plain[0], 2, BANK)
        finish_last(0, BANK, gated32)
        times_gate(nc.vector, term22[:, STEP:], last_plain[1], 2, T - STEP)
        finish_last(BANK, STEP, last_gated)
        finish_last(T - STEP, STEP, term22)
